import numpy as np
import ml_dtypes


def mxq(x, axis, fmt="e4m3"):
    dtype, down = {"e4m3": (ml_dtypes.float8_e4m3fn, 7), "e5m2": (ml_dtypes.float8_e5m2, 14)}[fmt]
    v = np.moveaxis(np.asarray(x, np.float32).astype(ml_dtypes.bfloat16).astype(np.float64), axis, -1)
    blocks = v.reshape(v.shape[:-1] + (-1, 32))
    amax = np.abs(blocks).max(-1, keepdims=True)
    byte = np.maximum(np.where(amax > 0, np.frexp(amax)[1] - 1 + 127, 0) - down, 1)
    scale = np.exp2(byte - 127.0)
    codes = (blocks / scale).astype(np.float32).astype(dtype).astype(np.float64)
    return np.moveaxis((codes * scale).reshape(v.shape), -1, axis)


WIDE = False


def mx_kscale(k):
    if not WIDE:
        return np.ones(k)
    levels = np.array([10, -10, 5, -5, 0])
    if k % 512:
        return np.exp2(np.random.permutation(np.resize(levels, k // 32))).repeat(32)
    a = np.empty((k // 512, 16))
    for p in range(k // 512):
        a[p, :8] = np.random.permutation(np.resize(levels, 8))
        for g in range(8):
            far = levels[np.abs(levels - a[p, g]) >= 10]
            a[p, g + 8] = far[np.random.randint(len(far))]
    return np.exp2(a.ravel()).repeat(32)


BF16 = ml_dtypes.bfloat16


def bf(x):
    return np.asarray(x, np.float32).astype(BF16)


def f64(x):
    return np.asarray(x).astype(np.float64)


E2M1 = np.array([0.0, 0.5, 1.0, 1.5, 2.0, 3.0, 4.0, 6.0, -0.0, -0.5, -1.0, -1.5, -2.0, -3.0, -4.0, -6.0])


def pack_weight(w, fmt):
    k, n = w.shape
    w = f64(bf(w)).reshape(k // 32, 32, n)
    amax = np.abs(w).max(1)
    if fmt == "e4m3":
        byte = np.frexp(amax)[1] - 1 + 127 - 7
    else:
        mant, ex = np.frexp(amax / 6.0)
        byte = np.where(mant > 0.5, ex, ex - 1) + 127
    byte = np.clip(np.where(amax > 0, byte, 1), 1, 254)
    scaled = (w * np.exp2(127.0 - byte)[:, None, :]).reshape(k, n).astype(np.float32)
    by_word = np.ascontiguousarray(scaled.reshape(k // 512, 128, 4, n).transpose(0, 1, 3, 2))
    if fmt == "e4m3":
        words = by_word.astype(ml_dtypes.float8_e4m3fn).view(np.uint8)
    else:
        c = by_word.astype(ml_dtypes.float4_e2m1fn).view(np.uint8) & 0xF
        words = c[..., 0::2] | (c[..., 1::2] << 4)
    return np.ascontiguousarray(words), np.ascontiguousarray(byte.astype(np.uint8).reshape(k // 512, 16, n))


def unpack_weight(words, scales, fmt):
    g, p, n, _ = words.shape
    if fmt == "e4m3":
        vals = np.ascontiguousarray(words).view(ml_dtypes.float8_e4m3fn).astype(np.float64)
    else:
        nib = np.empty((g, p, n, 4), np.uint8)
        nib[..., 0::2] = words & 0xF
        nib[..., 1::2] = words >> 4
        vals = E2M1[nib]
    vals = vals * np.repeat(np.exp2(scales.astype(np.float64) - 127.0), 8, axis=1)[..., None]
    return vals.transpose(0, 1, 3, 2).reshape(g * 512, n)
def pack4(w):
    words, scales = pack_weight(w, "e2m1")
    return words.reshape(words.shape[0], 128, -1), scales


def unpack4(words, scales):
    return unpack_weight(words.reshape(words.shape[0], 128, -1, 2), scales, "e2m1")


T, K, O, F, N = 1536, 1024, 512, 1024, 1024
OUTLIER = 6.0


def draw0():
    s, o = mx_kscale(K), mx_kscale(O)
    t = mx_kscale(T)
    x = np.random.standard_normal((T, K)) * s
    xo = OUTLIER * np.random.standard_normal((T, O)) * o
    w = np.random.standard_normal((K, F)) / np.sqrt(K) / s[:, None]
    wo = np.random.standard_normal((O, F)) / np.sqrt(O) / OUTLIER / o[:, None]
    gate = np.random.uniform(0.25, 1.0, T) * t
    dy = 2.0 * np.random.standard_normal((T, N)) / np.sqrt(T) / t[:, None]
    w_words, w_scales = pack4(w)
    dy_words, dy_scales = pack4(dy)
    return {"x": bf(x), "xo": bf(xo), "w_words": w_words, "w_scales": w_scales,
            "wo": bf(wo), "gate": bf(gate), "dy_words": dy_words, "dy_scales": dy_scales}


def core(x, xo, w_words, w_scales, wo, gate, dy_words, dy_scales):
    base = mxq(f64(x), 1, "e4m3") @ unpack4(w_words, w_scales)
    outl = mxq(f64(xo), 1, "e4m3") @ mxq(f64(wo), 0, "e4m3")
    h = np.maximum(base + outl, 0.0) * f64(gate)[:, None]
    dw = mxq(h, 0, "e4m3").T @ unpack4(dy_words, dy_scales)
    return dw


def e4m3fn_bytes(y):
    return np.clip(np.asarray(y, np.float64), -448.0, 448.0).astype(np.float32).astype(ml_dtypes.float8_e4m3fn).view(np.uint8)


def e4m3fn_values(b):
    return np.asarray(b, np.uint8).view(ml_dtypes.float8_e4m3fn).astype(np.float64)


def setup_inputs():
    d = draw0()
    x0 = np.asarray(d['x']).astype(np.float64)
    s = (np.max(np.abs(x0), axis=(0,), keepdims=True) / 448.0).astype(np.float32)
    out = {}
    for k, v in d.items():
        if k == 'x':
            out['x_bytes'] = e4m3fn_bytes(x0 / s.astype(np.float64))
            out['x_scale'] = s
        else:
            out[k] = v
    return out


def reference(x_bytes, x_scale, xo, w_words, w_scales, wo, gate, dy_words, dy_scales):
    return core(e4m3fn_values(x_bytes) * x_scale.astype(np.float64), xo, w_words, w_scales, wo, gate, dy_words, dy_scales)

@@ -1,0 +1,334 @@
+from contextlib import ExitStack
+
+import concourse.mybir as mybir
+from concourse.masks import make_identity
+
+T, K, O, F, N = 1536, 1024, 512, 1024, 1024
+FLOPS = 2 * T * F * (K + O) + 2 * T * F * N
+
+F32 = mybir.dt.float32
+BF16 = mybir.dt.bfloat16
+U32 = mybir.dt.uint32
+U8 = mybir.dt.uint8
+I32 = mybir.dt.int32
+FP8 = mybir.dt.float8_e4m3fn
+FP8X4 = mybir.dt.float8_e4m3fn_x4
+FP4X4 = mybir.dt.float4_e2m1fn_x4
+MULT = mybir.AluOpType.mult
+MAX = mybir.AluOpType.max
+
+P = 128
+G = T // 512
+PAIRS = 2 * G
+CH = F // P
+
+
+def tile_recomputed_hidden_weight_gradient_s3_kernel(
+    tc, x_bytes, x_scale, xo, w_words, w_scales, wo, gate, dy_words, dy_scales, out
+):
+    nc = tc.nc
+    with ExitStack() as ctx:
+        keep = ctx.enter_context(tc.tile_pool(name="keep", bufs=1))
+        hpool = ctx.enter_context(tc.tile_pool(name="hpool", bufs=4))
+        psum_a = ctx.enter_context(tc.psum_pool(name="psum_a", bufs=4))
+        psum_h = ctx.enter_context(tc.psum_pool(name="psum_h", bufs=4))
+        ctx.enter_context(tc.manual_schedule())
+
+        ident = keep.tile([P, P], F32, name="ident", align_bytes=64)
+        wt = keep.tile([P, 2, 2 * F], U8, name="wt", align_bytes=64)
+        ws = keep.tile([P, 2, F], U8, name="ws", align_bytes=64)
+        dyt = keep.tile([P, G, 2 * N], U8, name="dyt", align_bytes=64)
+        dys = keep.tile([P, G, N], U8, name="dys", align_bytes=64)
+        sc = keep.tile([P, 2, 4], F32, name="sc", align_bytes=64)
+        gt = keep.tile([P, G, 4], BF16, name="gt", align_bytes=64)
+        woq = keep.tile([P, F], U32, name="woq", align_bytes=64)
+        wos = keep.tile([P, F], U8, name="wos", align_bytes=64)
+
+        xbytes, xb, xor, xg, xog, xq, xs = [], [], [], [], [], [], []
+        for pr in range(PAIRS):
+            xbytes.append(keep.tile([P, 2, K], U8, name="xbytes%d" % pr, align_bytes=64))
+            xb.append(keep.tile([P, 2 * K], BF16, name="xb%d" % pr, align_bytes=64))
+            xor.append(keep.tile([P, 2 * O], BF16, name="xor%d" % pr, align_bytes=64))
+            xg.append(keep.tile([P, 2, 1024], BF16, name="xg%d" % pr, align_bytes=64))
+            xog.append(keep.tile([P, 1024], BF16, name="xog%d" % pr, align_bytes=64))
+            xq.append(keep.tile([P, 3, 256], U32, name="xq%d" % pr, align_bytes=64))
+            xs.append(keep.tile([P, 3, 256], U8, name="xs%d" % pr, align_bytes=64))
+        wor, wog = [], []
+        for hf in range(2):
+            wor.append(keep.tile([P, 4, 512], BF16, name="wor%d" % hf, align_bytes=64))
+            wog.append(keep.tile([P, 2048], BF16, name="wog%d" % hf, align_bytes=64))
+        hq, hs = [], []
+        for g in range(G):
+            hq.append(keep.tile([P, F], U32, name="hq%d" % g, align_bytes=64))
+            hs.append(keep.tile([P, F], U8, name="hs%d" % g, align_bytes=64))
+        ot = []
+        for m in range(CH):
+            ot.append(keep.tile([P, N], F32, name="ot%d" % m, align_bytes=64))
+
+        nc.vector.memset(ws[:].rearrange("p g n -> p (g n)").bitcast(I32), 0)
+        nc.vector.memset(dys[:].rearrange("p g n -> p (g n)").bitcast(I32), 0)
+        make_identity(nc, ident[:])
+
+        x_v = x_bytes.rearrange("(g m t) k -> g m t k", m=P, t=4)
+        xo_v = xo.rearrange("(g m t) k -> g m t k", m=P, t=4)
+        wo_v = wo.rearrange("(p j) f -> p j f", j=4)
+
+        def load_x(pr):
+            g, h = divmod(pr, 2)
+            nc.sync.dma_start(out=xbytes[pr][:], in_=x_v[g][:, 2 * h : 2 * h + 2, :])
+
+        def load_xo(pr):
+            g, h = divmod(pr, 2)
+            nc.sync.dma_start(
+                out=xor[pr][:].rearrange("p (t k) -> p t k", t=2),
+                in_=xo_v[g][:, 2 * h : 2 * h + 2, :],
+            )
+
+        def load_wo(hf):
+            nc.sync.dma_start(out=wor[hf][:], in_=wo_v[:, :, 512 * hf : 512 * hf + 512])
+
+        def load_scales(dst, src):
+            for q in range(4):
+                nc.sync.dma_start(
+                    out=dst[32 * q : 32 * q + 4, :, :].bitcast(I32),
+                    in_=src.rearrange("g q n -> q g n")[4 * q : 4 * q + 4, :, :].bitcast(I32),
+                )
+
+        load_x(0)
+        load_xo(0)
+        nc.sync.dma_start(
+            out=sc[:], in_=x_scale.rearrange("o (g p t) -> p (o g) t", p=P, t=4)
+        )
+        load_wo(0)
+        load_x(1)
+        load_xo(1)
+        load_scales(ws, w_scales)
+        nc.sync.dma_start(out=wt[:], in_=w_words.rearrange("g p n -> p g n"))
+        nc.sync.dma_start(out=gt[:], in_=gate.rearrange("(g m t) -> m g t", m=P, t=4))
+        load_x(2)
+        load_xo(2)
+        load_wo(1)
+        for pr in range(3, PAIRS):
+            load_x(pr)
+            load_xo(pr)
+        load_scales(dys, dy_scales)
+        nc.sync.dma_start(out=dyt[:], in_=dy_words.rearrange("g p n -> p g n"))
+
+        def cast_s(pr, t):
+            nc.scalar.copy(
+                out=xb[pr][:, K * t : K * t + K], in_=xbytes[pr][:, t, :].bitcast(FP8)
+            )
+
+        def cast_v(pr, t):
+            nc.vector.tensor_copy(
+                out=xb[pr][:, K * t : K * t + K], in_=xbytes[pr][:, t, :].bitcast(FP8)
+            )
+
+        xps = {}
+
+        def turn(pr):
+            po = psum_a.tile([P, 512], F32, name="a")
+            words = xor[pr][:].bitcast(F32)
+            for t in range(2):
+                for u in range(2):
+                    c0 = 256 * t + u
+                    nc.tensor.transpose(
+                        po[:, 256 * u + P * t : 256 * u + P * t + P],
+                        words[:, c0 : 256 * t + 256 : 2],
+                        ident[:],
+                    )
+            px = [psum_a.tile([P, 512], F32, name="a"), psum_a.tile([P, 512], F32, name="a")]
+            words = xb[pr][:].bitcast(F32)
+            for g in range(2):
+                for t in range(2):
+                    for u in range(2):
+                        c0 = 512 * t + 256 * g
+                        nc.tensor.transpose(
+                            px[g][:, 256 * u + P * t : 256 * u + P * t + P],
+                            words[:, c0 + u : c0 + 256 : 2],
+                            ident[:],
+                        )
+            xps[pr] = (px[0], px[1], po)
+
+        def xo_out(pr):
+            nc.scalar.copy(
+                out=xog[pr][:].bitcast(F32).rearrange("p (r u) -> p r u", u=2),
+                in_=xps[pr][2][:].rearrange("p (u r) -> p r u", u=2),
+            )
+
+        def prod(pr, g):
+            nc.vector.tensor_tensor(
+                out=xg[pr][:, g, :].rearrange("p (r u e) -> p r u e", u=2, e=2),
+                in0=xps[pr][g][:].bitcast(BF16).rearrange("p (u r e) -> p r u e", u=2, e=2),
+                in1=sc[:, g, :]
+                .rearrange("p (u e) -> p u e", e=2)
+                .unsqueeze(1)
+                .to_broadcast([P, 256, 2, 2]),
+                op=MULT,
+            )
+
+        def quant_x(pr, g):
+            nc.vector.quantize_mx(
+                out=xq[pr][:, g, :].bitcast(FP8X4), scales=xs[pr][:, g, :], in_=xg[pr][:, g, :]
+            )
+
+        def quant_xo(pr):
+            nc.vector.quantize_mx(
+                out=xq[pr][:, 2, :].bitcast(FP8X4), scales=xs[pr][:, 2, :], in_=xog[pr][:]
+            )
+
+        def wo_lay(engine_copy, hf):
+            engine_copy(
+                out=wog[hf][:].rearrange("p (c i t) -> p c t i", i=4, t=4),
+                in_=wor[hf][:].rearrange("p t (c i) -> p c t i", i=4),
+            )
+
+        def quant_wo(hf):
+            cols = slice(512 * hf, 512 * hf + 512)
+            nc.vector.quantize_mx(
+                out=woq[:, cols].bitcast(FP8X4), scales=wos[:, cols], in_=wog[hf][:]
+            )
+
+        hps = {}
+
+        def stage1(g, c, ts):
+            if 0 in ts:
+                hps[g, c] = psum_h.tile([P, 512], F32, name="h")
+            acc = hps[g, c]
+            f0 = P * c
+            for t in ts:
+                pr, tl = 2 * g + t // 2, t % 2
+                r = slice(P * tl, P * tl + P)
+                for kk in range(3):
+                    if kk < 2:
+                        rhs = wt[:, kk, 2 * f0 : 2 * f0 + 2 * P].bitcast(FP4X4)
+                        rsc = ws[:, kk, f0 : f0 + P]
+                    else:
+                        rhs = woq[:, f0 : f0 + P].bitcast(FP8X4)
+                        rsc = wos[:, f0 : f0 + P]
+                    nc.tensor.matmul_mx(
+                        out=acc[:, P * t : P * t + P],
+                        lhsT=xq[pr][:, kk, r].bitcast(FP8X4),
+                        lhsT_scale=xs[pr][:, kk, r],
+                        rhs=rhs,
+                        rhs_scale=rsc,
+                        start=(kk == 0),
+                        stop=(kk == 2),
+                    )
+
+        hgt = {}
+
+        def hid(g, c):
+            hgt[g, c] = hpool.tile([P, 512], BF16, name="hg", align_bytes=64)
+            nc.vector.scalar_tensor_tensor(
+                out=hgt[g, c][:].rearrange("p (f t) -> p f t", t=4),
+                in0=hps[g, c][:].rearrange("p (t f) -> p f t", t=4),
+                scalar=0.0,
+                in1=gt[:, g, :].unsqueeze(1).to_broadcast([P, P, 4]),
+                op0=MAX,
+                op1=MULT,
+            )
+
+        def quant_h(g, c):
+            cols = slice(P * c, P * c + P)
+            nc.vector.quantize_mx(
+                out=hq[g][:, cols].bitcast(FP8X4), scales=hs[g][:, cols], in_=hgt[g, c][:]
+            )
+
+        dwp = {}
+
+        def stage2(m):
+            cols = slice(P * m, P * m + P)
+            for nh in range(2):
+                acc = psum_a.tile([P, 512], F32, name="a")
+                for g in range(G):
+                    nc.tensor.matmul_mx(
+                        out=acc[:],
+                        lhsT=hq[g][:, cols].bitcast(FP8X4),
+                        lhsT_scale=hs[g][:, cols],
+                        rhs=dyt[:, g, 1024 * nh : 1024 * nh + 1024].bitcast(FP4X4),
+                        rhs_scale=dys[:, g, 512 * nh : 512 * nh + 512],
+                        start=(g == 0),
+                        stop=(g == G - 1),
+                    )
+                dwp[m, nh] = acc
+
+        def store(m):
+            nc.scalar.copy(out=ot[m][:, 0:512], in_=dwp[m, 0][:])
+            nc.vector.tensor_copy(out=ot[m][:, 512:1024], in_=dwp[m, 1][:])
+            for nh in range(2):
+                nc.sync.dma_start(
+                    out=out[P * m : P * m + P, 512 * nh : 512 * nh + 512],
+                    in_=ot[m][:, 512 * nh : 512 * nh + 512],
+                )
+
+        cast_v(0, 0)
+        cast_s(0, 1)
+        turn(0)
+        wo_lay(nc.vector.tensor_copy, 0)
+        cast_v(1, 0)
+        cast_s(1, 1)
+        xo_out(0)
+        prod(0, 0)
+        quant_wo(0)
+        prod(0, 1)
+        quant_x(0, 0)
+        quant_xo(0)
+        quant_x(0, 1)
+        turn(1)
+        for c in range(4):
+            stage1(0, c, (0, 1))
+        xo_out(1)
+        cast_s(2, 0)
+        cast_s(2, 1)
+        prod(1, 0)
+        prod(1, 1)
+        quant_x(1, 0)
+        quant_xo(1)
+        quant_x(1, 1)
+        wo_lay(nc.scalar.copy, 1)
+        turn(2)
+        xo_out(2)
+
+        def block(g, c0, pr, ts):
+            if pr + 1 < PAIRS:
+                cast_s(pr + 1, 0)
+                cast_s(pr + 1, 1)
+            prod(pr, 0)
+            stage1(g, c0, ts)
+            hid(g, c0)
+            prod(pr, 1)
+            quant_x(pr, 0)
+            quant_h(g, c0)
+            stage1(g, c0 + 1, ts)
+            hid(g, c0 + 1)
+            quant_xo(pr)
+            quant_x(pr, 1)
+            quant_h(g, c0 + 1)
+            stage1(g, c0 + 2, ts)
+            stage1(g, c0 + 3, ts)
+            hid(g, c0 + 2)
+            if g == 0 and c0 == 0:
+                quant_wo(1)
+            hid(g, c0 + 3)
+            quant_h(g, c0 + 2)
+            quant_h(g, c0 + 3)
+            if pr + 1 < PAIRS:
+                turn(pr + 1)
+                xo_out(pr + 1)
+
+        allt = (0, 1, 2, 3)
+        block(0, 0, 2, (2, 3))
+        block(0, 4, 3, allt)
+        block(1, 0, 4, allt)
+        block(1, 4, 5, allt)
+        for c in range(CH + 2):
+            if c < CH:
+                stage1(2, c, allt)
+                hid(2, c)
+            if c >= 2:
+                stage2(c - 2)
+            if c < CH:
+                quant_h(2, c)
+            if c >= 2:
+                store(c - 2)

@@ -21,6 +21,8 @@ P = 128
 G = T // 512
 PAIRS = 2 * G
 CH = F // P
+TURN_BANKS = 3
+H_BANKS = 5
 
 
 def tile_recomputed_hidden_weight_gradient_s3_kernel(
@@ -29,41 +31,35 @@ def tile_recomputed_hidden_weight_gradient_s3_kernel(
     nc = tc.nc
     with ExitStack() as ctx:
         keep = ctx.enter_context(tc.tile_pool(name="keep", bufs=1))
-        hpool = ctx.enter_context(tc.tile_pool(name="hpool", bufs=4))
-        psum_a = ctx.enter_context(tc.psum_pool(name="psum_a", bufs=4))
-        psum_h = ctx.enter_context(tc.psum_pool(name="psum_h", bufs=4))
+        ring = ctx.enter_context(tc.tile_pool(name="ring", bufs=3))
+        psum = ctx.enter_context(tc.psum_pool(name="psum", bufs=1))
         ctx.enter_context(tc.manual_schedule())
 
-        ident = keep.tile([P, P], F32, name="ident", align_bytes=64)
-        wt = keep.tile([P, 2, 2 * F], U8, name="wt", align_bytes=64)
-        ws = keep.tile([P, 2, F], U8, name="ws", align_bytes=64)
-        dyt = keep.tile([P, G, 2 * N], U8, name="dyt", align_bytes=64)
-        dys = keep.tile([P, G, N], U8, name="dys", align_bytes=64)
-        sc = keep.tile([P, 2, 4], F32, name="sc", align_bytes=64)
-        gt = keep.tile([P, G, 4], BF16, name="gt", align_bytes=64)
-        woq = keep.tile([P, F], U32, name="woq", align_bytes=64)
-        wos = keep.tile([P, F], U8, name="wos", align_bytes=64)
+        def kept(name, shape, dtype):
+            return keep.tile(shape, dtype, name=name, align_bytes=64)
 
-        xbytes, xb, xor, xg, xog, xq, xs = [], [], [], [], [], [], []
-        for pr in range(PAIRS):
-            xbytes.append(keep.tile([P, 2, K], U8, name="xbytes%d" % pr, align_bytes=64))
-            xb.append(keep.tile([P, 2 * K], BF16, name="xb%d" % pr, align_bytes=64))
-            xor.append(keep.tile([P, 2 * O], BF16, name="xor%d" % pr, align_bytes=64))
-            xg.append(keep.tile([P, 2, 1024], BF16, name="xg%d" % pr, align_bytes=64))
-            xog.append(keep.tile([P, 1024], BF16, name="xog%d" % pr, align_bytes=64))
-            xq.append(keep.tile([P, 3, 256], U32, name="xq%d" % pr, align_bytes=64))
-            xs.append(keep.tile([P, 3, 256], U8, name="xs%d" % pr, align_bytes=64))
-        wor, wog = [], []
-        for hf in range(2):
-            wor.append(keep.tile([P, 4, 512], BF16, name="wor%d" % hf, align_bytes=64))
-            wog.append(keep.tile([P, 2048], BF16, name="wog%d" % hf, align_bytes=64))
-        hq, hs = [], []
-        for g in range(G):
-            hq.append(keep.tile([P, F], U32, name="hq%d" % g, align_bytes=64))
-            hs.append(keep.tile([P, F], U8, name="hs%d" % g, align_bytes=64))
-        ot = []
-        for m in range(CH):
-            ot.append(keep.tile([P, N], F32, name="ot%d" % m, align_bytes=64))
+        def bank(b):
+            return psum.tile([P, 512], F32, name="bank%d" % b)
+
+        ident = kept("ident", [P, P], F32)
+        wt = [kept("wt%d" % hf, [P, 2, F], U8) for hf in range(2)]
+        ws = kept("ws", [P, 2, F], U8)
+        dyt = kept("dyt", [P, G, 2 * N], U8)
+        dys = kept("dys", [P, G, N], U8)
+        sc = kept("sc", [P, 2, 4], F32)
+        scb = kept("scb", [P, K], F32)
+        gt = kept("gt", [P, G, 4], BF16)
+        woq = kept("woq", [P, F], U32)
+        wos = kept("wos", [P, F], U8)
+        xbytes = [kept("xbytes%d" % pr, [P, 2, K], U8) for pr in range(PAIRS)]
+        xor = [kept("xor%d" % pr, [P, 2 * O], BF16) for pr in range(PAIRS)]
+        xq = [kept("xq%d" % pr, [P, 3 * 256], U32) for pr in range(PAIRS)]
+        xs = [kept("xs%d" % pr, [P, 3 * 256], U8) for pr in range(PAIRS)]
+        wor = [kept("wor%d" % q, [P, 4, 256], BF16) for q in range(4)]
+        wog = kept("wog", [P, 4 * F], BF16)
+        hg01 = [kept("hg01_%d" % c, [P, 1024], BF16) for c in range(CH)]
+        hq = [kept("hq%d" % c, [P, G * P], U32) for c in range(CH)]
+        hs = [kept("hs%d" % c, [P, G * P], U8) for c in range(CH)]
 
         nc.vector.memset(ws[:].rearrange("p g n -> p (g n)").bitcast(I32), 0)
         nc.vector.memset(dys[:].rearrange("p g n -> p (g n)").bitcast(I32), 0)
@@ -84,8 +80,13 @@ def tile_recomputed_hidden_weight_gradient_s3_kernel(
                 in_=xo_v[g][:, 2 * h : 2 * h + 2, :],
             )
 
-        def load_wo(hf):
-            nc.sync.dma_start(out=wor[hf][:], in_=wo_v[:, :, 512 * hf : 512 * hf + 512])
+        def load_wo(q):
+            nc.sync.dma_start(out=wor[q][:], in_=wo_v[:, :, 256 * q : 256 * q + 256])
+
+        def load_w(hf):
+            nc.sync.dma_start(
+                out=wt[hf][:], in_=w_words.rearrange("g p n -> p g n")[:, :, F * hf : F * hf + F]
+            )
 
         def load_scales(dst, src):
             for q in range(4):
@@ -94,241 +95,380 @@ def tile_recomputed_hidden_weight_gradient_s3_kernel(
                     in_=src.rearrange("g q n -> q g n")[4 * q : 4 * q + 4, :, :].bitcast(I32),
                 )
 
-        load_x(0)
-        load_xo(0)
-        nc.sync.dma_start(
-            out=sc[:], in_=x_scale.rearrange("o (g p t) -> p (o g) t", p=P, t=4)
-        )
-        load_wo(0)
-        load_x(1)
-        load_xo(1)
-        load_scales(ws, w_scales)
-        nc.sync.dma_start(out=wt[:], in_=w_words.rearrange("g p n -> p g n"))
-        nc.sync.dma_start(out=gt[:], in_=gate.rearrange("(g m t) -> m g t", m=P, t=4))
-        load_x(2)
-        load_xo(2)
-        load_wo(1)
-        for pr in range(3, PAIRS):
-            load_x(pr)
-            load_xo(pr)
-        load_scales(dys, dy_scales)
-        nc.sync.dma_start(out=dyt[:], in_=dy_words.rearrange("g p n -> p g n"))
+        def load_sc():
+            nc.sync.dma_start(
+                out=sc[:], in_=x_scale.rearrange("o (g p t) -> p (o g) t", p=P, t=4)
+            )
 
-        def cast_s(pr, t):
+        def load_gate():
+            nc.sync.dma_start(out=gt[:], in_=gate.rearrange("(g m t) -> m g t", m=P, t=4))
+
+        def load_dy():
+            load_scales(dys, dy_scales)
+            nc.sync.dma_start(out=dyt[:], in_=dy_words.rearrange("g p n -> p g n"))
+
+        xb, xp, xop, xg, turned = {}, {}, {}, {}, {}
+
+        def rows(pr):
+            if pr not in xb:
+                xb[pr] = ring.tile([P, 2 * K], BF16, name="xb", align_bytes=64)
+            return xb[pr]
+
+        def grouped(pr):
+            if pr not in xg:
+                xg[pr] = ring.tile([P, 3 * 1024], BF16, name="xg", align_bytes=64)
+            return xg[pr]
+
+        def widen(copy, pr, t, k0, k1):
+            copy(out=rows(pr)[:, K * t + k0 : K * t + k1], in_=xbytes[pr][:, t, k0:k1].bitcast(FP8))
+
+        def spread(g, b):
+            ps = bank(b)
+            for t in range(4):
+                nc.tensor.transpose(
+                    ps[:, P * t : P * t + P], sc[:, g, t : t + 1].to_broadcast([P, P]), ident[:]
+                )
+            return ps
+
+        def spread_out(g, ps):
             nc.scalar.copy(
-                out=xb[pr][:, K * t : K * t + K], in_=xbytes[pr][:, t, :].bitcast(FP8)
+                out=scb[:, 512 * g : 512 * g + 512].rearrange("p (n t) -> p n t", t=4),
+                in_=ps[:].rearrange("p (t n) -> p n t", t=4),
             )
 
-        def cast_v(pr, t):
-            nc.vector.tensor_copy(
-                out=xb[pr][:, K * t : K * t + K], in_=xbytes[pr][:, t, :].bitcast(FP8)
-            )
-
-        xps = {}
-
-        def turn(pr):
-            po = psum_a.tile([P, 512], F32, name="a")
-            words = xor[pr][:].bitcast(F32)
-            for t in range(2):
-                for u in range(2):
-                    c0 = 256 * t + u
-                    nc.tensor.transpose(
-                        po[:, 256 * u + P * t : 256 * u + P * t + P],
-                        words[:, c0 : 256 * t + 256 : 2],
-                        ident[:],
-                    )
-            px = [psum_a.tile([P, 512], F32, name="a"), psum_a.tile([P, 512], F32, name="a")]
-            words = xb[pr][:].bitcast(F32)
-            for g in range(2):
-                for t in range(2):
-                    for u in range(2):
-                        c0 = 512 * t + 256 * g
-                        nc.tensor.transpose(
-                            px[g][:, 256 * u + P * t : 256 * u + P * t + P],
-                            words[:, c0 + u : c0 + 256 : 2],
-                            ident[:],
-                        )
-            xps[pr] = (px[0], px[1], po)
-
-        def xo_out(pr):
-            nc.scalar.copy(
-                out=xog[pr][:].bitcast(F32).rearrange("p (r u) -> p r u", u=2),
-                in_=xps[pr][2][:].rearrange("p (u r) -> p r u", u=2),
-            )
-
-        def prod(pr, g):
+        def mul(pr, t):
             nc.vector.tensor_tensor(
-                out=xg[pr][:, g, :].rearrange("p (r u e) -> p r u e", u=2, e=2),
-                in0=xps[pr][g][:].bitcast(BF16).rearrange("p (u r e) -> p r u e", u=2, e=2),
-                in1=sc[:, g, :]
+                out=rows(pr)[:, K * t : K * t + K],
+                in0=xbytes[pr][:, t, :].bitcast(FP8),
+                in1=scb[:],
+                op=MULT,
+            )
+
+        def sort_x(pr, t):
+            if pr not in xp:
+                xp[pr] = ring.tile([P, K], F32, name="xp", align_bytes=64)
+            nc.scalar.copy(
+                out=xp[pr][:, 512 * t : 512 * t + 512].rearrange("p (g u m) -> p g u m", g=2, u=2),
+                in_=xb[pr][:].bitcast(F32)[:, 512 * t : 512 * t + 512].rearrange(
+                    "p (g m u) -> p g u m", g=2, u=2
+                ),
+            )
+
+        def sort_xo(pr):
+            xop[pr] = ring.tile([P, O], F32, name="xop", align_bytes=64)
+            nc.scalar.copy(
+                out=xop[pr][:].rearrange("p (t u m) -> p t u m", t=2, u=2),
+                in_=xor[pr][:].bitcast(F32).rearrange("p (t m u) -> p t u m", t=2, u=2),
+            )
+
+        def turn(pr, kk):
+            ps = bank(kk)
+            is_sorted = pr in (xp if kk < 2 else xop)
+            for t in range(2):
+                if kk < 2:
+                    c0 = 512 * t + 256 * kk
+                    words = xp[pr][:] if is_sorted else xb[pr][:].bitcast(F32)
+                else:
+                    c0 = 256 * t
+                    words = xop[pr][:] if is_sorted else xor[pr][:].bitcast(F32)
+                for u in range(2):
+                    if is_sorted:
+                        src = words[:, c0 + P * u : c0 + P * u + P]
+                    else:
+                        src = words[:, c0 + u : c0 + 256 : 2]
+                    nc.tensor.transpose(ps[:, 256 * u + P * t : 256 * u + P * t + P], src, ident[:])
+            turned[pr, kk] = ps
+
+        def turn_out(pr, kk):
+            nc.scalar.copy(
+                out=grouped(pr)[:, 1024 * kk : 1024 * kk + 1024]
+                .bitcast(F32)
+                .rearrange("p (r u) -> p r u", u=2),
+                in_=turned[pr, kk][:].rearrange("p (u r) -> p r u", u=2),
+            )
+
+        def prod(pr, kk):
+            nc.vector.tensor_tensor(
+                out=grouped(pr)[:, 1024 * kk : 1024 * kk + 1024].rearrange(
+                    "p (r u e) -> p r u e", u=2, e=2
+                ),
+                in0=turned[pr, kk][:].bitcast(BF16).rearrange("p (u r e) -> p r u e", u=2, e=2),
+                in1=sc[:, kk, :]
                 .rearrange("p (u e) -> p u e", e=2)
                 .unsqueeze(1)
                 .to_broadcast([P, 256, 2, 2]),
                 op=MULT,
             )
 
-        def quant_x(pr, g):
+        def quant_x(pr, k0, k1):
             nc.vector.quantize_mx(
-                out=xq[pr][:, g, :].bitcast(FP8X4), scales=xs[pr][:, g, :], in_=xg[pr][:, g, :]
+                out=xq[pr][:, 256 * k0 : 256 * k1].bitcast(FP8X4),
+                scales=xs[pr][:, 256 * k0 : 256 * k1],
+                in_=xg[pr][:, 1024 * k0 : 1024 * k1],
             )
 
-        def quant_xo(pr):
-            nc.vector.quantize_mx(
-                out=xq[pr][:, 2, :].bitcast(FP8X4), scales=xs[pr][:, 2, :], in_=xog[pr][:]
+        def wo_lay(copy, q):
+            copy(
+                out=wog[:, 1024 * q : 1024 * q + 1024].rearrange("p (c i t) -> p c t i", i=4, t=4),
+                in_=wor[q][:].rearrange("p t (c i) -> p c t i", i=4),
             )
 
-        def wo_lay(engine_copy, hf):
-            engine_copy(
-                out=wog[hf][:].rearrange("p (c i t) -> p c t i", i=4, t=4),
-                in_=wor[hf][:].rearrange("p t (c i) -> p c t i", i=4),
-            )
-
-        def quant_wo(hf):
-            cols = slice(512 * hf, 512 * hf + 512)
+        def quant_wo(q0, q1):
+            cols = slice(256 * q0, 256 * q1)
             nc.vector.quantize_mx(
-                out=woq[:, cols].bitcast(FP8X4), scales=wos[:, cols], in_=wog[hf][:]
+                out=woq[:, cols].bitcast(FP8X4), scales=wos[:, cols], in_=wog[:, 1024 * q0 : 1024 * q1]
             )
 
         hps = {}
 
-        def stage1(g, c, ts):
+        def stage1(g, c, ts=(0, 1, 2, 3)):
             if 0 in ts:
-                hps[g, c] = psum_h.tile([P, 512], F32, name="h")
+                hps[g, c] = bank(TURN_BANKS + len(hps) % H_BANKS)
             acc = hps[g, c]
             f0 = P * c
+            hf, w0 = divmod(2 * f0, F)
             for t in ts:
                 pr, tl = 2 * g + t // 2, t % 2
-                r = slice(P * tl, P * tl + P)
                 for kk in range(3):
+                    r = slice(256 * kk + P * tl, 256 * kk + P * tl + P)
                     if kk < 2:
-                        rhs = wt[:, kk, 2 * f0 : 2 * f0 + 2 * P].bitcast(FP4X4)
+                        rhs = wt[hf][:, kk, w0 : w0 + 2 * P].bitcast(FP4X4)
                         rsc = ws[:, kk, f0 : f0 + P]
                     else:
                         rhs = woq[:, f0 : f0 + P].bitcast(FP8X4)
                         rsc = wos[:, f0 : f0 + P]
                     nc.tensor.matmul_mx(
                         out=acc[:, P * t : P * t + P],
-                        lhsT=xq[pr][:, kk, r].bitcast(FP8X4),
-                        lhsT_scale=xs[pr][:, kk, r],
+                        lhsT=xq[pr][:, r].bitcast(FP8X4),
+                        lhsT_scale=xs[pr][:, r],
                         rhs=rhs,
                         rhs_scale=rsc,
                         start=(kk == 0),
                         stop=(kk == 2),
                     )
 
-        hgt = {}
+        hg2, parked = {}, {}
+
+        def park(g, c):
+            parked[g, c] = kept("parked%d_%d" % (g, c), [P, 512], F32)
+            nc.scalar.copy(
+                out=parked[g, c][:].rearrange("p (f t) -> p f t", t=4),
+                in_=hps[g, c][:].rearrange("p (t f) -> p f t", t=4),
+            )
 
         def hid(g, c):
-            hgt[g, c] = hpool.tile([P, 512], BF16, name="hg", align_bytes=64)
+            if (g, c) in parked:
+                sums = parked[g, c][:].rearrange("p (f t) -> p f t", t=4)
+            else:
+                sums = hps[g, c][:].rearrange("p (t f) -> p f t", t=4)
+            if g < 2:
+                dst = hg01[c][:, 512 * g : 512 * g + 512]
+            else:
+                hg2[c] = ring.tile([P, 512], BF16, name="hg2", align_bytes=64)
+                dst = hg2[c][:]
             nc.vector.scalar_tensor_tensor(
-                out=hgt[g, c][:].rearrange("p (f t) -> p f t", t=4),
-                in0=hps[g, c][:].rearrange("p (t f) -> p f t", t=4),
+                out=dst.rearrange("p (f t) -> p f t", t=4),
+                in0=sums,
                 scalar=0.0,
                 in1=gt[:, g, :].unsqueeze(1).to_broadcast([P, P, 4]),
                 op0=MAX,
                 op1=MULT,
             )
 
-        def quant_h(g, c):
-            cols = slice(P * c, P * c + P)
+        def quant_h01(c):
             nc.vector.quantize_mx(
-                out=hq[g][:, cols].bitcast(FP8X4), scales=hs[g][:, cols], in_=hgt[g, c][:]
+                out=hq[c][:, 0 : 2 * P].bitcast(FP8X4), scales=hs[c][:, 0 : 2 * P], in_=hg01[c][:]
             )
 
-        dwp = {}
+        def quant_h2(c):
+            nc.vector.quantize_mx(
+                out=hq[c][:, 2 * P :].bitcast(FP8X4), scales=hs[c][:, 2 * P :], in_=hg2[c][:]
+            )
 
-        def stage2(m):
-            cols = slice(P * m, P * m + P)
-            for nh in range(2):
-                acc = psum_a.tile([P, 512], F32, name="a")
+        def stage2(m, b, n0, width):
+            acc = bank(b)
+            step = 512 if width == 512 else P
+            for j in range(0, width, step):
                 for g in range(G):
+                    n1 = n0 + j
                     nc.tensor.matmul_mx(
-                        out=acc[:],
-                        lhsT=hq[g][:, cols].bitcast(FP8X4),
-                        lhsT_scale=hs[g][:, cols],
-                        rhs=dyt[:, g, 1024 * nh : 1024 * nh + 1024].bitcast(FP4X4),
-                        rhs_scale=dys[:, g, 512 * nh : 512 * nh + 512],
+                        out=acc[:, j : j + step],
+                        lhsT=hq[m][:, P * g : P * g + P].bitcast(FP8X4),
+                        lhsT_scale=hs[m][:, P * g : P * g + P],
+                        rhs=dyt[:, g, 2 * n1 : 2 * n1 + 2 * step].bitcast(FP4X4),
+                        rhs_scale=dys[:, g, n1 : n1 + step],
                         start=(g == 0),
                         stop=(g == G - 1),
                     )
-                dwp[m, nh] = acc
+            return acc
 
-        def store(m):
-            nc.scalar.copy(out=ot[m][:, 0:512], in_=dwp[m, 0][:])
-            nc.vector.tensor_copy(out=ot[m][:, 512:1024], in_=dwp[m, 1][:])
-            for nh in range(2):
-                nc.sync.dma_start(
-                    out=out[P * m : P * m + P, 512 * nh : 512 * nh + 512],
-                    in_=ot[m][:, 512 * nh : 512 * nh + 512],
-                )
+        def store(copy, m, acc, n0, width):
+            ot = ring.tile([P, 512], F32, name="ot", align_bytes=64, bufs=6)
+            copy(out=ot[:, 0:width], in_=acc[:, 0:width])
+            nc.sync.dma_start(out=out[P * m : P * m + P, n0 : n0 + width], in_=ot[:, 0:width])
 
-        cast_v(0, 0)
-        cast_s(0, 1)
-        turn(0)
+        load_x(0)
+        load_sc()
+        load_wo(0)
+        load_x(1)
+        load_xo(0)
+        load_scales(ws, w_scales)
+        load_wo(1)
+        load_w(0)
+        load_xo(1)
+        load_wo(2)
+        load_x(2)
+        load_wo(3)
+        load_gate()
+        load_w(1)
+        load_xo(2)
+        for pr in range(3, PAIRS):
+            load_x(pr)
+            load_xo(pr)
+        load_dy()
+
+        spread_ps = [spread(0, TURN_BANKS)]
+        widen(nc.vector.tensor_copy, 0, 0, 0, K)
+        widen(nc.scalar.copy, 0, 1, 0, 512)
+        widen(nc.vector.tensor_copy, 0, 1, 512, K)
+        turn(0, 0)
+        turn(0, 1)
+        spread_ps.append(spread(1, TURN_BANKS + 1))
+        spread_out(0, spread_ps[0])
         wo_lay(nc.vector.tensor_copy, 0)
-        cast_v(1, 0)
-        cast_s(1, 1)
-        xo_out(0)
         prod(0, 0)
-        quant_wo(0)
+        for t in range(2):
+            widen(nc.scalar.copy, 1, t, 0, 512)
+        spread_out(1, spread_ps[1])
+        turn(0, 2)
+        turn_out(0, 2)
+        quant_wo(0, 1)
         prod(0, 1)
-        quant_x(0, 0)
-        quant_xo(0)
-        quant_x(0, 1)
-        turn(1)
-        for c in range(4):
-            stage1(0, c, (0, 1))
-        xo_out(1)
-        cast_s(2, 0)
-        cast_s(2, 1)
-        prod(1, 0)
-        prod(1, 1)
-        quant_x(1, 0)
-        quant_xo(1)
-        quant_x(1, 1)
+        turn(1, 0)
+        for t in range(2):
+            widen(nc.scalar.copy, 1, t, 512, K)
+        quant_x(0, 0, 1)
+        quant_x(0, 2, 3)
+        quant_x(0, 1, 2)
+        turn(1, 1)
+        turn(1, 2)
         wo_lay(nc.scalar.copy, 1)
-        turn(2)
-        xo_out(2)
+        turn_out(1, 2)
+        prod(1, 0)
+        stage1(0, 0, (0, 1))
+        stage1(0, 1, (0, 1))
+        quant_wo(1, 2)
+        prod(1, 1)
+        stage1(0, 2, (0, 1))
+        stage1(0, 3, (0, 1))
+        wo_lay(nc.scalar.copy, 2)
+        wo_lay(nc.scalar.copy, 3)
+        quant_x(1, 0, 1)
+        quant_x(1, 2, 3)
+        quant_x(1, 1, 2)
+        for c in range(4):
+            stage1(0, c, (2, 3))
 
-        def block(g, c0, pr, ts):
-            if pr + 1 < PAIRS:
-                cast_s(pr + 1, 0)
-                cast_s(pr + 1, 1)
-            prod(pr, 0)
-            stage1(g, c0, ts)
-            hid(g, c0)
-            prod(pr, 1)
-            quant_x(pr, 0)
-            quant_h(g, c0)
-            stage1(g, c0 + 1, ts)
-            hid(g, c0 + 1)
-            quant_xo(pr)
-            quant_x(pr, 1)
-            quant_h(g, c0 + 1)
-            stage1(g, c0 + 2, ts)
-            stage1(g, c0 + 3, ts)
-            hid(g, c0 + 2)
-            if g == 0 and c0 == 0:
-                quant_wo(1)
-            hid(g, c0 + 3)
-            quant_h(g, c0 + 2)
-            quant_h(g, c0 + 3)
-            if pr + 1 < PAIRS:
-                turn(pr + 1)
-                xo_out(pr + 1)
+        def prepare(pr, t):
+            mul(pr, t)
+            sort_x(pr, t)
 
-        allt = (0, 1, 2, 3)
-        block(0, 0, 2, (2, 3))
-        block(0, 4, 3, allt)
-        block(1, 0, 4, allt)
-        block(1, 4, 5, allt)
-        for c in range(CH + 2):
-            if c < CH:
-                stage1(2, c, allt)
+        def turn_all(pr):
+            for kk in (2, 0, 1):
+                turn(pr, kk)
+
+        def out_all(pr):
+            for kk in (2, 0, 1):
+                turn_out(pr, kk)
+
+        def quant_all(pr):
+            quant_x(pr, 2, 3)
+            quant_x(pr, 0, 2)
+
+        sort_xo(2)
+        prepare(2, 0)
+        quant_wo(2, 4)
+        park(0, 0)
+        sort_xo(3)
+        prepare(2, 1)
+        park(0, 1)
+        stage1(0, 4)
+        stage1(0, 5)
+        prepare(3, 0)
+        turn_all(2)
+        turn_out(2, 2)
+        stage1(0, 6)
+        prepare(3, 1)
+        turn_out(2, 0)
+        turn_out(2, 1)
+        hid(0, 2)
+        hid(0, 3)
+        turn_all(3)
+        out_all(3)
+        stage1(0, 7)
+        mul(4, 0)
+        quant_all(2)
+        stage1(1, 4, (0, 1))
+        hid(0, 4)
+        stage1(1, 5, (0, 1))
+        quant_all(3)
+        stage1(1, 4, (2, 3))
+        stage1(1, 5, (2, 3))
+        sort_x(4, 0)
+        park(0, 5)
+        sort_xo(4)
+        prepare(4, 1)
+        stage1(1, 6)
+        sort_xo(5)
+        prepare(5, 0)
+        hid(0, 6)
+        turn_all(4)
+        turn_out(4, 2)
+        stage1(1, 7)
+        prepare(5, 1)
+        turn_out(4, 0)
+        turn_out(4, 1)
+        hid(0, 7)
+        stage1(1, 0)
+        hid(1, 4)
+        turn_all(5)
+        out_all(5)
+        stage1(1, 1)
+        hid(1, 5)
+        quant_all(4)
+        stage1(1, 2)
+        hid(1, 6)
+        quant_all(5)
+        stage1(1, 3)
+        hid(1, 7)
+        hid(0, 5)
+        for c in range(4):
+            park(1, c)
+
+        LAG = 2
+        order = [4, 5, 6, 7, 0, 1, 2, 3]
+        for i in range(CH + LAG):
+            if i < CH:
+                stage1(2, order[i])
+            if i >= LAG:
+                m = order[i - LAG]
+                if i - LAG < CH - 1:
+                    for nh in range(2):
+                        acc = stage2(m, (2 * i + nh) % TURN_BANKS, 512 * nh, 512)
+                        store(nc.scalar.copy, m, acc, 512 * nh, 512)
+                else:
+                    acc = stage2(m, (2 * i) % 3, 0, 512)
+                    store(nc.scalar.copy, m, acc, 0, 512)
+                    acc = stage2(m, (2 * i + 1) % 3, 512, 256)
+                    store(nc.vector.tensor_copy, m, acc, 512, 256)
+                    acc = stage2(m, (2 * i + 2) % 3, 768, 256)
+                    store(nc.scalar.copy, m, acc, 768, 256)
+            if i < CH:
+                c = order[i]
                 hid(2, c)
-            if c >= 2:
-                stage2(c - 2)
-            if c < CH:
-                quant_h(2, c)
-            if c >= 2:
-                store(c - 2)
+                quant_h01(c)
+                quant_h2(c)
+                if i + 2 < CH:
+                    for g in range(2):
+                        if (g, order[i + 2]) in parked:
+                            hid(g, order[i + 2])

@@ -145,10 +145,9 @@ def tile_recomputed_hidden_weight_gradient_s3_kernel(
             )
 
         def sort_x(pr, t):
-            if pr not in xp:
-                xp[pr] = ring.tile([P, K], F32, name="xp", align_bytes=64)
+            xp[pr, t] = ring.tile([P, 512], F32, name="xp", align_bytes=64, bufs=4)
             nc.scalar.copy(
-                out=xp[pr][:, 512 * t : 512 * t + 512].rearrange("p (g u m) -> p g u m", g=2, u=2),
+                out=xp[pr, t][:].rearrange("p (g u m) -> p g u m", g=2, u=2),
                 in_=xb[pr][:].bitcast(F32)[:, 512 * t : 512 * t + 512].rearrange(
                     "p (g m u) -> p g u m", g=2, u=2
                 ),
@@ -163,12 +162,13 @@ def tile_recomputed_hidden_weight_gradient_s3_kernel(
 
         def turn(pr, kk):
             ps = bank(kk)
-            is_sorted = pr in (xp if kk < 2 else xop)
             for t in range(2):
                 if kk < 2:
-                    c0 = 512 * t + 256 * kk
-                    words = xp[pr][:] if is_sorted else xb[pr][:].bitcast(F32)
+                    is_sorted = (pr, t) in xp
+                    c0 = 256 * kk if is_sorted else 512 * t + 256 * kk
+                    words = xp[pr, t][:] if is_sorted else xb[pr][:].bitcast(F32)
                 else:
+                    is_sorted = pr in xop
                     c0 = 256 * t
                     words = xop[pr][:] if is_sorted else xor[pr][:].bitcast(F32)
                 for u in range(2):
@@ -187,16 +187,18 @@ def tile_recomputed_hidden_weight_gradient_s3_kernel(
                 in_=turned[pr, kk][:].rearrange("p (u r) -> p r u", u=2),
             )
 
-        def prod(pr, kk):
+        def prod(pr, kk, r0=0, r1=256):
             nc.vector.tensor_tensor(
-                out=grouped(pr)[:, 1024 * kk : 1024 * kk + 1024].rearrange(
+                out=grouped(pr)[:, 1024 * kk + 4 * r0 : 1024 * kk + 4 * r1].rearrange(
                     "p (r u e) -> p r u e", u=2, e=2
                 ),
-                in0=turned[pr, kk][:].bitcast(BF16).rearrange("p (u r e) -> p r u e", u=2, e=2),
+                in0=turned[pr, kk][:]
+                .bitcast(BF16)
+                .rearrange("p (u r e) -> p r u e", u=2, e=2)[:, r0:r1, :, :],
                 in1=sc[:, kk, :]
                 .rearrange("p (u e) -> p u e", e=2)
                 .unsqueeze(1)
-                .to_broadcast([P, 256, 2, 2]),
+                .to_broadcast([P, r1 - r0, 2, 2]),
                 op=MULT,
             )
 
@@ -205,6 +207,14 @@ def tile_recomputed_hidden_weight_gradient_s3_kernel(
                 out=xq[pr][:, 256 * k0 : 256 * k1].bitcast(FP8X4),
                 scales=xs[pr][:, 256 * k0 : 256 * k1],
                 in_=xg[pr][:, 1024 * k0 : 1024 * k1],
+            )
+
+        def quant_slot(pr, kk, tl):
+            w0 = 256 * kk + P * tl
+            nc.vector.quantize_mx(
+                out=xq[pr][:, w0 : w0 + P].bitcast(FP8X4),
+                scales=xs[pr][:, w0 : w0 + P],
+                in_=xg[pr][:, 4 * w0 : 4 * w0 + 4 * P],
             )
 
         def wo_lay(copy, q):
@@ -221,31 +231,32 @@ def tile_recomputed_hidden_weight_gradient_s3_kernel(
 
         hps = {}
 
-        def stage1(g, c, ts=(0, 1, 2, 3)):
-            if 0 in ts:
-                hps[g, c] = bank(TURN_BANKS + len(hps) % H_BANKS)
-            acc = hps[g, c]
-            f0 = P * c
-            hf, w0 = divmod(2 * f0, F)
+        def stage1(g, cs, ts=(0, 1, 2, 3), passes=(0, 2, 1)):
+            for c in cs:
+                if (g, c) not in hps:
+                    hps[g, c] = bank(TURN_BANKS + len(hps) % H_BANKS)
             for t in ts:
                 pr, tl = 2 * g + t // 2, t % 2
-                for kk in range(3):
+                for kk in passes:
                     r = slice(256 * kk + P * tl, 256 * kk + P * tl + P)
-                    if kk < 2:
-                        rhs = wt[hf][:, kk, w0 : w0 + 2 * P].bitcast(FP4X4)
-                        rsc = ws[:, kk, f0 : f0 + P]
-                    else:
-                        rhs = woq[:, f0 : f0 + P].bitcast(FP8X4)
-                        rsc = wos[:, f0 : f0 + P]
-                    nc.tensor.matmul_mx(
-                        out=acc[:, P * t : P * t + P],
-                        lhsT=xq[pr][:, r].bitcast(FP8X4),
-                        lhsT_scale=xs[pr][:, r],
-                        rhs=rhs,
-                        rhs_scale=rsc,
-                        start=(kk == 0),
-                        stop=(kk == 2),
-                    )
+                    for c in cs:
+                        f0 = P * c
+                        hf, w0 = divmod(2 * f0, F)
+                        if kk < 2:
+                            rhs = wt[hf][:, kk, w0 : w0 + 2 * P].bitcast(FP4X4)
+                            rsc = ws[:, kk, f0 : f0 + P]
+                        else:
+                            rhs = woq[:, f0 : f0 + P].bitcast(FP8X4)
+                            rsc = wos[:, f0 : f0 + P]
+                        nc.tensor.matmul_mx(
+                            out=hps[g, c][:, P * t : P * t + P],
+                            lhsT=xq[pr][:, r].bitcast(FP8X4),
+                            lhsT_scale=xs[pr][:, r],
+                            rhs=rhs,
+                            rhs_scale=rsc,
+                            start=(kk == 0),
+                            stop=(kk == 1),
+                        )
 
         hg2, parked = {}, {}
 
@@ -314,8 +325,8 @@ def tile_recomputed_hidden_weight_gradient_s3_kernel(
         load_xo(0)
         load_scales(ws, w_scales)
         load_wo(1)
-        load_w(0)
         load_xo(1)
+        load_w(0)
         load_wo(2)
         load_x(2)
         load_wo(3)
@@ -333,41 +344,44 @@ def tile_recomputed_hidden_weight_gradient_s3_kernel(
         widen(nc.vector.tensor_copy, 0, 1, 512, K)
         turn(0, 0)
         turn(0, 1)
-        spread_ps.append(spread(1, TURN_BANKS + 1))
+        spread_ps.append(spread(1, TURN_BANKS + H_BANKS - 1))
         spread_out(0, spread_ps[0])
         wo_lay(nc.vector.tensor_copy, 0)
         prod(0, 0)
         for t in range(2):
             widen(nc.scalar.copy, 1, t, 0, 512)
-        spread_out(1, spread_ps[1])
         turn(0, 2)
+        widen(nc.scalar.copy, 1, 0, 512, K)
         turn_out(0, 2)
         quant_wo(0, 1)
         prod(0, 1)
         turn(1, 0)
-        for t in range(2):
-            widen(nc.scalar.copy, 1, t, 512, K)
+        widen(nc.scalar.copy, 1, 1, 512, K)
         quant_x(0, 0, 1)
         quant_x(0, 2, 3)
         quant_x(0, 1, 2)
-        turn(1, 1)
         turn(1, 2)
+        turn(1, 1)
         wo_lay(nc.scalar.copy, 1)
         turn_out(1, 2)
+        spread_out(1, spread_ps[1])
         prod(1, 0)
-        stage1(0, 0, (0, 1))
-        stage1(0, 1, (0, 1))
+        stage1(0, (0, 1), (0, 1))
         quant_wo(1, 2)
-        prod(1, 1)
-        stage1(0, 2, (0, 1))
-        stage1(0, 3, (0, 1))
+        quant_x(1, 0, 1)
+        quant_slot(1, 2, 0)
+        stage1(0, (2, 3), (0, 1))
+        stage1(0, (0, 1, 2, 3), (2,), (0, 2))
         wo_lay(nc.scalar.copy, 2)
         wo_lay(nc.scalar.copy, 3)
-        quant_x(1, 0, 1)
-        quant_x(1, 2, 3)
-        quant_x(1, 1, 2)
-        for c in range(4):
-            stage1(0, c, (2, 3))
+        for tl in range(2):
+            prod(1, 1, P * tl, P * tl + P)
+        quant_slot(1, 1, 0)
+        quant_slot(1, 2, 1)
+        quant_slot(1, 1, 1)
+        stage1(0, (0, 1, 2, 3), (2,), (1,))
+        stage1(0, (0, 1), (3,))
+        stage1(0, (2, 3), (3,))
 
         def prepare(pr, t):
             mul(pr, t)
@@ -385,90 +399,94 @@ def tile_recomputed_hidden_weight_gradient_s3_kernel(
             quant_x(pr, 2, 3)
             quant_x(pr, 0, 2)
 
+        quant_wo(2, 3)
         sort_xo(2)
-        prepare(2, 0)
-        quant_wo(2, 4)
         park(0, 0)
-        sort_xo(3)
-        prepare(2, 1)
+        prepare(2, 0)
+        quant_wo(3, 4)
+        stage1(0, (4,))
+        stage1(0, (5,))
         park(0, 1)
-        stage1(0, 4)
-        stage1(0, 5)
-        prepare(3, 0)
+        prepare(2, 1)
+        sort_xo(3)
+        mul(3, 0)
+        sort_x(3, 0)
         turn_all(2)
         turn_out(2, 2)
-        stage1(0, 6)
-        prepare(3, 1)
+        hid(0, 2)
+        mul(3, 1)
+        stage1(0, (6,))
         turn_out(2, 0)
         turn_out(2, 1)
-        hid(0, 2)
-        hid(0, 3)
+        stage1(0, (7,), (0, 1))
         turn_all(3)
         out_all(3)
-        stage1(0, 7)
-        mul(4, 0)
+        stage1(0, (7,), (2, 3))
+        hid(0, 3)
         quant_all(2)
-        stage1(1, 4, (0, 1))
         hid(0, 4)
-        stage1(1, 5, (0, 1))
+        hid(0, 5)
+        stage1(1, (4, 5), (0, 1))
+        stage1(1, (6,), (0, 1))
         quant_all(3)
-        stage1(1, 4, (2, 3))
-        stage1(1, 5, (2, 3))
-        sort_x(4, 0)
-        park(0, 5)
+        stage1(1, (4, 5, 6), (2, 3))
+        park(0, 6)
         sort_xo(4)
-        prepare(4, 1)
-        stage1(1, 6)
         sort_xo(5)
-        prepare(5, 0)
-        hid(0, 6)
+        prepare(4, 0)
+        park(0, 7)
+        prepare(4, 1)
+        stage1(1, (7,))
+        mul(5, 0)
+        sort_x(5, 0)
         turn_all(4)
         turn_out(4, 2)
-        stage1(1, 7)
-        prepare(5, 1)
         turn_out(4, 0)
-        turn_out(4, 1)
-        hid(0, 7)
-        stage1(1, 0)
         hid(1, 4)
+        mul(5, 1)
+        sort_x(5, 1)
+        turn_out(4, 1)
+        stage1(1, (0, 1))
+        hid(1, 5)
         turn_all(5)
         out_all(5)
-        stage1(1, 1)
-        hid(1, 5)
-        quant_all(4)
-        stage1(1, 2)
         hid(1, 6)
-        quant_all(5)
-        stage1(1, 3)
+        quant_all(4)
         hid(1, 7)
-        hid(0, 5)
+        stage1(1, (2, 3))
+
+        quant_all(5)
         for c in range(4):
             park(1, c)
 
-        LAG = 2
         order = [4, 5, 6, 7, 0, 1, 2, 3]
-        for i in range(CH + LAG):
-            if i < CH:
-                stage1(2, order[i])
-            if i >= LAG:
-                m = order[i - LAG]
-                if i - LAG < CH - 1:
-                    for nh in range(2):
-                        acc = stage2(m, (2 * i + nh) % TURN_BANKS, 512 * nh, 512)
-                        store(nc.scalar.copy, m, acc, 512 * nh, 512)
-                else:
-                    acc = stage2(m, (2 * i) % 3, 0, 512)
-                    store(nc.scalar.copy, m, acc, 0, 512)
-                    acc = stage2(m, (2 * i + 1) % 3, 512, 256)
-                    store(nc.vector.tensor_copy, m, acc, 512, 256)
-                    acc = stage2(m, (2 * i + 2) % 3, 768, 256)
-                    store(nc.scalar.copy, m, acc, 768, 256)
-            if i < CH:
-                c = order[i]
+        out_banks = []
+
+        def product(m, widths):
+            n0 = 0
+            for j, width in enumerate(widths):
+                b = len(out_banks) % TURN_BANKS if j < 2 else TURN_BANKS + j
+                out_banks.append(b)
+                acc = stage2(m, b, n0, width)
+                copy = nc.vector.tensor_copy if len(widths) > 2 and j % 2 else nc.scalar.copy
+                store(copy, m, acc, n0, width)
+                n0 += width
+
+        def finish(c):
+            for g in range(2):
+                if (g, c) in parked:
+                    hid(g, c)
+
+        for i in range(0, CH + 2, 2):
+            cs = order[i : i + 2]
+            if cs:
+                stage1(2, cs)
+            if i >= 2:
+                for m in order[i - 2 : i]:
+                    product(m, (256, 256, 256, 256) if m == order[-1] else (512, 512))
+            for c in cs:
                 hid(2, c)
                 quant_h01(c)
                 quant_h2(c)
-                if i + 2 < CH:
-                    for g in range(2):
-                        if (g, order[i + 2]) in parked:
-                            hid(g, order[i + 2])
+            for c in order[i + 2 : i + 4]:
+                finish(c)

@@ -15,7 +15,7 @@ FP8 = mybir.dt.float8_e4m3fn
 FP8X4 = mybir.dt.float8_e4m3fn_x4
 FP4X4 = mybir.dt.float4_e2m1fn_x4
 MULT = mybir.AluOpType.mult
-MAX = mybir.AluOpType.max
+ACT = mybir.ActivationFunctionType
 
 P = 128
 G = T // 512
@@ -49,13 +49,15 @@ def tile_recomputed_hidden_weight_gradient_s3_kernel(
         sc = kept("sc", [P, 2, 4], F32)
         scb = kept("scb", [P, K], F32)
         gt = kept("gt", [P, G, 4], BF16)
+        g_abs = kept("g_abs", [P, G * 4], F32)
+        g_sign = kept("g_sign", [P, G * 4], F32)
         woq = kept("woq", [P, F], U32)
         wos = kept("wos", [P, F], U8)
         xbytes = [kept("xbytes%d" % pr, [P, 2, K], U8) for pr in range(PAIRS)]
         xor = [kept("xor%d" % pr, [P, 2 * O], BF16) for pr in range(PAIRS)]
         xq = [kept("xq%d" % pr, [P, 3 * 256], U32) for pr in range(PAIRS)]
         xs = [kept("xs%d" % pr, [P, 3 * 256], U8) for pr in range(PAIRS)]
-        wor = [kept("wor%d" % q, [P, 4, 256], BF16) for q in range(4)]
+        wor = {}
         wog = kept("wog", [P, 4 * F], BF16)
         hg01 = [kept("hg01_%d" % c, [P, 1024], BF16) for c in range(CH)]
         hq = [kept("hq%d" % c, [P, G * P], U32) for c in range(CH)]
@@ -80,8 +82,11 @@ def tile_recomputed_hidden_weight_gradient_s3_kernel(
                 in_=xo_v[g][:, 2 * h : 2 * h + 2, :],
             )
 
-        def load_wo(q):
-            nc.sync.dma_start(out=wor[q][:], in_=wo_v[:, :, 256 * q : 256 * q + 256])
+        def load_wo(q0, q1):
+            rows_in = kept("wor%d" % q0, [P, 4, 256 * (q1 - q0)], BF16)
+            nc.sync.dma_start(out=rows_in[:], in_=wo_v[:, :, 256 * q0 : 256 * q1])
+            for q in range(q0, q1):
+                wor[q] = rows_in[:, :, 256 * (q - q0) : 256 * (q - q0) + 256]
 
         def load_w(hf):
             nc.sync.dma_start(
@@ -144,18 +149,18 @@ def tile_recomputed_hidden_weight_gradient_s3_kernel(
                 op=MULT,
             )
 
-        def sort_x(pr, t):
+        def sort_x(pr, t, copy=nc.scalar.copy):
             xp[pr, t] = ring.tile([P, 512], F32, name="xp", align_bytes=64, bufs=4)
-            nc.scalar.copy(
+            copy(
                 out=xp[pr, t][:].rearrange("p (g u m) -> p g u m", g=2, u=2),
                 in_=xb[pr][:].bitcast(F32)[:, 512 * t : 512 * t + 512].rearrange(
                     "p (g m u) -> p g u m", g=2, u=2
                 ),
             )
 
-        def sort_xo(pr):
+        def sort_xo(pr, copy=nc.scalar.copy):
             xop[pr] = ring.tile([P, O], F32, name="xop", align_bytes=64)
-            nc.scalar.copy(
+            copy(
                 out=xop[pr][:].rearrange("p (t u m) -> p t u m", t=2, u=2),
                 in_=xor[pr][:].bitcast(F32).rearrange("p (t m u) -> p t u m", t=2, u=2),
             )
@@ -179,8 +184,8 @@ def tile_recomputed_hidden_weight_gradient_s3_kernel(
                     nc.tensor.transpose(ps[:, 256 * u + P * t : 256 * u + P * t + P], src, ident[:])
             turned[pr, kk] = ps
 
-        def turn_out(pr, kk):
-            nc.scalar.copy(
+        def turn_out(pr, kk, copy=nc.scalar.copy):
+            copy(
                 out=grouped(pr)[:, 1024 * kk : 1024 * kk + 1024]
                 .bitcast(F32)
                 .rearrange("p (r u) -> p r u", u=2),
@@ -220,7 +225,7 @@ def tile_recomputed_hidden_weight_gradient_s3_kernel(
         def wo_lay(copy, q):
             copy(
                 out=wog[:, 1024 * q : 1024 * q + 1024].rearrange("p (c i t) -> p c t i", i=4, t=4),
-                in_=wor[q][:].rearrange("p t (c i) -> p c t i", i=4),
+                in_=wor[q].rearrange("p t (c i) -> p c t i", i=4),
             )
 
         def quant_wo(q0, q1):
@@ -231,59 +236,63 @@ def tile_recomputed_hidden_weight_gradient_s3_kernel(
 
         hps = {}
 
-        def stage1(g, cs, ts=(0, 1, 2, 3), passes=(0, 2, 1)):
-            for c in cs:
-                if (g, c) not in hps:
-                    hps[g, c] = bank(TURN_BANKS + len(hps) % H_BANKS)
-            for t in ts:
-                pr, tl = 2 * g + t // 2, t % 2
-                for kk in passes:
-                    r = slice(256 * kk + P * tl, 256 * kk + P * tl + P)
-                    for c in cs:
-                        f0 = P * c
-                        hf, w0 = divmod(2 * f0, F)
-                        if kk < 2:
-                            rhs = wt[hf][:, kk, w0 : w0 + 2 * P].bitcast(FP4X4)
-                            rsc = ws[:, kk, f0 : f0 + P]
-                        else:
-                            rhs = woq[:, f0 : f0 + P].bitcast(FP8X4)
-                            rsc = wos[:, f0 : f0 + P]
-                        nc.tensor.matmul_mx(
-                            out=hps[g, c][:, P * t : P * t + P],
-                            lhsT=xq[pr][:, r].bitcast(FP8X4),
-                            lhsT_scale=xs[pr][:, r],
-                            rhs=rhs,
-                            rhs_scale=rsc,
-                            start=(kk == 0),
-                            stop=(kk == 1),
-                        )
+        def wide(g, hf, t, passes=(0, 2, 1), last=1):
+            if (g, hf, t) not in hps:
+                hps[g, hf, t] = bank(TURN_BANKS + len(hps) % H_BANKS)
+            pr, tl = 2 * g + t // 2, t % 2
+            cols = slice(512 * hf, 512 * hf + 512)
+            for kk in passes:
+                r = slice(256 * kk + P * tl, 256 * kk + P * tl + P)
+                nc.tensor.matmul_mx(
+                    out=hps[g, hf, t][:],
+                    lhsT=xq[pr][:, r].bitcast(FP8X4),
+                    lhsT_scale=xs[pr][:, r],
+                    rhs=wt[hf][:, kk, :].bitcast(FP4X4) if kk < 2 else woq[:, cols].bitcast(FP8X4),
+                    rhs_scale=ws[:, kk, cols] if kk < 2 else wos[:, cols],
+                    start=(kk == 0),
+                    stop=(kk == last),
+                )
 
-        hg2, parked = {}, {}
+        hg2, planes = {}, {}
 
-        def park(g, c):
-            parked[g, c] = kept("parked%d_%d" % (g, c), [P, 512], F32)
-            nc.scalar.copy(
-                out=parked[g, c][:].rearrange("p (f t) -> p f t", t=4),
-                in_=hps[g, c][:].rearrange("p (t f) -> p f t", t=4),
+        def split_gate():
+            flat = gt[:].rearrange("p g t -> p (g t)")
+            nc.scalar.activation(out=g_abs[:], in_=flat, func=ACT.Abs)
+            nc.scalar.activation(out=g_sign[:], in_=flat, func=ACT.Sign)
+
+        def park(g, hf, t):
+            if (g, hf) not in planes:
+                planes[g, hf] = kept("planes%d_%d" % (g, hf), [P, 4 * 512], BF16)
+            nc.scalar.activation(
+                out=planes[g, hf][:, 512 * t : 512 * t + 512],
+                in_=hps[g, hf, t][:],
+                func=ACT.Relu,
+                scale=g_abs[:, 4 * g + t : 4 * g + t + 1],
             )
 
-        def hid(g, c):
-            if (g, c) in parked:
-                sums = parked[g, c][:].rearrange("p (f t) -> p f t", t=4)
-            else:
-                sums = hps[g, c][:].rearrange("p (t f) -> p f t", t=4)
+        def sign(g, hf, t):
+            plane = planes[g, hf][:, 512 * t : 512 * t + 512]
+            nc.vector.tensor_scalar(
+                out=plane,
+                in0=plane,
+                scalar1=g_sign[:, 4 * g + t : 4 * g + t + 1],
+                scalar2=None,
+                op0=MULT,
+            )
+
+        def h_rows(g, c):
             if g < 2:
-                dst = hg01[c][:, 512 * g : 512 * g + 512]
-            else:
-                hg2[c] = ring.tile([P, 512], BF16, name="hg2", align_bytes=64)
-                dst = hg2[c][:]
-            nc.vector.scalar_tensor_tensor(
-                out=dst.rearrange("p (f t) -> p f t", t=4),
-                in0=sums,
-                scalar=0.0,
-                in1=gt[:, g, :].unsqueeze(1).to_broadcast([P, P, 4]),
-                op0=MAX,
-                op1=MULT,
+                return hg01[c][:, 512 * g : 512 * g + 512]
+            hg2[c] = ring.tile([P, 512], BF16, name="hg2", align_bytes=64)
+            return hg2[c][:]
+
+        def weave(g, c):
+            hf, f0 = divmod(P * c, 512)
+            nc.vector.tensor_copy(
+                out=h_rows(g, c).rearrange("p (c i t) -> p c t i", i=4, t=4),
+                in_=planes[g, hf][:]
+                .rearrange("p (t f) -> p t f", t=4)[:, :, f0 : f0 + P]
+                .rearrange("p t (c i) -> p c t i", i=4),
             )
 
         def quant_h01(c):
@@ -320,17 +329,16 @@ def tile_recomputed_hidden_weight_gradient_s3_kernel(
 
         load_x(0)
         load_sc()
-        load_wo(0)
+        load_wo(0, 1)
         load_x(1)
         load_xo(0)
         load_scales(ws, w_scales)
-        load_wo(1)
+        load_wo(1, 2)
         load_xo(1)
         load_w(0)
-        load_wo(2)
-        load_x(2)
-        load_wo(3)
+        load_wo(2, 4)
         load_gate()
+        load_x(2)
         load_w(1)
         load_xo(2)
         for pr in range(3, PAIRS):
@@ -366,22 +374,24 @@ def tile_recomputed_hidden_weight_gradient_s3_kernel(
         turn_out(1, 2)
         spread_out(1, spread_ps[1])
         prod(1, 0)
-        stage1(0, (0, 1), (0, 1))
+        for t in range(2):
+            wide(0, 0, t, (0, 1), 2)
         quant_wo(1, 2)
         quant_x(1, 0, 1)
         quant_slot(1, 2, 0)
-        stage1(0, (2, 3), (0, 1))
-        stage1(0, (0, 1, 2, 3), (2,), (0, 2))
+        for t in range(2):
+            wide(0, 0, t, (2,), 2)
+        wide(0, 0, 2, (0, 2))
         wo_lay(nc.scalar.copy, 2)
+        split_gate()
         wo_lay(nc.scalar.copy, 3)
         for tl in range(2):
             prod(1, 1, P * tl, P * tl + P)
         quant_slot(1, 1, 0)
         quant_slot(1, 2, 1)
         quant_slot(1, 1, 1)
-        stage1(0, (0, 1, 2, 3), (2,), (1,))
-        stage1(0, (0, 1), (3,))
-        stage1(0, (2, 3), (3,))
+        wide(0, 0, 2, (1,))
+        wide(0, 0, 3)
 
         def prepare(pr, t):
             mul(pr, t)
@@ -399,67 +409,77 @@ def tile_recomputed_hidden_weight_gradient_s3_kernel(
             quant_x(pr, 2, 3)
             quant_x(pr, 0, 2)
 
-        quant_wo(2, 3)
+        def sort_pair(pr):
+            sort_xo(pr, nc.vector.tensor_copy)
+            for t in range(2):
+                sort_x(pr, t, nc.vector.tensor_copy)
+
+        park(0, 0, 0)
         sort_xo(2)
-        park(0, 0)
         prepare(2, 0)
-        quant_wo(3, 4)
-        stage1(0, (4,))
-        stage1(0, (5,))
-        park(0, 1)
-        prepare(2, 1)
-        sort_xo(3)
-        mul(3, 0)
-        sort_x(3, 0)
+        quant_wo(2, 4)
+        for t in range(2):
+            wide(0, 1, t, (0, 1), 2)
+        for t in range(2):
+            wide(0, 1, t, (2,), 2)
+        park(0, 0, 1)
+        park(0, 0, 2)
+        mul(2, 1)
         turn_all(2)
-        turn_out(2, 2)
-        hid(0, 2)
+        out_all(2)
+        wide(0, 1, 2)
+        wide(0, 1, 3)
+        mul(3, 0)
         mul(3, 1)
-        stage1(0, (6,))
-        turn_out(2, 0)
-        turn_out(2, 1)
-        stage1(0, (7,), (0, 1))
+        for kk in (2, 0, 1):
+            quant_x(2, kk, kk + 1)
+        sort_pair(3)
+        park(0, 0, 3)
+        wide(1, 1, 0)
+        park(0, 1, 0)
+        park(0, 1, 1)
+        park(0, 1, 2)
         turn_all(3)
         out_all(3)
-        stage1(0, (7,), (2, 3))
-        hid(0, 3)
-        quant_all(2)
-        hid(0, 4)
-        hid(0, 5)
-        stage1(1, (4, 5), (0, 1))
-        stage1(1, (6,), (0, 1))
+        wide(1, 1, 1)
+        wide(1, 0, 0)
+        wide(1, 0, 1)
+        mul(4, 0)
+        mul(4, 1)
+        sort_xo(4, nc.vector.tensor_copy)
+        sort_x(4, 0, nc.vector.tensor_copy)
         quant_all(3)
-        stage1(1, (4, 5, 6), (2, 3))
-        park(0, 6)
-        sort_xo(4)
-        sort_xo(5)
-        prepare(4, 0)
-        park(0, 7)
-        prepare(4, 1)
-        stage1(1, (7,))
-        mul(5, 0)
-        sort_x(5, 0)
+        sort_x(4, 1, nc.vector.tensor_copy)
+        park(0, 1, 3)
+        wide(1, 1, 2)
+        park(1, 1, 0)
+        park(1, 1, 1)
         turn_all(4)
-        turn_out(4, 2)
-        turn_out(4, 0)
-        hid(1, 4)
+        park(1, 0, 0)
+        out_all(4)
+        wide(1, 1, 3)
+        wide(1, 0, 2)
+        mul(5, 0)
         mul(5, 1)
-        sort_x(5, 1)
-        turn_out(4, 1)
-        stage1(1, (0, 1))
-        hid(1, 5)
+        sort_pair(5)
         turn_all(5)
+        park(1, 0, 1)
+        park(1, 1, 2)
         out_all(5)
-        hid(1, 6)
         quant_all(4)
-        hid(1, 7)
-        stage1(1, (2, 3))
-
+        wide(1, 0, 3)
+        for t in range(4):
+            sign(0, 1, t)
+        weave(0, 4)
+        wide(2, 1, 0)
+        park(1, 1, 3)
+        wide(2, 1, 1)
         quant_all(5)
-        for c in range(4):
-            park(1, c)
+        park(1, 0, 2)
+        park(1, 0, 3)
+        for t in range(4):
+            sign(1, 1, t)
 
-        order = [4, 5, 6, 7, 0, 1, 2, 3]
         out_banks = []
 
         def product(m, widths):
@@ -472,21 +492,38 @@ def tile_recomputed_hidden_weight_gradient_s3_kernel(
                 store(copy, m, acc, n0, width)
                 n0 += width
 
-        def finish(c):
-            for g in range(2):
-                if (g, c) in parked:
-                    hid(g, c)
-
-        for i in range(0, CH + 2, 2):
-            cs = order[i : i + 2]
-            if cs:
-                stage1(2, cs)
-            if i >= 2:
-                for m in order[i - 2 : i]:
-                    product(m, (256, 256, 256, 256) if m == order[-1] else (512, 512))
-            for c in cs:
-                hid(2, c)
-                quant_h01(c)
-                quant_h2(c)
-            for c in order[i + 2 : i + 4]:
-                finish(c)
+        for hf in (1, 0):
+            for t in range(4):
+                if (2, hf, t) not in hps:
+                    wide(2, hf, t)
+                park(2, hf, t)
+        weave(1, 4)
+        for c in range(5, 7):
+            weave(0, c)
+            weave(1, c)
+            quant_h01(c - 1)
+        for t in range(4):
+            sign(2, 1, t)
+        weave(0, 7)
+        weave(2, 4)
+        weave(2, 5)
+        quant_h2(4)
+        product(4, (512, 512))
+        weave(1, 7)
+        quant_h2(5)
+        product(5, (512, 512))
+        for c in range(6, 8):
+            weave(2, c)
+            quant_h01(c)
+            quant_h2(c)
+            product(c, (512, 512))
+        for g in range(G):
+            for t in range(4):
+                sign(g, 0, t)
+        for c in range(4):
+            for g in range(G):
+                weave(g, c)
+            quant_h01(c)
+            quant_h2(c)
+        for c in range(4):
+            product(c, (256, 256, 256, 256) if c == 3 else (512, 512))

@@ -94,10 +94,10 @@ def tile_recomputed_hidden_weight_gradient_s3_kernel(
             )
 
         def load_scales(dst, src):
-            for q in range(4):
+            for r in range(4):
                 nc.sync.dma_start(
-                    out=dst[32 * q : 32 * q + 4, :, :].bitcast(I32),
-                    in_=src.rearrange("g q n -> q g n")[4 * q : 4 * q + 4, :, :].bitcast(I32),
+                    out=dst[r:P:32, :, :].bitcast(I32),
+                    in_=src.rearrange("g (q r) n -> r q g n", r=4)[r].bitcast(I32),
                 )
 
         def load_sc():
@@ -234,6 +234,11 @@ def tile_recomputed_hidden_weight_gradient_s3_kernel(
                 out=woq[:, cols].bitcast(FP8X4), scales=wos[:, cols], in_=wog[:, 1024 * q0 : 1024 * q1]
             )
 
+        def warm_up(count):
+            ps = bank(TURN_BANKS + 2)
+            for j in range(count):
+                nc.tensor.matmul(ps[:], lhsT=xor[0][:, 0:P], rhs=xor[0][:, 0:512], start=True, stop=True)
+
         hps = {}
 
         def wide(g, hf, t, passes=(0, 2, 1), last=1):
@@ -327,33 +332,36 @@ def tile_recomputed_hidden_weight_gradient_s3_kernel(
             copy(out=ot[:, 0:width], in_=acc[:, 0:width])
             nc.sync.dma_start(out=out[P * m : P * m + P, n0 : n0 + width], in_=ot[:, 0:width])
 
-        load_x(0)
         load_sc()
+        load_x(0)
         load_wo(0, 1)
         load_x(1)
         load_xo(0)
-        load_scales(ws, w_scales)
-        load_wo(1, 2)
+        load_wo(1, 3)
         load_xo(1)
         load_w(0)
-        load_wo(2, 4)
+        load_scales(ws, w_scales)
         load_gate()
+        load_wo(3, 4)
         load_x(2)
         load_w(1)
         load_xo(2)
-        for pr in range(3, PAIRS):
-            load_x(pr)
-            load_xo(pr)
+        load_x(3)
+        load_xo(3)
+        load_x(4)
+        load_xo(4)
+        load_x(5)
+        load_xo(5)
         load_dy()
 
-        spread_ps = [spread(0, TURN_BANKS)]
+        spread_ps = [spread(g, TURN_BANKS + g) for g in range(2)]
         widen(nc.vector.tensor_copy, 0, 0, 0, K)
         widen(nc.scalar.copy, 0, 1, 0, 512)
         widen(nc.vector.tensor_copy, 0, 1, 512, K)
         turn(0, 0)
         turn(0, 1)
-        spread_ps.append(spread(1, TURN_BANKS + H_BANKS - 1))
-        spread_out(0, spread_ps[0])
+        for g in range(2):
+            spread_out(g, spread_ps[g])
         wo_lay(nc.vector.tensor_copy, 0)
         prod(0, 0)
         for t in range(2):
@@ -364,6 +372,7 @@ def tile_recomputed_hidden_weight_gradient_s3_kernel(
         quant_wo(0, 1)
         prod(0, 1)
         turn(1, 0)
+        warm_up(2)
         widen(nc.scalar.copy, 1, 1, 512, K)
         quant_x(0, 0, 1)
         quant_x(0, 2, 3)
@@ -372,26 +381,28 @@ def tile_recomputed_hidden_weight_gradient_s3_kernel(
         turn(1, 1)
         wo_lay(nc.scalar.copy, 1)
         turn_out(1, 2)
-        spread_out(1, spread_ps[1])
         prod(1, 0)
         for t in range(2):
             wide(0, 0, t, (0, 1), 2)
         quant_wo(1, 2)
         quant_x(1, 0, 1)
-        quant_slot(1, 2, 0)
+        quant_x(1, 2, 3)
         for t in range(2):
             wide(0, 0, t, (2,), 2)
-        wide(0, 0, 2, (0, 2))
-        wo_lay(nc.scalar.copy, 2)
+        for t in range(2, 4):
+            wide(0, 0, t, (0, 2))
         split_gate()
+        wo_lay(nc.scalar.copy, 2)
+        park(0, 0, 0)
+        park(0, 0, 1)
         wo_lay(nc.scalar.copy, 3)
+        sort_xo(2)
         for tl in range(2):
             prod(1, 1, P * tl, P * tl + P)
         quant_slot(1, 1, 0)
-        quant_slot(1, 2, 1)
         quant_slot(1, 1, 1)
-        wide(0, 0, 2, (1,))
-        wide(0, 0, 3)
+        for t in range(2, 4):
+            wide(0, 0, t, (1,))
 
         def prepare(pr, t):
             mul(pr, t)
@@ -406,34 +417,34 @@ def tile_recomputed_hidden_weight_gradient_s3_kernel(
                 turn_out(pr, kk)
 
         def quant_all(pr):
-            quant_x(pr, 2, 3)
-            quant_x(pr, 0, 2)
+            for kk in (2, 0, 1):
+                quant_x(pr, kk, kk + 1)
 
         def sort_pair(pr):
             sort_xo(pr, nc.vector.tensor_copy)
             for t in range(2):
                 sort_x(pr, t, nc.vector.tensor_copy)
 
-        park(0, 0, 0)
-        sort_xo(2)
         prepare(2, 0)
-        quant_wo(2, 4)
-        for t in range(2):
-            wide(0, 1, t, (0, 1), 2)
-        for t in range(2):
-            wide(0, 1, t, (2,), 2)
-        park(0, 0, 1)
-        park(0, 0, 2)
         mul(2, 1)
+        quant_wo(2, 4)
+        for t in range(3):
+            wide(0, 1, t, (0, 1), 2)
         turn_all(2)
+
+        park(0, 0, 2)
         out_all(2)
-        wide(0, 1, 2)
-        wide(0, 1, 3)
+        for t in range(3):
+            wide(0, 1, t, (2,), 2)
+        for t in range(3, 4):
+            wide(0, 1, t)
         mul(3, 0)
+        quant_x(2, 2, 3)
+        quant_x(2, 0, 1)
+        sort_xo(3, nc.vector.tensor_copy)
+        sort_x(3, 0, nc.vector.tensor_copy)
+        quant_x(2, 1, 2)
         mul(3, 1)
-        for kk in (2, 0, 1):
-            quant_x(2, kk, kk + 1)
-        sort_pair(3)
         park(0, 0, 3)
         wide(1, 1, 0)
         park(0, 1, 0)
@@ -446,10 +457,8 @@ def tile_recomputed_hidden_weight_gradient_s3_kernel(
         wide(1, 0, 1)
         mul(4, 0)
         mul(4, 1)
-        sort_xo(4, nc.vector.tensor_copy)
-        sort_x(4, 0, nc.vector.tensor_copy)
         quant_all(3)
-        sort_x(4, 1, nc.vector.tensor_copy)
+        sort_pair(4)
         park(0, 1, 3)
         wide(1, 1, 2)
         park(1, 1, 0)
@@ -485,7 +494,7 @@ def tile_recomputed_hidden_weight_gradient_s3_kernel(
         def product(m, widths):
             n0 = 0
             for j, width in enumerate(widths):
-                b = len(out_banks) % TURN_BANKS if j < 2 else TURN_BANKS + j
+                b = len(out_banks) % (TURN_BANKS + H_BANKS)
                 out_banks.append(b)
                 acc = stage2(m, b, n0, width)
                 copy = nc.vector.tensor_copy if len(widths) > 2 and j % 2 else nc.scalar.copy
@@ -498,12 +507,16 @@ def tile_recomputed_hidden_weight_gradient_s3_kernel(
                     wide(2, hf, t)
                 park(2, hf, t)
         weave(1, 4)
-        for c in range(5, 7):
-            weave(0, c)
-            weave(1, c)
-            quant_h01(c - 1)
-        for t in range(4):
-            sign(2, 1, t)
+        weave(0, 5)
+        weave(1, 5)
+        quant_h01(4)
+        weave(0, 6)
+        sign(2, 1, 0)
+        sign(2, 1, 1)
+        weave(1, 6)
+        sign(2, 1, 2)
+        quant_h01(5)
+        sign(2, 1, 3)
         weave(0, 7)
         weave(2, 4)
         weave(2, 5)

@@ -149,14 +149,16 @@ def tile_recomputed_hidden_weight_gradient_s3_kernel(
                 op=MULT,
             )
 
-        def sort_x(pr, t, copy=nc.scalar.copy):
-            xp[pr, t] = ring.tile([P, 512], F32, name="xp", align_bytes=64, bufs=4)
+        def sort_x(pr, t0, t1, copy=nc.scalar.copy):
+            words = ring.tile([P, 512 * (t1 - t0)], F32, name="xp", align_bytes=64)
             copy(
-                out=xp[pr, t][:].rearrange("p (g u m) -> p g u m", g=2, u=2),
-                in_=xb[pr][:].bitcast(F32)[:, 512 * t : 512 * t + 512].rearrange(
-                    "p (g m u) -> p g u m", g=2, u=2
+                out=words[:].rearrange("p (g u m) -> p g u m", u=2, m=P),
+                in_=xb[pr][:].bitcast(F32)[:, 512 * t0 : 512 * t1].rearrange(
+                    "p (g m u) -> p g u m", u=2, m=P
                 ),
             )
+            for t in range(t0, t1):
+                xp[pr, t] = words[:, 512 * (t - t0) : 512 * (t - t0) + 512]
 
         def sort_xo(pr, copy=nc.scalar.copy):
             xop[pr] = ring.tile([P, O], F32, name="xop", align_bytes=64)
@@ -171,7 +173,7 @@ def tile_recomputed_hidden_weight_gradient_s3_kernel(
                 if kk < 2:
                     is_sorted = (pr, t) in xp
                     c0 = 256 * kk if is_sorted else 512 * t + 256 * kk
-                    words = xp[pr, t][:] if is_sorted else xb[pr][:].bitcast(F32)
+                    words = xp[pr, t] if is_sorted else xb[pr][:].bitcast(F32)
                 else:
                     is_sorted = pr in xop
                     c0 = 256 * t
@@ -233,11 +235,6 @@ def tile_recomputed_hidden_weight_gradient_s3_kernel(
             nc.vector.quantize_mx(
                 out=woq[:, cols].bitcast(FP8X4), scales=wos[:, cols], in_=wog[:, 1024 * q0 : 1024 * q1]
             )
-
-        def warm_up(count):
-            ps = bank(TURN_BANKS + 2)
-            for j in range(count):
-                nc.tensor.matmul(ps[:], lhsT=xor[0][:, 0:P], rhs=xor[0][:, 0:512], start=True, stop=True)
 
         hps = {}
 
@@ -372,11 +369,9 @@ def tile_recomputed_hidden_weight_gradient_s3_kernel(
         quant_wo(0, 1)
         prod(0, 1)
         turn(1, 0)
-        warm_up(2)
         widen(nc.scalar.copy, 1, 1, 512, K)
-        quant_x(0, 0, 1)
         quant_x(0, 2, 3)
-        quant_x(0, 1, 2)
+        quant_x(0, 0, 2)
         turn(1, 2)
         turn(1, 1)
         wo_lay(nc.scalar.copy, 1)
@@ -406,7 +401,7 @@ def tile_recomputed_hidden_weight_gradient_s3_kernel(
 
         def prepare(pr, t):
             mul(pr, t)
-            sort_x(pr, t)
+            sort_x(pr, t, t + 1)
 
         def turn_all(pr):
             for kk in (2, 0, 1):
@@ -422,8 +417,7 @@ def tile_recomputed_hidden_weight_gradient_s3_kernel(
 
         def sort_pair(pr):
             sort_xo(pr, nc.vector.tensor_copy)
-            for t in range(2):
-                sort_x(pr, t, nc.vector.tensor_copy)
+            sort_x(pr, 0, 2, nc.vector.tensor_copy)
 
         prepare(2, 0)
         mul(2, 1)
@@ -442,7 +436,7 @@ def tile_recomputed_hidden_weight_gradient_s3_kernel(
         quant_x(2, 2, 3)
         quant_x(2, 0, 1)
         sort_xo(3, nc.vector.tensor_copy)
-        sort_x(3, 0, nc.vector.tensor_copy)
+        sort_x(3, 0, 1, nc.vector.tensor_copy)
         quant_x(2, 1, 2)
         mul(3, 1)
         park(0, 0, 3)
@@ -457,7 +451,8 @@ def tile_recomputed_hidden_weight_gradient_s3_kernel(
         wide(1, 0, 1)
         mul(4, 0)
         mul(4, 1)
-        quant_all(3)
+        quant_x(3, 2, 3)
+        quant_x(3, 0, 2)
         sort_pair(4)
         park(0, 1, 3)
         wide(1, 1, 2)
@@ -475,7 +470,8 @@ def tile_recomputed_hidden_weight_gradient_s3_kernel(
         park(1, 0, 1)
         park(1, 1, 2)
         out_all(5)
-        quant_all(4)
+        quant_x(4, 2, 3)
+        quant_x(4, 0, 2)
         wide(1, 0, 3)
         for t in range(4):
             sign(0, 1, t)
@@ -510,26 +506,28 @@ def tile_recomputed_hidden_weight_gradient_s3_kernel(
         weave(0, 5)
         weave(1, 5)
         quant_h01(4)
-        weave(0, 6)
         sign(2, 1, 0)
         sign(2, 1, 1)
-        weave(1, 6)
+        weave(0, 6)
         sign(2, 1, 2)
         quant_h01(5)
         sign(2, 1, 3)
-        weave(0, 7)
+        weave(1, 6)
         weave(2, 4)
         weave(2, 5)
         quant_h2(4)
         product(4, (512, 512))
-        weave(1, 7)
+        weave(2, 6)
         quant_h2(5)
         product(5, (512, 512))
-        for c in range(6, 8):
-            weave(2, c)
-            quant_h01(c)
-            quant_h2(c)
-            product(c, (512, 512))
+        quant_h01(6)
+        quant_h2(6)
+        product(6, (512, 512))
+        for g in range(G):
+            weave(g, 7)
+        quant_h01(7)
+        quant_h2(7)
+        product(7, (512, 512))
         for g in range(G):
             for t in range(4):
                 sign(g, 0, t)

@@ -18,17 +18,23 @@ MULT = mybir.AluOpType.mult
 ACT = mybir.ActivationFunctionType
 
 P = 128
-G = T // 512
-PAIRS = 2 * G
-CH = F // P
+BANK = 512
+GROUPS = T // 512
+PAIRS = 2 * GROUPS
+PAIR_ROWS = 2 * P
+QUARTER = F // 4
+CHUNKS = F // P
+XO_PASS = 2
 TURN_BANKS = 3
-H_BANKS = 5
+UNIT_BANKS = 5
+WARM_UPS = 2
 
 
 def tile_recomputed_hidden_weight_gradient_s3_kernel(
     tc, x_bytes, x_scale, xo, w_words, w_scales, wo, gate, dy_words, dy_scales, out
 ):
     nc = tc.nc
+    on_vector, on_scalar = nc.vector.tensor_copy, nc.scalar.copy
     with ExitStack() as ctx:
         keep = ctx.enter_context(tc.tile_pool(name="keep", bufs=1))
         ring = ctx.enter_context(tc.tile_pool(name="ring", bufs=3))
@@ -39,32 +45,32 @@ def tile_recomputed_hidden_weight_gradient_s3_kernel(
             return keep.tile(shape, dtype, name=name, align_bytes=64)
 
         def bank(b):
-            return psum.tile([P, 512], F32, name="bank%d" % b)
+            return psum.tile([P, BANK], F32, name="bank%d" % b)
 
         ident = kept("ident", [P, P], F32)
-        wt = [kept("wt%d" % hf, [P, 2, F], U8) for hf in range(2)]
-        ws = kept("ws", [P, 2, F], U8)
-        dyt = kept("dyt", [P, G, 2 * N], U8)
-        dys = kept("dys", [P, G, N], U8)
-        sc = kept("sc", [P, 2, 4], F32)
-        scb = kept("scb", [P, K], F32)
-        gt = kept("gt", [P, G, 4], BF16)
-        g_abs = kept("g_abs", [P, G * 4], F32)
-        g_sign = kept("g_sign", [P, G * 4], F32)
-        woq = kept("woq", [P, F], U32)
-        wos = kept("wos", [P, F], U8)
-        xbytes = [kept("xbytes%d" % pr, [P, 2, K], U8) for pr in range(PAIRS)]
-        xor = [kept("xor%d" % pr, [P, 2 * O], BF16) for pr in range(PAIRS)]
-        xq = [kept("xq%d" % pr, [P, 3 * 256], U32) for pr in range(PAIRS)]
-        xs = [kept("xs%d" % pr, [P, 3 * 256], U8) for pr in range(PAIRS)]
-        wor = {}
-        wog = kept("wog", [P, 4 * F], BF16)
-        hg01 = [kept("hg01_%d" % c, [P, 1024], BF16) for c in range(CH)]
-        hq = [kept("hq%d" % c, [P, G * P], U32) for c in range(CH)]
-        hs = [kept("hs%d" % c, [P, G * P], U8) for c in range(CH)]
+        w_codes = [kept("w_codes%d" % hf, [P, 2, F], U8) for hf in range(2)]
+        w_plane = kept("w_plane", [P, 2, F], U8)
+        dy_codes = kept("dy_codes", [P, GROUPS, 2 * N], U8)
+        dy_plane = kept("dy_plane", [P, GROUPS, N], U8)
+        scale_by_k = kept("scale_by_k", [P, 2, 4], F32)
+        scale_rows = kept("scale_rows", [P, K], F32)
+        gates = kept("gates", [P, GROUPS, 4], BF16)
+        gate_abs = kept("gate_abs", [P, GROUPS * 4], F32)
+        gate_sign = kept("gate_sign", [P, GROUPS * 4], F32)
+        wo_codes = kept("wo_codes", [P, F], U32)
+        wo_plane = kept("wo_plane", [P, F], U8)
+        x_raw = [kept("x_raw%d" % pr, [P, 2, K], U8) for pr in range(PAIRS)]
+        xo_raw = [kept("xo_raw%d" % pr, [P, 2 * O], BF16) for pr in range(PAIRS)]
+        x_codes = [kept("x_codes%d" % pr, [P, 3 * PAIR_ROWS], U32) for pr in range(PAIRS)]
+        x_plane = [kept("x_plane%d" % pr, [P, 3 * PAIR_ROWS], U8) for pr in range(PAIRS)]
+        wo_raw = {}
+        wo_laid = kept("wo_laid", [P, 4 * F], BF16)
+        h_early = [kept("h_early%d" % c, [P, 2 * 512], BF16) for c in range(CHUNKS)]
+        h_codes = [kept("h_codes%d" % c, [P, GROUPS * P], U32) for c in range(CHUNKS)]
+        h_plane = [kept("h_plane%d" % c, [P, GROUPS * P], U8) for c in range(CHUNKS)]
 
-        nc.vector.memset(ws[:].rearrange("p g n -> p (g n)").bitcast(I32), 0)
-        nc.vector.memset(dys[:].rearrange("p g n -> p (g n)").bitcast(I32), 0)
+        nc.vector.memset(w_plane[:].rearrange("p g n -> p (g n)").bitcast(I32), 0)
+        nc.vector.memset(dy_plane[:].rearrange("p g n -> p (g n)").bitcast(I32), 0)
         make_identity(nc, ident[:])
 
         x_v = x_bytes.rearrange("(g m t) k -> g m t k", m=P, t=4)
@@ -73,263 +79,266 @@ def tile_recomputed_hidden_weight_gradient_s3_kernel(
 
         def load_x(pr):
             g, h = divmod(pr, 2)
-            nc.sync.dma_start(out=xbytes[pr][:], in_=x_v[g][:, 2 * h : 2 * h + 2, :])
+            nc.sync.dma_start(out=x_raw[pr][:], in_=x_v[g][:, 2 * h : 2 * h + 2, :])
 
         def load_xo(pr):
             g, h = divmod(pr, 2)
             nc.sync.dma_start(
-                out=xor[pr][:].rearrange("p (t k) -> p t k", t=2),
+                out=xo_raw[pr][:].rearrange("p (t k) -> p t k", t=2),
                 in_=xo_v[g][:, 2 * h : 2 * h + 2, :],
             )
 
         def load_wo(q0, q1):
-            rows_in = kept("wor%d" % q0, [P, 4, 256 * (q1 - q0)], BF16)
-            nc.sync.dma_start(out=rows_in[:], in_=wo_v[:, :, 256 * q0 : 256 * q1])
+            rows_in = kept("wo_raw%d" % q0, [P, 4, QUARTER * (q1 - q0)], BF16)
+            nc.sync.dma_start(out=rows_in[:], in_=wo_v[:, :, QUARTER * q0 : QUARTER * q1])
             for q in range(q0, q1):
-                wor[q] = rows_in[:, :, 256 * (q - q0) : 256 * (q - q0) + 256]
+                wo_raw[q] = rows_in[:, :, QUARTER * (q - q0) : QUARTER * (q - q0 + 1)]
 
         def load_w(hf):
             nc.sync.dma_start(
-                out=wt[hf][:], in_=w_words.rearrange("g p n -> p g n")[:, :, F * hf : F * hf + F]
+                out=w_codes[hf][:],
+                in_=w_words.rearrange("g p n -> p g n")[:, :, F * hf : F * hf + F],
             )
 
-        def load_scales(dst, src):
+        def load_scale_bytes(dst, src):
             for r in range(4):
                 nc.sync.dma_start(
                     out=dst[r:P:32, :, :].bitcast(I32),
                     in_=src.rearrange("g (q r) n -> r q g n", r=4)[r].bitcast(I32),
                 )
 
-        def load_sc():
-            nc.sync.dma_start(
-                out=sc[:], in_=x_scale.rearrange("o (g p t) -> p (o g) t", p=P, t=4)
+        x_rows, x_sorted, xo_sorted, x_laid, turned = {}, {}, {}, {}, {}
+
+        def rows_of(pr):
+            if pr not in x_rows:
+                x_rows[pr] = ring.tile([P, 2 * K], BF16, name="x_rows", align_bytes=64)
+            return x_rows[pr]
+
+        def laid_of(pr):
+            if pr not in x_laid:
+                x_laid[pr] = ring.tile([P, 3 * 4 * PAIR_ROWS], BF16, name="x_laid", align_bytes=64)
+            return x_laid[pr]
+
+        def widen(copy, pr, tl, k0, k1):
+            copy(
+                out=rows_of(pr)[:, K * tl + k0 : K * tl + k1],
+                in_=x_raw[pr][:, tl, k0:k1].bitcast(FP8),
             )
 
-        def load_gate():
-            nc.sync.dma_start(out=gt[:], in_=gate.rearrange("(g m t) -> m g t", m=P, t=4))
-
-        def load_dy():
-            load_scales(dys, dy_scales)
-            nc.sync.dma_start(out=dyt[:], in_=dy_words.rearrange("g p n -> p g n"))
-
-        xb, xp, xop, xg, turned = {}, {}, {}, {}, {}
-
-        def rows(pr):
-            if pr not in xb:
-                xb[pr] = ring.tile([P, 2 * K], BF16, name="xb", align_bytes=64)
-            return xb[pr]
-
-        def grouped(pr):
-            if pr not in xg:
-                xg[pr] = ring.tile([P, 3 * 1024], BF16, name="xg", align_bytes=64)
-            return xg[pr]
-
-        def widen(copy, pr, t, k0, k1):
-            copy(out=rows(pr)[:, K * t + k0 : K * t + k1], in_=xbytes[pr][:, t, k0:k1].bitcast(FP8))
-
-        def spread(g, b):
+        def spread(kk, b):
             ps = bank(b)
-            for t in range(4):
+            for e in range(4):
                 nc.tensor.transpose(
-                    ps[:, P * t : P * t + P], sc[:, g, t : t + 1].to_broadcast([P, P]), ident[:]
+                    ps[:, P * e : P * e + P],
+                    scale_by_k[:, kk, e : e + 1].to_broadcast([P, P]),
+                    ident[:],
                 )
             return ps
 
-        def spread_out(g, ps):
+        def spread_out(kk, ps):
             nc.scalar.copy(
-                out=scb[:, 512 * g : 512 * g + 512].rearrange("p (n t) -> p n t", t=4),
-                in_=ps[:].rearrange("p (t n) -> p n t", t=4),
+                out=scale_rows[:, 512 * kk : 512 * kk + 512].rearrange("p (n e) -> p n e", e=4),
+                in_=ps[:].rearrange("p (e n) -> p n e", e=4),
             )
 
-        def mul(pr, t):
+        def scale_bytes(pr, tl):
             nc.vector.tensor_tensor(
-                out=rows(pr)[:, K * t : K * t + K],
-                in0=xbytes[pr][:, t, :].bitcast(FP8),
-                in1=scb[:],
+                out=rows_of(pr)[:, K * tl : K * tl + K],
+                in0=x_raw[pr][:, tl, :].bitcast(FP8),
+                in1=scale_rows[:],
                 op=MULT,
             )
 
-        def sort_x(pr, t0, t1, copy=nc.scalar.copy):
-            words = ring.tile([P, 512 * (t1 - t0)], F32, name="xp", align_bytes=64)
+        def sort_x(copy, pr, tl0, tl1):
+            words = ring.tile([P, 512 * (tl1 - tl0)], F32, name="x_sorted", align_bytes=64)
             copy(
                 out=words[:].rearrange("p (g u m) -> p g u m", u=2, m=P),
-                in_=xb[pr][:].bitcast(F32)[:, 512 * t0 : 512 * t1].rearrange(
-                    "p (g m u) -> p g u m", u=2, m=P
-                ),
+                in_=x_rows[pr][:]
+                .bitcast(F32)[:, 512 * tl0 : 512 * tl1]
+                .rearrange("p (g m u) -> p g u m", u=2, m=P),
             )
-            for t in range(t0, t1):
-                xp[pr, t] = words[:, 512 * (t - t0) : 512 * (t - t0) + 512]
+            for tl in range(tl0, tl1):
+                x_sorted[pr, tl] = words[:, 512 * (tl - tl0) : 512 * (tl - tl0) + 512]
 
-        def sort_xo(pr, copy=nc.scalar.copy):
-            xop[pr] = ring.tile([P, O], F32, name="xop", align_bytes=64)
+        def sort_xo(copy, pr):
+            xo_sorted[pr] = ring.tile([P, O], F32, name="xo_sorted", align_bytes=64)
             copy(
-                out=xop[pr][:].rearrange("p (t u m) -> p t u m", t=2, u=2),
-                in_=xor[pr][:].bitcast(F32).rearrange("p (t m u) -> p t u m", t=2, u=2),
+                out=xo_sorted[pr][:].rearrange("p (t u m) -> p t u m", t=2, u=2),
+                in_=xo_raw[pr][:].bitcast(F32).rearrange("p (t m u) -> p t u m", t=2, u=2),
             )
 
         def turn(pr, kk):
             ps = bank(kk)
-            for t in range(2):
-                if kk < 2:
-                    is_sorted = (pr, t) in xp
-                    c0 = 256 * kk if is_sorted else 512 * t + 256 * kk
-                    words = xp[pr, t] if is_sorted else xb[pr][:].bitcast(F32)
+            for tl in range(2):
+                if kk != XO_PASS:
+                    is_sorted = (pr, tl) in x_sorted
+                    c0 = 256 * kk if is_sorted else 512 * tl + 256 * kk
+                    words = x_sorted[pr, tl] if is_sorted else x_rows[pr][:].bitcast(F32)
                 else:
-                    is_sorted = pr in xop
-                    c0 = 256 * t
-                    words = xop[pr][:] if is_sorted else xor[pr][:].bitcast(F32)
+                    is_sorted = pr in xo_sorted
+                    c0 = 256 * tl
+                    words = xo_sorted[pr][:] if is_sorted else xo_raw[pr][:].bitcast(F32)
                 for u in range(2):
                     if is_sorted:
                         src = words[:, c0 + P * u : c0 + P * u + P]
                     else:
                         src = words[:, c0 + u : c0 + 256 : 2]
-                    nc.tensor.transpose(ps[:, 256 * u + P * t : 256 * u + P * t + P], src, ident[:])
+                    o0 = PAIR_ROWS * u + P * tl
+                    nc.tensor.transpose(ps[:, o0 : o0 + P], src, ident[:])
             turned[pr, kk] = ps
 
-        def turn_out(pr, kk, copy=nc.scalar.copy):
-            copy(
-                out=grouped(pr)[:, 1024 * kk : 1024 * kk + 1024]
+        def turn_out(pr, kk):
+            nc.scalar.copy(
+                out=laid_of(pr)[:, 1024 * kk : 1024 * kk + 1024]
                 .bitcast(F32)
                 .rearrange("p (r u) -> p r u", u=2),
                 in_=turned[pr, kk][:].rearrange("p (u r) -> p r u", u=2),
             )
 
-        def prod(pr, kk, r0=0, r1=256):
+        def scale_turned(pr, kk, r0=0, r1=PAIR_ROWS):
             nc.vector.tensor_tensor(
-                out=grouped(pr)[:, 1024 * kk + 4 * r0 : 1024 * kk + 4 * r1].rearrange(
+                out=laid_of(pr)[:, 1024 * kk + 4 * r0 : 1024 * kk + 4 * r1].rearrange(
                     "p (r u e) -> p r u e", u=2, e=2
                 ),
                 in0=turned[pr, kk][:]
                 .bitcast(BF16)
                 .rearrange("p (u r e) -> p r u e", u=2, e=2)[:, r0:r1, :, :],
-                in1=sc[:, kk, :]
+                in1=scale_by_k[:, kk, :]
                 .rearrange("p (u e) -> p u e", e=2)
                 .unsqueeze(1)
                 .to_broadcast([P, r1 - r0, 2, 2]),
                 op=MULT,
             )
 
-        def quant_x(pr, k0, k1):
+        def quantise(codes, plane, laid, w0, w1):
             nc.vector.quantize_mx(
-                out=xq[pr][:, 256 * k0 : 256 * k1].bitcast(FP8X4),
-                scales=xs[pr][:, 256 * k0 : 256 * k1],
-                in_=xg[pr][:, 1024 * k0 : 1024 * k1],
+                out=codes[:, w0:w1].bitcast(FP8X4), scales=plane[:, w0:w1], in_=laid
             )
+
+        def quant_x(pr, kk0, kk1):
+            w0, w1 = PAIR_ROWS * kk0, PAIR_ROWS * kk1
+            quantise(x_codes[pr], x_plane[pr], x_laid[pr][:, 4 * w0 : 4 * w1], w0, w1)
 
         def quant_slot(pr, kk, tl):
-            w0 = 256 * kk + P * tl
-            nc.vector.quantize_mx(
-                out=xq[pr][:, w0 : w0 + P].bitcast(FP8X4),
-                scales=xs[pr][:, w0 : w0 + P],
-                in_=xg[pr][:, 4 * w0 : 4 * w0 + 4 * P],
-            )
+            w0 = PAIR_ROWS * kk + P * tl
+            quantise(x_codes[pr], x_plane[pr], x_laid[pr][:, 4 * w0 : 4 * w0 + 4 * P], w0, w0 + P)
 
-        def wo_lay(copy, q):
+        def lay_wo(copy, q):
             copy(
-                out=wog[:, 1024 * q : 1024 * q + 1024].rearrange("p (c i t) -> p c t i", i=4, t=4),
-                in_=wor[q].rearrange("p t (c i) -> p c t i", i=4),
+                out=wo_laid[:, 4 * QUARTER * q : 4 * QUARTER * (q + 1)].rearrange(
+                    "p (c i e) -> p c e i", i=4, e=4
+                ),
+                in_=wo_raw[q].rearrange("p e (c i) -> p c e i", i=4),
             )
 
         def quant_wo(q0, q1):
-            cols = slice(256 * q0, 256 * q1)
-            nc.vector.quantize_mx(
-                out=woq[:, cols].bitcast(FP8X4), scales=wos[:, cols], in_=wog[:, 1024 * q0 : 1024 * q1]
-            )
+            w0, w1 = QUARTER * q0, QUARTER * q1
+            quantise(wo_codes, wo_plane, wo_laid[:, 4 * w0 : 4 * w1], w0, w1)
 
-        hps = {}
+        def warm_up():
+            ps = bank(TURN_BANKS + 2)
+            for j in range(WARM_UPS):
+                nc.tensor.matmul(
+                    ps[:], lhsT=xo_raw[0][:, 0:P], rhs=xo_raw[0][:, 0:BANK], start=True, stop=True
+                )
 
-        def wide(g, hf, t, passes=(0, 2, 1), last=1):
-            if (g, hf, t) not in hps:
-                hps[g, hf, t] = bank(TURN_BANKS + len(hps) % H_BANKS)
+        sums, planes, h_late = {}, {}, {}
+
+        def unit(g, hf, t, passes=(0, XO_PASS, 1), last=1):
+            if (g, hf, t) not in sums:
+                sums[g, hf, t] = bank(TURN_BANKS + len(sums) % UNIT_BANKS)
             pr, tl = 2 * g + t // 2, t % 2
-            cols = slice(512 * hf, 512 * hf + 512)
+            cols = slice(BANK * hf, BANK * hf + BANK)
             for kk in passes:
-                r = slice(256 * kk + P * tl, 256 * kk + P * tl + P)
+                r = slice(PAIR_ROWS * kk + P * tl, PAIR_ROWS * kk + P * tl + P)
+                if kk == XO_PASS:
+                    rhs, rhs_scale = wo_codes[:, cols].bitcast(FP8X4), wo_plane[:, cols]
+                else:
+                    rhs, rhs_scale = w_codes[hf][:, kk, :].bitcast(FP4X4), w_plane[:, kk, cols]
                 nc.tensor.matmul_mx(
-                    out=hps[g, hf, t][:],
-                    lhsT=xq[pr][:, r].bitcast(FP8X4),
-                    lhsT_scale=xs[pr][:, r],
-                    rhs=wt[hf][:, kk, :].bitcast(FP4X4) if kk < 2 else woq[:, cols].bitcast(FP8X4),
-                    rhs_scale=ws[:, kk, cols] if kk < 2 else wos[:, cols],
+                    out=sums[g, hf, t][:],
+                    lhsT=x_codes[pr][:, r].bitcast(FP8X4),
+                    lhsT_scale=x_plane[pr][:, r],
+                    rhs=rhs,
+                    rhs_scale=rhs_scale,
                     start=(kk == 0),
                     stop=(kk == last),
                 )
 
-        hg2, planes = {}, {}
-
         def split_gate():
-            flat = gt[:].rearrange("p g t -> p (g t)")
-            nc.scalar.activation(out=g_abs[:], in_=flat, func=ACT.Abs)
-            nc.scalar.activation(out=g_sign[:], in_=flat, func=ACT.Sign)
+            flat = gates[:].rearrange("p g t -> p (g t)")
+            nc.scalar.activation(out=gate_abs[:], in_=flat, func=ACT.Abs)
+            nc.scalar.activation(out=gate_sign[:], in_=flat, func=ACT.Sign)
 
-        def park(g, hf, t):
+        def empty(g, hf, t):
             if (g, hf) not in planes:
-                planes[g, hf] = kept("planes%d_%d" % (g, hf), [P, 4 * 512], BF16)
+                planes[g, hf] = kept("planes%d_%d" % (g, hf), [P, 4 * BANK], BF16)
             nc.scalar.activation(
-                out=planes[g, hf][:, 512 * t : 512 * t + 512],
-                in_=hps[g, hf, t][:],
+                out=planes[g, hf][:, BANK * t : BANK * t + BANK],
+                in_=sums[g, hf, t][:],
                 func=ACT.Relu,
-                scale=g_abs[:, 4 * g + t : 4 * g + t + 1],
+                scale=gate_abs[:, 4 * g + t : 4 * g + t + 1],
             )
 
         def sign(g, hf, t):
-            plane = planes[g, hf][:, 512 * t : 512 * t + 512]
+            plane = planes[g, hf][:, BANK * t : BANK * t + BANK]
             nc.vector.tensor_scalar(
                 out=plane,
                 in0=plane,
-                scalar1=g_sign[:, 4 * g + t : 4 * g + t + 1],
+                scalar1=gate_sign[:, 4 * g + t : 4 * g + t + 1],
                 scalar2=None,
                 op0=MULT,
             )
 
-        def h_rows(g, c):
-            if g < 2:
-                return hg01[c][:, 512 * g : 512 * g + 512]
-            hg2[c] = ring.tile([P, 512], BF16, name="hg2", align_bytes=64)
-            return hg2[c][:]
-
         def weave(g, c):
-            hf, f0 = divmod(P * c, 512)
+            if g < 2:
+                dst = h_early[c][:, 512 * g : 512 * g + 512]
+            else:
+                h_late[c] = ring.tile([P, 512], BF16, name="h_late", align_bytes=64)
+                dst = h_late[c][:]
+            hf, f0 = divmod(P * c, BANK)
             nc.vector.tensor_copy(
-                out=h_rows(g, c).rearrange("p (c i t) -> p c t i", i=4, t=4),
+                out=dst.rearrange("p (c i t) -> p c t i", i=4, t=4),
                 in_=planes[g, hf][:]
                 .rearrange("p (t f) -> p t f", t=4)[:, :, f0 : f0 + P]
                 .rearrange("p t (c i) -> p c t i", i=4),
             )
 
-        def quant_h01(c):
-            nc.vector.quantize_mx(
-                out=hq[c][:, 0 : 2 * P].bitcast(FP8X4), scales=hs[c][:, 0 : 2 * P], in_=hg01[c][:]
-            )
+        def quant_early(c):
+            quantise(h_codes[c], h_plane[c], h_early[c][:], 0, 2 * P)
 
-        def quant_h2(c):
-            nc.vector.quantize_mx(
-                out=hq[c][:, 2 * P :].bitcast(FP8X4), scales=hs[c][:, 2 * P :], in_=hg2[c][:]
-            )
+        def quant_late(c):
+            quantise(h_codes[c], h_plane[c], h_late[c][:], 2 * P, 3 * P)
 
-        def stage2(m, b, n0, width):
-            acc = bank(b)
-            step = 512 if width == 512 else P
-            for j in range(0, width, step):
-                for g in range(G):
+        pieces = []
+
+        def gradient(c, width):
+            step = BANK if width == BANK else P
+            for n0 in range(0, N, width):
+                acc = bank(len(pieces) % (TURN_BANKS + UNIT_BANKS))
+                pieces.append(acc)
+                for j in range(0, width, step):
                     n1 = n0 + j
-                    nc.tensor.matmul_mx(
-                        out=acc[:, j : j + step],
-                        lhsT=hq[m][:, P * g : P * g + P].bitcast(FP8X4),
-                        lhsT_scale=hs[m][:, P * g : P * g + P],
-                        rhs=dyt[:, g, 2 * n1 : 2 * n1 + 2 * step].bitcast(FP4X4),
-                        rhs_scale=dys[:, g, n1 : n1 + step],
-                        start=(g == 0),
-                        stop=(g == G - 1),
-                    )
-            return acc
+                    for g in range(GROUPS):
+                        nc.tensor.matmul_mx(
+                            out=acc[:, j : j + step],
+                            lhsT=h_codes[c][:, P * g : P * g + P].bitcast(FP8X4),
+                            lhsT_scale=h_plane[c][:, P * g : P * g + P],
+                            rhs=dy_codes[:, g, 2 * n1 : 2 * n1 + 2 * step].bitcast(FP4X4),
+                            rhs_scale=dy_plane[:, g, n1 : n1 + step],
+                            start=(g == 0),
+                            stop=(g == GROUPS - 1),
+                        )
+                copy = on_vector if width < BANK and (n0 // width) % 2 else on_scalar
+                result = ring.tile([P, BANK], F32, name="result", align_bytes=64, bufs=6)
+                copy(out=result[:, 0:width], in_=acc[:, 0:width])
+                nc.sync.dma_start(
+                    out=out[P * c : P * c + P, n0 : n0 + width], in_=result[:, 0:width]
+                )
 
-        def store(copy, m, acc, n0, width):
-            ot = ring.tile([P, 512], F32, name="ot", align_bytes=64, bufs=6)
-            copy(out=ot[:, 0:width], in_=acc[:, 0:width])
-            nc.sync.dma_start(out=out[P * m : P * m + P, n0 : n0 + width], in_=ot[:, 0:width])
-
-        load_sc()
+        nc.sync.dma_start(
+            out=scale_by_k[:], in_=x_scale.rearrange("o (g p t) -> p (o g) t", p=P, t=4)
+        )
         load_x(0)
         load_wo(0, 1)
         load_x(1)
@@ -337,204 +346,192 @@ def tile_recomputed_hidden_weight_gradient_s3_kernel(
         load_wo(1, 3)
         load_xo(1)
         load_w(0)
-        load_scales(ws, w_scales)
-        load_gate()
+        load_scale_bytes(w_plane, w_scales)
+        nc.sync.dma_start(out=gates[:], in_=gate.rearrange("(g m t) -> m g t", m=P, t=4))
         load_wo(3, 4)
         load_x(2)
         load_w(1)
         load_xo(2)
-        load_x(3)
-        load_xo(3)
-        load_x(4)
-        load_xo(4)
-        load_x(5)
-        load_xo(5)
-        load_dy()
+        for pr in range(3, PAIRS):
+            load_x(pr)
+            load_xo(pr)
+        load_scale_bytes(dy_plane, dy_scales)
+        nc.sync.dma_start(out=dy_codes[:], in_=dy_words.rearrange("g p n -> p g n"))
 
-        spread_ps = [spread(g, TURN_BANKS + g) for g in range(2)]
-        widen(nc.vector.tensor_copy, 0, 0, 0, K)
-        widen(nc.scalar.copy, 0, 1, 0, 512)
-        widen(nc.vector.tensor_copy, 0, 1, 512, K)
+        spread_banks = [spread(kk, TURN_BANKS + kk) for kk in range(2)]
+        widen(on_vector, 0, 0, 0, K)
+        widen(on_scalar, 0, 1, 0, 512)
+        widen(on_vector, 0, 1, 512, K)
         turn(0, 0)
         turn(0, 1)
-        for g in range(2):
-            spread_out(g, spread_ps[g])
-        wo_lay(nc.vector.tensor_copy, 0)
-        prod(0, 0)
-        for t in range(2):
-            widen(nc.scalar.copy, 1, t, 0, 512)
-        turn(0, 2)
-        widen(nc.scalar.copy, 1, 0, 512, K)
-        turn_out(0, 2)
+        for kk in range(2):
+            spread_out(kk, spread_banks[kk])
+        lay_wo(on_vector, 0)
+        scale_turned(0, 0)
+        for tl in range(2):
+            widen(on_scalar, 1, tl, 0, 512)
+        turn(0, XO_PASS)
+        widen(on_scalar, 1, 0, 512, K)
+        turn_out(0, XO_PASS)
         quant_wo(0, 1)
-        prod(0, 1)
+        scale_turned(0, 1)
         turn(1, 0)
-        widen(nc.scalar.copy, 1, 1, 512, K)
-        quant_x(0, 2, 3)
+        warm_up()
+        widen(on_scalar, 1, 1, 512, K)
+        quant_x(0, XO_PASS, XO_PASS + 1)
         quant_x(0, 0, 2)
-        turn(1, 2)
+        turn(1, XO_PASS)
         turn(1, 1)
-        wo_lay(nc.scalar.copy, 1)
-        turn_out(1, 2)
-        prod(1, 0)
+        lay_wo(on_scalar, 1)
+        turn_out(1, XO_PASS)
+        scale_turned(1, 0)
+
         for t in range(2):
-            wide(0, 0, t, (0, 1), 2)
+            unit(0, 0, t, (0, 1), XO_PASS)
         quant_wo(1, 2)
         quant_x(1, 0, 1)
-        quant_x(1, 2, 3)
+        quant_x(1, XO_PASS, XO_PASS + 1)
         for t in range(2):
-            wide(0, 0, t, (2,), 2)
+            unit(0, 0, t, (XO_PASS,), XO_PASS)
         for t in range(2, 4):
-            wide(0, 0, t, (0, 2))
+            unit(0, 0, t, (0, XO_PASS))
         split_gate()
-        wo_lay(nc.scalar.copy, 2)
-        park(0, 0, 0)
-        park(0, 0, 1)
-        wo_lay(nc.scalar.copy, 3)
-        sort_xo(2)
+        lay_wo(on_scalar, 2)
+        empty(0, 0, 0)
+        empty(0, 0, 1)
+        lay_wo(on_scalar, 3)
+        sort_xo(on_scalar, 2)
         for tl in range(2):
-            prod(1, 1, P * tl, P * tl + P)
-        quant_slot(1, 1, 0)
-        quant_slot(1, 1, 1)
+            scale_turned(1, 1, P * tl, P * tl + P)
+        for tl in range(2):
+            quant_slot(1, 1, tl)
         for t in range(2, 4):
-            wide(0, 0, t, (1,))
+            unit(0, 0, t, (1,))
 
-        def prepare(pr, t):
-            mul(pr, t)
-            sort_x(pr, t, t + 1)
-
-        def turn_all(pr):
-            for kk in (2, 0, 1):
+        def turn_pair(pr):
+            for kk in (XO_PASS, 0, 1):
                 turn(pr, kk)
 
-        def out_all(pr):
-            for kk in (2, 0, 1):
+        def turn_pair_out(pr):
+            for kk in (XO_PASS, 0, 1):
                 turn_out(pr, kk)
 
-        def quant_all(pr):
-            for kk in (2, 0, 1):
-                quant_x(pr, kk, kk + 1)
-
         def sort_pair(pr):
-            sort_xo(pr, nc.vector.tensor_copy)
-            sort_x(pr, 0, 2, nc.vector.tensor_copy)
+            sort_xo(on_vector, pr)
+            sort_x(on_vector, pr, 0, 2)
 
-        prepare(2, 0)
-        mul(2, 1)
+        scale_bytes(2, 0)
+        sort_x(on_scalar, 2, 0, 1)
+        scale_bytes(2, 1)
         quant_wo(2, 4)
         for t in range(3):
-            wide(0, 1, t, (0, 1), 2)
-        turn_all(2)
-
-        park(0, 0, 2)
-        out_all(2)
+            unit(0, 1, t, (0, 1), XO_PASS)
+        turn_pair(2)
+        empty(0, 0, 2)
+        turn_pair_out(2)
         for t in range(3):
-            wide(0, 1, t, (2,), 2)
-        for t in range(3, 4):
-            wide(0, 1, t)
-        mul(3, 0)
-        quant_x(2, 2, 3)
-        quant_x(2, 0, 1)
-        sort_xo(3, nc.vector.tensor_copy)
-        sort_x(3, 0, 1, nc.vector.tensor_copy)
-        quant_x(2, 1, 2)
-        mul(3, 1)
-        park(0, 0, 3)
-        wide(1, 1, 0)
-        park(0, 1, 0)
-        park(0, 1, 1)
-        park(0, 1, 2)
-        turn_all(3)
-        out_all(3)
-        wide(1, 1, 1)
-        wide(1, 0, 0)
-        wide(1, 0, 1)
-        mul(4, 0)
-        mul(4, 1)
-        quant_x(3, 2, 3)
-        quant_x(3, 0, 2)
+            unit(0, 1, t, (XO_PASS,), XO_PASS)
+        unit(0, 1, 3)
+
+        for tl in range(2):
+            scale_bytes(3, tl)
+        for kk in (0, XO_PASS, 1):
+            quant_x(2, kk, kk + 1)
+        sort_x(on_vector, 3, 0, 2)
+        empty(0, 0, 3)
+        sort_xo(on_scalar, 3)
+        unit(1, 1, 0)
+        empty(0, 1, 0)
+        empty(0, 1, 1)
+        turn_pair(3)
+        turn_out(3, XO_PASS)
+        turn_out(3, 0)
+        empty(0, 1, 2)
+        turn_out(3, 1)
+        unit(1, 1, 1)
+        unit(1, 0, 0)
+        unit(1, 0, 1)
+
+        for tl in range(2):
+            scale_bytes(4, tl)
+        quant_x(3, XO_PASS, XO_PASS + 1)
+        quant_x(3, 0, 1)
         sort_pair(4)
-        park(0, 1, 3)
-        wide(1, 1, 2)
-        park(1, 1, 0)
-        park(1, 1, 1)
-        turn_all(4)
-        park(1, 0, 0)
-        out_all(4)
-        wide(1, 1, 3)
-        wide(1, 0, 2)
-        mul(5, 0)
-        mul(5, 1)
+        quant_x(3, 1, 2)
+        empty(0, 1, 3)
+        unit(1, 1, 2)
+        empty(1, 1, 0)
+        empty(1, 1, 1)
+        turn_pair(4)
+        empty(1, 0, 0)
+        turn_pair_out(4)
+        unit(1, 1, 3)
+        unit(1, 0, 2)
+
+        for tl in range(2):
+            scale_bytes(5, tl)
         sort_pair(5)
-        turn_all(5)
-        park(1, 0, 1)
-        park(1, 1, 2)
-        out_all(5)
-        quant_x(4, 2, 3)
+        turn_pair(5)
+        empty(1, 0, 1)
+        empty(1, 1, 2)
+        turn_pair_out(5)
+        quant_x(4, XO_PASS, XO_PASS + 1)
         quant_x(4, 0, 2)
-        wide(1, 0, 3)
+        unit(1, 0, 3)
+
         for t in range(4):
             sign(0, 1, t)
         weave(0, 4)
-        wide(2, 1, 0)
-        park(1, 1, 3)
-        wide(2, 1, 1)
-        quant_all(5)
-        park(1, 0, 2)
-        park(1, 0, 3)
+        unit(2, 1, 0)
+        empty(1, 1, 3)
+        unit(2, 1, 1)
+        for kk in (XO_PASS, 0, 1):
+            quant_x(5, kk, kk + 1)
+        empty(1, 0, 2)
+        empty(1, 0, 3)
         for t in range(4):
             sign(1, 1, t)
+        for t in range(2):
+            empty(2, 1, t)
+        for hf, t in [(1, 2), (1, 3)] + [(0, t) for t in range(4)]:
+            unit(2, hf, t)
+            empty(2, hf, t)
 
-        out_banks = []
-
-        def product(m, widths):
-            n0 = 0
-            for j, width in enumerate(widths):
-                b = len(out_banks) % (TURN_BANKS + H_BANKS)
-                out_banks.append(b)
-                acc = stage2(m, b, n0, width)
-                copy = nc.vector.tensor_copy if len(widths) > 2 and j % 2 else nc.scalar.copy
-                store(copy, m, acc, n0, width)
-                n0 += width
-
-        for hf in (1, 0):
-            for t in range(4):
-                if (2, hf, t) not in hps:
-                    wide(2, hf, t)
-                park(2, hf, t)
         weave(1, 4)
         weave(0, 5)
         weave(1, 5)
-        quant_h01(4)
+        quant_early(4)
         sign(2, 1, 0)
         sign(2, 1, 1)
         weave(0, 6)
         sign(2, 1, 2)
-        quant_h01(5)
+        quant_early(5)
         sign(2, 1, 3)
         weave(1, 6)
         weave(2, 4)
         weave(2, 5)
-        quant_h2(4)
-        product(4, (512, 512))
+        quant_late(4)
+        gradient(4, BANK)
         weave(2, 6)
-        quant_h2(5)
-        product(5, (512, 512))
-        quant_h01(6)
-        quant_h2(6)
-        product(6, (512, 512))
-        for g in range(G):
+        quant_late(5)
+        gradient(5, BANK)
+        quant_early(6)
+        quant_late(6)
+        gradient(6, BANK)
+        for g in range(GROUPS):
             weave(g, 7)
-        quant_h01(7)
-        quant_h2(7)
-        product(7, (512, 512))
-        for g in range(G):
+        quant_early(7)
+        quant_late(7)
+        gradient(7, BANK)
+
+        for g in range(GROUPS):
             for t in range(4):
                 sign(g, 0, t)
         for c in range(4):
-            for g in range(G):
+            for g in range(GROUPS):
                 weave(g, c)
-            quant_h01(c)
-            quant_h2(c)
-        for c in range(4):
-            product(c, (256, 256, 256, 256) if c == 3 else (512, 512))
+            quant_early(c)
+            quant_late(c)
+        for c in range(3):
+            gradient(c, BANK)
+        gradient(3, N // 4)

@@ -25,6 +25,7 @@ PAIR_ROWS = 2 * P
 QUARTER = F // 4
 CHUNKS = F // P
 XO_PASS = 2
+PLACE = {0: 0, XO_PASS: 1, 1: 2}
 TURN_BANKS = 3
 UNIT_BANKS = 5
 WARM_UPS = 2
@@ -167,8 +168,8 @@ def tile_recomputed_hidden_weight_gradient_s3_kernel(
                 in_=xo_raw[pr][:].bitcast(F32).rearrange("p (t m u) -> p t u m", t=2, u=2),
             )
 
-        def turn(pr, kk):
-            ps = bank(kk)
+        def turn(pr, kk, b=None):
+            ps = bank(kk if b is None else b)
             for tl in range(2):
                 if kk != XO_PASS:
                     is_sorted = (pr, tl) in x_sorted
@@ -189,15 +190,16 @@ def tile_recomputed_hidden_weight_gradient_s3_kernel(
 
         def turn_out(pr, kk):
             nc.scalar.copy(
-                out=laid_of(pr)[:, 1024 * kk : 1024 * kk + 1024]
+                out=laid_of(pr)[:, 1024 * PLACE[kk] : 1024 * PLACE[kk] + 1024]
                 .bitcast(F32)
                 .rearrange("p (r u) -> p r u", u=2),
                 in_=turned[pr, kk][:].rearrange("p (u r) -> p r u", u=2),
             )
 
         def scale_turned(pr, kk, r0=0, r1=PAIR_ROWS):
+            c0 = 1024 * PLACE[kk]
             nc.vector.tensor_tensor(
-                out=laid_of(pr)[:, 1024 * kk + 4 * r0 : 1024 * kk + 4 * r1].rearrange(
+                out=laid_of(pr)[:, c0 + 4 * r0 : c0 + 4 * r1].rearrange(
                     "p (r u e) -> p r u e", u=2, e=2
                 ),
                 in0=turned[pr, kk][:]
@@ -215,12 +217,12 @@ def tile_recomputed_hidden_weight_gradient_s3_kernel(
                 out=codes[:, w0:w1].bitcast(FP8X4), scales=plane[:, w0:w1], in_=laid
             )
 
-        def quant_x(pr, kk0, kk1):
-            w0, w1 = PAIR_ROWS * kk0, PAIR_ROWS * kk1
+        def quant_x(pr, *passes):
+            w0, w1 = PAIR_ROWS * PLACE[passes[0]], PAIR_ROWS * (PLACE[passes[-1]] + 1)
             quantise(x_codes[pr], x_plane[pr], x_laid[pr][:, 4 * w0 : 4 * w1], w0, w1)
 
         def quant_slot(pr, kk, tl):
-            w0 = PAIR_ROWS * kk + P * tl
+            w0 = PAIR_ROWS * PLACE[kk] + P * tl
             quantise(x_codes[pr], x_plane[pr], x_laid[pr][:, 4 * w0 : 4 * w0 + 4 * P], w0, w0 + P)
 
         def lay_wo(copy, q):
@@ -250,7 +252,8 @@ def tile_recomputed_hidden_weight_gradient_s3_kernel(
             pr, tl = 2 * g + t // 2, t % 2
             cols = slice(BANK * hf, BANK * hf + BANK)
             for kk in passes:
-                r = slice(PAIR_ROWS * kk + P * tl, PAIR_ROWS * kk + P * tl + P)
+                w0 = PAIR_ROWS * PLACE[kk] + P * tl
+                r = slice(w0, w0 + P)
                 if kk == XO_PASS:
                     rhs, rhs_scale = wo_codes[:, cols].bitcast(FP8X4), wo_plane[:, cols]
                 else:
@@ -343,8 +346,8 @@ def tile_recomputed_hidden_weight_gradient_s3_kernel(
         load_wo(0, 1)
         load_x(1)
         load_xo(0)
-        load_wo(1, 3)
         load_xo(1)
+        load_wo(1, 3)
         load_w(0)
         load_scale_bytes(w_plane, w_scales)
         nc.sync.dma_start(out=gates[:], in_=gate.rearrange("(g m t) -> m g t", m=P, t=4))
@@ -371,6 +374,7 @@ def tile_recomputed_hidden_weight_gradient_s3_kernel(
         for tl in range(2):
             widen(on_scalar, 1, tl, 0, 512)
         turn(0, XO_PASS)
+        turn(1, XO_PASS, TURN_BANKS + UNIT_BANKS - 1)
         widen(on_scalar, 1, 0, 512, K)
         turn_out(0, XO_PASS)
         quant_wo(0, 1)
@@ -378,9 +382,8 @@ def tile_recomputed_hidden_weight_gradient_s3_kernel(
         turn(1, 0)
         warm_up()
         widen(on_scalar, 1, 1, 512, K)
-        quant_x(0, XO_PASS, XO_PASS + 1)
-        quant_x(0, 0, 2)
-        turn(1, XO_PASS)
+        quant_x(0, 0, XO_PASS)
+        quant_x(0, 1)
         turn(1, 1)
         lay_wo(on_scalar, 1)
         turn_out(1, XO_PASS)
@@ -389,8 +392,7 @@ def tile_recomputed_hidden_weight_gradient_s3_kernel(
         for t in range(2):
             unit(0, 0, t, (0, 1), XO_PASS)
         quant_wo(1, 2)
-        quant_x(1, 0, 1)
-        quant_x(1, XO_PASS, XO_PASS + 1)
+        quant_x(1, 0, XO_PASS)
         for t in range(2):
             unit(0, 0, t, (XO_PASS,), XO_PASS)
         for t in range(2, 4):
@@ -436,7 +438,7 @@ def tile_recomputed_hidden_weight_gradient_s3_kernel(
         for tl in range(2):
             scale_bytes(3, tl)
         for kk in (0, XO_PASS, 1):
-            quant_x(2, kk, kk + 1)
+            quant_x(2, kk)
         sort_x(on_vector, 3, 0, 2)
         empty(0, 0, 3)
         sort_xo(on_scalar, 3)
@@ -454,10 +456,9 @@ def tile_recomputed_hidden_weight_gradient_s3_kernel(
 
         for tl in range(2):
             scale_bytes(4, tl)
-        quant_x(3, XO_PASS, XO_PASS + 1)
-        quant_x(3, 0, 1)
+        quant_x(3, 0, XO_PASS)
         sort_pair(4)
-        quant_x(3, 1, 2)
+        quant_x(3, 1)
         empty(0, 1, 3)
         unit(1, 1, 2)
         empty(1, 1, 0)
@@ -475,8 +476,8 @@ def tile_recomputed_hidden_weight_gradient_s3_kernel(
         empty(1, 0, 1)
         empty(1, 1, 2)
         turn_pair_out(5)
-        quant_x(4, XO_PASS, XO_PASS + 1)
-        quant_x(4, 0, 2)
+        quant_x(4, 0, XO_PASS)
+        quant_x(4, 1)
         unit(1, 0, 3)
 
         for t in range(4):
@@ -485,8 +486,8 @@ def tile_recomputed_hidden_weight_gradient_s3_kernel(
         unit(2, 1, 0)
         empty(1, 1, 3)
         unit(2, 1, 1)
-        for kk in (XO_PASS, 0, 1):
-            quant_x(5, kk, kk + 1)
+        quant_x(5, 0, XO_PASS)
+        quant_x(5, 1)
         empty(1, 0, 2)
         empty(1, 0, 3)
         for t in range(4):

@@ -19,16 +19,13 @@ ACT = mybir.ActivationFunctionType
 
 P = 128
 BANK = 512
+BANKS = 8
 GROUPS = T // 512
-PAIRS = 2 * GROUPS
-PAIR_ROWS = 2 * P
+SLOTS = 4 * GROUPS
+PAIRS = SLOTS // 2
 QUARTER = F // 4
 CHUNKS = F // P
 XO_PASS = 2
-PLACE = {0: 0, XO_PASS: 1, 1: 2}
-TURN_BANKS = 3
-UNIT_BANKS = 5
-WARM_UPS = 2
 
 
 def tile_recomputed_hidden_weight_gradient_s3_kernel(
@@ -38,54 +35,57 @@ def tile_recomputed_hidden_weight_gradient_s3_kernel(
     on_vector, on_scalar = nc.vector.tensor_copy, nc.scalar.copy
     with ExitStack() as ctx:
         keep = ctx.enter_context(tc.tile_pool(name="keep", bufs=1))
-        ring = ctx.enter_context(tc.tile_pool(name="ring", bufs=3))
+        ring = ctx.enter_context(tc.tile_pool(name="ring", bufs=4))
         psum = ctx.enter_context(tc.psum_pool(name="psum", bufs=1))
         ctx.enter_context(tc.manual_schedule())
 
         def kept(name, shape, dtype):
             return keep.tile(shape, dtype, name=name, align_bytes=64)
 
+        def passing(name, shape, dtype, bufs=4):
+            return ring.tile(shape, dtype, name=name, align_bytes=64, bufs=bufs)
+
         def bank(b):
             return psum.tile([P, BANK], F32, name="bank%d" % b)
 
         ident = kept("ident", [P, P], F32)
+        ones = kept("ones", [P, 1], F32)
         w_codes = [kept("w_codes%d" % hf, [P, 2, F], U8) for hf in range(2)]
         w_plane = kept("w_plane", [P, 2, F], U8)
         dy_codes = kept("dy_codes", [P, GROUPS, 2 * N], U8)
         dy_plane = kept("dy_plane", [P, GROUPS, N], U8)
         scale_by_k = kept("scale_by_k", [P, 2, 4], F32)
-        scale_rows = kept("scale_rows", [P, K], F32)
-        gates = kept("gates", [P, GROUPS, 4], BF16)
-        gate_abs = kept("gate_abs", [P, GROUPS * 4], F32)
-        gate_sign = kept("gate_sign", [P, GROUPS * 4], F32)
+        gates = kept("gates", [P, SLOTS], BF16)
+        gate_abs = kept("gate_abs", [P, SLOTS], F32)
+        gate_sign = kept("gate_sign", [P, SLOTS], F32)
         wo_codes = kept("wo_codes", [P, F], U32)
         wo_plane = kept("wo_plane", [P, F], U8)
-        x_raw = [kept("x_raw%d" % pr, [P, 2, K], U8) for pr in range(PAIRS)]
-        xo_raw = [kept("xo_raw%d" % pr, [P, 2 * O], BF16) for pr in range(PAIRS)]
-        x_codes = [kept("x_codes%d" % pr, [P, 3 * PAIR_ROWS], U32) for pr in range(PAIRS)]
-        x_plane = [kept("x_plane%d" % pr, [P, 3 * PAIR_ROWS], U8) for pr in range(PAIRS)]
-        wo_raw = {}
         wo_laid = kept("wo_laid", [P, 4 * F], BF16)
+        x_codes = [kept("x_codes%d" % s, [P, 2 * P], U32) for s in range(SLOTS)]
+        x_plane = [kept("x_plane%d" % s, [P, 2 * P], U8) for s in range(SLOTS)]
+        xo_codes = [kept("xo_codes%d" % j, [P, 2 * P], U32) for j in range(PAIRS)]
+        xo_plane = [kept("xo_plane%d" % j, [P, 2 * P], U8) for j in range(PAIRS)]
         h_early = [kept("h_early%d" % c, [P, 2 * 512], BF16) for c in range(CHUNKS)]
         h_codes = [kept("h_codes%d" % c, [P, GROUPS * P], U32) for c in range(CHUNKS)]
         h_plane = [kept("h_plane%d" % c, [P, GROUPS * P], U8) for c in range(CHUNKS)]
 
-        nc.vector.memset(w_plane[:].rearrange("p g n -> p (g n)").bitcast(I32), 0)
-        nc.vector.memset(dy_plane[:].rearrange("p g n -> p (g n)").bitcast(I32), 0)
-        make_identity(nc, ident[:])
-
         x_v = x_bytes.rearrange("(g m t) k -> g m t k", m=P, t=4)
         xo_v = xo.rearrange("(g m t) k -> g m t k", m=P, t=4)
         wo_v = wo.rearrange("(p j) f -> p j f", j=4)
+        x_raw, xo_raw, wo_raw = {}, {}, {}
 
-        def load_x(pr):
-            g, h = divmod(pr, 2)
-            nc.sync.dma_start(out=x_raw[pr][:], in_=x_v[g][:, 2 * h : 2 * h + 2, :])
+        def load_x(s0, s1):
+            g, t0 = divmod(s0, 4)
+            rows_in = kept("x_raw%d" % s0, [P, s1 - s0, K], U8)
+            nc.sync.dma_start(out=rows_in[:], in_=x_v[g][:, t0 : t0 + s1 - s0, :])
+            for s in range(s0, s1):
+                x_raw[s] = rows_in[:, s - s0, :]
 
-        def load_xo(pr):
-            g, h = divmod(pr, 2)
+        def load_xo(j):
+            g, h = divmod(j, 2)
+            xo_raw[j] = kept("xo_raw%d" % j, [P, 2 * O], BF16)
             nc.sync.dma_start(
-                out=xo_raw[pr][:].rearrange("p (t k) -> p t k", t=2),
+                out=xo_raw[j][:].rearrange("p (t k) -> p t k", t=2),
                 in_=xo_v[g][:, 2 * h : 2 * h + 2, :],
             )
 
@@ -108,107 +108,83 @@ def tile_recomputed_hidden_weight_gradient_s3_kernel(
                     in_=src.rearrange("g (q r) n -> r q g n", r=4)[r].bitcast(I32),
                 )
 
-        x_rows, x_sorted, xo_sorted, x_laid, turned = {}, {}, {}, {}, {}
+        x_rows, x_sorted, xo_sorted, x_laid, xo_laid, turned = {}, {}, {}, {}, {}, {}
 
-        def rows_of(pr):
-            if pr not in x_rows:
-                x_rows[pr] = ring.tile([P, 2 * K], BF16, name="x_rows", align_bytes=64)
-            return x_rows[pr]
+        def widen(copy, s, k0=0, k1=K):
+            if s not in x_rows:
+                x_rows[s] = passing("x_rows", [P, K], BF16)
+            copy(out=x_rows[s][:, k0:k1], in_=x_raw[s][:, k0:k1].bitcast(FP8))
 
-        def laid_of(pr):
-            if pr not in x_laid:
-                x_laid[pr] = ring.tile([P, 3 * 4 * PAIR_ROWS], BF16, name="x_laid", align_bytes=64)
-            return x_laid[pr]
-
-        def widen(copy, pr, tl, k0, k1):
+        def sort_x(copy, s):
+            x_sorted[s] = passing("x_sorted", [P, K // 2], F32)
             copy(
-                out=rows_of(pr)[:, K * tl + k0 : K * tl + k1],
-                in_=x_raw[pr][:, tl, k0:k1].bitcast(FP8),
+                out=x_sorted[s][:].rearrange("p (g u m) -> p g u m", u=2, m=P),
+                in_=x_rows[s][:].bitcast(F32).rearrange("p (g m u) -> p g u m", u=2, m=P),
             )
 
-        def spread(kk, b):
-            ps = bank(b)
-            for e in range(4):
-                nc.tensor.transpose(
-                    ps[:, P * e : P * e + P],
-                    scale_by_k[:, kk, e : e + 1].to_broadcast([P, P]),
-                    ident[:],
+        def widen_sorted(s):
+            x_sorted[s] = passing("x_sorted", [P, K // 2], F32)
+            for kk in range(2):
+                cols = slice(512 * kk, 512 * kk + 512)
+                nc.vector.tensor_scalar(
+                    out=x_sorted[s][:].bitcast(BF16)[:, cols].rearrange("p (u m e) -> p m u e", u=2, e=2),
+                    in0=x_raw[s][:, cols].bitcast(FP8),
+                    scalar1=ones[:],
+                    scalar2=None,
+                    op0=MULT,
                 )
-            return ps
 
-        def spread_out(kk, ps):
-            nc.scalar.copy(
-                out=scale_rows[:, 512 * kk : 512 * kk + 512].rearrange("p (n e) -> p n e", e=4),
-                in_=ps[:].rearrange("p (e n) -> p n e", e=4),
-            )
-
-        def scale_bytes(pr, tl):
-            nc.vector.tensor_tensor(
-                out=rows_of(pr)[:, K * tl : K * tl + K],
-                in0=x_raw[pr][:, tl, :].bitcast(FP8),
-                in1=scale_rows[:],
-                op=MULT,
-            )
-
-        def sort_x(copy, pr, tl0, tl1):
-            words = ring.tile([P, 512 * (tl1 - tl0)], F32, name="x_sorted", align_bytes=64)
+        def sort_xo(copy, j):
+            xo_sorted[j] = passing("xo_sorted", [P, O], F32, 2)
             copy(
-                out=words[:].rearrange("p (g u m) -> p g u m", u=2, m=P),
-                in_=x_rows[pr][:]
-                .bitcast(F32)[:, 512 * tl0 : 512 * tl1]
-                .rearrange("p (g m u) -> p g u m", u=2, m=P),
-            )
-            for tl in range(tl0, tl1):
-                x_sorted[pr, tl] = words[:, 512 * (tl - tl0) : 512 * (tl - tl0) + 512]
-
-        def sort_xo(copy, pr):
-            xo_sorted[pr] = ring.tile([P, O], F32, name="xo_sorted", align_bytes=64)
-            copy(
-                out=xo_sorted[pr][:].rearrange("p (t u m) -> p t u m", t=2, u=2),
-                in_=xo_raw[pr][:].bitcast(F32).rearrange("p (t m u) -> p t u m", t=2, u=2),
+                out=xo_sorted[j][:].rearrange("p (t u m) -> p t u m", t=2, u=2),
+                in_=xo_raw[j][:].bitcast(F32).rearrange("p (t m u) -> p t u m", t=2, u=2),
             )
 
-        def turn(pr, kk, b=None):
-            ps = bank(kk if b is None else b)
-            for tl in range(2):
-                if kk != XO_PASS:
-                    is_sorted = (pr, tl) in x_sorted
-                    c0 = 256 * kk if is_sorted else 512 * tl + 256 * kk
-                    words = x_sorted[pr, tl] if is_sorted else x_rows[pr][:].bitcast(F32)
-                else:
-                    is_sorted = pr in xo_sorted
-                    c0 = 256 * tl
-                    words = xo_sorted[pr][:] if is_sorted else xo_raw[pr][:].bitcast(F32)
+        def transpose_words(ps, words, is_sorted, parts):
+            for i in parts:
                 for u in range(2):
                     if is_sorted:
-                        src = words[:, c0 + P * u : c0 + P * u + P]
+                        src = words[:, 256 * i + P * u : 256 * i + P * u + P]
                     else:
-                        src = words[:, c0 + u : c0 + 256 : 2]
-                    o0 = PAIR_ROWS * u + P * tl
+                        src = words[:, 256 * i + u : 256 * i + 256 : 2]
+                    o0 = 256 * u + P * i
                     nc.tensor.transpose(ps[:, o0 : o0 + P], src, ident[:])
-            turned[pr, kk] = ps
 
-        def turn_out(pr, kk):
+        def turn_x(s, b, passes=(0, 1)):
+            ps = bank(b)
+            words = x_sorted[s][:] if s in x_sorted else x_rows[s][:].bitcast(F32)
+            transpose_words(ps, words, s in x_sorted, passes)
+            for kk in passes:
+                turned[s, kk] = ps
+
+        def turn_xo(j, b):
+            ps = bank(b)
+            words = xo_sorted[j][:] if j in xo_sorted else xo_raw[j][:].bitcast(F32)
+            transpose_words(ps, words, j in xo_sorted, (0, 1))
+            turned[j, XO_PASS] = ps
+
+        def xo_out(j):
+            xo_laid[j] = passing("xo_laid", [P, 2 * 512], BF16, 2)
             nc.scalar.copy(
-                out=laid_of(pr)[:, 1024 * PLACE[kk] : 1024 * PLACE[kk] + 1024]
-                .bitcast(F32)
-                .rearrange("p (r u) -> p r u", u=2),
-                in_=turned[pr, kk][:].rearrange("p (u r) -> p r u", u=2),
+                out=xo_laid[j][:].bitcast(F32).rearrange("p (r u) -> p r u", u=2),
+                in_=turned[j, XO_PASS][:].rearrange("p (u r) -> p r u", u=2),
             )
 
-        def scale_turned(pr, kk, r0=0, r1=PAIR_ROWS):
-            c0 = 1024 * PLACE[kk]
+        def scale_x(s, k0=0, k1=2):
+            if s not in x_laid:
+                x_laid[s] = passing("x_laid", [P, K], BF16)
             nc.vector.tensor_tensor(
-                out=laid_of(pr)[:, c0 + 4 * r0 : c0 + 4 * r1].rearrange(
-                    "p (r u e) -> p r u e", u=2, e=2
+                out=x_laid[s][:, 512 * k0 : 512 * k1].rearrange(
+                    "p (g r u e) -> p g r u e", r=P, u=2, e=2
                 ),
-                in0=turned[pr, kk][:]
+                in0=turned[s, k0][:]
                 .bitcast(BF16)
-                .rearrange("p (u r e) -> p r u e", u=2, e=2)[:, r0:r1, :, :],
-                in1=scale_by_k[:, kk, :]
-                .rearrange("p (u e) -> p u e", e=2)
-                .unsqueeze(1)
-                .to_broadcast([P, r1 - r0, 2, 2]),
+                .rearrange("p (u g r e) -> p g r u e", u=2, g=2, e=2)[:, k0:k1, :, :, :],
+                in1=scale_by_k[:, k0:k1, :]
+                .rearrange("p g (u e) -> p g u e", e=2)
+                .unsqueeze(2)
+                .to_broadcast([P, k1 - k0, P, 2, 2]),
                 op=MULT,
             )
 
@@ -217,13 +193,11 @@ def tile_recomputed_hidden_weight_gradient_s3_kernel(
                 out=codes[:, w0:w1].bitcast(FP8X4), scales=plane[:, w0:w1], in_=laid
             )
 
-        def quant_x(pr, *passes):
-            w0, w1 = PAIR_ROWS * PLACE[passes[0]], PAIR_ROWS * (PLACE[passes[-1]] + 1)
-            quantise(x_codes[pr], x_plane[pr], x_laid[pr][:, 4 * w0 : 4 * w1], w0, w1)
+        def quant_x(s, k0=0, k1=2):
+            quantise(x_codes[s], x_plane[s], x_laid[s][:, 512 * k0 : 512 * k1], P * k0, P * k1)
 
-        def quant_slot(pr, kk, tl):
-            w0 = PAIR_ROWS * PLACE[kk] + P * tl
-            quantise(x_codes[pr], x_plane[pr], x_laid[pr][:, 4 * w0 : 4 * w0 + 4 * P], w0, w0 + P)
+        def quant_xo(j):
+            quantise(xo_codes[j], xo_plane[j], xo_laid[j][:], 0, 2 * P)
 
         def lay_wo(copy, q):
             copy(
@@ -237,70 +211,63 @@ def tile_recomputed_hidden_weight_gradient_s3_kernel(
             w0, w1 = QUARTER * q0, QUARTER * q1
             quantise(wo_codes, wo_plane, wo_laid[:, 4 * w0 : 4 * w1], w0, w1)
 
-        def warm_up():
-            ps = bank(TURN_BANKS + 2)
-            for j in range(WARM_UPS):
-                nc.tensor.matmul(
-                    ps[:], lhsT=xo_raw[0][:, 0:P], rhs=xo_raw[0][:, 0:BANK], start=True, stop=True
-                )
-
         sums, planes, h_late = {}, {}, {}
 
-        def unit(g, hf, t, passes=(0, XO_PASS, 1), last=1):
-            if (g, hf, t) not in sums:
-                sums[g, hf, t] = bank(TURN_BANKS + len(sums) % UNIT_BANKS)
-            pr, tl = 2 * g + t // 2, t % 2
+        def unit(s, hf, passes, b=None):
+            if b is not None:
+                sums[s, hf] = (bank(b), [])
+            ps, done = sums[s, hf]
             cols = slice(BANK * hf, BANK * hf + BANK)
             for kk in passes:
-                w0 = PAIR_ROWS * PLACE[kk] + P * tl
-                r = slice(w0, w0 + P)
                 if kk == XO_PASS:
+                    r = slice(P * (s % 2), P * (s % 2) + P)
+                    lhsT, lhsT_scale = xo_codes[s // 2][:, r], xo_plane[s // 2][:, r]
                     rhs, rhs_scale = wo_codes[:, cols].bitcast(FP8X4), wo_plane[:, cols]
                 else:
+                    r = slice(P * kk, P * kk + P)
+                    lhsT, lhsT_scale = x_codes[s][:, r], x_plane[s][:, r]
                     rhs, rhs_scale = w_codes[hf][:, kk, :].bitcast(FP4X4), w_plane[:, kk, cols]
+                done.append(kk)
                 nc.tensor.matmul_mx(
-                    out=sums[g, hf, t][:],
-                    lhsT=x_codes[pr][:, r].bitcast(FP8X4),
-                    lhsT_scale=x_plane[pr][:, r],
+                    out=ps[:],
+                    lhsT=lhsT.bitcast(FP8X4),
+                    lhsT_scale=lhsT_scale,
                     rhs=rhs,
                     rhs_scale=rhs_scale,
-                    start=(kk == 0),
-                    stop=(kk == last),
+                    start=(len(done) == 1),
+                    stop=(len(done) == 3),
                 )
 
         def split_gate():
-            flat = gates[:].rearrange("p g t -> p (g t)")
-            nc.scalar.activation(out=gate_abs[:], in_=flat, func=ACT.Abs)
-            nc.scalar.activation(out=gate_sign[:], in_=flat, func=ACT.Sign)
+            nc.scalar.activation(out=gate_abs[:], in_=gates[:], func=ACT.Abs)
+            nc.scalar.activation(out=gate_sign[:], in_=gates[:], func=ACT.Sign)
 
-        def empty(g, hf, t):
+        def empty(s, hf):
+            g, t = divmod(s, 4)
             if (g, hf) not in planes:
                 planes[g, hf] = kept("planes%d_%d" % (g, hf), [P, 4 * BANK], BF16)
             nc.scalar.activation(
                 out=planes[g, hf][:, BANK * t : BANK * t + BANK],
-                in_=sums[g, hf, t][:],
+                in_=sums[s, hf][0][:],
                 func=ACT.Relu,
-                scale=gate_abs[:, 4 * g + t : 4 * g + t + 1],
+                scale=gate_abs[:, s : s + 1],
             )
 
-        def sign(g, hf, t):
+        def sign(s, hf):
+            g, t = divmod(s, 4)
             plane = planes[g, hf][:, BANK * t : BANK * t + BANK]
             nc.vector.tensor_scalar(
-                out=plane,
-                in0=plane,
-                scalar1=gate_sign[:, 4 * g + t : 4 * g + t + 1],
-                scalar2=None,
-                op0=MULT,
+                out=plane, in0=plane, scalar1=gate_sign[:, s : s + 1], scalar2=None, op0=MULT
             )
 
-        def weave(g, c):
+        def weave(g, c, copy=on_vector):
             if g < 2:
                 dst = h_early[c][:, 512 * g : 512 * g + 512]
             else:
-                h_late[c] = ring.tile([P, 512], BF16, name="h_late", align_bytes=64)
+                h_late[c] = passing("h_late", [P, 512], BF16, 3)
                 dst = h_late[c][:]
             hf, f0 = divmod(P * c, BANK)
-            nc.vector.tensor_copy(
+            copy(
                 out=dst.rearrange("p (c i t) -> p c t i", i=4, t=4),
                 in_=planes[g, hf][:]
                 .rearrange("p (t f) -> p t f", t=4)[:, :, f0 : f0 + P]
@@ -313,226 +280,311 @@ def tile_recomputed_hidden_weight_gradient_s3_kernel(
         def quant_late(c):
             quantise(h_codes[c], h_plane[c], h_late[c][:], 2 * P, 3 * P)
 
-        pieces = []
+        pieces = {}
 
-        def gradient(c, width):
+        def piece(c, n0, width, b):
             step = BANK if width == BANK else P
-            for n0 in range(0, N, width):
-                acc = bank(len(pieces) % (TURN_BANKS + UNIT_BANKS))
-                pieces.append(acc)
-                for j in range(0, width, step):
-                    n1 = n0 + j
-                    for g in range(GROUPS):
-                        nc.tensor.matmul_mx(
-                            out=acc[:, j : j + step],
-                            lhsT=h_codes[c][:, P * g : P * g + P].bitcast(FP8X4),
-                            lhsT_scale=h_plane[c][:, P * g : P * g + P],
-                            rhs=dy_codes[:, g, 2 * n1 : 2 * n1 + 2 * step].bitcast(FP4X4),
-                            rhs_scale=dy_plane[:, g, n1 : n1 + step],
-                            start=(g == 0),
-                            stop=(g == GROUPS - 1),
-                        )
-                copy = on_vector if width < BANK and (n0 // width) % 2 else on_scalar
-                result = ring.tile([P, BANK], F32, name="result", align_bytes=64, bufs=6)
-                copy(out=result[:, 0:width], in_=acc[:, 0:width])
-                nc.sync.dma_start(
-                    out=out[P * c : P * c + P, n0 : n0 + width], in_=result[:, 0:width]
-                )
+            acc = bank(b)
+            pieces[c, n0] = (acc, width)
+            for j in range(0, width, step):
+                n1 = n0 + j
+                for g in range(GROUPS):
+                    nc.tensor.matmul_mx(
+                        out=acc[:, j : j + step],
+                        lhsT=h_codes[c][:, P * g : P * g + P].bitcast(FP8X4),
+                        lhsT_scale=h_plane[c][:, P * g : P * g + P],
+                        rhs=dy_codes[:, g, 2 * n1 : 2 * n1 + 2 * step].bitcast(FP4X4),
+                        rhs_scale=dy_plane[:, g, n1 : n1 + step],
+                        start=(g == 0),
+                        stop=(g == GROUPS - 1),
+                    )
 
-        nc.sync.dma_start(
-            out=scale_by_k[:], in_=x_scale.rearrange("o (g p t) -> p (o g) t", p=P, t=4)
-        )
-        load_x(0)
-        load_wo(0, 1)
-        load_x(1)
-        load_xo(0)
-        load_xo(1)
-        load_wo(1, 3)
+        def store(copy, c, n0):
+            acc, width = pieces[c, n0]
+            result = passing("result", [P, BANK], F32, 6)
+            copy(out=result[:, 0:width], in_=acc[:, 0:width])
+            nc.sync.dma_start(out=out[P * c : P * c + P, n0 : n0 + width], in_=result[:, 0:width])
+
+        def load_x_scale():
+            nc.sync.dma_start(
+                out=scale_by_k[:], in_=x_scale.rearrange("o (g p t) -> p (o g) t", p=P, t=4)
+            )
+
+        def load_gates():
+            nc.sync.dma_start(
+                out=gates[:].rearrange("p (g t) -> p g t", t=4),
+                in_=gate.rearrange("(g m t) -> m g t", m=P, t=4),
+            )
+
+        nc.vector.memset(w_plane[:].rearrange("p g n -> p (g n)").bitcast(I32), 0)
+        nc.vector.memset(ones[:], 1.0)
+        nc.vector.memset(dy_plane[:].rearrange("p g n -> p (g n)").bitcast(I32), 0)
+        make_identity(nc, ident[:])
+        load_x(0, 1)
+        load_x_scale()
+        load_x(1, 2)
+        load_x(2, 4)
+        load_wo(0, 2)
         load_w(0)
         load_scale_bytes(w_plane, w_scales)
-        nc.sync.dma_start(out=gates[:], in_=gate.rearrange("(g m t) -> m g t", m=P, t=4))
-        load_wo(3, 4)
-        load_x(2)
+        load_xo(0)
         load_w(1)
+        load_xo(1)
+        load_gates()
+        load_x(4, 6)
+        load_wo(2, 4)
         load_xo(2)
-        for pr in range(3, PAIRS):
-            load_x(pr)
-            load_xo(pr)
+        load_x(6, 8)
+        load_xo(3)
+        load_x(8, 10)
+        load_xo(4)
+        load_x(10, 12)
+        load_xo(5)
         load_scale_bytes(dy_plane, dy_scales)
         nc.sync.dma_start(out=dy_codes[:], in_=dy_words.rearrange("g p n -> p g n"))
 
-        spread_banks = [spread(kk, TURN_BANKS + kk) for kk in range(2)]
-        widen(on_vector, 0, 0, 0, K)
-        widen(on_scalar, 0, 1, 0, 512)
-        widen(on_vector, 0, 1, 512, K)
-        turn(0, 0)
-        turn(0, 1)
-        for kk in range(2):
-            spread_out(kk, spread_banks[kk])
-        lay_wo(on_vector, 0)
-        scale_turned(0, 0)
-        for tl in range(2):
-            widen(on_scalar, 1, tl, 0, 512)
-        turn(0, XO_PASS)
-        turn(1, XO_PASS, TURN_BANKS + UNIT_BANKS - 1)
-        widen(on_scalar, 1, 0, 512, K)
-        turn_out(0, XO_PASS)
-        quant_wo(0, 1)
-        scale_turned(0, 1)
-        turn(1, 0)
-        warm_up()
-        widen(on_scalar, 1, 1, 512, K)
-        quant_x(0, 0, XO_PASS)
-        quant_x(0, 1)
-        turn(1, 1)
+        X, XO, ALL = (0, 1), (XO_PASS,), (0, 1, XO_PASS)
+        widen(on_vector, 0, 0, 512)
+        widen(on_scalar, 0, 512, K)
+        turn_x(0, 0, (0,))
+        widen_sorted(1)
+        widen(on_scalar, 2)
+        turn_x(0, 1, (1,))
+        scale_x(0, 0, 1)
+        widen(on_scalar, 3)
+        turn_x(1, 2)
+        scale_x(0, 1, 2)
+        lay_wo(on_scalar, 0)
+        turn_x(2, 3)
+        quant_x(0, 0, 1)
         lay_wo(on_scalar, 1)
-        turn_out(1, XO_PASS)
-        scale_turned(1, 0)
-
-        for t in range(2):
-            unit(0, 0, t, (0, 1), XO_PASS)
-        quant_wo(1, 2)
-        quant_x(1, 0, XO_PASS)
-        for t in range(2):
-            unit(0, 0, t, (XO_PASS,), XO_PASS)
-        for t in range(2, 4):
-            unit(0, 0, t, (0, XO_PASS))
+        turn_x(3, 4)
+        quant_x(0, 1, 2)
+        unit(0, 0, X, 5)
+        scale_x(1)
+        turn_xo(0, 0)
+        quant_x(1)
+        xo_out(0)
+        unit(1, 0, X, 6)
+        scale_x(2)
         split_gate()
+        unit(0, 1, X, 1)
+        quant_wo(0, 2)
+        widen(on_scalar, 4)
+        unit(1, 1, X, 2)
+        quant_x(2)
+        widen(on_scalar, 5)
+        unit(2, 0, X, 7)
+        scale_x(3)
         lay_wo(on_scalar, 2)
-        empty(0, 0, 0)
-        empty(0, 0, 1)
-        lay_wo(on_scalar, 3)
-        sort_xo(on_scalar, 2)
-        for tl in range(2):
-            scale_turned(1, 1, P * tl, P * tl + P)
-        for tl in range(2):
-            quant_slot(1, 1, tl)
-        for t in range(2, 4):
-            unit(0, 0, t, (1,))
-
-        def turn_pair(pr):
-            for kk in (XO_PASS, 0, 1):
-                turn(pr, kk)
-
-        def turn_pair_out(pr):
-            for kk in (XO_PASS, 0, 1):
-                turn_out(pr, kk)
-
-        def sort_pair(pr):
-            sort_xo(on_vector, pr)
-            sort_x(on_vector, pr, 0, 2)
-
-        scale_bytes(2, 0)
-        sort_x(on_scalar, 2, 0, 1)
-        scale_bytes(2, 1)
+        turn_xo(1, 0)
+        quant_xo(0)
+        xo_out(1)
+        turn_x(4, 3)
+        quant_x(3)
+        unit(0, 0, XO)
+        sort_x(on_vector, 5)
+        empty(0, 0)
+        unit(1, 0, XO)
+        sort_xo(on_vector, 2)
+        empty(1, 0)
+        unit(3, 0, X, 4)
+        lay_wo(on_vector, 3)
+        widen(on_scalar, 6)
+        quant_xo(1)
+        unit(2, 0, XO)
+        scale_x(4)
+        empty(2, 0)
+        unit(3, 0, XO)
         quant_wo(2, 4)
-        for t in range(3):
-            unit(0, 1, t, (0, 1), XO_PASS)
-        turn_pair(2)
-        empty(0, 0, 2)
-        turn_pair_out(2)
-        for t in range(3):
-            unit(0, 1, t, (XO_PASS,), XO_PASS)
-        unit(0, 1, 3)
-
-        for tl in range(2):
-            scale_bytes(3, tl)
-        for kk in (0, XO_PASS, 1):
-            quant_x(2, kk)
-        sort_x(on_vector, 3, 0, 2)
-        empty(0, 0, 3)
-        sort_xo(on_scalar, 3)
-        unit(1, 1, 0)
-        empty(0, 1, 0)
-        empty(0, 1, 1)
-        turn_pair(3)
-        turn_out(3, XO_PASS)
-        turn_out(3, 0)
-        empty(0, 1, 2)
-        turn_out(3, 1)
-        unit(1, 1, 1)
-        unit(1, 0, 0)
-        unit(1, 0, 1)
-
-        for tl in range(2):
-            scale_bytes(4, tl)
-        quant_x(3, 0, XO_PASS)
-        sort_pair(4)
-        quant_x(3, 1)
-        empty(0, 1, 3)
-        unit(1, 1, 2)
-        empty(1, 1, 0)
-        empty(1, 1, 1)
-        turn_pair(4)
-        empty(1, 0, 0)
-        turn_pair_out(4)
-        unit(1, 1, 3)
-        unit(1, 0, 2)
-
-        for tl in range(2):
-            scale_bytes(5, tl)
-        sort_pair(5)
-        turn_pair(5)
-        empty(1, 0, 1)
-        empty(1, 1, 2)
-        turn_pair_out(5)
-        quant_x(4, 0, XO_PASS)
-        quant_x(4, 1)
-        unit(1, 0, 3)
-
-        for t in range(4):
-            sign(0, 1, t)
+        turn_x(5, 0)
+        quant_x(4)
+        turn_xo(2, 3)
+        scale_x(5)
+        xo_out(2)
+        unit(2, 1, X, 5)
+        quant_xo(2)
+        widen(on_scalar, 7)
+        unit(3, 1, X, 6)
+        sort_x(on_vector, 6)
+        empty(3, 0)
+        unit(0, 1, XO)
+        sort_xo(on_vector, 3)
+        empty(0, 1)
+        unit(1, 1, XO)
+        quant_x(5)
+        empty(1, 1)
+        unit(2, 1, XO)
+        sort_x(on_vector, 7)
+        empty(2, 1)
+        unit(3, 1, XO)
+        sign(0, 1)
+        unit(4, 1, ALL, 7)
+        sign(1, 1)
+        turn_x(6, 0)
+        scale_x(6)
+        turn_xo(3, 3)
+        sign(2, 1)
+        xo_out(3)
+        turn_x(7, 4)
+        quant_x(6)
+        empty(3, 1)
+        unit(4, 0, ALL, 1)
+        quant_xo(3)
+        widen(on_scalar, 8)
+        unit(5, 1, ALL, 2)
+        scale_x(7)
+        widen(on_scalar, 9)
+        unit(5, 0, ALL, 5)
+        sort_x(on_vector, 8)
+        empty(4, 1)
+        unit(6, 1, ALL, 6)
+        sort_xo(on_vector, 4)
+        empty(4, 0)
+        turn_x(8, 0)
+        sort_x(on_vector, 9)
+        empty(5, 1)
+        turn_xo(4, 3)
+        quant_x(7)
+        widen(on_scalar, 10)
+        turn_x(9, 4)
+        sign(3, 1)
+        xo_out(4)
+        unit(6, 0, ALL, 7)
+        scale_x(8)
+        widen(on_scalar, 11)
+        unit(7, 1, ALL, 1)
+        sort_x(on_vector, 10)
+        empty(5, 0)
+        quant_x(8)
+        empty(6, 1)
+        quant_xo(4)
+        empty(6, 0)
+        unit(8, 1, ALL, 2)
+        sort_x(on_vector, 11)
+        empty(7, 1)
+        turn_x(10, 0)
+        sort_xo(on_vector, 5)
+        turn_xo(5, 3)
+        scale_x(9)
+        xo_out(5)
+        turn_x(11, 4)
+        scale_x(10)
+        empty(8, 1)
+        unit(7, 0, ALL, 5)
+        quant_x(9)
+        empty(7, 0)
+        unit(9, 1, ALL, 6)
+        quant_xo(5)
+        empty(9, 1)
+        unit(8, 0, ALL, 7)
+        quant_x(10)
+        empty(8, 0)
+        unit(10, 1, ALL, 1)
+        scale_x(11)
+        empty(10, 1)
+        sign(4, 1)
+        quant_x(11)
+        unit(11, 1, ALL, 2)
         weave(0, 4)
-        unit(2, 1, 0)
-        empty(1, 1, 3)
-        unit(2, 1, 1)
-        quant_x(5, 0, XO_PASS)
-        quant_x(5, 1)
-        empty(1, 0, 2)
-        empty(1, 0, 3)
-        for t in range(4):
-            sign(1, 1, t)
-        for t in range(2):
-            empty(2, 1, t)
-        for hf, t in [(1, 2), (1, 3)] + [(0, t) for t in range(4)]:
-            unit(2, hf, t)
-            empty(2, hf, t)
-
+        empty(11, 1)
+        unit(9, 0, ALL, 5)
+        sign(5, 1)
+        empty(9, 0)
+        unit(10, 0, ALL, 6)
+        sign(6, 1)
+        empty(10, 0)
+        unit(11, 0, ALL, 7)
+        sign(7, 1)
+        empty(11, 0)
+        sign(8, 1)
         weave(1, 4)
         weave(0, 5)
+        sign(9, 1)
         weave(1, 5)
         quant_early(4)
-        sign(2, 1, 0)
-        sign(2, 1, 1)
-        weave(0, 6)
-        sign(2, 1, 2)
+        sign(10, 1)
+        sign(11, 1)
         quant_early(5)
-        sign(2, 1, 3)
-        weave(1, 6)
         weave(2, 4)
         weave(2, 5)
         quant_late(4)
-        gradient(4, BANK)
-        weave(2, 6)
+        piece(4, 0, BANK, 0)
+        weave(0, 6)
+        store(on_scalar, 4, 0)
+        piece(4, 512, BANK, 1)
+        weave(1, 6)
+        store(on_scalar, 4, 512)
         quant_late(5)
-        gradient(5, BANK)
+        piece(5, 0, BANK, 2)
+        weave(2, 6)
+        store(on_scalar, 5, 0)
+        piece(5, 512, BANK, 3)
         quant_early(6)
+        store(on_scalar, 5, 512)
         quant_late(6)
-        gradient(6, BANK)
-        for g in range(GROUPS):
-            weave(g, 7)
+        piece(6, 0, BANK, 4)
+        weave(0, 7)
+        store(on_scalar, 6, 0)
+        piece(6, 512, BANK, 5)
+        weave(1, 7)
+        store(on_scalar, 6, 512)
+        weave(2, 7)
         quant_early(7)
         quant_late(7)
-        gradient(7, BANK)
-
-        for g in range(GROUPS):
-            for t in range(4):
-                sign(g, 0, t)
-        for c in range(4):
-            for g in range(GROUPS):
-                weave(g, c)
-            quant_early(c)
-            quant_late(c)
-        for c in range(3):
-            gradient(c, BANK)
-        gradient(3, N // 4)
+        piece(7, 0, BANK, 6)
+        sign(0, 0)
+        store(on_scalar, 7, 0)
+        piece(7, 512, BANK, 7)
+        sign(1, 0)
+        store(on_scalar, 7, 512)
+        sign(2, 0)
+        sign(3, 0)
+        sign(4, 0)
+        sign(5, 0)
+        sign(6, 0)
+        sign(7, 0)
+        sign(8, 0)
+        sign(9, 0)
+        sign(10, 0)
+        sign(11, 0)
+        weave(0, 0)
+        weave(1, 0)
+        weave(2, 0)
+        quant_early(0)
+        quant_late(0)
+        piece(0, 0, BANK, 0)
+        weave(0, 1)
+        store(on_scalar, 0, 0)
+        piece(0, 512, BANK, 1)
+        weave(1, 1)
+        store(on_scalar, 0, 512)
+        weave(2, 1)
+        quant_early(1)
+        quant_late(1)
+        piece(1, 0, BANK, 2)
+        weave(0, 2)
+        store(on_scalar, 1, 0)
+        piece(1, 512, BANK, 3)
+        weave(1, 2)
+        store(on_scalar, 1, 512)
+        weave(2, 2)
+        quant_early(2)
+        quant_late(2)
+        piece(2, 0, BANK, 4)
+        weave(0, 3)
+        store(on_scalar, 2, 0)
+        piece(2, 512, BANK, 5)
+        weave(1, 3)
+        store(on_scalar, 2, 512)
+        weave(2, 3)
+        quant_early(3)
+        quant_late(3)
+        piece(3, 0, 256, 6)
+        store(on_scalar, 3, 0)
+        piece(3, 256, 256, 7)
+        store(on_vector, 3, 256)
+        piece(3, 512, 256, 0)
+        store(on_scalar, 3, 512)
+        piece(3, 768, 256, 1)
+        store(on_vector, 3, 768)

@@ -55,6 +55,7 @@ def tile_recomputed_hidden_weight_gradient_s3_kernel(
         dy_codes = kept("dy_codes", [P, GROUPS, 2 * N], U8)
         dy_plane = kept("dy_plane", [P, GROUPS, N], U8)
         scale_by_k = kept("scale_by_k", [P, 2, 4], F32)
+        scale_rows = kept("scale_rows", [P, K], F32)
         gates = kept("gates", [P, SLOTS], BF16)
         gate_abs = kept("gate_abs", [P, SLOTS], F32)
         gate_sign = kept("gate_sign", [P, SLOTS], F32)
@@ -114,6 +115,35 @@ def tile_recomputed_hidden_weight_gradient_s3_kernel(
             if s not in x_rows:
                 x_rows[s] = passing("x_rows", [P, K], BF16)
             copy(out=x_rows[s][:, k0:k1], in_=x_raw[s][:, k0:k1].bitcast(FP8))
+
+        def spread(kk, b):
+            ps = bank(b)
+            for e in range(4):
+                nc.tensor.transpose(
+                    ps[:, P * e : P * e + P],
+                    scale_by_k[:, kk, e : e + 1].to_broadcast([P, P]),
+                    ident[:],
+                )
+            turned["scale", kk] = ps
+
+        def spread_out(kk):
+            nc.scalar.copy(
+                out=scale_rows[:, 512 * kk : 512 * kk + 512].rearrange("p (n e) -> p n e", e=4),
+                in_=turned["scale", kk][:].rearrange("p (e n) -> p n e", e=4),
+            )
+
+        def scale_bytes(s):
+            x_rows[s] = passing("x_rows", [P, K], BF16)
+            nc.vector.tensor_tensor(
+                out=x_rows[s][:], in0=x_raw[s].bitcast(FP8), in1=scale_rows[:], op=MULT
+            )
+
+        def x_out(s):
+            x_laid[s] = passing("x_laid", [P, K], BF16)
+            nc.scalar.copy(
+                out=x_laid[s][:].bitcast(F32).rearrange("p (r u) -> p r u", u=2),
+                in_=turned[s, 0][:].rearrange("p (u r) -> p r u", u=2),
+            )
 
         def sort_x(copy, s):
             x_sorted[s] = passing("x_sorted", [P, K // 2], F32)
@@ -320,16 +350,16 @@ def tile_recomputed_hidden_weight_gradient_s3_kernel(
         nc.vector.memset(ones[:], 1.0)
         nc.vector.memset(dy_plane[:].rearrange("p g n -> p (g n)").bitcast(I32), 0)
         make_identity(nc, ident[:])
-        load_x(0, 1)
         load_x_scale()
+        load_x(0, 1)
         load_x(1, 2)
         load_x(2, 4)
+        load_xo(0)
+        load_xo(1)
         load_wo(0, 2)
         load_w(0)
         load_scale_bytes(w_plane, w_scales)
-        load_xo(0)
         load_w(1)
-        load_xo(1)
         load_gates()
         load_x(4, 6)
         load_wo(2, 4)
@@ -344,198 +374,201 @@ def tile_recomputed_hidden_weight_gradient_s3_kernel(
         nc.sync.dma_start(out=dy_codes[:], in_=dy_words.rearrange("g p n -> p g n"))
 
         X, XO, ALL = (0, 1), (XO_PASS,), (0, 1, XO_PASS)
+        spread(0, 5)
         widen(on_vector, 0, 0, 512)
         widen(on_scalar, 0, 512, K)
-        turn_x(0, 0, (0,))
+        spread(1, 7)
         widen_sorted(1)
+        spread_out(0)
+        turn_x(0, 0, (0,))
+        scale_x(0, 0, 1)
         widen(on_scalar, 2)
         turn_x(0, 1, (1,))
-        scale_x(0, 0, 1)
+        scale_x(0, 1, 2)
         widen(on_scalar, 3)
         turn_x(1, 2)
-        scale_x(0, 1, 2)
+        quant_x(0, 0, 1)
+        spread_out(1)
+        turn_xo(0, 6)
+        scale_x(1)
         lay_wo(on_scalar, 0)
         turn_x(2, 3)
-        quant_x(0, 0, 1)
+        quant_x(0, 1, 2)
+        xo_out(0)
+        turn_xo(1, 5)
+        quant_x(1)
         lay_wo(on_scalar, 1)
         turn_x(3, 4)
-        quant_x(0, 1, 2)
-        unit(0, 0, X, 5)
-        scale_x(1)
-        turn_xo(0, 0)
-        quant_x(1)
-        xo_out(0)
-        unit(1, 0, X, 6)
         scale_x(2)
+        xo_out(1)
+        unit(0, 0, X, 7)
+        scale_x(3)
         split_gate()
+        unit(1, 0, X, 0)
+        quant_x(2)
+        lay_wo(on_scalar, 2)
         unit(0, 1, X, 1)
         quant_wo(0, 2)
-        widen(on_scalar, 4)
+        sort_xo(on_scalar, 2)
         unit(1, 1, X, 2)
-        quant_x(2)
-        widen(on_scalar, 5)
-        unit(2, 0, X, 7)
-        scale_x(3)
-        lay_wo(on_scalar, 2)
-        turn_xo(1, 0)
-        quant_xo(0)
-        xo_out(1)
-        turn_x(4, 3)
         quant_x(3)
+        unit(2, 0, X, 3)
+        quant_xo(0)
+        unit(2, 1, X, 6)
+        quant_xo(1)
         unit(0, 0, XO)
-        sort_x(on_vector, 5)
+        scale_bytes(4)
         empty(0, 0)
         unit(1, 0, XO)
-        sort_xo(on_vector, 2)
-        empty(1, 0)
-        unit(3, 0, X, 4)
         lay_wo(on_vector, 3)
-        widen(on_scalar, 6)
-        quant_xo(1)
+        sort_x(on_scalar, 4)
         unit(2, 0, XO)
-        scale_x(4)
-        empty(2, 0)
-        unit(3, 0, XO)
+        scale_bytes(5)
+        empty(1, 0)
+        unit(3, 0, ALL, 4)
         quant_wo(2, 4)
-        turn_x(5, 0)
+        empty(2, 0)
+        unit(3, 1, X, 5)
+        sort_xo(on_vector, 3)
+        turn_x(4, 7)
+        scale_bytes(6)
+        x_out(4)
+        turn_xo(2, 0)
         quant_x(4)
-        turn_xo(2, 3)
-        scale_x(5)
         xo_out(2)
-        unit(2, 1, X, 5)
+        turn_x(5, 3)
         quant_xo(2)
-        widen(on_scalar, 7)
-        unit(3, 1, X, 6)
-        sort_x(on_vector, 6)
         empty(3, 0)
         unit(0, 1, XO)
-        sort_xo(on_vector, 3)
-        empty(0, 1)
+        scale_bytes(7)
+        x_out(5)
         unit(1, 1, XO)
+        sort_x(on_vector, 6)
+        empty(0, 1)
+        unit(2, 1, XO)
         quant_x(5)
         empty(1, 1)
-        unit(2, 1, XO)
+        unit(3, 1, XO)
         sort_x(on_vector, 7)
         empty(2, 1)
-        unit(3, 1, XO)
-        sign(0, 1)
-        unit(4, 1, ALL, 7)
-        sign(1, 1)
-        turn_x(6, 0)
-        scale_x(6)
-        turn_xo(3, 3)
-        sign(2, 1)
-        xo_out(3)
-        turn_x(7, 4)
-        quant_x(6)
+        unit(4, 1, ALL, 4)
+        scale_bytes(8)
         empty(3, 1)
         unit(4, 0, ALL, 1)
-        quant_xo(3)
-        widen(on_scalar, 8)
-        unit(5, 1, ALL, 2)
-        scale_x(7)
-        widen(on_scalar, 9)
-        unit(5, 0, ALL, 5)
-        sort_x(on_vector, 8)
-        empty(4, 1)
-        unit(6, 1, ALL, 6)
         sort_xo(on_vector, 4)
+        turn_x(6, 0)
+        x_out(6)
+        turn_xo(3, 7)
+        quant_x(6)
+        xo_out(3)
+        turn_x(7, 3)
+        quant_xo(3)
+        x_out(7)
+        unit(5, 1, ALL, 2)
+        scale_bytes(9)
+        empty(4, 1)
+        unit(5, 0, ALL, 6)
+        sort_x(on_vector, 8)
         empty(4, 0)
-        turn_x(8, 0)
+        unit(6, 1, ALL, 5)
         sort_x(on_vector, 9)
         empty(5, 1)
-        turn_xo(4, 3)
+        turn_xo(4, 7)
         quant_x(7)
-        widen(on_scalar, 10)
-        turn_x(9, 4)
-        sign(3, 1)
         xo_out(4)
-        unit(6, 0, ALL, 7)
-        scale_x(8)
-        widen(on_scalar, 11)
+        turn_x(8, 0)
+        scale_bytes(10)
+        x_out(8)
+        turn_x(9, 3)
+        sort_xo(on_vector, 5)
+        x_out(9)
+        unit(6, 0, ALL, 4)
+        scale_bytes(11)
+        empty(5, 0)
         unit(7, 1, ALL, 1)
         sort_x(on_vector, 10)
-        empty(5, 0)
-        quant_x(8)
         empty(6, 1)
-        quant_xo(4)
+        unit(7, 0, ALL, 2)
+        quant_x(8)
         empty(6, 0)
-        unit(8, 1, ALL, 2)
-        sort_x(on_vector, 11)
-        empty(7, 1)
         turn_x(10, 0)
-        sort_xo(on_vector, 5)
-        turn_xo(5, 3)
-        scale_x(9)
+        quant_xo(4)
+        x_out(10)
+        turn_xo(5, 7)
+        sort_x(on_vector, 11)
         xo_out(5)
-        turn_x(11, 4)
-        scale_x(10)
-        empty(8, 1)
-        unit(7, 0, ALL, 5)
+        turn_x(11, 3)
         quant_x(9)
+        x_out(11)
+        unit(8, 1, ALL, 6)
+        sign(0, 1)
+        empty(7, 1)
+        unit(9, 1, ALL, 5)
+        sign(1, 1)
         empty(7, 0)
-        unit(9, 1, ALL, 6)
-        quant_xo(5)
+        sign(2, 1)
+        empty(8, 1)
+        sign(3, 1)
         empty(9, 1)
-        unit(8, 0, ALL, 7)
-        quant_x(10)
-        empty(8, 0)
-        unit(10, 1, ALL, 1)
-        scale_x(11)
-        empty(10, 1)
         sign(4, 1)
-        quant_x(11)
-        unit(11, 1, ALL, 2)
-        weave(0, 4)
-        empty(11, 1)
-        unit(9, 0, ALL, 5)
         sign(5, 1)
-        empty(9, 0)
-        unit(10, 0, ALL, 6)
         sign(6, 1)
-        empty(10, 0)
-        unit(11, 0, ALL, 7)
+        weave(0, 4)
+        quant_x(10)
+        quant_xo(5)
+        unit(10, 1, ALL, 4)
+        quant_x(11)
+        empty(10, 1)
+        unit(11, 1, ALL, 1)
         sign(7, 1)
+        empty(11, 1)
+        unit(8, 0, ALL, 2)
+        weave(0, 5)
+        empty(8, 0)
+        unit(9, 0, ALL, 6)
+        weave(1, 4)
+        empty(9, 0)
+        unit(10, 0, ALL, 5)
+        weave(1, 5)
+        empty(10, 0)
+        unit(11, 0, ALL, 4)
+        quant_early(4)
         empty(11, 0)
         sign(8, 1)
-        weave(1, 4)
-        weave(0, 5)
         sign(9, 1)
-        weave(1, 5)
-        quant_early(4)
         sign(10, 1)
         sign(11, 1)
         quant_early(5)
         weave(2, 4)
         weave(2, 5)
         quant_late(4)
-        piece(4, 0, BANK, 0)
+        piece(4, 0, BANK, 7)
         weave(0, 6)
         store(on_scalar, 4, 0)
-        piece(4, 512, BANK, 1)
+        piece(4, 512, BANK, 0)
         weave(1, 6)
         store(on_scalar, 4, 512)
         quant_late(5)
-        piece(5, 0, BANK, 2)
+        piece(5, 0, BANK, 1)
         weave(2, 6)
         store(on_scalar, 5, 0)
-        piece(5, 512, BANK, 3)
+        piece(5, 512, BANK, 2)
         quant_early(6)
         store(on_scalar, 5, 512)
         quant_late(6)
-        piece(6, 0, BANK, 4)
+        piece(6, 0, BANK, 3)
         weave(0, 7)
         store(on_scalar, 6, 0)
-        piece(6, 512, BANK, 5)
+        piece(6, 512, BANK, 4)
         weave(1, 7)
         store(on_scalar, 6, 512)
         weave(2, 7)
         quant_early(7)
         quant_late(7)
-        piece(7, 0, BANK, 6)
+        piece(7, 0, BANK, 5)
         sign(0, 0)
         store(on_scalar, 7, 0)
-        piece(7, 512, BANK, 7)
+        piece(7, 512, BANK, 6)
         sign(1, 0)
         store(on_scalar, 7, 512)
         sign(2, 0)
@@ -553,38 +586,38 @@ def tile_recomputed_hidden_weight_gradient_s3_kernel(
         weave(2, 0)
         quant_early(0)
         quant_late(0)
-        piece(0, 0, BANK, 0)
+        piece(0, 0, BANK, 7)
         weave(0, 1)
         store(on_scalar, 0, 0)
-        piece(0, 512, BANK, 1)
+        piece(0, 512, BANK, 0)
         weave(1, 1)
         store(on_scalar, 0, 512)
         weave(2, 1)
         quant_early(1)
         quant_late(1)
-        piece(1, 0, BANK, 2)
+        piece(1, 0, BANK, 1)
         weave(0, 2)
         store(on_scalar, 1, 0)
-        piece(1, 512, BANK, 3)
+        piece(1, 512, BANK, 2)
         weave(1, 2)
         store(on_scalar, 1, 512)
         weave(2, 2)
         quant_early(2)
         quant_late(2)
-        piece(2, 0, BANK, 4)
+        piece(2, 0, BANK, 3)
         weave(0, 3)
         store(on_scalar, 2, 0)
-        piece(2, 512, BANK, 5)
+        piece(2, 512, BANK, 4)
         weave(1, 3)
         store(on_scalar, 2, 512)
         weave(2, 3)
         quant_early(3)
         quant_late(3)
-        piece(3, 0, 256, 6)
+        piece(3, 0, 256, 5)
         store(on_scalar, 3, 0)
-        piece(3, 256, 256, 7)
+        piece(3, 256, 256, 6)
         store(on_vector, 3, 256)
-        piece(3, 512, 256, 0)
+        piece(3, 512, 256, 7)
         store(on_scalar, 3, 512)
-        piece(3, 768, 256, 1)
+        piece(3, 768, 256, 0)
         store(on_vector, 3, 768)

@@ -26,6 +26,8 @@ PAIRS = SLOTS // 2
 QUARTER = F // 4
 CHUNKS = F // P
 XO_PASS = 2
+XO_PART = 2
+PLACE = {0: 0, XO_PART: 1, 1: 2}
 
 
 def tile_recomputed_hidden_weight_gradient_s3_kernel(
@@ -49,7 +51,7 @@ def tile_recomputed_hidden_weight_gradient_s3_kernel(
             return psum.tile([P, BANK], F32, name="bank%d" % b)
 
         ident = kept("ident", [P, P], F32)
-        ones = kept("ones", [P, 1], F32)
+        zeros = kept("zeros", [P, BANK], BF16)
         w_codes = [kept("w_codes%d" % hf, [P, 2, F], U8) for hf in range(2)]
         w_plane = kept("w_plane", [P, 2, F], U8)
         dy_codes = kept("dy_codes", [P, GROUPS, 2 * N], U8)
@@ -62,18 +64,19 @@ def tile_recomputed_hidden_weight_gradient_s3_kernel(
         wo_codes = kept("wo_codes", [P, F], U32)
         wo_plane = kept("wo_plane", [P, F], U8)
         wo_laid = kept("wo_laid", [P, 4 * F], BF16)
-        x_codes = [kept("x_codes%d" % s, [P, 2 * P], U32) for s in range(SLOTS)]
-        x_plane = [kept("x_plane%d" % s, [P, 2 * P], U8) for s in range(SLOTS)]
-        xo_codes = [kept("xo_codes%d" % j, [P, 2 * P], U32) for j in range(PAIRS)]
-        xo_plane = [kept("xo_plane%d" % j, [P, 2 * P], U8) for j in range(PAIRS)]
-        h_early = [kept("h_early%d" % c, [P, 2 * 512], BF16) for c in range(CHUNKS)]
-        h_codes = [kept("h_codes%d" % c, [P, GROUPS * P], U32) for c in range(CHUNKS)]
-        h_plane = [kept("h_plane%d" % c, [P, GROUPS * P], U8) for c in range(CHUNKS)]
+        x_codes = [kept("x_codes%d" % j, [P, 6 * P], U32) for j in range(PAIRS)]
+        x_plane = [kept("x_plane%d" % j, [P, 6 * P], U8) for j in range(PAIRS)]
+        rows = [kept("rows%d" % j, [P, 3 * K], BF16) for j in range(PAIRS)]
+        h_laid = [kept("h_laid%d" % g, [P, 4 * F], BF16) for g in range(GROUPS)]
+        h_codes = [kept("h_codes%d" % g, [P, F], U32) for g in range(GROUPS)]
+        h_plane = [kept("h_plane%d" % g, [P, F], U8) for g in range(GROUPS)]
+        both = [kept("planes%d" % g, [P, 4 * F], BF16) for g in range(2)]
+        last = [kept("planes2_%d" % hf, [P, 4 * BANK], BF16) for hf in range(2)]
 
         x_v = x_bytes.rearrange("(g m t) k -> g m t k", m=P, t=4)
         xo_v = xo.rearrange("(g m t) k -> g m t k", m=P, t=4)
         wo_v = wo.rearrange("(p j) f -> p j f", j=4)
-        x_raw, xo_raw, wo_raw = {}, {}, {}
+        x_raw, wo_raw = {}, {}
 
         def load_x(s0, s1):
             g, t0 = divmod(s0, 4)
@@ -84,9 +87,8 @@ def tile_recomputed_hidden_weight_gradient_s3_kernel(
 
         def load_xo(j):
             g, h = divmod(j, 2)
-            xo_raw[j] = kept("xo_raw%d" % j, [P, 2 * O], BF16)
             nc.sync.dma_start(
-                out=xo_raw[j][:].rearrange("p (t k) -> p t k", t=2),
+                out=rows[j][:, 2 * K : 3 * K].rearrange("p (t k) -> p t k", t=2),
                 in_=xo_v[g][:, 2 * h : 2 * h + 2, :],
             )
 
@@ -109,12 +111,11 @@ def tile_recomputed_hidden_weight_gradient_s3_kernel(
                     in_=src.rearrange("g (q r) n -> r q g n", r=4)[r].bitcast(I32),
                 )
 
-        x_rows, x_sorted, xo_sorted, x_laid, xo_laid, turned = {}, {}, {}, {}, {}, {}
+        in_order, laid, turned, is_sorted = {}, {}, {}, set()
 
         def widen(copy, s, k0=0, k1=K):
-            if s not in x_rows:
-                x_rows[s] = passing("x_rows", [P, K], BF16)
-            copy(out=x_rows[s][:, k0:k1], in_=x_raw[s][:, k0:k1].bitcast(FP8))
+            c0 = K * (s % 2)
+            copy(out=rows[s // 2][:, c0 + k0 : c0 + k1], in_=x_raw[s][:, k0:k1].bitcast(FP8))
 
         def spread(kk, b):
             ps = bank(b)
@@ -133,82 +134,56 @@ def tile_recomputed_hidden_weight_gradient_s3_kernel(
             )
 
         def scale_bytes(s):
-            x_rows[s] = passing("x_rows", [P, K], BF16)
+            c0 = K * (s % 2)
             nc.vector.tensor_tensor(
-                out=x_rows[s][:], in0=x_raw[s].bitcast(FP8), in1=scale_rows[:], op=MULT
+                out=rows[s // 2][:, c0 : c0 + K],
+                in0=x_raw[s].bitcast(FP8),
+                in1=scale_rows[:],
+                op=MULT,
             )
 
-        def x_out(s):
-            x_laid[s] = passing("x_laid", [P, K], BF16)
-            nc.scalar.copy(
-                out=x_laid[s][:].bitcast(F32).rearrange("p (r u) -> p r u", u=2),
-                in_=turned[s, 0][:].rearrange("p (u r) -> p r u", u=2),
-            )
-
-        def sort_x(copy, s):
-            x_sorted[s] = passing("x_sorted", [P, K // 2], F32)
+        def sort(copy, j, part0, part1):
+            if j not in in_order:
+                in_order[j] = passing("in_order", [P, 3 * 512], F32, 2)
+            words = slice(512 * part0, 512 * part1)
             copy(
-                out=x_sorted[s][:].rearrange("p (g u m) -> p g u m", u=2, m=P),
-                in_=x_rows[s][:].bitcast(F32).rearrange("p (g m u) -> p g u m", u=2, m=P),
+                out=in_order[j][:, words].rearrange("p (g u m) -> p g u m", u=2, m=P),
+                in_=rows[j][:].bitcast(F32)[:, words].rearrange("p (g m u) -> p g u m", u=2, m=P),
             )
+            for part in range(part0, part1):
+                is_sorted.add((j, part))
 
-        def widen_sorted(s):
-            x_sorted[s] = passing("x_sorted", [P, K // 2], F32)
-            for kk in range(2):
-                cols = slice(512 * kk, 512 * kk + 512)
-                nc.vector.tensor_scalar(
-                    out=x_sorted[s][:].bitcast(BF16)[:, cols].rearrange("p (u m e) -> p m u e", u=2, e=2),
-                    in0=x_raw[s][:, cols].bitcast(FP8),
-                    scalar1=ones[:],
-                    scalar2=None,
-                    op0=MULT,
-                )
-
-        def sort_xo(copy, j):
-            xo_sorted[j] = passing("xo_sorted", [P, O], F32, 2)
-            copy(
-                out=xo_sorted[j][:].rearrange("p (t u m) -> p t u m", t=2, u=2),
-                in_=xo_raw[j][:].bitcast(F32).rearrange("p (t m u) -> p t u m", t=2, u=2),
-            )
-
-        def transpose_words(ps, words, is_sorted, parts):
-            for i in parts:
+        def turn(j, part, b, runs=(0, 1)):
+            ps = bank(b)
+            for i in runs:
+                c0 = 512 * part + 256 * i
                 for u in range(2):
-                    if is_sorted:
-                        src = words[:, 256 * i + P * u : 256 * i + P * u + P]
+                    if (j, part) in is_sorted:
+                        src = in_order[j][:, c0 + P * u : c0 + P * u + P]
                     else:
-                        src = words[:, 256 * i + u : 256 * i + 256 : 2]
+                        src = rows[j][:].bitcast(F32)[:, c0 + u : c0 + 256 : 2]
                     o0 = 256 * u + P * i
                     nc.tensor.transpose(ps[:, o0 : o0 + P], src, ident[:])
+                turned[j, part, i] = ps
 
-        def turn_x(s, b, passes=(0, 1)):
-            ps = bank(b)
-            words = x_sorted[s][:] if s in x_sorted else x_rows[s][:].bitcast(F32)
-            transpose_words(ps, words, s in x_sorted, passes)
-            for kk in passes:
-                turned[s, kk] = ps
+        def laid_part(j, part):
+            if j not in laid:
+                laid[j] = passing("laid", [P, 3 * K], BF16, 3)
+            return laid[j][:, K * PLACE[part] : K * PLACE[part] + K]
 
-        def turn_xo(j, b):
-            ps = bank(b)
-            words = xo_sorted[j][:] if j in xo_sorted else xo_raw[j][:].bitcast(F32)
-            transpose_words(ps, words, j in xo_sorted, (0, 1))
-            turned[j, XO_PASS] = ps
-
-        def xo_out(j):
-            xo_laid[j] = passing("xo_laid", [P, 2 * 512], BF16, 2)
+        def turn_out(j, part):
             nc.scalar.copy(
-                out=xo_laid[j][:].bitcast(F32).rearrange("p (r u) -> p r u", u=2),
-                in_=turned[j, XO_PASS][:].rearrange("p (u r) -> p r u", u=2),
+                out=laid_part(j, part).bitcast(F32).rearrange("p (r u) -> p r u", u=2),
+                in_=turned[j, part, 0][:].rearrange("p (u r) -> p r u", u=2),
             )
 
-        def scale_x(s, k0=0, k1=2):
-            if s not in x_laid:
-                x_laid[s] = passing("x_laid", [P, K], BF16)
+        def scale_turned(s, k0=0, k1=2):
+            j, part = divmod(s, 2)
             nc.vector.tensor_tensor(
-                out=x_laid[s][:, 512 * k0 : 512 * k1].rearrange(
+                out=laid_part(j, part)[:, 512 * k0 : 512 * k1].rearrange(
                     "p (g r u e) -> p g r u e", r=P, u=2, e=2
                 ),
-                in0=turned[s, k0][:]
+                in0=turned[j, part, k0][:]
                 .bitcast(BF16)
                 .rearrange("p (u g r e) -> p g r u e", u=2, g=2, e=2)[:, k0:k1, :, :, :],
                 in1=scale_by_k[:, k0:k1, :]
@@ -218,16 +193,15 @@ def tile_recomputed_hidden_weight_gradient_s3_kernel(
                 op=MULT,
             )
 
-        def quantise(codes, plane, laid, w0, w1):
+        def quantise(codes, plane, values, w0, w1):
             nc.vector.quantize_mx(
-                out=codes[:, w0:w1].bitcast(FP8X4), scales=plane[:, w0:w1], in_=laid
+                out=codes[:, w0:w1].bitcast(FP8X4),
+                scales=plane[:, w0:w1],
+                in_=values[:, 4 * w0 : 4 * w1],
             )
 
-        def quant_x(s, k0=0, k1=2):
-            quantise(x_codes[s], x_plane[s], x_laid[s][:, 512 * k0 : 512 * k1], P * k0, P * k1)
-
-        def quant_xo(j):
-            quantise(xo_codes[j], xo_plane[j], xo_laid[j][:], 0, 2 * P)
+        def quant_x(j, run0, run1):
+            quantise(x_codes[j], x_plane[j], laid[j], P * run0, P * run1)
 
         def lay_wo(copy, q):
             copy(
@@ -239,29 +213,28 @@ def tile_recomputed_hidden_weight_gradient_s3_kernel(
 
         def quant_wo(q0, q1):
             w0, w1 = QUARTER * q0, QUARTER * q1
-            quantise(wo_codes, wo_plane, wo_laid[:, 4 * w0 : 4 * w1], w0, w1)
+            quantise(wo_codes, wo_plane, wo_laid, w0, w1)
 
-        sums, planes, h_late = {}, {}, {}
+        sums = {}
 
         def unit(s, hf, passes, b=None):
             if b is not None:
                 sums[s, hf] = (bank(b), [])
             ps, done = sums[s, hf]
+            j, part = divmod(s, 2)
             cols = slice(BANK * hf, BANK * hf + BANK)
             for kk in passes:
                 if kk == XO_PASS:
-                    r = slice(P * (s % 2), P * (s % 2) + P)
-                    lhsT, lhsT_scale = xo_codes[s // 2][:, r], xo_plane[s // 2][:, r]
+                    w0 = 2 * P * PLACE[XO_PART] + P * part
                     rhs, rhs_scale = wo_codes[:, cols].bitcast(FP8X4), wo_plane[:, cols]
                 else:
-                    r = slice(P * kk, P * kk + P)
-                    lhsT, lhsT_scale = x_codes[s][:, r], x_plane[s][:, r]
+                    w0 = 2 * P * PLACE[part] + P * kk
                     rhs, rhs_scale = w_codes[hf][:, kk, :].bitcast(FP4X4), w_plane[:, kk, cols]
                 done.append(kk)
                 nc.tensor.matmul_mx(
                     out=ps[:],
-                    lhsT=lhsT.bitcast(FP8X4),
-                    lhsT_scale=lhsT_scale,
+                    lhsT=x_codes[j][:, w0 : w0 + P].bitcast(FP8X4),
+                    lhsT_scale=x_plane[j][:, w0 : w0 + P],
                     rhs=rhs,
                     rhs_scale=rhs_scale,
                     start=(len(done) == 1),
@@ -272,43 +245,36 @@ def tile_recomputed_hidden_weight_gradient_s3_kernel(
             nc.scalar.activation(out=gate_abs[:], in_=gates[:], func=ACT.Abs)
             nc.scalar.activation(out=gate_sign[:], in_=gates[:], func=ACT.Sign)
 
+        def plane(g, f0, f1):
+            if g < 2:
+                return both[g][:].rearrange("p (t f) -> p t f", t=4)[:, :, f0:f1]
+            f00 = f0 // BANK * BANK
+            return last[f0 // BANK][:].rearrange("p (t f) -> p t f", t=4)[:, :, f0 - f00 : f1 - f00]
+
         def empty(s, hf):
             g, t = divmod(s, 4)
-            if (g, hf) not in planes:
-                planes[g, hf] = kept("planes%d_%d" % (g, hf), [P, 4 * BANK], BF16)
             nc.scalar.activation(
-                out=planes[g, hf][:, BANK * t : BANK * t + BANK],
+                out=plane(g, BANK * hf, BANK * hf + BANK)[:, t, :],
                 in_=sums[s, hf][0][:],
                 func=ACT.Relu,
                 scale=gate_abs[:, s : s + 1],
             )
 
-        def sign(s, hf):
+        def sign(s, hf0, hf1):
             g, t = divmod(s, 4)
-            plane = planes[g, hf][:, BANK * t : BANK * t + BANK]
+            row = plane(g, BANK * hf0, BANK * hf1)[:, t, :]
             nc.vector.tensor_scalar(
-                out=plane, in0=plane, scalar1=gate_sign[:, s : s + 1], scalar2=None, op0=MULT
+                out=row, in0=row, scalar1=gate_sign[:, s : s + 1], scalar2=None, op0=MULT
             )
 
-        def weave(g, c, copy=on_vector):
-            if g < 2:
-                dst = h_early[c][:, 512 * g : 512 * g + 512]
-            else:
-                h_late[c] = passing("h_late", [P, 512], BF16, 3)
-                dst = h_late[c][:]
-            hf, f0 = divmod(P * c, BANK)
+        def weave(g, c0, c1, copy=on_vector):
             copy(
-                out=dst.rearrange("p (c i t) -> p c t i", i=4, t=4),
-                in_=planes[g, hf][:]
-                .rearrange("p (t f) -> p t f", t=4)[:, :, f0 : f0 + P]
-                .rearrange("p t (c i) -> p c t i", i=4),
+                out=h_laid[g][:, 512 * c0 : 512 * c1].rearrange("p (c i t) -> p c t i", i=4, t=4),
+                in_=plane(g, P * c0, P * c1).rearrange("p t (c i) -> p c t i", i=4),
             )
 
-        def quant_early(c):
-            quantise(h_codes[c], h_plane[c], h_early[c][:], 0, 2 * P)
-
-        def quant_late(c):
-            quantise(h_codes[c], h_plane[c], h_late[c][:], 2 * P, 3 * P)
+        def quant_h(g, c0, c1):
+            quantise(h_codes[g], h_plane[g], h_laid[g], P * c0, P * c1)
 
         pieces = {}
 
@@ -321,8 +287,8 @@ def tile_recomputed_hidden_weight_gradient_s3_kernel(
                 for g in range(GROUPS):
                     nc.tensor.matmul_mx(
                         out=acc[:, j : j + step],
-                        lhsT=h_codes[c][:, P * g : P * g + P].bitcast(FP8X4),
-                        lhsT_scale=h_plane[c][:, P * g : P * g + P],
+                        lhsT=h_codes[g][:, P * c : P * c + P].bitcast(FP8X4),
+                        lhsT_scale=h_plane[g][:, P * c : P * c + P],
                         rhs=dy_codes[:, g, 2 * n1 : 2 * n1 + 2 * step].bitcast(FP4X4),
                         rhs_scale=dy_plane[:, g, n1 : n1 + step],
                         start=(g == 0),
@@ -346,8 +312,13 @@ def tile_recomputed_hidden_weight_gradient_s3_kernel(
                 in_=gate.rearrange("(g m t) -> m g t", m=P, t=4),
             )
 
+        def warm_up(count, b):
+            ps = bank(b)
+            for j in range(count):
+                nc.tensor.matmul(ps[:], lhsT=zeros[:, 0:P], rhs=zeros[:], start=True, stop=True)
+
+        nc.vector.memset(zeros[:].bitcast(I32), 0)
         nc.vector.memset(w_plane[:].rearrange("p g n -> p (g n)").bitcast(I32), 0)
-        nc.vector.memset(ones[:], 1.0)
         nc.vector.memset(dy_plane[:].rearrange("p g n -> p (g n)").bitcast(I32), 0)
         make_identity(nc, ident[:])
         load_x_scale()
@@ -355,14 +326,14 @@ def tile_recomputed_hidden_weight_gradient_s3_kernel(
         load_x(1, 2)
         load_x(2, 4)
         load_xo(0)
-        load_xo(1)
         load_wo(0, 2)
+        load_xo(1)
         load_w(0)
         load_scale_bytes(w_plane, w_scales)
-        load_w(1)
         load_gates()
-        load_x(4, 6)
+        load_w(1)
         load_wo(2, 4)
+        load_x(4, 6)
         load_xo(2)
         load_x(6, 8)
         load_xo(3)
@@ -374,245 +345,215 @@ def tile_recomputed_hidden_weight_gradient_s3_kernel(
         nc.sync.dma_start(out=dy_codes[:], in_=dy_words.rearrange("g p n -> p g n"))
 
         X, XO, ALL = (0, 1), (XO_PASS,), (0, 1, XO_PASS)
-        spread(0, 5)
+        warm_up(3, 4)
         widen(on_vector, 0, 0, 512)
         widen(on_scalar, 0, 512, K)
-        spread(1, 7)
-        widen_sorted(1)
+        spread(0, 5)
+        widen(on_vector, 1)
         spread_out(0)
-        turn_x(0, 0, (0,))
-        scale_x(0, 0, 1)
+        spread(1, 7)
         widen(on_scalar, 2)
-        turn_x(0, 1, (1,))
-        scale_x(0, 1, 2)
+        turn(0, 0, 0, (0,))
+        scale_turned(0, 0, 1)
         widen(on_scalar, 3)
-        turn_x(1, 2)
-        quant_x(0, 0, 1)
+        turn(0, 0, 1, (1,))
+        scale_turned(0, 1, 2)
         spread_out(1)
-        turn_xo(0, 6)
-        scale_x(1)
+        warm_up(1, 4)
         lay_wo(on_scalar, 0)
-        turn_x(2, 3)
-        quant_x(0, 1, 2)
-        xo_out(0)
-        turn_xo(1, 5)
-        quant_x(1)
+        turn(0, 1, 2)
+        scale_turned(1)
+        turn(1, 0, 3)
+        quant_x(0, 0, 2)
+        warm_up(1, 4)
+        quant_x(0, 4, 6)
+        turn(0, 2, 6)
+        scale_turned(2)
+        turn_out(0, 2)
+        turn(1, 1, 4)
+        quant_x(0, 2, 4)
         lay_wo(on_scalar, 1)
-        turn_x(3, 4)
-        scale_x(2)
-        xo_out(1)
+        turn(1, 2, 5)
+        quant_x(1, 0, 2)
+        turn_out(1, 2)
         unit(0, 0, X, 7)
-        scale_x(3)
+        scale_turned(3)
         split_gate()
         unit(1, 0, X, 0)
-        quant_x(2)
+        quant_wo(0, 2)
         lay_wo(on_scalar, 2)
         unit(0, 1, X, 1)
-        quant_wo(0, 2)
-        sort_xo(on_scalar, 2)
+        quant_x(1, 2, 6)
+        lay_wo(on_scalar, 3)
         unit(1, 1, X, 2)
-        quant_x(3)
-        unit(2, 0, X, 3)
-        quant_xo(0)
-        unit(2, 1, X, 6)
-        quant_xo(1)
-        unit(0, 0, XO)
         scale_bytes(4)
+        unit(2, 0, X, 3)
+        scale_bytes(5)
+        unit(2, 1, X, 6)
+        quant_wo(2, 4)
+        unit(0, 0, XO)
+        scale_bytes(6)
         empty(0, 0)
         unit(1, 0, XO)
-        lay_wo(on_vector, 3)
-        sort_x(on_scalar, 4)
-        unit(2, 0, XO)
-        scale_bytes(5)
         empty(1, 0)
+        unit(2, 0, XO)
+        sort(on_scalar, 2, 2, 3)
         unit(3, 0, ALL, 4)
-        quant_wo(2, 4)
         empty(2, 0)
         unit(3, 1, X, 5)
-        sort_xo(on_vector, 3)
-        turn_x(4, 7)
-        scale_bytes(6)
-        x_out(4)
-        turn_xo(2, 0)
-        quant_x(4)
-        xo_out(2)
-        turn_x(5, 3)
-        quant_xo(2)
+        turn(2, 0, 7)
+        turn_out(2, 0)
+        turn(2, 2, 0)
+        turn_out(2, 2)
+        turn(2, 1, 3)
+        quant_x(2, 0, 4)
         empty(3, 0)
         unit(0, 1, XO)
         scale_bytes(7)
-        x_out(5)
+        turn_out(2, 1)
         unit(1, 1, XO)
-        sort_x(on_vector, 6)
+        sort(on_vector, 3, 0, 1)
         empty(0, 1)
         unit(2, 1, XO)
-        quant_x(5)
+        sort(on_vector, 3, 1, 2)
         empty(1, 1)
         unit(3, 1, XO)
-        sort_x(on_vector, 7)
-        empty(2, 1)
+        quant_x(2, 4, 6)
+        sort(on_scalar, 3, 2, 3)
         unit(4, 1, ALL, 4)
         scale_bytes(8)
-        empty(3, 1)
+        empty(2, 1)
         unit(4, 0, ALL, 1)
-        sort_xo(on_vector, 4)
-        turn_x(6, 0)
-        x_out(6)
-        turn_xo(3, 7)
-        quant_x(6)
-        xo_out(3)
-        turn_x(7, 3)
-        quant_xo(3)
-        x_out(7)
-        unit(5, 1, ALL, 2)
         scale_bytes(9)
-        empty(4, 1)
+        turn(3, 0, 7)
+        turn_out(3, 0)
+        turn(3, 2, 0)
+        turn_out(3, 2)
+        turn(3, 1, 3)
+        quant_x(3, 0, 4)
+        empty(3, 1)
+        unit(5, 1, ALL, 2)
+        sort(on_vector, 4, 0, 3)
+        turn_out(3, 1)
         unit(5, 0, ALL, 6)
-        sort_x(on_vector, 8)
-        empty(4, 0)
+        quant_x(3, 4, 6)
+        empty(4, 1)
         unit(6, 1, ALL, 5)
-        sort_x(on_vector, 9)
-        empty(5, 1)
-        turn_xo(4, 7)
-        quant_x(7)
-        xo_out(4)
-        turn_x(8, 0)
         scale_bytes(10)
-        x_out(8)
-        turn_x(9, 3)
-        sort_xo(on_vector, 5)
-        x_out(9)
-        unit(6, 0, ALL, 4)
+        empty(4, 0)
+        turn(4, 0, 7)
         scale_bytes(11)
+        empty(5, 1)
+        turn(4, 2, 0)
+        turn_out(4, 0)
+        turn(4, 1, 3)
+        turn_out(4, 2)
+        unit(6, 0, ALL, 4)
+        quant_x(4, 0, 4)
         empty(5, 0)
         unit(7, 1, ALL, 1)
-        sort_x(on_vector, 10)
-        empty(6, 1)
+        sort(on_vector, 5, 0, 3)
+        turn_out(4, 1)
         unit(7, 0, ALL, 2)
-        quant_x(8)
-        empty(6, 0)
-        turn_x(10, 0)
-        quant_xo(4)
-        x_out(10)
-        turn_xo(5, 7)
-        sort_x(on_vector, 11)
-        xo_out(5)
-        turn_x(11, 3)
-        quant_x(9)
-        x_out(11)
+        quant_x(4, 4, 6)
+        empty(6, 1)
         unit(8, 1, ALL, 6)
-        sign(0, 1)
+        sign(0, 0, 2)
+        empty(6, 0)
+        turn(5, 0, 7)
+        sign(1, 0, 2)
         empty(7, 1)
-        unit(9, 1, ALL, 5)
-        sign(1, 1)
+        turn(5, 2, 0)
+        sign(2, 0, 2)
         empty(7, 0)
-        sign(2, 1)
+        turn(5, 1, 3)
+        sign(3, 0, 2)
+        turn_out(5, 0)
+        unit(9, 1, ALL, 5)
+        sign(4, 0, 2)
+        turn_out(5, 2)
+        unit(8, 0, ALL, 4)
+        weave(0, 4, 6)
+        turn_out(5, 1)
+        quant_x(5, 0, 4)
         empty(8, 1)
-        sign(3, 1)
+        unit(10, 1, ALL, 1)
+        sign(5, 0, 2)
         empty(9, 1)
-        sign(4, 1)
-        sign(5, 1)
-        sign(6, 1)
-        weave(0, 4)
-        quant_x(10)
-        quant_xo(5)
-        unit(10, 1, ALL, 4)
-        quant_x(11)
-        empty(10, 1)
-        unit(11, 1, ALL, 1)
-        sign(7, 1)
-        empty(11, 1)
-        unit(8, 0, ALL, 2)
-        weave(0, 5)
+        quant_x(5, 4, 6)
         empty(8, 0)
+        unit(11, 1, ALL, 2)
+        sign(6, 0, 2)
+        empty(10, 1)
         unit(9, 0, ALL, 6)
-        weave(1, 4)
-        empty(9, 0)
+        sign(7, 0, 2)
+        empty(11, 1)
         unit(10, 0, ALL, 5)
-        weave(1, 5)
-        empty(10, 0)
+        quant_h(0, 4, 6)
+        empty(9, 0)
         unit(11, 0, ALL, 4)
-        quant_early(4)
+        weave(1, 4, 6)
+        empty(10, 0)
+        sign(8, 1, 2)
         empty(11, 0)
-        sign(8, 1)
-        sign(9, 1)
-        sign(10, 1)
-        sign(11, 1)
-        quant_early(5)
-        weave(2, 4)
-        weave(2, 5)
-        quant_late(4)
+        sign(9, 1, 2)
+        sign(10, 1, 2)
+        sign(11, 1, 2)
+        quant_h(1, 4, 6)
+        weave(2, 4, 5)
+        weave(2, 5, 6)
+        quant_h(2, 4, 5)
         piece(4, 0, BANK, 7)
-        weave(0, 6)
+        quant_h(2, 5, 6)
         store(on_scalar, 4, 0)
         piece(4, 512, BANK, 0)
-        weave(1, 6)
+        weave(0, 6, 8)
         store(on_scalar, 4, 512)
-        quant_late(5)
         piece(5, 0, BANK, 1)
-        weave(2, 6)
+        weave(1, 6, 8)
         store(on_scalar, 5, 0)
         piece(5, 512, BANK, 2)
-        quant_early(6)
+        weave(2, 6, 8)
         store(on_scalar, 5, 512)
-        quant_late(6)
+        quant_h(0, 6, 8)
+        quant_h(1, 6, 8)
+        quant_h(2, 6, 8)
         piece(6, 0, BANK, 3)
-        weave(0, 7)
+        sign(8, 0, 1)
         store(on_scalar, 6, 0)
         piece(6, 512, BANK, 4)
-        weave(1, 7)
+        sign(9, 0, 1)
         store(on_scalar, 6, 512)
-        weave(2, 7)
-        quant_early(7)
-        quant_late(7)
         piece(7, 0, BANK, 5)
-        sign(0, 0)
+        sign(10, 0, 1)
         store(on_scalar, 7, 0)
         piece(7, 512, BANK, 6)
-        sign(1, 0)
+        sign(11, 0, 1)
         store(on_scalar, 7, 512)
-        sign(2, 0)
-        sign(3, 0)
-        sign(4, 0)
-        sign(5, 0)
-        sign(6, 0)
-        sign(7, 0)
-        sign(8, 0)
-        sign(9, 0)
-        sign(10, 0)
-        sign(11, 0)
-        weave(0, 0)
-        weave(1, 0)
-        weave(2, 0)
-        quant_early(0)
-        quant_late(0)
+        weave(0, 0, 2)
+        weave(1, 0, 2)
+        weave(2, 0, 2)
+        quant_h(0, 0, 2)
+        quant_h(1, 0, 2)
+        quant_h(2, 0, 2)
         piece(0, 0, BANK, 7)
-        weave(0, 1)
+        weave(0, 2, 4)
         store(on_scalar, 0, 0)
         piece(0, 512, BANK, 0)
-        weave(1, 1)
+        weave(1, 2, 4)
         store(on_scalar, 0, 512)
-        weave(2, 1)
-        quant_early(1)
-        quant_late(1)
         piece(1, 0, BANK, 1)
-        weave(0, 2)
+        weave(2, 2, 4)
         store(on_scalar, 1, 0)
         piece(1, 512, BANK, 2)
-        weave(1, 2)
+        quant_h(0, 2, 4)
         store(on_scalar, 1, 512)
-        weave(2, 2)
-        quant_early(2)
-        quant_late(2)
+        quant_h(1, 2, 4)
+        quant_h(2, 2, 4)
         piece(2, 0, BANK, 3)
-        weave(0, 3)
         store(on_scalar, 2, 0)
         piece(2, 512, BANK, 4)
-        weave(1, 3)
         store(on_scalar, 2, 512)
-        weave(2, 3)
-        quant_early(3)
-        quant_late(3)
         piece(3, 0, 256, 5)
         store(on_scalar, 3, 0)
         piece(3, 256, 256, 6)

@@ -324,241 +324,234 @@ def tile_recomputed_hidden_weight_gradient_s3_kernel(
         load_x_scale()
         load_x(0, 1)
         load_x(1, 2)
+        load_wo(0, 1)
         load_x(2, 4)
         load_xo(0)
-        load_wo(0, 2)
         load_xo(1)
+        load_wo(1, 3)
         load_w(0)
         load_scale_bytes(w_plane, w_scales)
         load_gates()
+        load_wo(3, 4)
         load_w(1)
-        load_wo(2, 4)
         load_x(4, 6)
         load_xo(2)
         load_x(6, 8)
         load_xo(3)
-        load_x(8, 10)
+        load_x(8, 12)
         load_xo(4)
-        load_x(10, 12)
         load_xo(5)
         load_scale_bytes(dy_plane, dy_scales)
         nc.sync.dma_start(out=dy_codes[:], in_=dy_words.rearrange("g p n -> p g n"))
 
         X, XO, ALL = (0, 1), (XO_PASS,), (0, 1, XO_PASS)
-        warm_up(3, 4)
+        spread(0, 3)
         widen(on_vector, 0, 0, 512)
         widen(on_scalar, 0, 512, K)
-        spread(0, 5)
-        widen(on_vector, 1)
-        spread_out(0)
-        spread(1, 7)
-        widen(on_scalar, 2)
-        turn(0, 0, 0, (0,))
-        scale_turned(0, 0, 1)
-        widen(on_scalar, 3)
-        turn(0, 0, 1, (1,))
-        scale_turned(0, 1, 2)
+        spread(1, 4)
+        widen(on_vector, 1, 512, K)
+        widen(on_scalar, 1, 0, 512)
+        turn(0, 0, 0)
+        lay_wo(on_vector, 0)
         spread_out(1)
-        warm_up(1, 4)
-        lay_wo(on_scalar, 0)
-        turn(0, 1, 2)
+        turn(0, 1, 1)
+        scale_turned(0)
+        spread_out(0)
+        turn(0, 2, 2)
         scale_turned(1)
-        turn(1, 0, 3)
+        widen(on_scalar, 2)
+        turn(1, 2, 7)
         quant_x(0, 0, 2)
-        warm_up(1, 4)
-        quant_x(0, 4, 6)
-        turn(0, 2, 6)
+        widen(on_scalar, 3)
+        turn(1, 0, 0)
         scale_turned(2)
         turn_out(0, 2)
-        turn(1, 1, 4)
-        quant_x(0, 2, 4)
+        warm_up(2, 5)
+        quant_x(0, 2, 6)
         lay_wo(on_scalar, 1)
-        turn(1, 2, 5)
-        quant_x(1, 0, 2)
-        turn_out(1, 2)
-        unit(0, 0, X, 7)
-        scale_turned(3)
-        split_gate()
-        unit(1, 0, X, 0)
+        turn(1, 1, 1)
         quant_wo(0, 2)
+        turn_out(1, 2)
+        unit(0, 0, X, 3)
+        quant_x(1, 0, 4)
+        split_gate()
+        unit(1, 0, X, 4)
+        scale_turned(3)
         lay_wo(on_scalar, 2)
-        unit(0, 1, X, 1)
-        quant_x(1, 2, 6)
-        lay_wo(on_scalar, 3)
-        unit(1, 1, X, 2)
-        scale_bytes(4)
-        unit(2, 0, X, 3)
-        scale_bytes(5)
-        unit(2, 1, X, 6)
-        quant_wo(2, 4)
         unit(0, 0, XO)
-        scale_bytes(6)
-        empty(0, 0)
+        scale_bytes(4)
+        lay_wo(on_scalar, 3)
         unit(1, 0, XO)
+        quant_x(1, 4, 6)
         empty(1, 0)
-        unit(2, 0, XO)
+        unit(2, 0, ALL, 5)
+        scale_bytes(5)
+        empty(0, 0)
+        unit(0, 1, X, 6)
+        quant_wo(2, 4)
         sort(on_scalar, 2, 2, 3)
-        unit(3, 0, ALL, 4)
-        empty(2, 0)
-        unit(3, 1, X, 5)
-        turn(2, 0, 7)
-        turn_out(2, 0)
-        turn(2, 2, 0)
-        turn_out(2, 2)
-        turn(2, 1, 3)
-        quant_x(2, 0, 4)
-        empty(3, 0)
-        unit(0, 1, XO)
+        unit(1, 1, X, 7)
+        scale_bytes(6)
+        sort(on_scalar, 2, 0, 1)
+        unit(2, 1, X, 4)
         scale_bytes(7)
+        empty(2, 0)
+        unit(3, 0, ALL, 3)
+        empty(3, 0)
+        turn(2, 0, 0)
+        turn_out(2, 0)
+        turn(2, 2, 2)
+        turn_out(2, 2)
+        turn(2, 1, 1)
+        quant_x(2, 0, 4)
         turn_out(2, 1)
+        unit(0, 1, XO)
+        sort(on_vector, 3, 0, 3)
         unit(1, 1, XO)
-        sort(on_vector, 3, 0, 1)
-        empty(0, 1)
-        unit(2, 1, XO)
-        sort(on_vector, 3, 1, 2)
-        empty(1, 1)
-        unit(3, 1, XO)
         quant_x(2, 4, 6)
-        sort(on_scalar, 3, 2, 3)
-        unit(4, 1, ALL, 4)
+        unit(2, 1, XO)
         scale_bytes(8)
         empty(2, 1)
-        unit(4, 0, ALL, 1)
+        unit(3, 1, ALL, 5)
         scale_bytes(9)
-        turn(3, 0, 7)
-        turn_out(3, 0)
-        turn(3, 2, 0)
-        turn_out(3, 2)
-        turn(3, 1, 3)
-        quant_x(3, 0, 4)
+        empty(0, 1)
+        unit(4, 1, ALL, 3)
+        empty(1, 1)
+        turn(3, 0, 0)
         empty(3, 1)
-        unit(5, 1, ALL, 2)
-        sort(on_vector, 4, 0, 3)
+        turn(3, 2, 2)
+        turn_out(3, 0)
+        turn(3, 1, 1)
+        turn_out(3, 2)
+        unit(4, 0, ALL, 4)
+        quant_x(3, 0, 4)
         turn_out(3, 1)
-        unit(5, 0, ALL, 6)
-        quant_x(3, 4, 6)
+        unit(5, 1, ALL, 6)
+        sort(on_vector, 4, 0, 3)
         empty(4, 1)
+        unit(5, 0, ALL, 7)
+        quant_x(3, 4, 6)
+        empty(4, 0)
         unit(6, 1, ALL, 5)
         scale_bytes(10)
-        empty(4, 0)
-        turn(4, 0, 7)
-        scale_bytes(11)
         empty(5, 1)
-        turn(4, 2, 0)
-        turn_out(4, 0)
-        turn(4, 1, 3)
-        turn_out(4, 2)
-        unit(6, 0, ALL, 4)
-        quant_x(4, 0, 4)
+        turn(4, 0, 0)
+        scale_bytes(11)
         empty(5, 0)
-        unit(7, 1, ALL, 1)
+        turn(4, 2, 2)
         sort(on_vector, 5, 0, 3)
+        turn_out(4, 0)
+        turn(4, 1, 1)
+        turn_out(4, 2)
+        unit(6, 0, ALL, 3)
+        quant_x(4, 0, 4)
         turn_out(4, 1)
-        unit(7, 0, ALL, 2)
+        unit(7, 1, ALL, 4)
         quant_x(4, 4, 6)
         empty(6, 1)
-        unit(8, 1, ALL, 6)
-        sign(0, 0, 2)
-        empty(6, 0)
-        turn(5, 0, 7)
-        sign(1, 0, 2)
-        empty(7, 1)
-        turn(5, 2, 0)
-        sign(2, 0, 2)
-        empty(7, 0)
-        turn(5, 1, 3)
+        unit(7, 0, ALL, 6)
         sign(3, 0, 2)
+        empty(6, 0)
+        turn(5, 0, 0)
+        sign(2, 0, 2)
+        empty(7, 1)
+        turn(5, 2, 2)
+        sign(1, 0, 2)
         turn_out(5, 0)
-        unit(9, 1, ALL, 5)
-        sign(4, 0, 2)
+        turn(5, 1, 1)
+        sign(0, 0, 2)
         turn_out(5, 2)
-        unit(8, 0, ALL, 4)
-        weave(0, 4, 6)
+        unit(8, 1, ALL, 7)
+        sign(4, 0, 2)
         turn_out(5, 1)
+        unit(9, 1, ALL, 5)
+        weave(0, 4, 6)
+        empty(7, 0)
+        unit(8, 0, ALL, 3)
         quant_x(5, 0, 4)
         empty(8, 1)
-        unit(10, 1, ALL, 1)
-        sign(5, 0, 2)
-        empty(9, 1)
+        unit(10, 1, ALL, 4)
         quant_x(5, 4, 6)
-        empty(8, 0)
-        unit(11, 1, ALL, 2)
-        sign(6, 0, 2)
-        empty(10, 1)
-        unit(9, 0, ALL, 6)
+        empty(9, 1)
+        unit(11, 1, ALL, 6)
         sign(7, 0, 2)
+        empty(10, 1)
+        unit(9, 0, ALL, 7)
+        sign(6, 0, 2)
         empty(11, 1)
         unit(10, 0, ALL, 5)
+        sign(5, 0, 2)
+        empty(8, 0)
+        unit(11, 0, ALL, 0)
         quant_h(0, 4, 6)
         empty(9, 0)
-        unit(11, 0, ALL, 4)
         weave(1, 4, 6)
         empty(10, 0)
-        sign(8, 1, 2)
+        sign(10, 1, 2)
         empty(11, 0)
         sign(9, 1, 2)
-        sign(10, 1, 2)
-        sign(11, 1, 2)
+        sign(8, 1, 2)
         quant_h(1, 4, 6)
+        sign(11, 1, 2)
         weave(2, 4, 5)
         weave(2, 5, 6)
         quant_h(2, 4, 5)
-        piece(4, 0, BANK, 7)
-        quant_h(2, 5, 6)
+        piece(4, 0, BANK, 1)
+        weave(2, 6, 8)
         store(on_scalar, 4, 0)
-        piece(4, 512, BANK, 0)
-        weave(0, 6, 8)
+        piece(4, 512, BANK, 2)
+        quant_h(2, 5, 6)
         store(on_scalar, 4, 512)
-        piece(5, 0, BANK, 1)
+        piece(5, 0, BANK, 3)
+        weave(0, 6, 8)
+        weave(0, 0, 2, on_scalar)
+        piece(5, 512, BANK, 4)
         weave(1, 6, 8)
         store(on_scalar, 5, 0)
-        piece(5, 512, BANK, 2)
-        weave(2, 6, 8)
-        store(on_scalar, 5, 512)
         quant_h(0, 6, 8)
-        quant_h(1, 6, 8)
+        store(on_scalar, 5, 512)
         quant_h(2, 6, 8)
-        piece(6, 0, BANK, 3)
-        sign(8, 0, 1)
-        store(on_scalar, 6, 0)
-        piece(6, 512, BANK, 4)
-        sign(9, 0, 1)
-        store(on_scalar, 6, 512)
-        piece(7, 0, BANK, 5)
-        sign(10, 0, 1)
-        store(on_scalar, 7, 0)
-        piece(7, 512, BANK, 6)
+        quant_h(1, 6, 8)
+        piece(6, 0, BANK, 5)
         sign(11, 0, 1)
+        store(on_scalar, 6, 0)
+        piece(6, 512, BANK, 6)
+        sign(10, 0, 1)
+        store(on_scalar, 6, 512)
+        piece(7, 0, BANK, 7)
+        sign(9, 0, 1)
+        store(on_scalar, 7, 0)
+        piece(7, 512, BANK, 0)
+        sign(8, 0, 1)
         store(on_scalar, 7, 512)
-        weave(0, 0, 2)
         weave(1, 0, 2)
         weave(2, 0, 2)
         quant_h(0, 0, 2)
-        quant_h(1, 0, 2)
         quant_h(2, 0, 2)
-        piece(0, 0, BANK, 7)
+        quant_h(1, 0, 2)
+        piece(0, 0, BANK, 1)
         weave(0, 2, 4)
         store(on_scalar, 0, 0)
-        piece(0, 512, BANK, 0)
-        weave(1, 2, 4)
-        store(on_scalar, 0, 512)
-        piece(1, 0, BANK, 1)
+        piece(0, 512, BANK, 2)
         weave(2, 2, 4)
+        store(on_scalar, 0, 512)
+        piece(1, 0, BANK, 3)
+        weave(1, 2, 4)
         store(on_scalar, 1, 0)
-        piece(1, 512, BANK, 2)
-        quant_h(0, 2, 4)
-        store(on_scalar, 1, 512)
-        quant_h(1, 2, 4)
+        piece(1, 512, BANK, 4)
         quant_h(2, 2, 4)
-        piece(2, 0, BANK, 3)
+        store(on_scalar, 1, 512)
+        quant_h(0, 2, 4)
+        quant_h(1, 2, 4)
+        piece(2, 0, BANK, 5)
         store(on_scalar, 2, 0)
-        piece(2, 512, BANK, 4)
+        piece(2, 512, BANK, 6)
         store(on_scalar, 2, 512)
-        piece(3, 0, 256, 5)
+        piece(3, 0, 256, 7)
         store(on_scalar, 3, 0)
-        piece(3, 256, 256, 6)
+        piece(3, 256, 256, 0)
         store(on_vector, 3, 256)
-        piece(3, 512, 256, 7)
+        piece(3, 512, 256, 1)
         store(on_scalar, 3, 512)
-        piece(3, 768, 256, 0)
+        piece(3, 768, 256, 2)
         store(on_vector, 3, 768)

@@ -15,6 +15,7 @@ FP8 = mybir.dt.float8_e4m3fn
 FP8X4 = mybir.dt.float8_e4m3fn_x4
 FP4X4 = mybir.dt.float4_e2m1fn_x4
 MULT = mybir.AluOpType.mult
+ADD = mybir.AluOpType.add
 ACT = mybir.ActivationFunctionType
 
 P = 128
@@ -35,6 +36,10 @@ def tile_recomputed_hidden_weight_gradient_s3_kernel(
 ):
     nc = tc.nc
     on_vector, on_scalar = nc.vector.tensor_copy, nc.scalar.copy
+
+    def on_gpsimd(out, in_):
+        nc.gpsimd.tensor_scalar(out=out, in0=in_, scalar1=1.0, scalar2=0.0, op0=MULT, op1=ADD)
+
     with ExitStack() as ctx:
         keep = ctx.enter_context(tc.tile_pool(name="keep", bufs=1))
         ring = ctx.enter_context(tc.tile_pool(name="ring", bufs=4))
@@ -348,100 +353,103 @@ def tile_recomputed_hidden_weight_gradient_s3_kernel(
         spread(0, 3)
         widen(on_vector, 0, 0, 512)
         widen(on_scalar, 0, 512, K)
-        spread(1, 4)
-        widen(on_vector, 1, 512, K)
-        widen(on_scalar, 1, 0, 512)
-        turn(0, 0, 0)
-        lay_wo(on_vector, 0)
-        spread_out(1)
-        turn(0, 1, 1)
-        scale_turned(0)
+        lay_wo(on_gpsimd, 0)
+        turn(0, 0, 0, (0,))
+        widen(on_vector, 1)
         spread_out(0)
-        turn(0, 2, 2)
-        scale_turned(1)
+        turn(0, 0, 5, (1,))
+        scale_turned(0, 0, 1)
         widen(on_scalar, 2)
-        turn(1, 2, 7)
-        quant_x(0, 0, 2)
+        turn(0, 1, 1)
+        scale_turned(0, 1, 2)
         widen(on_scalar, 3)
+        spread(1, 4)
+        scale_turned(1)
+        spread_out(1)
+        turn(0, 2, 2)
+        quant_x(0, 0, 2)
+        turn_out(0, 2)
         turn(1, 0, 0)
         scale_turned(2)
-        turn_out(0, 2)
-        warm_up(2, 5)
-        quant_x(0, 2, 6)
         lay_wo(on_scalar, 1)
-        turn(1, 1, 1)
-        quant_wo(0, 2)
+        turn(1, 2, 7)
+        quant_x(0, 2, 6)
         turn_out(1, 2)
-        unit(0, 0, X, 3)
-        quant_x(1, 0, 4)
+        warm_up(2, 5)
+        quant_wo(0, 2)
         split_gate()
-        unit(1, 0, X, 4)
-        scale_turned(3)
+        turn(1, 1, 1)
+        quant_x(1, 0, 4)
         lay_wo(on_scalar, 2)
-        unit(0, 0, XO)
-        scale_bytes(4)
+        unit(0, 0, X, 3)
+        scale_turned(3)
         lay_wo(on_scalar, 3)
-        unit(1, 0, XO)
+        unit(1, 0, X, 4)
+        scale_bytes(4)
+        unit(0, 0, XO)
         quant_x(1, 4, 6)
+        unit(1, 0, XO)
+        scale_bytes(5)
         empty(1, 0)
         unit(2, 0, ALL, 5)
-        scale_bytes(5)
+        quant_wo(2, 4)
         empty(0, 0)
         unit(0, 1, X, 6)
-        quant_wo(2, 4)
+        scale_bytes(6)
         sort(on_scalar, 2, 2, 3)
         unit(1, 1, X, 7)
-        scale_bytes(6)
+        scale_bytes(7)
         sort(on_scalar, 2, 0, 1)
         unit(2, 1, X, 4)
-        scale_bytes(7)
         empty(2, 0)
         unit(3, 0, ALL, 3)
         empty(3, 0)
         turn(2, 0, 0)
         turn_out(2, 0)
         turn(2, 2, 2)
+        quant_x(2, 0, 2)
         turn_out(2, 2)
         turn(2, 1, 1)
-        quant_x(2, 0, 4)
+        sort(on_vector, 3, 0, 3)
         turn_out(2, 1)
         unit(0, 1, XO)
-        sort(on_vector, 3, 0, 3)
+        quant_x(2, 2, 6)
         unit(1, 1, XO)
-        quant_x(2, 4, 6)
-        unit(2, 1, XO)
         scale_bytes(8)
+        unit(2, 1, XO)
+        scale_bytes(9)
         empty(2, 1)
         unit(3, 1, ALL, 5)
-        scale_bytes(9)
         empty(0, 1)
-        unit(4, 1, ALL, 3)
+        unit(4, 1, X, 3)
         empty(1, 1)
-        turn(3, 0, 0)
+        unit(4, 0, X, 4)
         empty(3, 1)
-        turn(3, 2, 2)
+        turn(3, 0, 0)
         turn_out(3, 0)
         turn(3, 1, 1)
+        turn(3, 2, 2)
         turn_out(3, 2)
-        unit(4, 0, ALL, 4)
+        unit(4, 1, XO)
         quant_x(3, 0, 4)
         turn_out(3, 1)
-        unit(5, 1, ALL, 6)
+        unit(4, 0, XO)
         sort(on_vector, 4, 0, 3)
+        empty(4, 0)
+        unit(5, 1, ALL, 6)
+        quant_x(3, 4, 6)
         empty(4, 1)
         unit(5, 0, ALL, 7)
-        quant_x(3, 4, 6)
-        empty(4, 0)
-        unit(6, 1, ALL, 5)
         scale_bytes(10)
         empty(5, 1)
-        turn(4, 0, 0)
+        unit(6, 1, ALL, 5)
         scale_bytes(11)
         empty(5, 0)
-        turn(4, 2, 2)
+        turn(4, 0, 0)
         sort(on_vector, 5, 0, 3)
         turn_out(4, 0)
         turn(4, 1, 1)
+        turn(4, 2, 2)
         turn_out(4, 2)
         unit(6, 0, ALL, 3)
         quant_x(4, 0, 4)
@@ -451,14 +459,14 @@ def tile_recomputed_hidden_weight_gradient_s3_kernel(
         empty(6, 1)
         unit(7, 0, ALL, 6)
         sign(3, 0, 2)
-        empty(6, 0)
+        empty(7, 1)
         turn(5, 0, 0)
         sign(2, 0, 2)
-        empty(7, 1)
-        turn(5, 2, 2)
+        empty(6, 0)
+        turn(5, 1, 1)
         sign(1, 0, 2)
         turn_out(5, 0)
-        turn(5, 1, 1)
+        turn(5, 2, 2)
         sign(0, 0, 2)
         turn_out(5, 2)
         unit(8, 1, ALL, 7)

@@ -28,6 +28,7 @@ QUARTER = F // 4
 CHUNKS = F // P
 XO_PASS = 2
 XO_PART = 2
+BF16_ONES = 0x3F803F80
 PLACE = {0: 0, XO_PART: 1, 1: 2}
 
 
@@ -56,7 +57,7 @@ def tile_recomputed_hidden_weight_gradient_s3_kernel(
             return psum.tile([P, BANK], F32, name="bank%d" % b)
 
         ident = kept("ident", [P, P], F32)
-        zeros = kept("zeros", [P, BANK], BF16)
+        ones = kept("ones", [P, BANK], BF16)
         w_codes = [kept("w_codes%d" % hf, [P, 2, F], U8) for hf in range(2)]
         w_plane = kept("w_plane", [P, 2, F], U8)
         dy_codes = kept("dy_codes", [P, GROUPS, 2 * N], U8)
@@ -320,9 +321,9 @@ def tile_recomputed_hidden_weight_gradient_s3_kernel(
         def warm_up(count, b):
             ps = bank(b)
             for j in range(count):
-                nc.tensor.matmul(ps[:], lhsT=zeros[:, 0:P], rhs=zeros[:], start=True, stop=True)
+                nc.tensor.matmul(ps[:], lhsT=ones[:, 0:P], rhs=ones[:], start=True, stop=True)
 
-        nc.vector.memset(zeros[:].bitcast(I32), 0)
+        nc.vector.memset(ones[:].bitcast(I32), BF16_ONES)
         nc.vector.memset(w_plane[:].rearrange("p g n -> p (g n)").bitcast(I32), 0)
         nc.vector.memset(dy_plane[:].rearrange("p g n -> p (g n)").bitcast(I32), 0)
         make_identity(nc, ident[:])
@@ -350,57 +351,59 @@ def tile_recomputed_hidden_weight_gradient_s3_kernel(
         nc.sync.dma_start(out=dy_codes[:], in_=dy_words.rearrange("g p n -> p g n"))
 
         X, XO, ALL = (0, 1), (XO_PASS,), (0, 1, XO_PASS)
-        spread(0, 3)
+        warm_up(4, 6)
         widen(on_vector, 0, 0, 512)
         widen(on_scalar, 0, 512, K)
         lay_wo(on_gpsimd, 0)
-        turn(0, 0, 0, (0,))
+        spread(0, 3)
         widen(on_vector, 1)
         spread_out(0)
-        turn(0, 0, 5, (1,))
+        turn(0, 0, 0, (0,))
         scale_turned(0, 0, 1)
         widen(on_scalar, 2)
-        turn(0, 1, 1)
+        turn(0, 0, 5, (1,))
         scale_turned(0, 1, 2)
         widen(on_scalar, 3)
-        spread(1, 4)
+        warm_up(2, 6)
+        turn(0, 1, 1)
         scale_turned(1)
+        spread(1, 4)
+        quant_x(0, 0, 2)
         spread_out(1)
         turn(0, 2, 2)
-        quant_x(0, 0, 2)
         turn_out(0, 2)
+        warm_up(2, 6)
+        lay_wo(on_scalar, 1)
         turn(1, 0, 0)
         scale_turned(2)
-        lay_wo(on_scalar, 1)
         turn(1, 2, 7)
         quant_x(0, 2, 6)
         turn_out(1, 2)
-        warm_up(2, 5)
+        turn(1, 1, 1)
         quant_wo(0, 2)
         split_gate()
-        turn(1, 1, 1)
+        unit(0, 0, X, 3)
         quant_x(1, 0, 4)
         lay_wo(on_scalar, 2)
-        unit(0, 0, X, 3)
+        unit(1, 0, X, 4)
         scale_turned(3)
         lay_wo(on_scalar, 3)
-        unit(1, 0, X, 4)
-        scale_bytes(4)
         unit(0, 0, XO)
-        quant_x(1, 4, 6)
+        scale_bytes(4)
         unit(1, 0, XO)
-        scale_bytes(5)
+        quant_x(1, 4, 6)
         empty(1, 0)
         unit(2, 0, ALL, 5)
-        quant_wo(2, 4)
+        scale_bytes(5)
         empty(0, 0)
         unit(0, 1, X, 6)
+        quant_wo(2, 4)
+        sort(on_scalar, 2, 0, 1)
+        unit(1, 1, X, 7)
         scale_bytes(6)
         sort(on_scalar, 2, 2, 3)
-        unit(1, 1, X, 7)
-        scale_bytes(7)
-        sort(on_scalar, 2, 0, 1)
         unit(2, 1, X, 4)
+        scale_bytes(7)
         empty(2, 0)
         unit(3, 0, ALL, 3)
         empty(3, 0)

@@ -333,12 +333,12 @@ def tile_recomputed_hidden_weight_gradient_s3_kernel(
         load_wo(0, 1)
         load_x(2, 4)
         load_xo(0)
+        load_wo(1, 2)
         load_xo(1)
-        load_wo(1, 3)
         load_w(0)
         load_scale_bytes(w_plane, w_scales)
         load_gates()
-        load_wo(3, 4)
+        load_wo(2, 4)
         load_w(1)
         load_x(4, 6)
         load_xo(2)
@@ -358,6 +358,7 @@ def tile_recomputed_hidden_weight_gradient_s3_kernel(
         spread(0, 3)
         widen(on_vector, 1)
         spread_out(0)
+        lay_wo(on_gpsimd, 1)
         turn(0, 0, 0, (0,))
         scale_turned(0, 0, 1)
         widen(on_scalar, 2)
@@ -368,14 +369,13 @@ def tile_recomputed_hidden_weight_gradient_s3_kernel(
         turn(0, 1, 1)
         scale_turned(1)
         spread(1, 4)
-        quant_x(0, 0, 2)
         spread_out(1)
-        turn(0, 2, 2)
-        turn_out(0, 2)
         warm_up(2, 6)
-        lay_wo(on_scalar, 1)
         turn(1, 0, 0)
         scale_turned(2)
+        turn(0, 2, 2)
+        quant_x(0, 0, 2)
+        turn_out(0, 2)
         turn(1, 2, 7)
         quant_x(0, 2, 6)
         turn_out(1, 2)

@@ -28,7 +28,6 @@ QUARTER = F // 4
 CHUNKS = F // P
 XO_PASS = 2
 XO_PART = 2
-BF16_ONES = 0x3F803F80
 PLACE = {0: 0, XO_PART: 1, 1: 2}
 
 
@@ -57,7 +56,7 @@ def tile_recomputed_hidden_weight_gradient_s3_kernel(
             return psum.tile([P, BANK], F32, name="bank%d" % b)
 
         ident = kept("ident", [P, P], F32)
-        ones = kept("ones", [P, BANK], BF16)
+        ones = kept("ones", [P, 256], F32)
         w_codes = [kept("w_codes%d" % hf, [P, 2, F], U8) for hf in range(2)]
         w_plane = kept("w_plane", [P, 2, F], U8)
         dy_codes = kept("dy_codes", [P, GROUPS, 2 * N], U8)
@@ -321,9 +320,11 @@ def tile_recomputed_hidden_weight_gradient_s3_kernel(
         def warm_up(count, b):
             ps = bank(b)
             for j in range(count):
-                nc.tensor.matmul(ps[:], lhsT=ones[:, 0:P], rhs=ones[:], start=True, stop=True)
+                nc.tensor.matmul(
+                    ps[:, 0:256], lhsT=ones[:, 0:P], rhs=ones[:], start=True, stop=True
+                )
 
-        nc.vector.memset(ones[:].bitcast(I32), BF16_ONES)
+        nc.vector.memset(ones[:], 1.0)
         nc.vector.memset(w_plane[:].rearrange("p g n -> p (g n)").bitcast(I32), 0)
         nc.vector.memset(dy_plane[:].rearrange("p g n -> p (g n)").bitcast(I32), 0)
         make_identity(nc, ident[:])
@@ -351,7 +352,7 @@ def tile_recomputed_hidden_weight_gradient_s3_kernel(
         nc.sync.dma_start(out=dy_codes[:], in_=dy_words.rearrange("g p n -> p g n"))
 
         X, XO, ALL = (0, 1), (XO_PASS,), (0, 1, XO_PASS)
-        warm_up(4, 6)
+        warm_up(2, 6)
         widen(on_vector, 0, 0, 512)
         widen(on_scalar, 0, 512, K)
         lay_wo(on_gpsimd, 0)
@@ -365,12 +366,12 @@ def tile_recomputed_hidden_weight_gradient_s3_kernel(
         turn(0, 0, 5, (1,))
         scale_turned(0, 1, 2)
         widen(on_scalar, 3)
-        warm_up(2, 6)
+        warm_up(1, 6)
         turn(0, 1, 1)
         scale_turned(1)
         spread(1, 4)
         spread_out(1)
-        warm_up(2, 6)
+        warm_up(1, 6)
         turn(1, 0, 0)
         scale_turned(2)
         turn(0, 2, 2)
@@ -414,23 +415,23 @@ def tile_recomputed_hidden_weight_gradient_s3_kernel(
         turn_out(2, 2)
         turn(2, 1, 1)
         sort(on_vector, 3, 0, 3)
-        turn_out(2, 1)
         unit(0, 1, XO)
-        quant_x(2, 2, 6)
         unit(1, 1, XO)
-        scale_bytes(8)
         unit(2, 1, XO)
-        scale_bytes(9)
         empty(2, 1)
         unit(3, 1, ALL, 5)
-        empty(0, 1)
+        turn_out(2, 1)
         unit(4, 1, X, 3)
-        empty(1, 1)
+        quant_x(2, 2, 6)
+        empty(0, 1)
         unit(4, 0, X, 4)
-        empty(3, 1)
+        scale_bytes(8)
+        empty(1, 1)
         turn(3, 0, 0)
-        turn_out(3, 0)
+        scale_bytes(9)
+        empty(3, 1)
         turn(3, 1, 1)
+        turn_out(3, 0)
         turn(3, 2, 2)
         turn_out(3, 2)
         unit(4, 1, XO)

@@ -25,9 +25,9 @@ GROUPS = T // 512
 SLOTS = 4 * GROUPS
 PAIRS = SLOTS // 2
 QUARTER = F // 4
-CHUNKS = F // P
 XO_PASS = 2
 XO_PART = 2
+BF16_ONES = 0x3F803F80
 PLACE = {0: 0, XO_PART: 1, 1: 2}
 
 
@@ -42,21 +42,21 @@ def tile_recomputed_hidden_weight_gradient_s3_kernel(
 
     with ExitStack() as ctx:
         keep = ctx.enter_context(tc.tile_pool(name="keep", bufs=1))
-        ring = ctx.enter_context(tc.tile_pool(name="ring", bufs=4))
+        ring = ctx.enter_context(tc.tile_pool(name="ring", bufs=2))
         psum = ctx.enter_context(tc.psum_pool(name="psum", bufs=1))
         ctx.enter_context(tc.manual_schedule())
 
         def kept(name, shape, dtype):
             return keep.tile(shape, dtype, name=name, align_bytes=64)
 
-        def passing(name, shape, dtype, bufs=4):
+        def passing(name, shape, dtype, bufs):
             return ring.tile(shape, dtype, name=name, align_bytes=64, bufs=bufs)
 
         def bank(b):
             return psum.tile([P, BANK], F32, name="bank%d" % b)
 
         ident = kept("ident", [P, P], F32)
-        ones = kept("ones", [P, 256], F32)
+        ones = kept("ones", [P, BANK], BF16)
         w_codes = [kept("w_codes%d" % hf, [P, 2, F], U8) for hf in range(2)]
         w_plane = kept("w_plane", [P, 2, F], U8)
         dy_codes = kept("dy_codes", [P, GROUPS, 2 * N], U8)
@@ -320,14 +320,15 @@ def tile_recomputed_hidden_weight_gradient_s3_kernel(
         def warm_up(count, b):
             ps = bank(b)
             for j in range(count):
-                nc.tensor.matmul(
-                    ps[:, 0:256], lhsT=ones[:, 0:P], rhs=ones[:], start=True, stop=True
-                )
+                nc.tensor.matmul(ps[:], lhsT=ones[:, 0:P], rhs=ones[:], start=True, stop=True)
 
-        nc.vector.memset(ones[:], 1.0)
+        X, XO, ALL = (0, 1), (XO_PASS,), (0, 1, XO_PASS)
+
+        nc.vector.memset(ones[:].bitcast(I32), BF16_ONES)
         nc.vector.memset(w_plane[:].rearrange("p g n -> p (g n)").bitcast(I32), 0)
         nc.vector.memset(dy_plane[:].rearrange("p g n -> p (g n)").bitcast(I32), 0)
         make_identity(nc, ident[:])
+
         load_x_scale()
         load_x(0, 1)
         load_x(1, 2)
@@ -351,219 +352,166 @@ def tile_recomputed_hidden_weight_gradient_s3_kernel(
         load_scale_bytes(dy_plane, dy_scales)
         nc.sync.dma_start(out=dy_codes[:], in_=dy_words.rearrange("g p n -> p g n"))
 
-        X, XO, ALL = (0, 1), (XO_PASS,), (0, 1, XO_PASS)
-        warm_up(2, 6)
+        warm_up(4, 6)
         widen(on_vector, 0, 0, 512)
         widen(on_scalar, 0, 512, K)
-        lay_wo(on_gpsimd, 0)
-        spread(0, 3)
         widen(on_vector, 1)
+        for q in range(2):
+            lay_wo(on_gpsimd, q)
+        spread(0, 3)
         spread_out(0)
-        lay_wo(on_gpsimd, 1)
-        turn(0, 0, 0, (0,))
-        scale_turned(0, 0, 1)
         widen(on_scalar, 2)
-        turn(0, 0, 5, (1,))
-        scale_turned(0, 1, 2)
         widen(on_scalar, 3)
-        warm_up(1, 6)
+        for kk, b in ((0, 0), (1, 5)):
+            turn(0, 0, b, (kk,))
+            scale_turned(0, kk, kk + 1)
         turn(0, 1, 1)
         scale_turned(1)
         spread(1, 4)
         spread_out(1)
-        warm_up(1, 6)
+        warm_up(2, 6)
         turn(1, 0, 0)
         scale_turned(2)
-        turn(0, 2, 2)
-        quant_x(0, 0, 2)
-        turn_out(0, 2)
-        turn(1, 2, 7)
-        quant_x(0, 2, 6)
-        turn_out(1, 2)
+        for j, b in ((0, 2), (1, 7)):
+            turn(j, XO_PART, b)
+            turn_out(j, XO_PART)
         turn(1, 1, 1)
-        quant_wo(0, 2)
         split_gate()
-        unit(0, 0, X, 3)
+        for q in range(2, 4):
+            lay_wo(on_scalar, q)
+        quant_x(0, 0, 2)
+        quant_x(0, 2, 6)
+        quant_wo(0, 2)
         quant_x(1, 0, 4)
-        lay_wo(on_scalar, 2)
-        unit(1, 0, X, 4)
         scale_turned(3)
-        lay_wo(on_scalar, 3)
+
+        unit(0, 0, X, 3)
+        unit(1, 0, X, 4)
         unit(0, 0, XO)
-        scale_bytes(4)
         unit(1, 0, XO)
-        quant_x(1, 4, 6)
         empty(1, 0)
-        unit(2, 0, ALL, 5)
-        scale_bytes(5)
         empty(0, 0)
-        unit(0, 1, X, 6)
+        scale_bytes(4)
+        quant_x(1, 4, 6)
+        scale_bytes(5)
         quant_wo(2, 4)
-        sort(on_scalar, 2, 0, 1)
-        unit(1, 1, X, 7)
         scale_bytes(6)
-        sort(on_scalar, 2, 2, 3)
-        unit(2, 1, X, 4)
         scale_bytes(7)
-        empty(2, 0)
+        sort(on_scalar, 2, 0, 1)
+        sort(on_scalar, 2, XO_PART, XO_PART + 1)
+        unit(2, 0, ALL, 5)
+        for s, b in ((0, 6), (1, 7), (2, 4)):
+            unit(s, 1, X, b)
         unit(3, 0, ALL, 3)
+        empty(2, 0)
         empty(3, 0)
-        turn(2, 0, 0)
+        for part, b in ((0, 0), (XO_PART, 2), (1, 1)):
+            turn(2, part, b)
         turn_out(2, 0)
-        turn(2, 2, 2)
-        quant_x(2, 0, 2)
-        turn_out(2, 2)
-        turn(2, 1, 1)
-        sort(on_vector, 3, 0, 3)
-        unit(0, 1, XO)
-        unit(1, 1, XO)
-        unit(2, 1, XO)
+        turn_out(2, XO_PART)
+        for s in range(3):
+            unit(s, 1, XO)
         empty(2, 1)
-        unit(3, 1, ALL, 5)
         turn_out(2, 1)
-        unit(4, 1, X, 3)
+        unit(3, 1, ALL, 5)
+
+        quant_x(2, 0, 2)
+        sort(on_vector, 3, 0, 3)
         quant_x(2, 2, 6)
-        empty(0, 1)
+        unit(4, 1, X, 3)
         unit(4, 0, X, 4)
+        for s in (0, 1, 3):
+            empty(s, 1)
+
+        def next_pair(j):
+            for part, b in ((0, 0), (1, 1), (XO_PART, 2)):
+                turn(j, part, b)
+            for part in (0, XO_PART, 1):
+                turn_out(j, part)
+
         scale_bytes(8)
-        empty(1, 1)
-        turn(3, 0, 0)
         scale_bytes(9)
-        empty(3, 1)
-        turn(3, 1, 1)
-        turn_out(3, 0)
-        turn(3, 2, 2)
-        turn_out(3, 2)
+        next_pair(3)
         unit(4, 1, XO)
-        quant_x(3, 0, 4)
-        turn_out(3, 1)
         unit(4, 0, XO)
-        sort(on_vector, 4, 0, 3)
         empty(4, 0)
-        unit(5, 1, ALL, 6)
-        quant_x(3, 4, 6)
         empty(4, 1)
-        unit(5, 0, ALL, 7)
+        quant_x(3, 0, 4)
+        sort(on_vector, 4, 0, 3)
+        quant_x(3, 4, 6)
         scale_bytes(10)
-        empty(5, 1)
-        unit(6, 1, ALL, 5)
         scale_bytes(11)
-        empty(5, 0)
-        turn(4, 0, 0)
         sort(on_vector, 5, 0, 3)
-        turn_out(4, 0)
-        turn(4, 1, 1)
-        turn(4, 2, 2)
-        turn_out(4, 2)
-        unit(6, 0, ALL, 3)
+        for hf, b in ((1, 6), (0, 7)):
+            unit(5, hf, ALL, b)
+            empty(5, hf)
+        unit(6, 1, ALL, 5)
+
+        next_pair(4)
         quant_x(4, 0, 4)
-        turn_out(4, 1)
-        unit(7, 1, ALL, 4)
         quant_x(4, 4, 6)
-        empty(6, 1)
+        unit(6, 0, ALL, 3)
+        unit(7, 1, ALL, 4)
         unit(7, 0, ALL, 6)
-        sign(3, 0, 2)
-        empty(7, 1)
-        turn(5, 0, 0)
-        sign(2, 0, 2)
-        empty(6, 0)
-        turn(5, 1, 1)
-        sign(1, 0, 2)
-        turn_out(5, 0)
-        turn(5, 2, 2)
-        sign(0, 0, 2)
-        turn_out(5, 2)
-        unit(8, 1, ALL, 7)
-        sign(4, 0, 2)
-        turn_out(5, 1)
-        unit(9, 1, ALL, 5)
-        weave(0, 4, 6)
+        for s, hf in ((6, 1), (7, 1), (6, 0)):
+            empty(s, hf)
+
+        next_pair(5)
         empty(7, 0)
-        unit(8, 0, ALL, 3)
+        for s in (3, 2, 1, 0, 4):
+            sign(s, 0, 2)
+        weave(0, 4, 6)
         quant_x(5, 0, 4)
-        empty(8, 1)
-        unit(10, 1, ALL, 4)
         quant_x(5, 4, 6)
-        empty(9, 1)
-        unit(11, 1, ALL, 6)
-        sign(7, 0, 2)
-        empty(10, 1)
-        unit(9, 0, ALL, 7)
-        sign(6, 0, 2)
-        empty(11, 1)
-        unit(10, 0, ALL, 5)
-        sign(5, 0, 2)
+        for s, hf, b in ((8, 1, 7), (9, 1, 5), (8, 0, 3), (10, 1, 4), (11, 1, 6)):
+            unit(s, hf, ALL, b)
+            if hf == 1:
+                empty(s, hf)
         empty(8, 0)
-        unit(11, 0, ALL, 0)
+        for s, b in ((9, 7), (10, 5), (11, 0)):
+            unit(s, 0, ALL, b)
+            empty(s, 0)
+        for s in (7, 6, 5):
+            sign(s, 0, 2)
         quant_h(0, 4, 6)
-        empty(9, 0)
         weave(1, 4, 6)
-        empty(10, 0)
-        sign(10, 1, 2)
-        empty(11, 0)
-        sign(9, 1, 2)
-        sign(8, 1, 2)
+        for s in (10, 9, 8):
+            sign(s, 1, 2)
         quant_h(1, 4, 6)
         sign(11, 1, 2)
         weave(2, 4, 5)
         weave(2, 5, 6)
         quant_h(2, 4, 5)
-        piece(4, 0, BANK, 1)
         weave(2, 6, 8)
-        store(on_scalar, 4, 0)
-        piece(4, 512, BANK, 2)
         quant_h(2, 5, 6)
-        store(on_scalar, 4, 512)
-        piece(5, 0, BANK, 3)
-        weave(0, 6, 8)
+
+        def gradient(c, first_bank):
+            for h in range(2):
+                piece(c, BANK * h, BANK, (first_bank + h) % BANKS)
+                store(on_scalar, c, BANK * h)
+
+        gradient(4, 1)
         weave(0, 0, 2, on_scalar)
-        piece(5, 512, BANK, 4)
+        gradient(5, 3)
+        weave(0, 6, 8)
         weave(1, 6, 8)
-        store(on_scalar, 5, 0)
-        quant_h(0, 6, 8)
-        store(on_scalar, 5, 512)
-        quant_h(2, 6, 8)
-        quant_h(1, 6, 8)
-        piece(6, 0, BANK, 5)
-        sign(11, 0, 1)
-        store(on_scalar, 6, 0)
-        piece(6, 512, BANK, 6)
-        sign(10, 0, 1)
-        store(on_scalar, 6, 512)
-        piece(7, 0, BANK, 7)
-        sign(9, 0, 1)
-        store(on_scalar, 7, 0)
-        piece(7, 512, BANK, 0)
-        sign(8, 0, 1)
-        store(on_scalar, 7, 512)
+        for g in (0, 2, 1):
+            quant_h(g, 6, 8)
+        gradient(6, 5)
+        gradient(7, 7)
+        for s in (11, 10, 9, 8):
+            sign(s, 0, 1)
         weave(1, 0, 2)
         weave(2, 0, 2)
-        quant_h(0, 0, 2)
-        quant_h(2, 0, 2)
-        quant_h(1, 0, 2)
-        piece(0, 0, BANK, 1)
-        weave(0, 2, 4)
-        store(on_scalar, 0, 0)
-        piece(0, 512, BANK, 2)
-        weave(2, 2, 4)
-        store(on_scalar, 0, 512)
-        piece(1, 0, BANK, 3)
-        weave(1, 2, 4)
-        store(on_scalar, 1, 0)
-        piece(1, 512, BANK, 4)
-        quant_h(2, 2, 4)
-        store(on_scalar, 1, 512)
-        quant_h(0, 2, 4)
-        quant_h(1, 2, 4)
-        piece(2, 0, BANK, 5)
-        store(on_scalar, 2, 0)
-        piece(2, 512, BANK, 6)
-        store(on_scalar, 2, 512)
-        piece(3, 0, 256, 7)
-        store(on_scalar, 3, 0)
-        piece(3, 256, 256, 0)
-        store(on_vector, 3, 256)
-        piece(3, 512, 256, 1)
-        store(on_scalar, 3, 512)
-        piece(3, 768, 256, 2)
-        store(on_vector, 3, 768)
+        for g in (0, 2, 1):
+            quant_h(g, 0, 2)
+        gradient(0, 1)
+        gradient(1, 3)
+        for g in (0, 2, 1):
+            weave(g, 2, 4)
+        for g in (2, 0, 1):
+            quant_h(g, 2, 4)
+        gradient(2, 5)
+        for i in range(4):
+            piece(3, 256 * i, 256, (7 + i) % BANKS)
+            store(on_vector if i % 2 else on_scalar, 3, 256 * i)

@@ -352,7 +352,7 @@ def tile_recomputed_hidden_weight_gradient_s3_kernel(
         load_scale_bytes(dy_plane, dy_scales)
         nc.sync.dma_start(out=dy_codes[:], in_=dy_words.rearrange("g p n -> p g n"))
 
-        warm_up(4, 6)
+        warm_up(2, 6)
         widen(on_vector, 0, 0, 512)
         widen(on_scalar, 0, 512, K)
         widen(on_vector, 1)
@@ -365,6 +365,7 @@ def tile_recomputed_hidden_weight_gradient_s3_kernel(
         for kk, b in ((0, 0), (1, 5)):
             turn(0, 0, b, (kk,))
             scale_turned(0, kk, kk + 1)
+        warm_up(2, 6)
         turn(0, 1, 1)
         scale_turned(1)
         spread(1, 4)

@@ -28,7 +28,6 @@ QUARTER = F // 4
 XO_PASS = 2
 XO_PART = 2
 BF16_ONES = 0x3F803F80
-PLACE = {0: 0, XO_PART: 1, 1: 2}
 
 
 def tile_recomputed_hidden_weight_gradient_s3_kernel(
@@ -62,7 +61,6 @@ def tile_recomputed_hidden_weight_gradient_s3_kernel(
         dy_codes = kept("dy_codes", [P, GROUPS, 2 * N], U8)
         dy_plane = kept("dy_plane", [P, GROUPS, N], U8)
         scale_by_k = kept("scale_by_k", [P, 2, 4], F32)
-        scale_rows = kept("scale_rows", [P, K], F32)
         gates = kept("gates", [P, SLOTS], BF16)
         gate_abs = kept("gate_abs", [P, SLOTS], F32)
         gate_sign = kept("gate_sign", [P, SLOTS], F32)
@@ -71,7 +69,9 @@ def tile_recomputed_hidden_weight_gradient_s3_kernel(
         wo_laid = kept("wo_laid", [P, 4 * F], BF16)
         x_codes = [kept("x_codes%d" % j, [P, 6 * P], U32) for j in range(PAIRS)]
         x_plane = [kept("x_plane%d" % j, [P, 6 * P], U8) for j in range(PAIRS)]
-        rows = [kept("rows%d" % j, [P, 3 * K], BF16) for j in range(PAIRS)]
+        xo_raw = [kept("xo_raw%d" % j, [P, K], BF16) for j in range(PAIRS)]
+        stage = [kept("stage%d" % i, [P, 3 * K], BF16) for i in range(3)]
+        head_rows = kept("head_rows", [P, 6 * K], BF16)
         h_laid = [kept("h_laid%d" % g, [P, 4 * F], BF16) for g in range(GROUPS)]
         h_codes = [kept("h_codes%d" % g, [P, F], U32) for g in range(GROUPS)]
         h_plane = [kept("h_plane%d" % g, [P, F], U8) for g in range(GROUPS)]
@@ -81,7 +81,7 @@ def tile_recomputed_hidden_weight_gradient_s3_kernel(
         x_v = x_bytes.rearrange("(g m t) k -> g m t k", m=P, t=4)
         xo_v = xo.rearrange("(g m t) k -> g m t k", m=P, t=4)
         wo_v = wo.rearrange("(p j) f -> p j f", j=4)
-        x_raw, wo_raw = {}, {}
+        x_raw, x_pair, wo_raw = {}, {}, {}
 
         def load_x(s0, s1):
             g, t0 = divmod(s0, 4)
@@ -89,11 +89,13 @@ def tile_recomputed_hidden_weight_gradient_s3_kernel(
             nc.sync.dma_start(out=rows_in[:], in_=x_v[g][:, t0 : t0 + s1 - s0, :])
             for s in range(s0, s1):
                 x_raw[s] = rows_in[:, s - s0, :]
+            for s in range(s0, s1 - 1, 2):
+                x_pair[s // 2] = rows_in[:, s - s0 : s - s0 + 2, :].rearrange("p t k -> p (t k)")
 
         def load_xo(j):
             g, h = divmod(j, 2)
             nc.sync.dma_start(
-                out=rows[j][:, 2 * K : 3 * K].rearrange("p (t k) -> p t k", t=2),
+                out=xo_raw[j][:].rearrange("p (t k) -> p t k", t=2),
                 in_=xo_v[g][:, 2 * h : 2 * h + 2, :],
             )
 
@@ -116,68 +118,50 @@ def tile_recomputed_hidden_weight_gradient_s3_kernel(
                     in_=src.rearrange("g (q r) n -> r q g n", r=4)[r].bitcast(I32),
                 )
 
-        in_order, laid, turned, is_sorted = {}, {}, {}, set()
+        in_order, turned, is_sorted = {}, {}, set()
+
+        def rows(j, part):
+            if part == XO_PART:
+                return xo_raw[j][:]
+            if j < 3:
+                return head_rows[:, K * (2 * j + part) : K * (2 * j + part + 1)]
+            return stage[(j - 2) % 3][:, K * part : K * part + K]
 
         def widen(copy, s, k0=0, k1=K):
-            c0 = K * (s % 2)
-            copy(out=rows[s // 2][:, c0 + k0 : c0 + k1], in_=x_raw[s][:, k0:k1].bitcast(FP8))
+            copy(out=rows(s // 2, s % 2)[:, k0:k1], in_=x_raw[s][:, k0:k1].bitcast(FP8))
 
-        def spread(kk, b):
-            ps = bank(b)
-            for e in range(4):
-                nc.tensor.transpose(
-                    ps[:, P * e : P * e + P],
-                    scale_by_k[:, kk, e : e + 1].to_broadcast([P, P]),
-                    ident[:],
-                )
-            turned["scale", kk] = ps
-
-        def spread_out(kk):
-            nc.scalar.copy(
-                out=scale_rows[:, 512 * kk : 512 * kk + 512].rearrange("p (n e) -> p n e", e=4),
-                in_=turned["scale", kk][:].rearrange("p (e n) -> p n e", e=4),
+        def widen_pair(j):
+            nc.gpsimd.tensor_copy(
+                out=stage[(j - 2) % 3][:, 0 : 2 * K], in_=x_pair[j].bitcast(FP8)
             )
 
-        def scale_bytes(s):
-            c0 = K * (s % 2)
-            nc.vector.tensor_tensor(
-                out=rows[s // 2][:, c0 : c0 + K],
-                in0=x_raw[s].bitcast(FP8),
-                in1=scale_rows[:],
-                op=MULT,
-            )
-
-        def sort(copy, j, part0, part1):
+        def sort(copy, j, part):
             if j not in in_order:
                 in_order[j] = passing("in_order", [P, 3 * 512], F32, 2)
-            words = slice(512 * part0, 512 * part1)
             copy(
-                out=in_order[j][:, words].rearrange("p (g u m) -> p g u m", u=2, m=P),
-                in_=rows[j][:].bitcast(F32)[:, words].rearrange("p (g m u) -> p g u m", u=2, m=P),
+                out=in_order[j][:, 512 * part : 512 * part + 512].rearrange("p (u m) -> p u m", u=2),
+                in_=rows(j, part).bitcast(F32).rearrange("p (m u) -> p u m", u=2),
             )
-            for part in range(part0, part1):
-                is_sorted.add((j, part))
+            is_sorted.add((j, part))
 
         def turn(j, part, b, runs=(0, 1)):
             ps = bank(b)
             for i in runs:
-                c0 = 512 * part + 256 * i
                 for u in range(2):
                     if (j, part) in is_sorted:
-                        src = in_order[j][:, c0 + P * u : c0 + P * u + P]
+                        c0 = 512 * part + 256 * u + P * i
+                        src = in_order[j][:, c0 : c0 + P]
                     else:
-                        src = rows[j][:].bitcast(F32)[:, c0 + u : c0 + 256 : 2]
+                        src = rows(j, part).bitcast(F32)[:, 256 * i + u : 256 * i + 256 : 2]
                     o0 = 256 * u + P * i
                     nc.tensor.transpose(ps[:, o0 : o0 + P], src, ident[:])
                 turned[j, part, i] = ps
 
         def laid_part(j, part):
-            if j not in laid:
-                laid[j] = passing("laid", [P, 3 * K], BF16, 3)
-            return laid[j][:, K * PLACE[part] : K * PLACE[part] + K]
+            return stage[j % 3][:, K * part : K * part + K]
 
-        def turn_out(j, part):
-            nc.scalar.copy(
+        def turn_out(j, part, copy=on_scalar):
+            copy(
                 out=laid_part(j, part).bitcast(F32).rearrange("p (r u) -> p r u", u=2),
                 in_=turned[j, part, 0][:].rearrange("p (u r) -> p r u", u=2),
             )
@@ -206,7 +190,7 @@ def tile_recomputed_hidden_weight_gradient_s3_kernel(
             )
 
         def quant_x(j, run0, run1):
-            quantise(x_codes[j], x_plane[j], laid[j], P * run0, P * run1)
+            quantise(x_codes[j], x_plane[j], stage[j % 3], P * run0, P * run1)
 
         def lay_wo(copy, q):
             copy(
@@ -230,10 +214,10 @@ def tile_recomputed_hidden_weight_gradient_s3_kernel(
             cols = slice(BANK * hf, BANK * hf + BANK)
             for kk in passes:
                 if kk == XO_PASS:
-                    w0 = 2 * P * PLACE[XO_PART] + P * part
+                    w0 = 2 * P * XO_PART + P * part
                     rhs, rhs_scale = wo_codes[:, cols].bitcast(FP8X4), wo_plane[:, cols]
                 else:
-                    w0 = 2 * P * PLACE[part] + P * kk
+                    w0 = 2 * P * part + P * kk
                     rhs, rhs_scale = w_codes[hf][:, kk, :].bitcast(FP4X4), w_plane[:, kk, cols]
                 done.append(kk)
                 nc.tensor.matmul_mx(
@@ -283,22 +267,20 @@ def tile_recomputed_hidden_weight_gradient_s3_kernel(
 
         pieces = {}
 
-        def piece(c, n0, width, b):
-            step = BANK if width == BANK else P
-            acc = bank(b)
-            pieces[c, n0] = (acc, width)
-            for j in range(0, width, step):
-                n1 = n0 + j
-                for g in range(GROUPS):
-                    nc.tensor.matmul_mx(
-                        out=acc[:, j : j + step],
-                        lhsT=h_codes[g][:, P * c : P * c + P].bitcast(FP8X4),
-                        lhsT_scale=h_plane[g][:, P * c : P * c + P],
-                        rhs=dy_codes[:, g, 2 * n1 : 2 * n1 + 2 * step].bitcast(FP4X4),
-                        rhs_scale=dy_plane[:, g, n1 : n1 + step],
-                        start=(g == 0),
-                        stop=(g == GROUPS - 1),
-                    )
+        def piece(c, n0, width, b, groups=(0, 1, 2)):
+            if groups[0] == 0:
+                pieces[c, n0] = (bank(b), width)
+            acc = pieces[c, n0][0]
+            for g in groups:
+                nc.tensor.matmul_mx(
+                    out=acc[:, 0:width],
+                    lhsT=h_codes[g][:, P * c : P * c + P].bitcast(FP8X4),
+                    lhsT_scale=h_plane[g][:, P * c : P * c + P],
+                    rhs=dy_codes[:, g, 2 * n0 : 2 * n0 + 2 * width].bitcast(FP4X4),
+                    rhs_scale=dy_plane[:, g, n0 : n0 + width],
+                    start=(g == 0),
+                    stop=(g == GROUPS - 1),
+                )
 
         def store(copy, c, n0):
             acc, width = pieces[c, n0]
@@ -323,6 +305,7 @@ def tile_recomputed_hidden_weight_gradient_s3_kernel(
                 nc.tensor.matmul(ps[:], lhsT=ones[:, 0:P], rhs=ones[:], start=True, stop=True)
 
         X, XO, ALL = (0, 1), (XO_PASS,), (0, 1, XO_PASS)
+        widen_on_gpsimd = nc.gpsimd.tensor_copy
 
         nc.vector.memset(ones[:].bitcast(I32), BF16_ONES)
         nc.vector.memset(w_plane[:].rearrange("p g n -> p (g n)").bitcast(I32), 0)
@@ -332,17 +315,16 @@ def tile_recomputed_hidden_weight_gradient_s3_kernel(
         load_x_scale()
         load_x(0, 1)
         load_x(1, 2)
-        load_wo(0, 1)
         load_x(2, 4)
-        load_xo(0)
-        load_wo(1, 2)
-        load_xo(1)
         load_w(0)
         load_scale_bytes(w_plane, w_scales)
-        load_gates()
-        load_wo(2, 4)
+        load_wo(0, 2)
         load_w(1)
+        load_gates()
+        load_xo(0)
         load_x(4, 6)
+        load_xo(1)
+        load_wo(2, 4)
         load_xo(2)
         load_x(6, 8)
         load_xo(3)
@@ -352,167 +334,145 @@ def tile_recomputed_hidden_weight_gradient_s3_kernel(
         load_scale_bytes(dy_plane, dy_scales)
         nc.sync.dma_start(out=dy_codes[:], in_=dy_words.rearrange("g p n -> p g n"))
 
-        warm_up(2, 6)
+        warm_up(4, 6)
         widen(on_vector, 0, 0, 512)
         widen(on_scalar, 0, 512, K)
         widen(on_vector, 1)
-        for q in range(2):
-            lay_wo(on_gpsimd, q)
-        spread(0, 3)
-        spread_out(0)
         widen(on_scalar, 2)
-        widen(on_scalar, 3)
+        widen(widen_on_gpsimd, 3)
         for kk, b in ((0, 0), (1, 5)):
             turn(0, 0, b, (kk,))
             scale_turned(0, kk, kk + 1)
-        warm_up(2, 6)
         turn(0, 1, 1)
-        scale_turned(1)
-        spread(1, 4)
-        spread_out(1)
         warm_up(2, 6)
+        quant_x(0, 0, 1)
+        quant_x(0, 1, 2)
+        scale_turned(1)
         turn(1, 0, 0)
         scale_turned(2)
-        for j, b in ((0, 2), (1, 7)):
-            turn(j, XO_PART, b)
-            turn_out(j, XO_PART)
-        turn(1, 1, 1)
-        split_gate()
-        for q in range(2, 4):
-            lay_wo(on_scalar, q)
-        quant_x(0, 0, 2)
-        quant_x(0, 2, 6)
-        quant_wo(0, 2)
-        quant_x(1, 0, 4)
-        scale_turned(3)
-
+        sort(on_scalar, 1, 1)
+        lay_wo(on_scalar, 0)
+        lay_wo(on_gpsimd, 1)
         unit(0, 0, X, 3)
-        unit(1, 0, X, 4)
-        unit(0, 0, XO)
-        unit(1, 0, XO)
-        empty(1, 0)
-        empty(0, 0)
-        scale_bytes(4)
+        turn(1, 1, 2)
+        unit(0, 1, X, 4)
+        quant_x(0, 2, 4)
+        quant_x(1, 0, 2)
+        quant_wo(0, 2)
+        scale_turned(3)
+        split_gate()
+        widen(on_scalar, 5)
+        widen(widen_on_gpsimd, 4)
+        turn(0, XO_PART, 1)
+        unit(1, 0, X, 5)
+        turn(1, XO_PART, 0)
+        turn_out(0, XO_PART)
+        turn_out(1, XO_PART)
+        unit(1, 1, X, 6)
+        quant_x(0, 4, 6)
         quant_x(1, 4, 6)
-        scale_bytes(5)
-        quant_wo(2, 4)
-        scale_bytes(6)
-        scale_bytes(7)
-        sort(on_scalar, 2, 0, 1)
-        sort(on_scalar, 2, XO_PART, XO_PART + 1)
-        unit(2, 0, ALL, 5)
-        for s, b in ((0, 6), (1, 7), (2, 4)):
-            unit(s, 1, X, b)
-        unit(3, 0, ALL, 3)
-        empty(2, 0)
-        empty(3, 0)
-        for part, b in ((0, 0), (XO_PART, 2), (1, 1)):
-            turn(2, part, b)
-        turn_out(2, 0)
-        turn_out(2, XO_PART)
+        lay_wo(on_scalar, 2)
+        unit(2, 0, X, 7)
         for s in range(3):
-            unit(s, 1, XO)
-        empty(2, 1)
-        turn_out(2, 1)
-        unit(3, 1, ALL, 5)
+            unit(s, 0, XO)
+        lay_wo(on_vector, 3)
+        sort(on_vector, 2, XO_PART)
+        quant_x(1, 2, 4)
+        quant_wo(2, 4)
+        empty(0, 0)
+        empty(1, 0)
+        empty(2, 0)
 
-        quant_x(2, 0, 2)
-        sort(on_vector, 3, 0, 3)
-        quant_x(2, 2, 6)
-        unit(4, 1, X, 3)
-        unit(4, 0, X, 4)
-        for s in (0, 1, 3):
-            empty(s, 1)
+        waiting = [(3, 0, ALL), (0, 1, XO), (1, 1, XO), (2, 1, ALL), (3, 1, ALL)]
+        banks = [3, 5, 7, 4, 6]
+        early = {}
+        sort_at = {2: 1}
+        prep = {
+            3: [(sign, 0, 0, 2), (sign, 1, 0, 2), (sign, 2, 0, 2)],
+            4: [(sign, 3, 0, 2), (sign, 4, 0, 2), (weave, 0, 4, 6)],
+            5: [],
+        }
 
-        def next_pair(j):
+        n_units = 0
+        for j in range(2, PAIRS):
             for part, b in ((0, 0), (1, 1), (XO_PART, 2)):
                 turn(j, part, b)
-            for part in (0, XO_PART, 1):
-                turn_out(j, part)
-
-        scale_bytes(8)
-        scale_bytes(9)
-        next_pair(3)
-        unit(4, 1, XO)
-        unit(4, 0, XO)
-        empty(4, 0)
-        empty(4, 1)
-        quant_x(3, 0, 4)
-        sort(on_vector, 4, 0, 3)
-        quant_x(3, 4, 6)
-        scale_bytes(10)
-        scale_bytes(11)
-        sort(on_vector, 5, 0, 3)
-        for hf, b in ((1, 6), (0, 7)):
-            unit(5, hf, ALL, b)
-            empty(5, hf)
-        unit(6, 1, ALL, 5)
-
-        next_pair(4)
-        quant_x(4, 0, 4)
-        quant_x(4, 4, 6)
-        unit(6, 0, ALL, 3)
-        unit(7, 1, ALL, 4)
-        unit(7, 0, ALL, 6)
-        for s, hf in ((6, 1), (7, 1), (6, 0)):
+            scale_turned(2 * j)
+            scale_turned(2 * j + 1)
+            if j + 1 < PAIRS:
+                widen_pair(j + 1)
+            for step in early.get(j, []):
+                step[0](*step[1:])
+            for i, (s, hf, passes) in enumerate(waiting):
+                if (s, hf) in sums:
+                    unit(s, hf, passes)
+                else:
+                    unit(s, hf, passes, banks[n_units % 5])
+                    n_units += 1
+                if i == 0:
+                    turn_out(j, XO_PART)
+                if passes != X:
+                    empty(s, hf)
+                if i == sort_at.get(j, 0) and j + 1 < PAIRS:
+                    sort(on_scalar, j + 1, 0)
+                    sort(on_scalar, j + 1, 1)
+            if j + 1 < PAIRS:
+                sort(on_vector, j + 1, XO_PART)
+            for step in prep.get(j, []):
+                step[0](*step[1:])
+            quant_x(j, 0, 4)
+            quant_x(j, 4, 6)
+            waiting = [(2 * j, 1, ALL), (2 * j + 1, 1, ALL), (2 * j, 0, ALL), (2 * j + 1, 0, ALL)]
+        for s, hf, passes in waiting:
+            unit(s, hf, ALL, banks[n_units % 5])
+            n_units += 1
             empty(s, hf)
-
-        next_pair(5)
-        empty(7, 0)
-        for s in (3, 2, 1, 0, 4):
-            sign(s, 0, 2)
-        weave(0, 4, 6)
-        quant_x(5, 0, 4)
-        quant_x(5, 4, 6)
-        for s, hf, b in ((8, 1, 7), (9, 1, 5), (8, 0, 3), (10, 1, 4), (11, 1, 6)):
-            unit(s, hf, ALL, b)
-            if hf == 1:
-                empty(s, hf)
-        empty(8, 0)
-        for s, b in ((9, 7), (10, 5), (11, 0)):
-            unit(s, 0, ALL, b)
-            empty(s, 0)
         for s in (7, 6, 5):
-            sign(s, 0, 2)
-        quant_h(0, 4, 6)
-        weave(1, 4, 6)
-        for s in (10, 9, 8):
             sign(s, 1, 2)
+        quant_h(0, 4, 6)
+        for s in (9, 8):
+            sign(s, 1, 2)
+        weave(1, 4, 6)
+        weave(0, 6, 8)
         quant_h(1, 4, 6)
+        sign(10, 1, 2)
         sign(11, 1, 2)
-        weave(2, 4, 5)
-        weave(2, 5, 6)
-        quant_h(2, 4, 5)
+        sign(7, 0, 1)
+        weave(2, 4, 6)
+        sign(6, 0, 1)
+        sign(5, 0, 1)
+        quant_h(2, 4, 6)
+        weave(1, 6, 8)
         weave(2, 6, 8)
-        quant_h(2, 5, 6)
 
         def gradient(c, first_bank):
             for h in range(2):
                 piece(c, BANK * h, BANK, (first_bank + h) % BANKS)
                 store(on_scalar, c, BANK * h)
 
-        gradient(4, 1)
-        weave(0, 0, 2, on_scalar)
-        gradient(5, 3)
-        weave(0, 6, 8)
-        weave(1, 6, 8)
-        for g in (0, 2, 1):
+        for h in range(2):
+            piece(4, BANK * h, BANK, h, (0, 1))
+        for h in range(2):
+            piece(4, BANK * h, BANK, h, (2,))
+            store(on_scalar, 4, BANK * h)
+        gradient(5, 2)
+        for g in (0, 1, 2):
             quant_h(g, 6, 8)
-        gradient(6, 5)
-        gradient(7, 7)
+        gradient(6, 4)
+        gradient(7, 6)
         for s in (11, 10, 9, 8):
             sign(s, 0, 1)
-        weave(1, 0, 2)
-        weave(2, 0, 2)
-        for g in (0, 2, 1):
+        for g in (0, 1, 2):
+            weave(g, 0, 2)
+        for g in (0, 1, 2):
             quant_h(g, 0, 2)
-        gradient(0, 1)
-        gradient(1, 3)
+        gradient(0, 0)
+        gradient(1, 2)
         for g in (0, 2, 1):
             weave(g, 2, 4)
-        for g in (2, 0, 1):
+        for g in (0, 2, 1):
             quant_h(g, 2, 4)
-        gradient(2, 5)
+        gradient(2, 4)
         for i in range(4):
-            piece(3, 256 * i, 256, (7 + i) % BANKS)
+            piece(3, 256 * i, 256, (6 + i) % BANKS)
             store(on_vector if i % 2 else on_scalar, 3, 256 * i)

@@ -66,7 +66,7 @@ def tile_recomputed_hidden_weight_gradient_s3_kernel(
         gate_sign = kept("gate_sign", [P, SLOTS], F32)
         wo_codes = kept("wo_codes", [P, F], U32)
         wo_plane = kept("wo_plane", [P, F], U8)
-        wo_laid = kept("wo_laid", [P, 4 * F], BF16)
+        wo_rest = kept("wo_rest", [P, 4 * F], BF16)
         x_codes = [kept("x_codes%d" % j, [P, 6 * P], U32) for j in range(PAIRS)]
         x_plane = [kept("x_plane%d" % j, [P, 6 * P], U8) for j in range(PAIRS)]
         xo_raw = [kept("xo_raw%d" % j, [P, K], BF16) for j in range(PAIRS)]
@@ -123,6 +123,8 @@ def tile_recomputed_hidden_weight_gradient_s3_kernel(
         def rows(j, part):
             if part == XO_PART:
                 return xo_raw[j][:]
+            if (j, part) == (2, 0):
+                return stage[1][:, 0:K]
             if j < 3:
                 return head_rows[:, K * (2 * j + part) : K * (2 * j + part + 1)]
             return stage[(j - 2) % 3][:, K * part : K * part + K]
@@ -184,25 +186,27 @@ def tile_recomputed_hidden_weight_gradient_s3_kernel(
 
         def quantise(codes, plane, values, w0, w1):
             nc.vector.quantize_mx(
-                out=codes[:, w0:w1].bitcast(FP8X4),
-                scales=plane[:, w0:w1],
-                in_=values[:, 4 * w0 : 4 * w1],
+                out=codes[:, w0:w1].bitcast(FP8X4), scales=plane[:, w0:w1], in_=values
             )
 
         def quant_x(j, run0, run1):
-            quantise(x_codes[j], x_plane[j], stage[j % 3], P * run0, P * run1)
+            values = stage[j % 3][:, 512 * run0 : 512 * run1]
+            quantise(x_codes[j], x_plane[j], values, P * run0, P * run1)
+
+        def wo_laid(q0, q1):
+            if q0 == 1:
+                return stage[0][:, 0:K]
+            return wo_rest[:, K * q0 : K * q1]
 
         def lay_wo(copy, q):
             copy(
-                out=wo_laid[:, 4 * QUARTER * q : 4 * QUARTER * (q + 1)].rearrange(
-                    "p (c i e) -> p c e i", i=4, e=4
-                ),
+                out=wo_laid(q, q + 1).rearrange("p (c i e) -> p c e i", i=4, e=4),
                 in_=wo_raw[q].rearrange("p e (c i) -> p c e i", i=4),
             )
 
         def quant_wo(q0, q1):
             w0, w1 = QUARTER * q0, QUARTER * q1
-            quantise(wo_codes, wo_plane, wo_laid, w0, w1)
+            quantise(wo_codes, wo_plane, wo_laid(q0, q1), w0, w1)
 
         sums = {}
 
@@ -263,7 +267,8 @@ def tile_recomputed_hidden_weight_gradient_s3_kernel(
             )
 
         def quant_h(g, c0, c1):
-            quantise(h_codes[g], h_plane[g], h_laid[g], P * c0, P * c1)
+            values = h_laid[g][:, 512 * c0 : 512 * c1]
+            quantise(h_codes[g], h_plane[g], values, P * c0, P * c1)
 
         pieces = {}
 
@@ -284,7 +289,7 @@ def tile_recomputed_hidden_weight_gradient_s3_kernel(
 
         def store(copy, c, n0):
             acc, width = pieces[c, n0]
-            result = passing("result", [P, BANK], F32, 6)
+            result = passing("result%d" % width, [P, width], F32, 6)
             copy(out=result[:, 0:width], in_=acc[:, 0:width])
             nc.sync.dma_start(out=out[P * c : P * c + P, n0 : n0 + width], in_=result[:, 0:width])
 
@@ -299,10 +304,11 @@ def tile_recomputed_hidden_weight_gradient_s3_kernel(
                 in_=gate.rearrange("(g m t) -> m g t", m=P, t=4),
             )
 
-        def warm_up(count, b):
+        def warm_up(count, b, behind=None):
             ps = bank(b)
+            weights = ones[:, 0:P] if behind is None else behind.to_broadcast([P, P])
             for j in range(count):
-                nc.tensor.matmul(ps[:], lhsT=ones[:, 0:P], rhs=ones[:], start=True, stop=True)
+                nc.tensor.matmul(ps[:], lhsT=weights, rhs=ones[:], start=True, stop=True)
 
         X, XO, ALL = (0, 1), (XO_PASS,), (0, 1, XO_PASS)
         widen_on_gpsimd = nc.gpsimd.tensor_copy
@@ -312,20 +318,20 @@ def tile_recomputed_hidden_weight_gradient_s3_kernel(
         nc.vector.memset(dy_plane[:].rearrange("p g n -> p (g n)").bitcast(I32), 0)
         make_identity(nc, ident[:])
 
-        load_x_scale()
         load_x(0, 1)
+        load_x_scale()
         load_x(1, 2)
         load_x(2, 4)
         load_w(0)
-        load_scale_bytes(w_plane, w_scales)
         load_wo(0, 2)
-        load_w(1)
-        load_gates()
+        load_scale_bytes(w_plane, w_scales)
         load_xo(0)
+        load_w(1)
         load_x(4, 6)
         load_xo(1)
         load_wo(2, 4)
         load_xo(2)
+        load_gates()
         load_x(6, 8)
         load_xo(3)
         load_x(8, 12)
@@ -334,7 +340,8 @@ def tile_recomputed_hidden_weight_gradient_s3_kernel(
         load_scale_bytes(dy_plane, dy_scales)
         nc.sync.dma_start(out=dy_codes[:], in_=dy_words.rearrange("g p n -> p g n"))
 
-        warm_up(4, 6)
+        warm_up(2, 6)
+        warm_up(2, 6, scale_by_k[:, 0, :].bitcast(BF16)[:, 1:2])
         widen(on_vector, 0, 0, 512)
         widen(on_scalar, 0, 512, K)
         widen(on_vector, 1)
@@ -355,23 +362,24 @@ def tile_recomputed_hidden_weight_gradient_s3_kernel(
         lay_wo(on_gpsimd, 1)
         unit(0, 0, X, 3)
         turn(1, 1, 2)
+        turn(0, XO_PART, 1)
         unit(0, 1, X, 4)
         quant_x(0, 2, 4)
+        quant_wo(0, 1)
         quant_x(1, 0, 2)
-        quant_wo(0, 2)
+        quant_wo(1, 2)
         scale_turned(3)
-        split_gate()
+        turn_out(0, XO_PART)
         widen(on_scalar, 5)
         widen(widen_on_gpsimd, 4)
-        turn(0, XO_PART, 1)
         unit(1, 0, X, 5)
         turn(1, XO_PART, 0)
-        turn_out(0, XO_PART)
         turn_out(1, XO_PART)
         unit(1, 1, X, 6)
         quant_x(0, 4, 6)
         quant_x(1, 4, 6)
         lay_wo(on_scalar, 2)
+        split_gate()
         unit(2, 0, X, 7)
         for s in range(3):
             unit(s, 0, XO)
@@ -388,19 +396,20 @@ def tile_recomputed_hidden_weight_gradient_s3_kernel(
         early = {}
         sort_at = {2: 1}
         prep = {
-            3: [(sign, 0, 0, 2), (sign, 1, 0, 2), (sign, 2, 0, 2)],
-            4: [(sign, 3, 0, 2), (sign, 4, 0, 2), (weave, 0, 4, 6)],
-            5: [],
+            3: [(sign, s, 1, 2) for s in range(3)],
+            4: [(sign, s, 1, 2) for s in (4, 5)],
         }
 
         n_units = 0
         for j in range(2, PAIRS):
-            for part, b in ((0, 0), (1, 1), (XO_PART, 2)):
+            for part, b in ((0, 0), (XO_PART, 2), (1, 1)):
                 turn(j, part, b)
             scale_turned(2 * j)
             scale_turned(2 * j + 1)
             if j + 1 < PAIRS:
                 widen_pair(j + 1)
+            else:
+                weave(0, 4, 7, on_gpsimd)
             for step in early.get(j, []):
                 step[0](*step[1:])
             for i, (s, hf, passes) in enumerate(waiting):
@@ -420,59 +429,74 @@ def tile_recomputed_hidden_weight_gradient_s3_kernel(
                 sort(on_vector, j + 1, XO_PART)
             for step in prep.get(j, []):
                 step[0](*step[1:])
-            quant_x(j, 0, 4)
-            quant_x(j, 4, 6)
+            if j + 1 < PAIRS:
+                quant_x(j, 0, 4)
+                if j == PAIRS - 2:
+                    sign(3, 1, 2)
+                quant_x(j, 4, 6)
+            else:
+                for run0 in (0, 4, 2):
+                    quant_x(j, run0, run0 + 2)
             waiting = [(2 * j, 1, ALL), (2 * j + 1, 1, ALL), (2 * j, 0, ALL), (2 * j + 1, 0, ALL)]
         for s, hf, passes in waiting:
             unit(s, hf, ALL, banks[n_units % 5])
             n_units += 1
             empty(s, hf)
-        for s in (7, 6, 5):
+        for s in (7, 6):
             sign(s, 1, 2)
         quant_h(0, 4, 6)
-        for s in (9, 8):
-            sign(s, 1, 2)
         weave(1, 4, 6)
-        weave(0, 6, 8)
+        for s in (8, 9):
+            sign(s, 1, 2)
+        weave(0, 7, 8)
         quant_h(1, 4, 6)
-        sign(10, 1, 2)
-        sign(11, 1, 2)
-        sign(7, 0, 1)
+        for s in range(4):
+            sign(s, 0, 1)
+        for s in (10, 11):
+            sign(s, 1, 2)
+        quant_h(0, 6, 8)
         weave(2, 4, 6)
-        sign(6, 0, 1)
+        sign(4, 0, 1)
         sign(5, 0, 1)
         quant_h(2, 4, 6)
         weave(1, 6, 8)
         weave(2, 6, 8)
+        quant_h(1, 6, 8)
+        quant_h(2, 6, 8)
+        weave(0, 0, 2, on_scalar)
 
         def gradient(c, first_bank):
             for h in range(2):
                 piece(c, BANK * h, BANK, (first_bank + h) % BANKS)
                 store(on_scalar, c, BANK * h)
 
-        for h in range(2):
-            piece(4, BANK * h, BANK, h, (0, 1))
-        for h in range(2):
-            piece(4, BANK * h, BANK, h, (2,))
-            store(on_scalar, 4, BANK * h)
-        gradient(5, 2)
-        for g in (0, 1, 2):
-            quant_h(g, 6, 8)
-        gradient(6, 4)
-        gradient(7, 6)
-        for s in (11, 10, 9, 8):
+        opened = ((4, 0), (4, BANK), (5, 0))
+        for b, (c, n0) in enumerate(opened):
+            piece(c, n0, BANK, b, (0, 1))
+        for b, (c, n0) in enumerate(opened):
+            piece(c, n0, BANK, b, (2,))
+            store(on_scalar, c, n0)
+        piece(5, BANK, BANK, 3)
+        store(on_scalar, 5, BANK)
+        for s in range(6, SLOTS):
             sign(s, 0, 1)
-        for g in (0, 1, 2):
+        gradient(6, 4)
+        weave(0, 2, 4, on_scalar)
+        gradient(7, 6)
+        for g in (1, 2):
             weave(g, 0, 2)
         for g in (0, 1, 2):
             quant_h(g, 0, 2)
         gradient(0, 0)
         gradient(1, 2)
-        for g in (0, 2, 1):
+        for g in (1, 2):
             weave(g, 2, 4)
-        for g in (0, 2, 1):
+        for g in (0, 1, 2):
             quant_h(g, 2, 4)
-        gradient(2, 4)
-        for i in range(4):
-            piece(3, 256 * i, 256, (6 + i) % BANKS)
-            store(on_vector if i % 2 else on_scalar, 3, 256 * i)
+        piece(2, 0, BANK, 4)
+        store(on_scalar, 2, 0)
+        last_pieces = [(2, 512, 256), (2, 768, 256), (3, 0, 256), (3, 256, 256), (3, 512, 256)]
+        last_pieces += [(3, 768, P), (3, 896, P)]
+        for i, (c, n0, width) in enumerate(last_pieces):
+            piece(c, n0, width, (5 + i) % BANKS)
+            store(on_scalar if i % 2 else on_vector, c, n0)

@@ -120,21 +120,23 @@ def tile_recomputed_hidden_weight_gradient_s3_kernel(
 
         in_order, turned, is_sorted = {}, {}, set()
 
+        def wide_pair(j):
+            c0 = K if j == 3 else 0
+            return stage[(j - 2) % 3][:, c0 : c0 + 2 * K]
+
         def rows(j, part):
             if part == XO_PART:
                 return xo_raw[j][:]
-            if (j, part) == (2, 0):
-                return stage[1][:, 0:K]
             if j < 3:
                 return head_rows[:, K * (2 * j + part) : K * (2 * j + part + 1)]
-            return stage[(j - 2) % 3][:, K * part : K * part + K]
+            return wide_pair(j)[:, K * part : K * part + K]
 
         def widen(copy, s, k0=0, k1=K):
             copy(out=rows(s // 2, s % 2)[:, k0:k1], in_=x_raw[s][:, k0:k1].bitcast(FP8))
 
         def widen_pair(j):
             nc.gpsimd.tensor_copy(
-                out=stage[(j - 2) % 3][:, 0 : 2 * K], in_=x_pair[j].bitcast(FP8)
+                out=wide_pair(j), in_=x_pair[j].bitcast(FP8)
             )
 
         def sort(copy, j, part):
@@ -195,7 +197,7 @@ def tile_recomputed_hidden_weight_gradient_s3_kernel(
 
         def wo_laid(q0, q1):
             if q0 == 1:
-                return stage[0][:, 0:K]
+                return stage[0][:, K : 2 * K]
             return wo_rest[:, K * q0 : K * q1]
 
         def lay_wo(copy, q):
@@ -319,13 +321,13 @@ def tile_recomputed_hidden_weight_gradient_s3_kernel(
         make_identity(nc, ident[:])
 
         load_x(0, 1)
-        load_x_scale()
         load_x(1, 2)
+        load_x_scale()
+        load_xo(0)
         load_x(2, 4)
         load_w(0)
-        load_wo(0, 2)
         load_scale_bytes(w_plane, w_scales)
-        load_xo(0)
+        load_wo(0, 2)
         load_w(1)
         load_x(4, 6)
         load_xo(1)
@@ -340,8 +342,7 @@ def tile_recomputed_hidden_weight_gradient_s3_kernel(
         load_scale_bytes(dy_plane, dy_scales)
         nc.sync.dma_start(out=dy_codes[:], in_=dy_words.rearrange("g p n -> p g n"))
 
-        warm_up(2, 6)
-        warm_up(2, 6, scale_by_k[:, 0, :].bitcast(BF16)[:, 1:2])
+        warm_up(4, 6)
         widen(on_vector, 0, 0, 512)
         widen(on_scalar, 0, 512, K)
         widen(on_vector, 1)
@@ -351,47 +352,43 @@ def tile_recomputed_hidden_weight_gradient_s3_kernel(
             turn(0, 0, b, (kk,))
             scale_turned(0, kk, kk + 1)
         turn(0, 1, 1)
+        turn(0, XO_PART, 2)
         warm_up(2, 6)
-        quant_x(0, 0, 1)
-        quant_x(0, 1, 2)
         scale_turned(1)
+        turn_out(0, XO_PART)
+        quant_x(0, 0, 2)
+        quant_x(0, 2, 4)
         turn(1, 0, 0)
+        turn(1, 1, 1)
         scale_turned(2)
-        sort(on_scalar, 1, 1)
+        scale_turned(3)
         lay_wo(on_scalar, 0)
         lay_wo(on_gpsimd, 1)
-        unit(0, 0, X, 3)
-        turn(1, 1, 2)
-        turn(0, XO_PART, 1)
-        unit(0, 1, X, 4)
-        quant_x(0, 2, 4)
-        quant_wo(0, 1)
-        quant_x(1, 0, 2)
-        quant_wo(1, 2)
-        scale_turned(3)
-        turn_out(0, XO_PART)
+        widen(widen_on_gpsimd, 4, 0, 512)
         widen(on_scalar, 5)
-        widen(widen_on_gpsimd, 4)
-        unit(1, 0, X, 5)
-        turn(1, XO_PART, 0)
-        turn_out(1, XO_PART)
-        unit(1, 1, X, 6)
-        quant_x(0, 4, 6)
-        quant_x(1, 4, 6)
+        widen(on_scalar, 4, 512, K)
+        for s, hf, b in ((0, 0, 3), (0, 1, 4), (1, 0, 5), (1, 1, 6)):
+            unit(s, hf, X, b)
+        turn(1, XO_PART, 2)
         lay_wo(on_scalar, 2)
-        split_gate()
+        turn_out(1, XO_PART)
+        quant_x(1, 0, 2)
+        quant_x(0, 4, 6)
+        quant_wo(0, 1)
+        quant_wo(1, 2)
         unit(2, 0, X, 7)
-        for s in range(3):
-            unit(s, 0, XO)
+        unit(0, 0, XO)
+        unit(1, 0, XO)
         lay_wo(on_vector, 3)
         sort(on_vector, 2, XO_PART)
         quant_x(1, 2, 4)
         quant_wo(2, 4)
+        quant_x(1, 4, 6)
+        split_gate()
         empty(0, 0)
         empty(1, 0)
-        empty(2, 0)
 
-        waiting = [(3, 0, ALL), (0, 1, XO), (1, 1, XO), (2, 1, ALL), (3, 1, ALL)]
+        waiting = [(2, 0, XO), (3, 0, ALL), (0, 1, XO), (1, 1, XO), (2, 1, ALL), (3, 1, ALL)]
         banks = [3, 5, 7, 4, 6]
         early = {}
         sort_at = {2: 1}
@@ -402,8 +399,8 @@ def tile_recomputed_hidden_weight_gradient_s3_kernel(
 
         n_units = 0
         for j in range(2, PAIRS):
-            for part, b in ((0, 0), (XO_PART, 2), (1, 1)):
-                turn(j, part, b)
+            for part in (0, 1, XO_PART) if j == 2 else (0, XO_PART, 1):
+                turn(j, part, part)
             scale_turned(2 * j)
             scale_turned(2 * j + 1)
             if j + 1 < PAIRS:
@@ -424,9 +421,12 @@ def tile_recomputed_hidden_weight_gradient_s3_kernel(
                     empty(s, hf)
                 if i == sort_at.get(j, 0) and j + 1 < PAIRS:
                     sort(on_scalar, j + 1, 0)
-                    sort(on_scalar, j + 1, 1)
+                    if j > 3:
+                        sort(on_scalar, j + 1, 1)
             if j + 1 < PAIRS:
                 sort(on_vector, j + 1, XO_PART)
+            if j <= 3:
+                sort(on_vector, j + 1, 1)
             for step in prep.get(j, []):
                 step[0](*step[1:])
             if j + 1 < PAIRS:

@@ -24,8 +24,8 @@ BANKS = 8
 GROUPS = T // 512
 SLOTS = 4 * GROUPS
 PAIRS = SLOTS // 2
-QUARTER = F // 4
 XO_PASS = 2
+GPSIMD_SHARE = 1792
 XO_PART = 2
 BF16_ONES = 0x3F803F80
 
@@ -55,6 +55,7 @@ def tile_recomputed_hidden_weight_gradient_s3_kernel(
             return psum.tile([P, BANK], F32, name="bank%d" % b)
 
         ident = kept("ident", [P, P], F32)
+        one = kept("one", [P, 1], F32)
         ones = kept("ones", [P, BANK], BF16)
         w_codes = [kept("w_codes%d" % hf, [P, 2, F], U8) for hf in range(2)]
         w_plane = kept("w_plane", [P, 2, F], U8)
@@ -66,7 +67,7 @@ def tile_recomputed_hidden_weight_gradient_s3_kernel(
         gate_sign = kept("gate_sign", [P, SLOTS], F32)
         wo_codes = kept("wo_codes", [P, F], U32)
         wo_plane = kept("wo_plane", [P, F], U8)
-        wo_rest = kept("wo_rest", [P, 4 * F], BF16)
+        wo_rest = kept("wo_rest", [P, 2 * K], BF16)
         x_codes = [kept("x_codes%d" % j, [P, 6 * P], U32) for j in range(PAIRS)]
         x_plane = [kept("x_plane%d" % j, [P, 6 * P], U8) for j in range(PAIRS)]
         xo_raw = [kept("xo_raw%d" % j, [P, K], BF16) for j in range(PAIRS)]
@@ -81,7 +82,8 @@ def tile_recomputed_hidden_weight_gradient_s3_kernel(
         x_v = x_bytes.rearrange("(g m t) k -> g m t k", m=P, t=4)
         xo_v = xo.rearrange("(g m t) k -> g m t k", m=P, t=4)
         wo_v = wo.rearrange("(p j) f -> p j f", j=4)
-        x_raw, x_pair, wo_raw = {}, {}, {}
+        x_raw, x_pair = {}, {}
+        wo_raw = [kept("wo_raw%d" % hf, [P, 4, BANK], BF16) for hf in range(2)]
 
         def load_x(s0, s1):
             g, t0 = divmod(s0, 4)
@@ -99,11 +101,8 @@ def tile_recomputed_hidden_weight_gradient_s3_kernel(
                 in_=xo_v[g][:, 2 * h : 2 * h + 2, :],
             )
 
-        def load_wo(q0, q1):
-            rows_in = kept("wo_raw%d" % q0, [P, 4, QUARTER * (q1 - q0)], BF16)
-            nc.sync.dma_start(out=rows_in[:], in_=wo_v[:, :, QUARTER * q0 : QUARTER * q1])
-            for q in range(q0, q1):
-                wo_raw[q] = rows_in[:, :, QUARTER * (q - q0) : QUARTER * (q - q0 + 1)]
+        def load_wo(hf):
+            nc.sync.dma_start(out=wo_raw[hf][:], in_=wo_v[:, :, BANK * hf : BANK * hf + BANK])
 
         def load_w(hf):
             nc.sync.dma_start(
@@ -136,23 +135,41 @@ def tile_recomputed_hidden_weight_gradient_s3_kernel(
 
         def widen_pair(j):
             nc.gpsimd.tensor_copy(
-                out=wide_pair(j), in_=x_pair[j].bitcast(FP8)
+                out=wide_pair(j)[:, 0:GPSIMD_SHARE], in_=x_pair[j][:, 0:GPSIMD_SHARE].bitcast(FP8)
             )
 
-        def sort(copy, j, part):
+        def sorted_words(j, part):
             if j not in in_order:
                 in_order[j] = passing("in_order", [P, 3 * 512], F32, 2)
+            return in_order[j][:, 512 * part : 512 * part + 512]
+
+        def sort(copy, j, part):
             copy(
-                out=in_order[j][:, 512 * part : 512 * part + 512].rearrange("p (u m) -> p u m", u=2),
+                out=sorted_words(j, part).rearrange("p (u m) -> p u m", u=2),
                 in_=rows(j, part).bitcast(F32).rearrange("p (m u) -> p u m", u=2),
             )
-            is_sorted.add((j, part))
+            is_sorted.update((j, part, i) for i in range(2))
+
+        def widen_sorted(s, i0, i1):
+            j, part = divmod(s, 2)
+            nc.vector.tensor_scalar(
+                out=sorted_words(j, part)
+                .bitcast(BF16)
+                .rearrange("p (u m e) -> p m u e", u=2, e=2)[:, P * i0 : P * i1, :, :],
+                in0=x_raw[s][:, 512 * i0 : 512 * i1]
+                .bitcast(FP8)
+                .rearrange("p (m u e) -> p m u e", u=2, e=2),
+                scalar1=one[:],
+                scalar2=None,
+                op0=MULT,
+            )
+            is_sorted.update((j, part, i) for i in range(i0, i1))
 
         def turn(j, part, b, runs=(0, 1)):
             ps = bank(b)
             for i in runs:
                 for u in range(2):
-                    if (j, part) in is_sorted:
+                    if (j, part, i) in is_sorted:
                         c0 = 512 * part + 256 * u + P * i
                         src = in_order[j][:, c0 : c0 + P]
                     else:
@@ -195,20 +212,17 @@ def tile_recomputed_hidden_weight_gradient_s3_kernel(
             values = stage[j % 3][:, 512 * run0 : 512 * run1]
             quantise(x_codes[j], x_plane[j], values, P * run0, P * run1)
 
-        def wo_laid(q0, q1):
-            if q0 == 1:
-                return stage[0][:, K : 2 * K]
-            return wo_rest[:, K * q0 : K * q1]
+        def wo_laid(hf):
+            return wo_rest[:] if hf else stage[0][:, 0 : 2 * K]
 
-        def lay_wo(copy, q):
+        def lay_wo(copy, hf, c0, c1):
             copy(
-                out=wo_laid(q, q + 1).rearrange("p (c i e) -> p c e i", i=4, e=4),
-                in_=wo_raw[q].rearrange("p e (c i) -> p c e i", i=4),
+                out=wo_laid(hf)[:, 512 * c0 : 512 * c1].rearrange("p (c i e) -> p c e i", i=4, e=4),
+                in_=wo_raw[hf][:, :, P * c0 : P * c1].rearrange("p e (c i) -> p c e i", i=4),
             )
 
-        def quant_wo(q0, q1):
-            w0, w1 = QUARTER * q0, QUARTER * q1
-            quantise(wo_codes, wo_plane, wo_laid(q0, q1), w0, w1)
+        def quant_wo(hf):
+            quantise(wo_codes, wo_plane, wo_laid(hf), BANK * hf, BANK * hf + BANK)
 
         sums = {}
 
@@ -316,6 +330,7 @@ def tile_recomputed_hidden_weight_gradient_s3_kernel(
         widen_on_gpsimd = nc.gpsimd.tensor_copy
 
         nc.vector.memset(ones[:].bitcast(I32), BF16_ONES)
+        nc.vector.memset(one[:], 1.0)
         nc.vector.memset(w_plane[:].rearrange("p g n -> p (g n)").bitcast(I32), 0)
         nc.vector.memset(dy_plane[:].rearrange("p g n -> p (g n)").bitcast(I32), 0)
         make_identity(nc, ident[:])
@@ -325,15 +340,15 @@ def tile_recomputed_hidden_weight_gradient_s3_kernel(
         load_x_scale()
         load_xo(0)
         load_x(2, 4)
+        load_wo(0)
         load_w(0)
         load_scale_bytes(w_plane, w_scales)
-        load_wo(0, 2)
-        load_w(1)
         load_x(4, 6)
+        load_w(1)
         load_xo(1)
-        load_wo(2, 4)
-        load_xo(2)
+        load_wo(1)
         load_gates()
+        load_xo(2)
         load_x(6, 8)
         load_xo(3)
         load_x(8, 12)
@@ -343,10 +358,11 @@ def tile_recomputed_hidden_weight_gradient_s3_kernel(
         nc.sync.dma_start(out=dy_codes[:], in_=dy_words.rearrange("g p n -> p g n"))
 
         warm_up(4, 6)
-        widen(on_vector, 0, 0, 512)
+        widen_sorted(0, 0, 1)
         widen(on_scalar, 0, 512, K)
-        widen(on_vector, 1)
-        widen(on_scalar, 2)
+        widen_sorted(1, 0, 2)
+        widen(on_scalar, 2, 0, 512)
+        widen(on_scalar, 2, 512, K)
         widen(widen_on_gpsimd, 3)
         for kk, b in ((0, 0), (1, 5)):
             turn(0, 0, b, (kk,))
@@ -362,29 +378,26 @@ def tile_recomputed_hidden_weight_gradient_s3_kernel(
         turn(1, 1, 1)
         scale_turned(2)
         scale_turned(3)
-        lay_wo(on_scalar, 0)
-        lay_wo(on_gpsimd, 1)
-        widen(widen_on_gpsimd, 4, 0, 512)
+        lay_wo(on_scalar, 0, 0, 1)
+        lay_wo(on_gpsimd, 0, 1, 4)
+        widen(on_scalar, 4)
         widen(on_scalar, 5)
-        widen(on_scalar, 4, 512, K)
-        for s, hf, b in ((0, 0, 3), (0, 1, 4), (1, 0, 5), (1, 1, 6)):
+        sort(on_scalar, 2, 0)
+        for s, hf, b in ((0, 0, 3), (1, 0, 5), (0, 1, 4), (1, 1, 6)):
             unit(s, hf, X, b)
         turn(1, XO_PART, 2)
-        lay_wo(on_scalar, 2)
         turn_out(1, XO_PART)
+        split_gate()
+        sort(on_scalar, 2, XO_PART)
         quant_x(1, 0, 2)
         quant_x(0, 4, 6)
-        quant_wo(0, 1)
-        quant_wo(1, 2)
+        quant_wo(0)
         unit(2, 0, X, 7)
         unit(0, 0, XO)
         unit(1, 0, XO)
-        lay_wo(on_vector, 3)
-        sort(on_vector, 2, XO_PART)
-        quant_x(1, 2, 4)
-        quant_wo(2, 4)
-        quant_x(1, 4, 6)
-        split_gate()
+        lay_wo(on_vector, 1, 0, 4)
+        quant_x(1, 2, 6)
+        quant_wo(1)
         empty(0, 0)
         empty(1, 0)
 
@@ -397,6 +410,8 @@ def tile_recomputed_hidden_weight_gradient_s3_kernel(
             4: [(sign, s, 1, 2) for s in (4, 5)],
         }
 
+        on_scalar_of = {2: (XO_PART,), 3: (XO_PART,), 4: (0, 1)}
+        on_vector_of = {2: (0, 1), 3: (0, 1), 4: (XO_PART,)}
         n_units = 0
         for j in range(2, PAIRS):
             for part in (0, 1, XO_PART) if j == 2 else (0, XO_PART, 1):
@@ -419,16 +434,15 @@ def tile_recomputed_hidden_weight_gradient_s3_kernel(
                     turn_out(j, XO_PART)
                 if passes != X:
                     empty(s, hf)
+                if i == 0 and j + 1 < PAIRS:
+                    widen(on_scalar, 2 * j + 3, GPSIMD_SHARE - K, K)
                 if i == sort_at.get(j, 0) and j + 1 < PAIRS:
-                    sort(on_scalar, j + 1, 0)
-                    if j > 3:
-                        sort(on_scalar, j + 1, 1)
-            if j + 1 < PAIRS:
-                sort(on_vector, j + 1, XO_PART)
-            if j <= 3:
-                sort(on_vector, j + 1, 1)
+                    for part in on_scalar_of[j]:
+                        sort(on_scalar, j + 1, part)
             for step in prep.get(j, []):
                 step[0](*step[1:])
+            for part in on_vector_of.get(j, ()):
+                sort(on_vector, j + 1, part)
             if j + 1 < PAIRS:
                 quant_x(j, 0, 4)
                 if j == PAIRS - 2:

@@ -338,11 +338,11 @@ def tile_recomputed_hidden_weight_gradient_s3_kernel(
         load_x(0, 1)
         load_x(1, 2)
         load_x_scale()
-        load_xo(0)
         load_x(2, 4)
-        load_wo(0)
+        load_xo(0)
         load_w(0)
         load_scale_bytes(w_plane, w_scales)
+        load_wo(0)
         load_x(4, 6)
         load_w(1)
         load_xo(1)
@@ -368,14 +368,14 @@ def tile_recomputed_hidden_weight_gradient_s3_kernel(
             turn(0, 0, b, (kk,))
             scale_turned(0, kk, kk + 1)
         turn(0, 1, 1)
-        turn(0, XO_PART, 2)
         warm_up(2, 6)
         scale_turned(1)
-        turn_out(0, XO_PART)
         quant_x(0, 0, 2)
         quant_x(0, 2, 4)
+        turn(0, XO_PART, 2)
+        turn_out(0, XO_PART)
         turn(1, 0, 0)
-        turn(1, 1, 1)
+        turn(1, 1, 3)
         scale_turned(2)
         scale_turned(3)
         lay_wo(on_scalar, 0, 0, 1)
@@ -383,7 +383,7 @@ def tile_recomputed_hidden_weight_gradient_s3_kernel(
         widen(on_scalar, 4)
         widen(on_scalar, 5)
         sort(on_scalar, 2, 0)
-        for s, hf, b in ((0, 0, 3), (1, 0, 5), (0, 1, 4), (1, 1, 6)):
+        for s, hf, b in ((0, 0, 7), (1, 0, 5), (0, 1, 4), (1, 1, 6)):
             unit(s, hf, X, b)
         turn(1, XO_PART, 2)
         turn_out(1, XO_PART)
@@ -392,7 +392,7 @@ def tile_recomputed_hidden_weight_gradient_s3_kernel(
         quant_x(1, 0, 2)
         quant_x(0, 4, 6)
         quant_wo(0)
-        unit(2, 0, X, 7)
+        unit(2, 0, X, 3)
         unit(0, 0, XO)
         unit(1, 0, XO)
         lay_wo(on_vector, 1, 0, 4)
@@ -402,7 +402,7 @@ def tile_recomputed_hidden_weight_gradient_s3_kernel(
         empty(1, 0)
 
         waiting = [(2, 0, XO), (3, 0, ALL), (0, 1, XO), (1, 1, XO), (2, 1, ALL), (3, 1, ALL)]
-        banks = [3, 5, 7, 4, 6]
+        banks = [7, 5, 3, 4, 6]
         early = {}
         sort_at = {2: 1}
         prep = {

@@ -25,8 +25,6 @@ GROUPS = T // 512
 SLOTS = 4 * GROUPS
 PAIRS = SLOTS // 2
 XO_PASS = 2
-GPSIMD_SHARE = 1792
-XO_PART = 2
 BF16_ONES = 0x3F803F80
 
 
@@ -55,7 +53,6 @@ def tile_recomputed_hidden_weight_gradient_s3_kernel(
             return psum.tile([P, BANK], F32, name="bank%d" % b)
 
         ident = kept("ident", [P, P], F32)
-        one = kept("one", [P, 1], F32)
         ones = kept("ones", [P, BANK], BF16)
         w_codes = [kept("w_codes%d" % hf, [P, 2, F], U8) for hf in range(2)]
         w_plane = kept("w_plane", [P, 2, F], U8)
@@ -67,32 +64,34 @@ def tile_recomputed_hidden_weight_gradient_s3_kernel(
         gate_sign = kept("gate_sign", [P, SLOTS], F32)
         wo_codes = kept("wo_codes", [P, F], U32)
         wo_plane = kept("wo_plane", [P, F], U8)
-        wo_rest = kept("wo_rest", [P, 2 * K], BF16)
-        x_codes = [kept("x_codes%d" % j, [P, 6 * P], U32) for j in range(PAIRS)]
-        x_plane = [kept("x_plane%d" % j, [P, 6 * P], U8) for j in range(PAIRS)]
+        wo_rest = kept("wo_rest", [P, 4 * BANK], BF16)
+        x_codes = [kept("x_codes%d" % s, [P, 2 * P], U32) for s in range(SLOTS)]
+        x_plane = [kept("x_plane%d" % s, [P, 2 * P], U8) for s in range(SLOTS)]
+        xo_codes = [kept("xo_codes%d" % j, [P, 2 * P], U32) for j in range(PAIRS)]
+        xo_plane = [kept("xo_plane%d" % j, [P, 2 * P], U8) for j in range(PAIRS)]
         xo_raw = [kept("xo_raw%d" % j, [P, K], BF16) for j in range(PAIRS)]
         stage = [kept("stage%d" % i, [P, 3 * K], BF16) for i in range(3)]
-        head_rows = kept("head_rows", [P, 6 * K], BF16)
         h_laid = [kept("h_laid%d" % g, [P, 4 * F], BF16) for g in range(GROUPS)]
         h_codes = [kept("h_codes%d" % g, [P, F], U32) for g in range(GROUPS)]
         h_plane = [kept("h_plane%d" % g, [P, F], U8) for g in range(GROUPS)]
-        both = [kept("planes%d" % g, [P, 4 * F], BF16) for g in range(2)]
-        last = [kept("planes2_%d" % hf, [P, 4 * BANK], BF16) for hf in range(2)]
+        planes = [
+            [kept("planes%d_%d" % (g, hf), [P, 4 * BANK], BF16) for hf in range(2)]
+            for g in range(GROUPS)
+        ]
 
         x_v = x_bytes.rearrange("(g m t) k -> g m t k", m=P, t=4)
         xo_v = xo.rearrange("(g m t) k -> g m t k", m=P, t=4)
         wo_v = wo.rearrange("(p j) f -> p j f", j=4)
-        x_raw, x_pair = {}, {}
-        wo_raw = [kept("wo_raw%d" % hf, [P, 4, BANK], BF16) for hf in range(2)]
+        x_raw, wo_raw = {}, {}
 
         def load_x(s0, s1):
             g, t0 = divmod(s0, 4)
-            rows_in = kept("x_raw%d" % s0, [P, s1 - s0, K], U8)
-            nc.sync.dma_start(out=rows_in[:], in_=x_v[g][:, t0 : t0 + s1 - s0, :])
+            rows_in = kept("x_raw%d" % s0, [P, (s1 - s0) * K], U8)
+            nc.sync.dma_start(
+                out=rows_in[:].rearrange("p (t k) -> p t k", k=K), in_=x_v[g][:, t0 : t0 + s1 - s0, :]
+            )
             for s in range(s0, s1):
-                x_raw[s] = rows_in[:, s - s0, :]
-            for s in range(s0, s1 - 1, 2):
-                x_pair[s // 2] = rows_in[:, s - s0 : s - s0 + 2, :].rearrange("p t k -> p (t k)")
+                x_raw[s] = (rows_in, K * (s - s0))
 
         def load_xo(j):
             g, h = divmod(j, 2)
@@ -101,8 +100,11 @@ def tile_recomputed_hidden_weight_gradient_s3_kernel(
                 in_=xo_v[g][:, 2 * h : 2 * h + 2, :],
             )
 
-        def load_wo(hf):
-            nc.sync.dma_start(out=wo_raw[hf][:], in_=wo_v[:, :, BANK * hf : BANK * hf + BANK])
+        def load_wo(c0, c1):
+            rows_in = kept("wo_raw%d" % c0, [P, 4, P * (c1 - c0)], BF16)
+            nc.sync.dma_start(out=rows_in[:], in_=wo_v[:, :, P * c0 : P * c1])
+            for c in range(c0, c1):
+                wo_raw[c] = (rows_in, P * (c - c0))
 
         def load_w(hf):
             nc.sync.dma_start(
@@ -117,83 +119,87 @@ def tile_recomputed_hidden_weight_gradient_s3_kernel(
                     in_=src.rearrange("g (q r) n -> r q g n", r=4)[r].bitcast(I32),
                 )
 
-        in_order, turned, is_sorted = {}, {}, set()
-
-        def wide_pair(j):
-            c0 = K if j == 3 else 0
-            return stage[(j - 2) % 3][:, c0 : c0 + 2 * K]
-
-        def rows(j, part):
-            if part == XO_PART:
-                return xo_raw[j][:]
-            if j < 3:
-                return head_rows[:, K * (2 * j + part) : K * (2 * j + part + 1)]
-            return wide_pair(j)[:, K * part : K * part + K]
-
-        def widen(copy, s, k0=0, k1=K):
-            copy(out=rows(s // 2, s % 2)[:, k0:k1], in_=x_raw[s][:, k0:k1].bitcast(FP8))
-
-        def widen_pair(j):
-            nc.gpsimd.tensor_copy(
-                out=wide_pair(j)[:, 0:GPSIMD_SHARE], in_=x_pair[j][:, 0:GPSIMD_SHARE].bitcast(FP8)
+        def load_x_scale():
+            nc.sync.dma_start(
+                out=scale_by_k[:], in_=x_scale.rearrange("o (g p t) -> p (o g) t", p=P, t=4)
             )
 
-        def sorted_words(j, part):
-            if j not in in_order:
-                in_order[j] = passing("in_order", [P, 3 * 512], F32, 2)
-            return in_order[j][:, 512 * part : 512 * part + 512]
+        def load_gates():
+            nc.sync.dma_start(
+                out=gates[:].rearrange("p (g t) -> p g t", t=4),
+                in_=gate.rearrange("(g m t) -> m g t", m=P, t=4),
+            )
 
-        def sort(copy, j, part):
+        wide, xo_sorted, turned = {}, {}, {}
+
+        def raw_passes(s, kk, count):
+            rows_in, c0 = x_raw[s]
+            return rows_in[:, c0 + 512 * kk : c0 + 512 * (kk + count)].bitcast(FP8)
+
+        def place(s, kk, count, values):
+            for i in range(count):
+                wide[s + (kk + i) // 2, (kk + i) % 2] = values[:, 512 * i : 512 * i + 512]
+
+        def widen_writing(copy, s, kk, count, values):
+            place(s, kk, count, values)
             copy(
-                out=sorted_words(j, part).rearrange("p (u m) -> p u m", u=2),
-                in_=rows(j, part).bitcast(F32).rearrange("p (m u) -> p u m", u=2),
+                out=values.rearrange("p (g u m e) -> p g m u e", u=2, m=P, e=2),
+                in_=raw_passes(s, kk, count).rearrange("p (g m u e) -> p g m u e", u=2, m=P, e=2),
             )
-            is_sorted.update((j, part, i) for i in range(2))
 
-        def widen_sorted(s, i0, i1):
-            j, part = divmod(s, 2)
-            nc.vector.tensor_scalar(
-                out=sorted_words(j, part)
-                .bitcast(BF16)
-                .rearrange("p (u m e) -> p m u e", u=2, e=2)[:, P * i0 : P * i1, :, :],
-                in0=x_raw[s][:, 512 * i0 : 512 * i1]
-                .bitcast(FP8)
-                .rearrange("p (m u e) -> p m u e", u=2, e=2),
-                scalar1=one[:],
-                scalar2=None,
-                op0=MULT,
+        def widen_reading(s, kk, count, values):
+            place(s, kk, count, values)
+            on_scalar(
+                out=values.rearrange("p (g u m e) -> p g u m e", u=2, m=P, e=2),
+                in_=raw_passes(s, kk, count).rearrange("p (g m u e) -> p g u m e", u=2, m=P, e=2),
             )
-            is_sorted.update((j, part, i) for i in range(i0, i1))
 
-        def turn(j, part, b, runs=(0, 1)):
+        def sort_xo(copy, j):
+            xo_sorted[j] = passing("xo_sorted", [P, 512], F32, 2)
+            copy(
+                out=xo_sorted[j][:].rearrange("p (i u m) -> p i u m", i=2, u=2),
+                in_=xo_raw[j][:].bitcast(F32).rearrange("p (i m u) -> p i u m", i=2, u=2),
+            )
+
+        def turn_x(s, b, runs=(0, 1)):
             ps = bank(b)
-            for i in runs:
+            for kk in runs:
                 for u in range(2):
-                    if (j, part, i) in is_sorted:
-                        c0 = 512 * part + 256 * u + P * i
-                        src = in_order[j][:, c0 : c0 + P]
-                    else:
-                        src = rows(j, part).bitcast(F32)[:, 256 * i + u : 256 * i + 256 : 2]
-                    o0 = 256 * u + P * i
+                    o0 = 256 * u + P * kk
+                    src = wide[s, kk].bitcast(F32)[:, P * u : P * u + P]
                     nc.tensor.transpose(ps[:, o0 : o0 + P], src, ident[:])
-                turned[j, part, i] = ps
+                turned[s, kk] = ps
 
-        def laid_part(j, part):
-            return stage[j % 3][:, K * part : K * part + K]
+        def turn_xo(j, b):
+            ps = bank(b)
+            for i in range(2):
+                for u in range(2):
+                    o0 = 256 * u + P * i
+                    if j in xo_sorted:
+                        src = xo_sorted[j][:, 256 * i + P * u : 256 * i + P * u + P]
+                    else:
+                        src = xo_raw[j][:].bitcast(F32)[:, 256 * i + u : 256 * i + 256 : 2]
+                    nc.tensor.transpose(ps[:, o0 : o0 + P], src, ident[:])
+            turned["xo", j] = ps
 
-        def turn_out(j, part, copy=on_scalar):
+        def laid_x(s):
+            return stage[s // 2 % 3][:, K * (s % 2) : K * (s % 2) + K]
+
+        def laid_xo(j):
+            return stage[j % 3][:, 2 * K : 3 * K]
+
+        def empty_xo(j, copy=on_scalar):
             copy(
-                out=laid_part(j, part).bitcast(F32).rearrange("p (r u) -> p r u", u=2),
-                in_=turned[j, part, 0][:].rearrange("p (u r) -> p r u", u=2),
+                out=laid_xo(j).bitcast(F32).rearrange("p (r u) -> p r u", u=2),
+                in_=turned["xo", j][:].rearrange("p (u r) -> p r u", u=2),
             )
 
-        def scale_turned(s, k0=0, k1=2):
-            j, part = divmod(s, 2)
+        def scale_x(s, k0=0, k1=2):
             nc.vector.tensor_tensor(
-                out=laid_part(j, part)[:, 512 * k0 : 512 * k1].rearrange(
+                out=laid_x(s)[:, 512 * k0 : 512 * k1].rearrange(
                     "p (g r u e) -> p g r u e", r=P, u=2, e=2
                 ),
-                in0=turned[j, part, k0][:]
+                in0=turned[s, k0][:]
                 .bitcast(BF16)
                 .rearrange("p (u g r e) -> p g r u e", u=2, g=2, e=2)[:, k0:k1, :, :, :],
                 in1=scale_by_k[:, k0:k1, :]
@@ -208,21 +214,28 @@ def tile_recomputed_hidden_weight_gradient_s3_kernel(
                 out=codes[:, w0:w1].bitcast(FP8X4), scales=plane[:, w0:w1], in_=values
             )
 
-        def quant_x(j, run0, run1):
-            values = stage[j % 3][:, 512 * run0 : 512 * run1]
-            quantise(x_codes[j], x_plane[j], values, P * run0, P * run1)
+        def quant_x(s, k0=0, k1=2):
+            quantise(x_codes[s], x_plane[s], laid_x(s)[:, 512 * k0 : 512 * k1], P * k0, P * k1)
 
-        def wo_laid(hf):
-            return wo_rest[:] if hf else stage[0][:, 0 : 2 * K]
+        def quant_xo(j):
+            quantise(xo_codes[j], xo_plane[j], laid_xo(j), 0, 2 * P)
 
-        def lay_wo(copy, hf, c0, c1):
+        def wo_laid(f0, f1):
+            if f0 >= BANK:
+                return wo_rest[:, 4 * (f0 - BANK) : 4 * (f1 - BANK)]
+            q, f = divmod(f0, 256)
+            return stage[q][:, 4 * f : 4 * (f + f1 - f0)]
+
+        def lay_wo(copy, f0, f1):
+            rows_in, c0 = wo_raw[f0 // P]
+            c0 += f0 % P
             copy(
-                out=wo_laid(hf)[:, 512 * c0 : 512 * c1].rearrange("p (c i e) -> p c e i", i=4, e=4),
-                in_=wo_raw[hf][:, :, P * c0 : P * c1].rearrange("p e (c i) -> p c e i", i=4),
+                out=wo_laid(f0, f1).rearrange("p (c i e) -> p c e i", i=4, e=4),
+                in_=rows_in[:, :, c0 : c0 + f1 - f0].rearrange("p e (c i) -> p c e i", i=4),
             )
 
-        def quant_wo(hf):
-            quantise(wo_codes, wo_plane, wo_laid(hf), BANK * hf, BANK * hf + BANK)
+        def quant_wo(f0, f1):
+            quantise(wo_codes, wo_plane, wo_laid(f0, f1), f0, f1)
 
         sums = {}
 
@@ -230,20 +243,21 @@ def tile_recomputed_hidden_weight_gradient_s3_kernel(
             if b is not None:
                 sums[s, hf] = (bank(b), [])
             ps, done = sums[s, hf]
-            j, part = divmod(s, 2)
             cols = slice(BANK * hf, BANK * hf + BANK)
             for kk in passes:
                 if kk == XO_PASS:
-                    w0 = 2 * P * XO_PART + P * part
+                    rows = slice(P * (s % 2), P * (s % 2) + P)
+                    codes, scales = xo_codes[s // 2][:, rows], xo_plane[s // 2][:, rows]
                     rhs, rhs_scale = wo_codes[:, cols].bitcast(FP8X4), wo_plane[:, cols]
                 else:
-                    w0 = 2 * P * part + P * kk
+                    rows = slice(P * kk, P * kk + P)
+                    codes, scales = x_codes[s][:, rows], x_plane[s][:, rows]
                     rhs, rhs_scale = w_codes[hf][:, kk, :].bitcast(FP4X4), w_plane[:, kk, cols]
                 done.append(kk)
                 nc.tensor.matmul_mx(
                     out=ps[:],
-                    lhsT=x_codes[j][:, w0 : w0 + P].bitcast(FP8X4),
-                    lhsT_scale=x_plane[j][:, w0 : w0 + P],
+                    lhsT=codes.bitcast(FP8X4),
+                    lhsT_scale=scales,
                     rhs=rhs,
                     rhs_scale=rhs_scale,
                     start=(len(done) == 1),
@@ -254,32 +268,27 @@ def tile_recomputed_hidden_weight_gradient_s3_kernel(
             nc.scalar.activation(out=gate_abs[:], in_=gates[:], func=ACT.Abs)
             nc.scalar.activation(out=gate_sign[:], in_=gates[:], func=ACT.Sign)
 
-        def plane(g, f0, f1):
-            if g < 2:
-                return both[g][:].rearrange("p (t f) -> p t f", t=4)[:, :, f0:f1]
-            f00 = f0 // BANK * BANK
-            return last[f0 // BANK][:].rearrange("p (t f) -> p t f", t=4)[:, :, f0 - f00 : f1 - f00]
+        def plane(s, hf):
+            g, t = divmod(s, 4)
+            return planes[g][hf][:, BANK * t : BANK * t + BANK]
 
         def empty(s, hf):
-            g, t = divmod(s, 4)
             nc.scalar.activation(
-                out=plane(g, BANK * hf, BANK * hf + BANK)[:, t, :],
-                in_=sums[s, hf][0][:],
-                func=ACT.Relu,
-                scale=gate_abs[:, s : s + 1],
+                out=plane(s, hf), in_=sums[s, hf][0][:], func=ACT.Relu, scale=gate_abs[:, s : s + 1]
             )
 
-        def sign(s, hf0, hf1):
-            g, t = divmod(s, 4)
-            row = plane(g, BANK * hf0, BANK * hf1)[:, t, :]
+        def sign(s, hf):
+            row = plane(s, hf)
             nc.vector.tensor_scalar(
                 out=row, in0=row, scalar1=gate_sign[:, s : s + 1], scalar2=None, op0=MULT
             )
 
         def weave(g, c0, c1, copy=on_vector):
+            hf, c = divmod(c0, 4)
+            rows = planes[g][hf][:].rearrange("p (t f) -> p t f", t=4)
             copy(
                 out=h_laid[g][:, 512 * c0 : 512 * c1].rearrange("p (c i t) -> p c t i", i=4, t=4),
-                in_=plane(g, P * c0, P * c1).rearrange("p t (c i) -> p c t i", i=4),
+                in_=rows[:, :, P * c : P * (c + c1 - c0)].rearrange("p t (c i) -> p c t i", i=4),
             )
 
         def quant_h(g, c0, c1):
@@ -309,28 +318,15 @@ def tile_recomputed_hidden_weight_gradient_s3_kernel(
             copy(out=result[:, 0:width], in_=acc[:, 0:width])
             nc.sync.dma_start(out=out[P * c : P * c + P, n0 : n0 + width], in_=result[:, 0:width])
 
-        def load_x_scale():
-            nc.sync.dma_start(
-                out=scale_by_k[:], in_=x_scale.rearrange("o (g p t) -> p (o g) t", p=P, t=4)
-            )
-
-        def load_gates():
-            nc.sync.dma_start(
-                out=gates[:].rearrange("p (g t) -> p g t", t=4),
-                in_=gate.rearrange("(g m t) -> m g t", m=P, t=4),
-            )
-
-        def warm_up(count, b, behind=None):
+        def warm_up(count, b):
             ps = bank(b)
-            weights = ones[:, 0:P] if behind is None else behind.to_broadcast([P, P])
             for j in range(count):
-                nc.tensor.matmul(ps[:], lhsT=weights, rhs=ones[:], start=True, stop=True)
+                nc.tensor.matmul(ps[:], lhsT=ones[:, 0:P], rhs=ones[:], start=True, stop=True)
 
         X, XO, ALL = (0, 1), (XO_PASS,), (0, 1, XO_PASS)
         widen_on_gpsimd = nc.gpsimd.tensor_copy
 
         nc.vector.memset(ones[:].bitcast(I32), BF16_ONES)
-        nc.vector.memset(one[:], 1.0)
         nc.vector.memset(w_plane[:].rearrange("p g n -> p (g n)").bitcast(I32), 0)
         nc.vector.memset(dy_plane[:].rearrange("p g n -> p (g n)").bitcast(I32), 0)
         make_identity(nc, ident[:])
@@ -338,18 +334,19 @@ def tile_recomputed_hidden_weight_gradient_s3_kernel(
         load_x(0, 1)
         load_x(1, 2)
         load_x_scale()
-        load_x(2, 4)
-        load_xo(0)
+        load_x(2, 3)
+        load_x(3, 4)
         load_w(0)
         load_scale_bytes(w_plane, w_scales)
-        load_wo(0)
         load_x(4, 6)
         load_w(1)
+        load_xo(0)
+        load_wo(0, 4)
         load_xo(1)
-        load_wo(1)
         load_gates()
-        load_xo(2)
+        load_wo(4, 8)
         load_x(6, 8)
+        load_xo(2)
         load_xo(3)
         load_x(8, 12)
         load_xo(4)
@@ -357,160 +354,198 @@ def tile_recomputed_hidden_weight_gradient_s3_kernel(
         load_scale_bytes(dy_plane, dy_scales)
         nc.sync.dma_start(out=dy_codes[:], in_=dy_words.rearrange("g p n -> p g n"))
 
-        warm_up(4, 6)
-        widen_sorted(0, 0, 1)
-        widen(on_scalar, 0, 512, K)
-        widen_sorted(1, 0, 2)
-        widen(on_scalar, 2, 0, 512)
-        widen(on_scalar, 2, 512, K)
-        widen(widen_on_gpsimd, 3)
-        for kk, b in ((0, 0), (1, 5)):
-            turn(0, 0, b, (kk,))
-            scale_turned(0, kk, kk + 1)
-        turn(0, 1, 1)
-        warm_up(2, 6)
-        scale_turned(1)
-        quant_x(0, 0, 2)
-        quant_x(0, 2, 4)
-        turn(0, XO_PART, 2)
-        turn_out(0, XO_PART)
-        turn(1, 0, 0)
-        turn(1, 1, 3)
-        scale_turned(2)
-        scale_turned(3)
-        lay_wo(on_scalar, 0, 0, 1)
-        lay_wo(on_gpsimd, 0, 1, 4)
-        widen(on_scalar, 4)
-        widen(on_scalar, 5)
-        sort(on_scalar, 2, 0)
-        for s, hf, b in ((0, 0, 7), (1, 0, 5), (0, 1, 4), (1, 1, 6)):
-            unit(s, hf, X, b)
-        turn(1, XO_PART, 2)
-        turn_out(1, XO_PART)
+        first = [kept("first%d" % i, [P, 512], BF16) for i in range(4)]
+        own = {s: kept("wide%d" % s, [P, K], BF16) for s in (1, 2, 4, 5, 7, 10, 11)}
+        warm_up(4, 7)
+        widen_writing(on_vector, 0, 0, 1, first[0][:])
+        widen_reading(0, 1, 1, first[1][:])
+        widen_writing(on_vector, 1, 0, 2, own[1][:])
+        widen_reading(2, 0, 2, own[2][:])
+        widen_writing(widen_on_gpsimd, 3, 0, 1, first[2][:])
+        widen_reading(3, 1, 1, first[3][:])
+        widen_reading(4, 0, 2, own[4][:])
+        widen_reading(5, 0, 2, own[5][:])
+        turn_x(0, 0, (0,))
+        turn_x(0, 4, (1,))
+        scale_x(0, 0, 1)
+        scale_x(0, 1, 2)
+        turn_x(1, 1)
+        warm_up(2, 7)
+        turn_x(2, 2)
+        turn_x(3, 0)
+        quant_x(0, 0, 1)
+        quant_x(0, 1, 2)
+        scale_x(1, 0, 1)
+        scale_x(1, 1, 2)
+        quant_x(1, 0, 1)
+        quant_x(1, 1, 2)
+        unit(0, 0, X, 7)
+        unit(0, 1, X, 6)
+        turn_xo(0, 3)
+        empty_xo(0)
+        scale_x(2, 0, 1)
+        scale_x(2, 1, 2)
+        quant_x(2, 0, 1)
+        quant_x(2, 1, 2)
+        unit(1, 0, X, 5)
+        unit(1, 1, X, 4)
+        lay_wo(on_scalar, 0, 256)
+        lay_wo(on_scalar, 256, 320)
+        lay_wo(on_gpsimd, 320, 512)
+        scale_x(3)
+        quant_xo(0)
+        quant_wo(0, 256)
+        quant_wo(256, 512)
+        quant_x(3)
+        unit(2, 0, X, 1)
+        turn_xo(1, 3)
+        turn_x(4, 2)
+        turn_x(5, 0)
         split_gate()
-        sort(on_scalar, 2, XO_PART)
-        quant_x(1, 0, 2)
-        quant_x(0, 4, 6)
-        quant_wo(0)
-        unit(2, 0, X, 3)
+        empty_xo(1)
         unit(0, 0, XO)
         unit(1, 0, XO)
-        lay_wo(on_vector, 1, 0, 4)
-        quant_x(1, 2, 6)
-        quant_wo(1)
         empty(0, 0)
         empty(1, 0)
-
-        waiting = [(2, 0, XO), (3, 0, ALL), (0, 1, XO), (1, 1, XO), (2, 1, ALL), (3, 1, ALL)]
-        banks = [7, 5, 3, 4, 6]
-        early = {}
-        sort_at = {2: 1}
-        prep = {
-            3: [(sign, s, 1, 2) for s in range(3)],
-            4: [(sign, s, 1, 2) for s in (4, 5)],
-        }
-
-        on_scalar_of = {2: (XO_PART,), 3: (XO_PART,), 4: (0, 1)}
-        on_vector_of = {2: (0, 1), 3: (0, 1), 4: (XO_PART,)}
-        n_units = 0
-        for j in range(2, PAIRS):
-            for part in (0, 1, XO_PART) if j == 2 else (0, XO_PART, 1):
-                turn(j, part, part)
-            scale_turned(2 * j)
-            scale_turned(2 * j + 1)
-            if j + 1 < PAIRS:
-                widen_pair(j + 1)
-            else:
-                weave(0, 4, 7, on_gpsimd)
-            for step in early.get(j, []):
-                step[0](*step[1:])
-            for i, (s, hf, passes) in enumerate(waiting):
-                if (s, hf) in sums:
-                    unit(s, hf, passes)
-                else:
-                    unit(s, hf, passes, banks[n_units % 5])
-                    n_units += 1
-                if i == 0:
-                    turn_out(j, XO_PART)
-                if passes != X:
-                    empty(s, hf)
-                if i == 0 and j + 1 < PAIRS:
-                    widen(on_scalar, 2 * j + 3, GPSIMD_SHARE - K, K)
-                if i == sort_at.get(j, 0) and j + 1 < PAIRS:
-                    for part in on_scalar_of[j]:
-                        sort(on_scalar, j + 1, part)
-            for step in prep.get(j, []):
-                step[0](*step[1:])
-            for part in on_vector_of.get(j, ()):
-                sort(on_vector, j + 1, part)
-            if j + 1 < PAIRS:
-                quant_x(j, 0, 4)
-                if j == PAIRS - 2:
-                    sign(3, 1, 2)
-                quant_x(j, 4, 6)
-            else:
-                for run0 in (0, 4, 2):
-                    quant_x(j, run0, run0 + 2)
-            waiting = [(2 * j, 1, ALL), (2 * j + 1, 1, ALL), (2 * j, 0, ALL), (2 * j + 1, 0, ALL)]
-        for s, hf, passes in waiting:
-            unit(s, hf, ALL, banks[n_units % 5])
-            n_units += 1
-            empty(s, hf)
-        for s in (7, 6):
-            sign(s, 1, 2)
-        quant_h(0, 4, 6)
-        weave(1, 4, 6)
-        for s in (8, 9):
-            sign(s, 1, 2)
-        weave(0, 7, 8)
-        quant_h(1, 4, 6)
+        quant_xo(1)
+        lay_wo(on_vector, 512, 1024)
+        unit(3, 0, X, 3)
+        unit(2, 0, XO)
+        unit(3, 0, XO)
+        sort_xo(on_scalar, 2)
+        empty(2, 0)
+        empty(3, 0)
+        sort_xo(on_vector, 3)
+        widen_writing(on_vector, 7, 0, 1, own[7][:, 0:512])
+        quant_wo(512, 1024)
+        unit(2, 1, X, 7)
+        unit(3, 1, X, 5)
+        scale_x(4)
+        scale_x(5)
+        widen_writing(widen_on_gpsimd, 6, 0, 2, wo_rest[:, 0:1024])
+        widen_reading(7, 1, 1, first[1][:])
         for s in range(4):
-            sign(s, 0, 1)
-        for s in (10, 11):
-            sign(s, 1, 2)
-        quant_h(0, 6, 8)
-        weave(2, 4, 6)
-        sign(4, 0, 1)
-        sign(5, 0, 1)
-        quant_h(2, 4, 6)
-        weave(1, 6, 8)
-        weave(2, 6, 8)
-        quant_h(1, 6, 8)
-        quant_h(2, 6, 8)
-        weave(0, 0, 2, on_scalar)
+            unit(s, 1, XO)
+        quant_x(4)
+        quant_x(5)
+        turn_xo(2, 3)
+        turn_xo(3, 1)
+        turn_x(6, 2)
+        turn_x(7, 0)
+        empty(0, 1)
+        empty_xo(2)
+        empty(1, 1)
+        quant_xo(2)
+        scale_x(6)
+        scale_x(7)
+        widen_writing(widen_on_gpsimd, 8, 0, 3, stage[2][:, 1536:3072])
+        unit(4, 1, ALL, 6)
+        empty(2, 1)
+        unit(5, 1, ALL, 4)
+        empty_xo(3)
+        empty(3, 1)
+        empty(4, 1)
+        quant_x(6)
+        quant_xo(3)
+        quant_x(7)
+        widen_writing(on_vector, 10, 0, 2, own[10][:])
+        widen_writing(on_vector, 11, 0, 2, own[11][:])
+        unit(4, 0, ALL, 3)
+        empty(5, 1)
+        widen_reading(9, 1, 1, first[0][:])
+        unit(5, 0, ALL, 7)
+        empty(4, 0)
+        sort_xo(on_scalar, 4)
+        sort_xo(on_vector, 5)
+        unit(6, 1, ALL, 1)
+        empty(5, 0)
+        unit(7, 1, ALL, 5)
+        empty(6, 1)
+        for s in range(6):
+            sign(s, 1)
+        turn_xo(4, 2)
+        turn_x(8, 0)
+        turn_x(9, 6)
+        turn_xo(5, 4)
+        turn_x(10, 3)
+        turn_x(11, 7)
+        empty_xo(4)
+        empty(7, 1)
+        scale_x(8)
+        scale_x(9)
+        weave(0, 4, 7, on_gpsimd)
+        empty_xo(5)
+        quant_x(8)
+        quant_xo(4)
+        sign(6, 1)
+        sign(7, 1)
+        quant_x(9)
+        scale_x(10)
+        scale_x(11)
+        weave(1, 4, 7, on_gpsimd)
+        quant_x(10)
+        quant_xo(5)
+        quant_x(11)
+        rest = ((6, 0, 1), (7, 0, 2), (8, 1, 5), (9, 1, 4), (8, 0, 0), (9, 0, 1), (10, 1, 2), (11, 1, 6), (10, 0, 5), (11, 0, 4))
+        for s, hf, b in rest:
+            unit(s, hf, ALL, b)
+            empty(s, hf)
+            if (s, hf) == (7, 0):
+                weave(0, 7, 8, on_scalar)
+            if (s, hf) == (8, 0):
+                weave(1, 7, 8, on_scalar)
 
         def gradient(c, first_bank):
             for h in range(2):
                 piece(c, BANK * h, BANK, (first_bank + h) % BANKS)
                 store(on_scalar, c, BANK * h)
 
-        opened = ((4, 0), (4, BANK), (5, 0))
-        for b, (c, n0) in enumerate(opened):
+        quant_h(0, 4, 8)
+        for s in (8, 9):
+            sign(s, 1)
+        quant_h(1, 4, 8)
+        for s in range(4):
+            sign(s, 0)
+        for s in (10, 11):
+            sign(s, 1)
+        for s in range(4, 6):
+            sign(s, 0)
+        weave(2, 4, 6)
+        for s in range(6, 8):
+            sign(s, 0)
+        quant_h(2, 4, 6)
+        weave(2, 6, 8)
+        weave(0, 0, 2, on_scalar)
+        for s in range(8, 10):
+            sign(s, 0)
+        quant_h(2, 6, 8)
+
+        opened = ((4, 0, 3), (4, BANK, 7), (5, 0, 0))
+        for c, n0, b in opened:
             piece(c, n0, BANK, b, (0, 1))
-        for b, (c, n0) in enumerate(opened):
+        for c, n0, b in opened:
             piece(c, n0, BANK, b, (2,))
             store(on_scalar, c, n0)
-        piece(5, BANK, BANK, 3)
+        piece(5, BANK, BANK, 1)
         store(on_scalar, 5, BANK)
-        for s in range(6, SLOTS):
-            sign(s, 0, 1)
-        gradient(6, 4)
-        weave(0, 2, 4, on_scalar)
-        gradient(7, 6)
+        for s in range(10, SLOTS):
+            sign(s, 0)
+        gradient(6, 2)
+        gradient(7, 4)
         for g in (1, 2):
             weave(g, 0, 2)
         for g in (0, 1, 2):
             quant_h(g, 0, 2)
-        gradient(0, 0)
-        gradient(1, 2)
-        for g in (1, 2):
+        gradient(0, 6)
+        gradient(1, 0)
+        for g in (0, 1, 2):
             weave(g, 2, 4)
         for g in (0, 1, 2):
             quant_h(g, 2, 4)
-        piece(2, 0, BANK, 4)
+        piece(2, 0, BANK, 2)
         store(on_scalar, 2, 0)
         last_pieces = [(2, 512, 256), (2, 768, 256), (3, 0, 256), (3, 256, 256), (3, 512, 256)]
         last_pieces += [(3, 768, P), (3, 896, P)]
         for i, (c, n0, width) in enumerate(last_pieces):
-            piece(c, n0, width, (5 + i) % BANKS)
+            piece(c, n0, width, (3 + i) % BANKS)
             store(on_scalar if i % 2 else on_vector, c, n0)

@@ -65,13 +65,12 @@ def tile_recomputed_hidden_weight_gradient_s3_kernel(
         wo_codes = kept("wo_codes", [P, F], U32)
         wo_plane = kept("wo_plane", [P, F], U8)
         wo_rest = kept("wo_rest", [P, 4 * BANK], BF16)
-        x_codes = [kept("x_codes%d" % s, [P, 2 * P], U32) for s in range(SLOTS)]
-        x_plane = [kept("x_plane%d" % s, [P, 2 * P], U8) for s in range(SLOTS)]
-        xo_codes = [kept("xo_codes%d" % j, [P, 2 * P], U32) for j in range(PAIRS)]
-        xo_plane = [kept("xo_plane%d" % j, [P, 2 * P], U8) for j in range(PAIRS)]
+        x_codes = [kept("x_codes%d" % j, [P, 6 * P], U32) for j in range(PAIRS)]
+        x_plane = [kept("x_plane%d" % j, [P, 6 * P], U8) for j in range(PAIRS)]
         xo_raw = [kept("xo_raw%d" % j, [P, K], BF16) for j in range(PAIRS)]
         stage = [kept("stage%d" % i, [P, 3 * K], BF16) for i in range(3)]
         h_laid = [kept("h_laid%d" % g, [P, 4 * F], BF16) for g in range(GROUPS)]
+        h_moved = {}
         h_codes = [kept("h_codes%d" % g, [P, F], U32) for g in range(GROUPS)]
         h_plane = [kept("h_plane%d" % g, [P, F], U8) for g in range(GROUPS)]
         planes = [
@@ -214,28 +213,26 @@ def tile_recomputed_hidden_weight_gradient_s3_kernel(
                 out=codes[:, w0:w1].bitcast(FP8X4), scales=plane[:, w0:w1], in_=values
             )
 
-        def quant_x(s, k0=0, k1=2):
-            quantise(x_codes[s], x_plane[s], laid_x(s)[:, 512 * k0 : 512 * k1], P * k0, P * k1)
+        def quant_x(j, run0, run1):
+            values = stage[j % 3][:, 512 * run0 : 512 * run1]
+            quantise(x_codes[j], x_plane[j], values, P * run0, P * run1)
 
-        def quant_xo(j):
-            quantise(xo_codes[j], xo_plane[j], laid_xo(j), 0, 2 * P)
-
-        def wo_laid(f0, f1):
-            if f0 >= BANK:
-                return wo_rest[:, 4 * (f0 - BANK) : 4 * (f1 - BANK)]
-            q, f = divmod(f0, 256)
-            return stage[q][:, 4 * f : 4 * (f + f1 - f0)]
+        def wo_laid(hf):
+            return wo_rest[:] if hf else stage[0][:, 0 : 2 * K]
 
         def lay_wo(copy, f0, f1):
             rows_in, c0 = wo_raw[f0 // P]
             c0 += f0 % P
+            hf, f = divmod(f0, BANK)
             copy(
-                out=wo_laid(f0, f1).rearrange("p (c i e) -> p c e i", i=4, e=4),
+                out=wo_laid(hf)[:, 4 * f : 4 * (f + f1 - f0)].rearrange(
+                    "p (c i e) -> p c e i", i=4, e=4
+                ),
                 in_=rows_in[:, :, c0 : c0 + f1 - f0].rearrange("p e (c i) -> p c e i", i=4),
             )
 
-        def quant_wo(f0, f1):
-            quantise(wo_codes, wo_plane, wo_laid(f0, f1), f0, f1)
+        def quant_wo(hf):
+            quantise(wo_codes, wo_plane, wo_laid(hf), BANK * hf, BANK * hf + BANK)
 
         sums = {}
 
@@ -246,18 +243,16 @@ def tile_recomputed_hidden_weight_gradient_s3_kernel(
             cols = slice(BANK * hf, BANK * hf + BANK)
             for kk in passes:
                 if kk == XO_PASS:
-                    rows = slice(P * (s % 2), P * (s % 2) + P)
-                    codes, scales = xo_codes[s // 2][:, rows], xo_plane[s // 2][:, rows]
+                    w0 = P * (4 + s % 2)
                     rhs, rhs_scale = wo_codes[:, cols].bitcast(FP8X4), wo_plane[:, cols]
                 else:
-                    rows = slice(P * kk, P * kk + P)
-                    codes, scales = x_codes[s][:, rows], x_plane[s][:, rows]
+                    w0 = P * (2 * (s % 2) + kk)
                     rhs, rhs_scale = w_codes[hf][:, kk, :].bitcast(FP4X4), w_plane[:, kk, cols]
                 done.append(kk)
                 nc.tensor.matmul_mx(
                     out=ps[:],
-                    lhsT=codes.bitcast(FP8X4),
-                    lhsT_scale=scales,
+                    lhsT=x_codes[s // 2][:, w0 : w0 + P].bitcast(FP8X4),
+                    lhsT_scale=x_plane[s // 2][:, w0 : w0 + P],
                     rhs=rhs,
                     rhs_scale=rhs_scale,
                     start=(len(done) == 1),
@@ -283,16 +278,21 @@ def tile_recomputed_hidden_weight_gradient_s3_kernel(
                 out=row, in0=row, scalar1=gate_sign[:, s : s + 1], scalar2=None, op0=MULT
             )
 
+        def woven(g, c0, c1):
+            hf, c = divmod(c0, 4)
+            values = h_moved.get((g, hf), h_laid[g][:, 4 * BANK * hf : 4 * BANK * (hf + 1)])
+            return values[:, 512 * c : 512 * (c + c1 - c0)]
+
         def weave(g, c0, c1, copy=on_vector):
             hf, c = divmod(c0, 4)
             rows = planes[g][hf][:].rearrange("p (t f) -> p t f", t=4)
             copy(
-                out=h_laid[g][:, 512 * c0 : 512 * c1].rearrange("p (c i t) -> p c t i", i=4, t=4),
+                out=woven(g, c0, c1).rearrange("p (c i t) -> p c t i", i=4, t=4),
                 in_=rows[:, :, P * c : P * (c + c1 - c0)].rearrange("p t (c i) -> p c t i", i=4),
             )
 
         def quant_h(g, c0, c1):
-            values = h_laid[g][:, 512 * c0 : 512 * c1]
+            values = woven(g, c0, c1)
             quantise(h_codes[g], h_plane[g], values, P * c0, P * c1)
 
         pieces = {}
@@ -334,19 +334,18 @@ def tile_recomputed_hidden_weight_gradient_s3_kernel(
         load_x(0, 1)
         load_x(1, 2)
         load_x_scale()
-        load_x(2, 3)
-        load_x(3, 4)
+        load_x(2, 4)
+        load_xo(0)
         load_w(0)
         load_scale_bytes(w_plane, w_scales)
+        load_wo(0, 4)
         load_x(4, 6)
         load_w(1)
-        load_xo(0)
-        load_wo(0, 4)
         load_xo(1)
         load_gates()
         load_wo(4, 8)
-        load_x(6, 8)
         load_xo(2)
+        load_x(6, 8)
         load_xo(3)
         load_x(8, 12)
         load_xo(4)
@@ -354,198 +353,155 @@ def tile_recomputed_hidden_weight_gradient_s3_kernel(
         load_scale_bytes(dy_plane, dy_scales)
         nc.sync.dma_start(out=dy_codes[:], in_=dy_words.rearrange("g p n -> p g n"))
 
-        first = [kept("first%d" % i, [P, 512], BF16) for i in range(4)]
-        own = {s: kept("wide%d" % s, [P, K], BF16) for s in (1, 2, 4, 5, 7, 10, 11)}
-        warm_up(4, 7)
+        first = [kept("first%d" % i, [P, 512], BF16) for i in range(2)]
+        own = {s: kept("wide%d" % s, [P, K], BF16) for s in range(1, 6)}
+        warm_up(4, 6)
         widen_writing(on_vector, 0, 0, 1, first[0][:])
         widen_reading(0, 1, 1, first[1][:])
         widen_writing(on_vector, 1, 0, 2, own[1][:])
         widen_reading(2, 0, 2, own[2][:])
-        widen_writing(widen_on_gpsimd, 3, 0, 1, first[2][:])
-        widen_reading(3, 1, 1, first[3][:])
+        widen_writing(widen_on_gpsimd, 3, 0, 2, own[3][:])
+        for kk, b in ((0, 0), (1, 5)):
+            turn_x(0, b, (kk,))
+            scale_x(0, kk, kk + 1)
+        turn_x(1, 1)
+        warm_up(2, 6)
+        scale_x(1)
+        quant_x(0, 0, 2)
+        quant_x(0, 2, 4)
+        turn_xo(0, 2)
+        empty_xo(0)
+        turn_x(2, 0)
+        turn_x(3, 3)
+        scale_x(2)
+        scale_x(3)
+        lay_wo(on_scalar, 0, 128)
+        lay_wo(on_gpsimd, 128, 512)
         widen_reading(4, 0, 2, own[4][:])
         widen_reading(5, 0, 2, own[5][:])
-        turn_x(0, 0, (0,))
-        turn_x(0, 4, (1,))
-        scale_x(0, 0, 1)
-        scale_x(0, 1, 2)
-        turn_x(1, 1)
-        warm_up(2, 7)
-        turn_x(2, 2)
-        turn_x(3, 0)
-        quant_x(0, 0, 1)
-        quant_x(0, 1, 2)
-        scale_x(1, 0, 1)
-        scale_x(1, 1, 2)
-        quant_x(1, 0, 1)
-        quant_x(1, 1, 2)
-        unit(0, 0, X, 7)
-        unit(0, 1, X, 6)
-        turn_xo(0, 3)
-        empty_xo(0)
-        scale_x(2, 0, 1)
-        scale_x(2, 1, 2)
-        quant_x(2, 0, 1)
-        quant_x(2, 1, 2)
-        unit(1, 0, X, 5)
-        unit(1, 1, X, 4)
-        lay_wo(on_scalar, 0, 256)
-        lay_wo(on_scalar, 256, 320)
-        lay_wo(on_gpsimd, 320, 512)
-        scale_x(3)
-        quant_xo(0)
-        quant_wo(0, 256)
-        quant_wo(256, 512)
-        quant_x(3)
-        unit(2, 0, X, 1)
-        turn_xo(1, 3)
-        turn_x(4, 2)
-        turn_x(5, 0)
+        for s, hf, b in ((0, 0, 7), (1, 0, 5), (0, 1, 4), (1, 1, 6)):
+            unit(s, hf, X, b)
+        turn_xo(1, 2)
+        turn_x(4, 0)
+        turn_x(5, 1)
         split_gate()
         empty_xo(1)
+        lay_wo(on_scalar, 512, 768)
+        quant_x(1, 0, 2)
+        quant_x(0, 4, 6)
+        quant_wo(0)
+        unit(2, 0, X, 3)
         unit(0, 0, XO)
         unit(1, 0, XO)
+        turn_xo(2, 2)
+        lay_wo(on_vector, 768, 1024)
+        quant_x(1, 2, 6)
         empty(0, 0)
         empty(1, 0)
-        quant_xo(1)
-        lay_wo(on_vector, 512, 1024)
-        unit(3, 0, X, 3)
-        unit(2, 0, XO)
-        unit(3, 0, XO)
-        sort_xo(on_scalar, 2)
-        empty(2, 0)
-        empty(3, 0)
-        sort_xo(on_vector, 3)
-        widen_writing(on_vector, 7, 0, 1, own[7][:, 0:512])
-        quant_wo(512, 1024)
-        unit(2, 1, X, 7)
-        unit(3, 1, X, 5)
-        scale_x(4)
-        scale_x(5)
-        widen_writing(widen_on_gpsimd, 6, 0, 2, wo_rest[:, 0:1024])
-        widen_reading(7, 1, 1, first[1][:])
-        for s in range(4):
-            unit(s, 1, XO)
-        quant_x(4)
-        quant_x(5)
-        turn_xo(2, 3)
-        turn_xo(3, 1)
-        turn_x(6, 2)
-        turn_x(7, 0)
-        empty(0, 1)
-        empty_xo(2)
-        empty(1, 1)
-        quant_xo(2)
-        scale_x(6)
-        scale_x(7)
-        widen_writing(widen_on_gpsimd, 8, 0, 3, stage[2][:, 1536:3072])
-        unit(4, 1, ALL, 6)
-        empty(2, 1)
-        unit(5, 1, ALL, 4)
-        empty_xo(3)
-        empty(3, 1)
-        empty(4, 1)
-        quant_x(6)
-        quant_xo(3)
-        quant_x(7)
-        widen_writing(on_vector, 10, 0, 2, own[10][:])
-        widen_writing(on_vector, 11, 0, 2, own[11][:])
-        unit(4, 0, ALL, 3)
-        empty(5, 1)
-        widen_reading(9, 1, 1, first[0][:])
-        unit(5, 0, ALL, 7)
-        empty(4, 0)
-        sort_xo(on_scalar, 4)
-        sort_xo(on_vector, 5)
-        unit(6, 1, ALL, 1)
-        empty(5, 0)
-        unit(7, 1, ALL, 5)
-        empty(6, 1)
-        for s in range(6):
-            sign(s, 1)
-        turn_xo(4, 2)
-        turn_x(8, 0)
-        turn_x(9, 6)
-        turn_xo(5, 4)
-        turn_x(10, 3)
-        turn_x(11, 7)
-        empty_xo(4)
-        empty(7, 1)
-        scale_x(8)
-        scale_x(9)
-        weave(0, 4, 7, on_gpsimd)
-        empty_xo(5)
-        quant_x(8)
-        quant_xo(4)
-        sign(6, 1)
-        sign(7, 1)
-        quant_x(9)
-        scale_x(10)
-        scale_x(11)
-        weave(1, 4, 7, on_gpsimd)
-        quant_x(10)
-        quant_xo(5)
-        quant_x(11)
-        rest = ((6, 0, 1), (7, 0, 2), (8, 1, 5), (9, 1, 4), (8, 0, 0), (9, 0, 1), (10, 1, 2), (11, 1, 6), (10, 0, 5), (11, 0, 4))
-        for s, hf, b in rest:
-            unit(s, hf, ALL, b)
+        quant_wo(1)
+
+        waiting = [(2, 0, XO), (3, 0, ALL), (2, 1, X), (0, 1, XO), (1, 1, XO), (2, 1, XO), (3, 1, ALL)]
+        banks = [7, 5, 3, 4, 6]
+        prep = {
+            3: [(s, 1) for s in (3, 2, 1, 0)],
+            4: [(5, 1), (4, 1)] + [(s, 0) for s in range(4)],
+        }
+        n_units = 0
+        for j in range(2, PAIRS):
+            if j > 2:
+                turn_x(2 * j, 0)
+                turn_xo(j, 2)
+                turn_x(2 * j + 1, 1)
+            scale_x(2 * j)
+            scale_x(2 * j + 1)
+            ahead = wo_rest[:] if j == 2 else stage[(j - 1) % 3][:, 0 : 2 * K]
+            if j + 1 < PAIRS:
+                widen_writing(widen_on_gpsimd, 2 * j + 2, 0, 3, ahead[:, 0:1536])
+            else:
+                h_moved[0, 1] = ahead
+                weave(0, 4, 7, on_gpsimd)
+            for i, (s, hf, passes) in enumerate(waiting):
+                if (s, hf) in sums:
+                    unit(s, hf, passes)
+                else:
+                    unit(s, hf, passes, banks[n_units % 5])
+                    n_units += 1
+                if i == 0:
+                    empty_xo(j)
+                    if j + 1 == PAIRS:
+                        weave(0, 0, 2, on_scalar)
+                if passes != X:
+                    empty(s, hf)
+                if i == 0 and j + 1 < PAIRS:
+                    widen_reading(2 * j + 3, 1, 1, ahead[:, 1536:2048])
+            if j + 1 < PAIRS:
+                sort_xo(on_vector, j + 1)
+            for s, hf in prep.get(j, []):
+                sign(s, hf)
+            if j + 1 < PAIRS:
+                quant_x(j, 0, 4)
+                quant_x(j, 4, 6)
+            else:
+                for run0 in (0, 4, 2):
+                    quant_x(j, run0, run0 + 2)
+            waiting = [(2 * j, 1, ALL), (2 * j + 1, 1, ALL), (2 * j, 0, ALL), (2 * j + 1, 0, ALL)]
+        for s, hf, passes in waiting:
+            unit(s, hf, ALL, banks[n_units % 5])
+            n_units += 1
             empty(s, hf)
-            if (s, hf) == (7, 0):
-                weave(0, 7, 8, on_scalar)
-            if (s, hf) == (8, 0):
-                weave(1, 7, 8, on_scalar)
 
         def gradient(c, first_bank):
             for h in range(2):
                 piece(c, BANK * h, BANK, (first_bank + h) % BANKS)
                 store(on_scalar, c, BANK * h)
 
-        quant_h(0, 4, 8)
-        for s in (8, 9):
+        for s in (7, 6):
             sign(s, 1)
-        quant_h(1, 4, 8)
-        for s in range(4):
-            sign(s, 0)
+        quant_h(0, 4, 6)
+        weave(1, 4, 6)
+        for s in (9, 8):
+            sign(s, 1)
+        weave(0, 7, 8)
+        quant_h(1, 4, 6)
         for s in (10, 11):
             sign(s, 1)
-        for s in range(4, 6):
-            sign(s, 0)
+        quant_h(0, 6, 8)
         weave(2, 4, 6)
-        for s in range(6, 8):
-            sign(s, 0)
+        sign(4, 0)
+        sign(5, 0)
         quant_h(2, 4, 6)
+        weave(1, 6, 8)
         weave(2, 6, 8)
-        weave(0, 0, 2, on_scalar)
-        for s in range(8, 10):
-            sign(s, 0)
+        quant_h(1, 6, 8)
         quant_h(2, 6, 8)
+        weave(0, 2, 4, on_scalar)
 
-        opened = ((4, 0, 3), (4, BANK, 7), (5, 0, 0))
-        for c, n0, b in opened:
+        opened = ((4, 0), (4, BANK), (5, 0))
+        for b, (c, n0) in enumerate(opened):
             piece(c, n0, BANK, b, (0, 1))
-        for c, n0, b in opened:
+        for b, (c, n0) in enumerate(opened):
             piece(c, n0, BANK, b, (2,))
             store(on_scalar, c, n0)
-        piece(5, BANK, BANK, 1)
+        piece(5, BANK, BANK, 3)
         store(on_scalar, 5, BANK)
-        for s in range(10, SLOTS):
+        for s in range(SLOTS - 1, 5, -1):
             sign(s, 0)
-        gradient(6, 2)
-        gradient(7, 4)
+        gradient(6, 4)
+        weave(1, 2, 4, on_scalar)
+        gradient(7, 6)
         for g in (1, 2):
             weave(g, 0, 2)
         for g in (0, 1, 2):
             quant_h(g, 0, 2)
-        gradient(0, 6)
-        gradient(1, 0)
-        for g in (0, 1, 2):
-            weave(g, 2, 4)
+        gradient(0, 0)
+        gradient(1, 2)
+        weave(2, 2, 4)
         for g in (0, 1, 2):
             quant_h(g, 2, 4)
-        piece(2, 0, BANK, 2)
+        piece(2, 0, BANK, 4)
         store(on_scalar, 2, 0)
         last_pieces = [(2, 512, 256), (2, 768, 256), (3, 0, 256), (3, 256, 256), (3, 512, 256)]
         last_pieces += [(3, 768, P), (3, 896, P)]
         for i, (c, n0, width) in enumerate(last_pieces):
-            piece(c, n0, width, (3 + i) % BANKS)
+            piece(c, n0, width, (5 + i) % BANKS)
             store(on_scalar if i % 2 else on_vector, c, n0)

@@ -314,7 +314,7 @@ def tile_recomputed_hidden_weight_gradient_s3_kernel(
 
         def store(copy, c, n0):
             acc, width = pieces[c, n0]
-            result = passing("result%d" % width, [P, width], F32, 6)
+            result = kept("result%d_%d" % (c, n0), [P, width], F32)
             copy(out=result[:, 0:width], in_=acc[:, 0:width])
             nc.sync.dma_start(out=out[P * c : P * c + P, n0 : n0 + width], in_=result[:, 0:width])
 
@@ -371,29 +371,30 @@ def tile_recomputed_hidden_weight_gradient_s3_kernel(
         quant_x(0, 2, 4)
         turn_xo(0, 2)
         empty_xo(0)
-        turn_x(2, 0)
-        turn_x(3, 3)
+        turn_x(2, 3)
+        turn_x(3, 4)
         scale_x(2)
         scale_x(3)
         lay_wo(on_scalar, 0, 128)
         lay_wo(on_gpsimd, 128, 512)
+        widen_reading(5, 0, 1, own[5][:, 0:512])
         widen_reading(4, 0, 2, own[4][:])
-        widen_reading(5, 0, 2, own[5][:])
-        for s, hf, b in ((0, 0, 7), (1, 0, 5), (0, 1, 4), (1, 1, 6)):
+        widen_reading(5, 1, 1, own[5][:, 512:1024])
+        for s, hf, b in ((0, 0, 7), (1, 0, 6), (0, 1, 0), (1, 1, 5)):
             unit(s, hf, X, b)
-        turn_xo(1, 2)
-        turn_x(4, 0)
-        turn_x(5, 1)
+        turn_xo(1, 1)
+        turn_x(4, 2)
+        turn_x(5, 3)
         split_gate()
         empty_xo(1)
         lay_wo(on_scalar, 512, 768)
         quant_x(1, 0, 2)
         quant_x(0, 4, 6)
         quant_wo(0)
-        unit(2, 0, X, 3)
+        unit(2, 0, X, 4)
         unit(0, 0, XO)
         unit(1, 0, XO)
-        turn_xo(2, 2)
+        turn_xo(2, 1)
         lay_wo(on_vector, 768, 1024)
         quant_x(1, 2, 6)
         empty(0, 0)
@@ -401,17 +402,18 @@ def tile_recomputed_hidden_weight_gradient_s3_kernel(
         quant_wo(1)
 
         waiting = [(2, 0, XO), (3, 0, ALL), (2, 1, X), (0, 1, XO), (1, 1, XO), (2, 1, XO), (3, 1, ALL)]
-        banks = [7, 5, 3, 4, 6]
+        opens_in = {(3, 0): 7, (2, 1): 6, (3, 1): 4}
         prep = {
             3: [(s, 1) for s in (3, 2, 1, 0)],
             4: [(5, 1), (4, 1)] + [(s, 0) for s in range(4)],
         }
-        n_units = 0
+        xo_bank = {3: 1, 4: 6, 5: 5}
+        unit_banks = {2: (7, 0, 5, 4), 3: (1, 7, 0, 4), 4: (6, 1, 7, 0), 5: (2, 3, 5, 6)}
         for j in range(2, PAIRS):
             if j > 2:
-                turn_x(2 * j, 0)
-                turn_xo(j, 2)
-                turn_x(2 * j + 1, 1)
+                turn_xo(j, xo_bank[j])
+                turn_x(2 * j, 2)
+                turn_x(2 * j + 1, 3)
             scale_x(2 * j)
             scale_x(2 * j + 1)
             ahead = wo_rest[:] if j == 2 else stage[(j - 1) % 3][:, 0 : 2 * K]
@@ -424,15 +426,14 @@ def tile_recomputed_hidden_weight_gradient_s3_kernel(
                 if (s, hf) in sums:
                     unit(s, hf, passes)
                 else:
-                    unit(s, hf, passes, banks[n_units % 5])
-                    n_units += 1
+                    unit(s, hf, passes, opens_in[s, hf])
                 if i == 0:
                     empty_xo(j)
                     if j + 1 == PAIRS:
                         weave(0, 0, 2, on_scalar)
                 if passes != X:
                     empty(s, hf)
-                if i == 0 and j + 1 < PAIRS:
+                if i == (1 if j == 2 else 0) and j + 1 < PAIRS:
                     widen_reading(2 * j + 3, 1, 1, ahead[:, 1536:2048])
             if j + 1 < PAIRS:
                 sort_xo(on_vector, j + 1)
@@ -445,14 +446,15 @@ def tile_recomputed_hidden_weight_gradient_s3_kernel(
                 for run0 in (0, 4, 2):
                     quant_x(j, run0, run0 + 2)
             waiting = [(2 * j, 1, ALL), (2 * j + 1, 1, ALL), (2 * j, 0, ALL), (2 * j + 1, 0, ALL)]
+            for (s, hf, passes), b in zip(waiting, unit_banks[j]):
+                opens_in[s, hf] = b
         for s, hf, passes in waiting:
-            unit(s, hf, ALL, banks[n_units % 5])
-            n_units += 1
+            unit(s, hf, ALL, opens_in[s, hf])
             empty(s, hf)
 
-        def gradient(c, first_bank):
+        def gradient(c, banks):
             for h in range(2):
-                piece(c, BANK * h, BANK, (first_bank + h) % BANKS)
+                piece(c, BANK * h, BANK, banks[h])
                 store(on_scalar, c, BANK * h)
 
         for s in (7, 6):
@@ -476,32 +478,32 @@ def tile_recomputed_hidden_weight_gradient_s3_kernel(
         quant_h(2, 6, 8)
         weave(0, 2, 4, on_scalar)
 
-        opened = ((4, 0), (4, BANK), (5, 0))
-        for b, (c, n0) in enumerate(opened):
+        opened = ((4, 0, 4), (4, BANK, 1), (5, 0, 7))
+        for c, n0, b in opened:
             piece(c, n0, BANK, b, (0, 1))
-        for b, (c, n0) in enumerate(opened):
+        for c, n0, b in opened:
             piece(c, n0, BANK, b, (2,))
             store(on_scalar, c, n0)
-        piece(5, BANK, BANK, 3)
+        piece(5, BANK, BANK, 0)
         store(on_scalar, 5, BANK)
         for s in range(SLOTS - 1, 5, -1):
             sign(s, 0)
-        gradient(6, 4)
+        gradient(6, (2, 3))
         weave(1, 2, 4, on_scalar)
-        gradient(7, 6)
+        gradient(7, (5, 1))
         for g in (1, 2):
             weave(g, 0, 2)
         for g in (0, 1, 2):
             quant_h(g, 0, 2)
-        gradient(0, 0)
-        gradient(1, 2)
+        gradient(0, (6, 4))
+        gradient(1, (7, 2))
         weave(2, 2, 4)
         for g in (0, 1, 2):
             quant_h(g, 2, 4)
-        piece(2, 0, BANK, 4)
+        piece(2, 0, BANK, 0)
         store(on_scalar, 2, 0)
         last_pieces = [(2, 512, 256), (2, 768, 256), (3, 0, 256), (3, 256, 256), (3, 512, 256)]
         last_pieces += [(3, 768, P), (3, 896, P)]
         for i, (c, n0, width) in enumerate(last_pieces):
-            piece(c, n0, width, (5 + i) % BANKS)
+            piece(c, n0, width, (3, 5, 1, 6, 4, 7, 2)[i])
             store(on_scalar if i % 2 else on_vector, c, n0)

@@ -25,6 +25,7 @@ GROUPS = T // 512
 SLOTS = 4 * GROUPS
 PAIRS = SLOTS // 2
 XO_PASS = 2
+GPSIMD_SHARE = 1280
 BF16_ONES = 0x3F803F80
 
 
@@ -83,14 +84,17 @@ def tile_recomputed_hidden_weight_gradient_s3_kernel(
         wo_v = wo.rearrange("(p j) f -> p j f", j=4)
         x_raw, wo_raw = {}, {}
 
-        def load_x(s0, s1):
-            g, t0 = divmod(s0, 4)
-            rows_in = kept("x_raw%d" % s0, [P, (s1 - s0) * K], U8)
-            nc.sync.dma_start(
-                out=rows_in[:].rearrange("p (t k) -> p t k", k=K), in_=x_v[g][:, t0 : t0 + s1 - s0, :]
-            )
-            for s in range(s0, s1):
-                x_raw[s] = (rows_in, K * (s - s0))
+        def load_x(*edges):
+            rows_in = kept("x_raw%d" % edges[0], [P, (edges[-1] - edges[0]) * K], U8)
+            for s in range(edges[0], edges[-1]):
+                x_raw[s] = (rows_in, K * (s - edges[0]))
+            for s0, s1 in zip(edges, edges[1:]):
+                g, t0 = divmod(s0, 4)
+                c0 = x_raw[s0][1]
+                nc.sync.dma_start(
+                    out=rows_in[:, c0 : c0 + K * (s1 - s0)].rearrange("p (t k) -> p t k", k=K),
+                    in_=x_v[g][:, t0 : t0 + s1 - s0, :],
+                )
 
         def load_xo(j):
             g, h = divmod(j, 2)
@@ -136,21 +140,29 @@ def tile_recomputed_hidden_weight_gradient_s3_kernel(
             return rows_in[:, c0 + 512 * kk : c0 + 512 * (kk + count)].bitcast(FP8)
 
         def place(s, kk, count, values):
+            words = values.bitcast(F32).rearrange("p (u w) -> p u w", u=2)
             for i in range(count):
-                wide[s + (kk + i) // 2, (kk + i) % 2] = values[:, 512 * i : 512 * i + 512]
+                wide[s + (kk + i) // 2, (kk + i) % 2] = words[:, :, P * i : P * i + P]
 
-        def widen_writing(copy, s, kk, count, values):
+        def widen_writing(copy, s, kk, count, values, k0=0, k1=None):
             place(s, kk, count, values)
+            k1 = 512 * count if k1 is None else k1
             copy(
-                out=values.rearrange("p (g u m e) -> p g m u e", u=2, m=P, e=2),
-                in_=raw_passes(s, kk, count).rearrange("p (g m u e) -> p g m u e", u=2, m=P, e=2),
+                out=values.rearrange("p (u m e) -> p m u e", u=2, e=2)[:, k0 // 4 : k1 // 4, :, :],
+                in_=raw_passes(s, kk, count)[:, k0:k1].rearrange("p (m u e) -> p m u e", u=2, e=2),
             )
+
+        def widen_plainly(copy, s, kk, count, values):
+            words = values.bitcast(F32).rearrange("p (w u) -> p u w", u=2)
+            for i in range(count):
+                wide[s + (kk + i) // 2, (kk + i) % 2] = words[:, :, P * i : P * i + P]
+            copy(out=values, in_=raw_passes(s, kk, count))
 
         def widen_reading(s, kk, count, values):
             place(s, kk, count, values)
             on_scalar(
-                out=values.rearrange("p (g u m e) -> p g u m e", u=2, m=P, e=2),
-                in_=raw_passes(s, kk, count).rearrange("p (g m u e) -> p g u m e", u=2, m=P, e=2),
+                out=values.rearrange("p (u m e) -> p u m e", u=2, e=2),
+                in_=raw_passes(s, kk, count).rearrange("p (m u e) -> p u m e", u=2, e=2),
             )
 
         def sort_xo(copy, j):
@@ -165,7 +177,7 @@ def tile_recomputed_hidden_weight_gradient_s3_kernel(
             for kk in runs:
                 for u in range(2):
                     o0 = 256 * u + P * kk
-                    src = wide[s, kk].bitcast(F32)[:, P * u : P * u + P]
+                    src = wide[s, kk][:, u, :]
                     nc.tensor.transpose(ps[:, o0 : o0 + P], src, ident[:])
                 turned[s, kk] = ps
 
@@ -318,10 +330,10 @@ def tile_recomputed_hidden_weight_gradient_s3_kernel(
             copy(out=result[:, 0:width], in_=acc[:, 0:width])
             nc.sync.dma_start(out=out[P * c : P * c + P, n0 : n0 + width], in_=result[:, 0:width])
 
-        def warm_up(count, b):
+        def warm_up(count, b, width=BANK):
             ps = bank(b)
             for j in range(count):
-                nc.tensor.matmul(ps[:], lhsT=ones[:, 0:P], rhs=ones[:], start=True, stop=True)
+                nc.tensor.matmul(ps[:, 0:width], lhsT=ones[:, 0:P], rhs=ones[:, 0:width], start=True, stop=True)
 
         X, XO, ALL = (0, 1), (XO_PASS,), (0, 1, XO_PASS)
         widen_on_gpsimd = nc.gpsimd.tensor_copy
@@ -334,17 +346,16 @@ def tile_recomputed_hidden_weight_gradient_s3_kernel(
         load_x(0, 1)
         load_x(1, 2)
         load_x_scale()
-        load_x(2, 4)
+        load_x(2, 4, 6)
         load_xo(0)
         load_w(0)
         load_scale_bytes(w_plane, w_scales)
         load_wo(0, 4)
-        load_x(4, 6)
         load_w(1)
         load_xo(1)
-        load_gates()
-        load_wo(4, 8)
         load_xo(2)
+        load_wo(4, 8)
+        load_gates()
         load_x(6, 8)
         load_xo(3)
         load_x(8, 12)
@@ -354,70 +365,77 @@ def tile_recomputed_hidden_weight_gradient_s3_kernel(
         nc.sync.dma_start(out=dy_codes[:], in_=dy_words.rearrange("g p n -> p g n"))
 
         first = [kept("first%d" % i, [P, 512], BF16) for i in range(2)]
+        early = kept("early", [P, 512], BF16)
         own = {s: kept("wide%d" % s, [P, K], BF16) for s in range(1, 6)}
         warm_up(4, 6)
         widen_writing(on_vector, 0, 0, 1, first[0][:])
-        widen_reading(0, 1, 1, first[1][:])
-        widen_writing(on_vector, 1, 0, 2, own[1][:])
-        widen_reading(2, 0, 2, own[2][:])
+        widen_plainly(on_scalar, 0, 1, 1, first[1][:])
+        widen_plainly(on_vector, 1, 0, 2, own[1][:])
+        widen_plainly(on_scalar, 2, 0, 2, own[2][:])
         widen_writing(widen_on_gpsimd, 3, 0, 2, own[3][:])
+        widen_plainly(widen_on_gpsimd, 4, 0, 1, early[:])
+        widen_reading(4, 1, 1, own[4][:, 0:512])
         for kk, b in ((0, 0), (1, 5)):
             turn_x(0, b, (kk,))
             scale_x(0, kk, kk + 1)
         turn_x(1, 1)
         warm_up(2, 6)
         scale_x(1)
-        quant_x(0, 0, 2)
-        quant_x(0, 2, 4)
         turn_xo(0, 2)
         empty_xo(0)
+        quant_x(0, 0, 2)
+        quant_x(0, 2, 6)
         turn_x(2, 3)
         turn_x(3, 4)
+        turn_x(4, 6)
         scale_x(2)
         scale_x(3)
-        lay_wo(on_scalar, 0, 128)
-        lay_wo(on_gpsimd, 128, 512)
-        widen_reading(5, 0, 1, own[5][:, 0:512])
-        widen_reading(4, 0, 2, own[4][:])
-        widen_reading(5, 1, 1, own[5][:, 512:1024])
-        for s, hf, b in ((0, 0, 7), (1, 0, 6), (0, 1, 0), (1, 1, 5)):
+        widen_reading(5, 0, 2, own[5][:])
+        lay_wo(on_scalar, 0, 256)
+        lay_wo(on_gpsimd, 256, 512)
+        sort_xo(on_scalar, 2)
+        for s, hf, b in ((0, 0, 7), (1, 0, 0), (0, 1, 5), (1, 1, 1)):
             unit(s, hf, X, b)
-        turn_xo(1, 1)
-        turn_x(4, 2)
-        turn_x(5, 3)
-        split_gate()
+        turn_xo(1, 3)
+        turn_x(5, 4)
+        turn_xo(2, 2)
         empty_xo(1)
-        lay_wo(on_scalar, 512, 768)
-        quant_x(1, 0, 2)
-        quant_x(0, 4, 6)
+        empty_xo(2)
+        split_gate()
         quant_wo(0)
-        unit(2, 0, X, 4)
+        quant_x(1, 0, 4)
         unit(0, 0, XO)
         unit(1, 0, XO)
-        turn_xo(2, 1)
+        lay_wo(on_vector, 512, 768)
+        quant_x(1, 4, 6)
         lay_wo(on_vector, 768, 1024)
-        quant_x(1, 2, 6)
+        sort_xo(on_vector, 3)
         empty(0, 0)
         empty(1, 0)
         quant_wo(1)
 
-        waiting = [(2, 0, XO), (3, 0, ALL), (2, 1, X), (0, 1, XO), (1, 1, XO), (2, 1, XO), (3, 1, ALL)]
-        opens_in = {(3, 0): 7, (2, 1): 6, (3, 1): 4}
+        waiting = [(2, 0, X), (3, 0, X), (2, 0, XO), (3, 0, XO), (2, 1, X), (3, 1, X)]
+        waiting += [(s, 1, XO) for s in range(4)]
+        opens_in = {(2, 0): 3, (3, 0): 2, (2, 1): 7, (3, 1): 0}
         prep = {
             3: [(s, 1) for s in (3, 2, 1, 0)],
-            4: [(5, 1), (4, 1)] + [(s, 0) for s in range(4)],
+            4: [(s, 0) for s in range(4)],
         }
-        xo_bank = {3: 1, 4: 6, 5: 5}
-        unit_banks = {2: (7, 0, 5, 4), 3: (1, 7, 0, 4), 4: (6, 1, 7, 0), 5: (2, 3, 5, 6)}
+        unit_banks = {2: (2, 5, 1, 7), 3: (0, 2, 5, 1), 4: (7, 0, 2, 5), 5: (1, 7, 0, 2)}
         for j in range(2, PAIRS):
+            if j == 3:
+                turn_xo(j, 3)
             if j > 2:
-                turn_xo(j, xo_bank[j])
-                turn_x(2 * j, 2)
-                turn_x(2 * j + 1, 3)
+                turn_x(2 * j, 6)
+                if j > 3:
+                    turn_xo(j, 3)
+                turn_x(2 * j + 1, 4)
             scale_x(2 * j)
             scale_x(2 * j + 1)
             ahead = wo_rest[:] if j == 2 else stage[(j - 1) % 3][:, 0 : 2 * K]
-            if j + 1 < PAIRS:
+            if j == 2:
+                widen_writing(widen_on_gpsimd, 6, 0, 2, ahead[:, 0:K])
+            elif j + 1 < PAIRS:
                 widen_writing(widen_on_gpsimd, 2 * j + 2, 0, 3, ahead[:, 0:1536])
             else:
                 h_moved[0, 1] = ahead
@@ -427,19 +445,24 @@ def tile_recomputed_hidden_weight_gradient_s3_kernel(
                     unit(s, hf, passes)
                 else:
                     unit(s, hf, passes, opens_in[s, hf])
-                if i == 0:
+                if i == 0 and j > 2:
                     empty_xo(j)
                     if j + 1 == PAIRS:
                         weave(0, 0, 2, on_scalar)
                 if passes != X:
                     empty(s, hf)
-                if i == (1 if j == 2 else 0) and j + 1 < PAIRS:
+                if j == 2 and i == 2:
+                    widen_reading(7, 0, 2, own[1][:])
+                if i == 0 and 2 < j < PAIRS - 1:
                     widen_reading(2 * j + 3, 1, 1, ahead[:, 1536:2048])
-            if j + 1 < PAIRS:
+            if 2 < j < PAIRS - 1:
                 sort_xo(on_vector, j + 1)
             for s, hf in prep.get(j, []):
                 sign(s, hf)
-            if j + 1 < PAIRS:
+            if j == 2:
+                quant_x(j, 0, 2)
+                quant_x(j, 2, 6)
+            elif j + 1 < PAIRS:
                 quant_x(j, 0, 4)
                 quant_x(j, 4, 6)
             else:
@@ -457,7 +480,7 @@ def tile_recomputed_hidden_weight_gradient_s3_kernel(
                 piece(c, BANK * h, BANK, banks[h])
                 store(on_scalar, c, BANK * h)
 
-        for s in (7, 6):
+        for s in (7, 6, 5, 4):
             sign(s, 1)
         quant_h(0, 4, 6)
         weave(1, 4, 6)
@@ -478,32 +501,32 @@ def tile_recomputed_hidden_weight_gradient_s3_kernel(
         quant_h(2, 6, 8)
         weave(0, 2, 4, on_scalar)
 
-        opened = ((4, 0, 4), (4, BANK, 1), (5, 0, 7))
+        opened = ((4, 0, 6), (4, BANK, 4), (5, 0, 3))
         for c, n0, b in opened:
             piece(c, n0, BANK, b, (0, 1))
         for c, n0, b in opened:
             piece(c, n0, BANK, b, (2,))
             store(on_scalar, c, n0)
-        piece(5, BANK, BANK, 0)
+        piece(5, BANK, BANK, 5)
         store(on_scalar, 5, BANK)
         for s in range(SLOTS - 1, 5, -1):
             sign(s, 0)
-        gradient(6, (2, 3))
+        gradient(6, (1, 7))
         weave(1, 2, 4, on_scalar)
-        gradient(7, (5, 1))
+        gradient(7, (0, 2))
         for g in (1, 2):
             weave(g, 0, 2)
         for g in (0, 1, 2):
             quant_h(g, 0, 2)
         gradient(0, (6, 4))
-        gradient(1, (7, 2))
+        gradient(1, (3, 5))
         weave(2, 2, 4)
         for g in (0, 1, 2):
             quant_h(g, 2, 4)
-        piece(2, 0, BANK, 0)
+        piece(2, 0, BANK, 1)
         store(on_scalar, 2, 0)
         last_pieces = [(2, 512, 256), (2, 768, 256), (3, 0, 256), (3, 256, 256), (3, 512, 256)]
         last_pieces += [(3, 768, P), (3, 896, P)]
         for i, (c, n0, width) in enumerate(last_pieces):
-            piece(c, n0, width, (3, 5, 1, 6, 4, 7, 2)[i])
+            piece(c, n0, width, (7, 0, 2, 6, 4, 3, 5)[i])
             store(on_scalar if i % 2 else on_vector, c, n0)

@@ -59,8 +59,8 @@ def tile_recomputed_hidden_weight_gradient_s3_kernel(
         w_plane = kept("w_plane", [P, 2, F], U8)
         dy_codes = kept("dy_codes", [P, GROUPS, 2 * N], U8)
         dy_plane = kept("dy_plane", [P, GROUPS, N], U8)
-        scale_by_k = kept("scale_by_k", [P, 2, 4], F32)
-        gates = kept("gates", [P, SLOTS], BF16)
+        scale_by_k = kept("scale_by_k", [P, 2, 8], F32)[:, :, 0:4]
+        gates = kept("gates", [P, GROUPS, 16], BF16)[:, :, 0:4]
         gate_abs = kept("gate_abs", [P, SLOTS], F32)
         gate_sign = kept("gate_sign", [P, SLOTS], F32)
         wo_codes = kept("wo_codes", [P, F], U32)
@@ -70,10 +70,12 @@ def tile_recomputed_hidden_weight_gradient_s3_kernel(
         x_plane = [kept("x_plane%d" % j, [P, 6 * P], U8) for j in range(PAIRS)]
         xo_raw = [kept("xo_raw%d" % j, [P, K], BF16) for j in range(PAIRS)]
         stage = [kept("stage%d" % i, [P, 3 * K], BF16) for i in range(3)]
-        h_laid = [kept("h_laid%d" % g, [P, 4 * F], BF16) for g in range(GROUPS)]
-        h_moved = {}
-        h_codes = [kept("h_codes%d" % g, [P, F], U32) for g in range(GROUPS)]
-        h_plane = [kept("h_plane%d" % g, [P, F], U8) for g in range(GROUPS)]
+        by_group = [kept("by_group%d" % g, [P, 4 * BANK], BF16)[:] for g in range(GROUPS)]
+        by_chunk = [kept("by_chunk%d" % c, [P, GROUPS * 512], BF16)[:] for c in range(4)]
+        group_codes = [kept("group_codes%d" % g, [P, BANK], U32) for g in range(GROUPS)]
+        group_plane = [kept("group_plane%d" % g, [P, BANK], U8) for g in range(GROUPS)]
+        chunk_codes = [kept("chunk_codes%d" % c, [P, GROUPS * P], U32) for c in range(4)]
+        chunk_plane = [kept("chunk_plane%d" % c, [P, GROUPS * P], U8) for c in range(4)]
         planes = [
             [kept("planes%d_%d" % (g, hf), [P, 4 * BANK], BF16) for hf in range(2)]
             for g in range(GROUPS)
@@ -124,13 +126,12 @@ def tile_recomputed_hidden_weight_gradient_s3_kernel(
 
         def load_x_scale():
             nc.sync.dma_start(
-                out=scale_by_k[:], in_=x_scale.rearrange("o (g p t) -> p (o g) t", p=P, t=4)
+                out=scale_by_k, in_=x_scale.rearrange("o (g p t) -> p (o g) t", p=P, t=4)
             )
 
-        def load_gates():
+        def load_gates(g0, g1):
             nc.sync.dma_start(
-                out=gates[:].rearrange("p (g t) -> p g t", t=4),
-                in_=gate.rearrange("(g m t) -> m g t", m=P, t=4),
+                out=gates[:, g0:g1, :], in_=gate.rearrange("(g m t) -> m g t", m=P, t=4)[:, g0:g1, :]
             )
 
         wide, xo_sorted, turned = {}, {}, {}
@@ -158,11 +159,11 @@ def tile_recomputed_hidden_weight_gradient_s3_kernel(
                 wide[s + (kk + i) // 2, (kk + i) % 2] = words[:, :, P * i : P * i + P]
             copy(out=values, in_=raw_passes(s, kk, count))
 
-        def widen_reading(s, kk, count, values):
+        def widen_reading(s, kk, count, values, k0=0):
             place(s, kk, count, values)
             on_scalar(
-                out=values.rearrange("p (u m e) -> p u m e", u=2, e=2),
-                in_=raw_passes(s, kk, count).rearrange("p (m u e) -> p u m e", u=2, e=2),
+                out=values.rearrange("p (u m e) -> p u m e", u=2, e=2)[:, :, k0 // 4 :, :],
+                in_=raw_passes(s, kk, count)[:, k0:].rearrange("p (m u e) -> p u m e", u=2, e=2),
             )
 
         def sort_xo(copy, j):
@@ -259,7 +260,8 @@ def tile_recomputed_hidden_weight_gradient_s3_kernel(
                     rhs, rhs_scale = wo_codes[:, cols].bitcast(FP8X4), wo_plane[:, cols]
                 else:
                     w0 = P * (2 * (s % 2) + kk)
-                    rhs, rhs_scale = w_codes[hf][:, kk, :].bitcast(FP4X4), w_plane[:, kk, cols]
+                    rhs = w_codes[hf][:, kk, :].bitcast(FP4X4)
+                    rhs_scale = w_plane[:, kk, cols]
                 done.append(kk)
                 nc.tensor.matmul_mx(
                     out=ps[:],
@@ -271,9 +273,13 @@ def tile_recomputed_hidden_weight_gradient_s3_kernel(
                     stop=(len(done) == 3),
                 )
 
-        def split_gate():
-            nc.scalar.activation(out=gate_abs[:], in_=gates[:], func=ACT.Abs)
-            nc.scalar.activation(out=gate_sign[:], in_=gates[:], func=ACT.Sign)
+        def split_gate(g0, g1):
+            for dst, func in ((gate_abs, ACT.Abs), (gate_sign, ACT.Sign)):
+                nc.scalar.activation(
+                    out=dst[:, 4 * g0 : 4 * g1].rearrange("p (g t) -> p g t", t=4),
+                    in_=gates[:, g0:g1, :],
+                    func=func,
+                )
 
         def plane(s, hf):
             g, t = divmod(s, 4)
@@ -284,16 +290,16 @@ def tile_recomputed_hidden_weight_gradient_s3_kernel(
                 out=plane(s, hf), in_=sums[s, hf][0][:], func=ACT.Relu, scale=gate_abs[:, s : s + 1]
             )
 
-        def sign(s, hf):
-            row = plane(s, hf)
+        def sign(s, hf, f0=0, f1=BANK):
+            row = plane(s, hf)[:, f0:f1]
             nc.vector.tensor_scalar(
                 out=row, in0=row, scalar1=gate_sign[:, s : s + 1], scalar2=None, op0=MULT
             )
 
         def woven(g, c0, c1):
-            hf, c = divmod(c0, 4)
-            values = h_moved.get((g, hf), h_laid[g][:, 4 * BANK * hf : 4 * BANK * (hf + 1)])
-            return values[:, 512 * c : 512 * (c + c1 - c0)]
+            if c0 < 4:
+                return by_chunk[c0][:, 512 * g : 512 * g + 512]
+            return by_group[g][:, 512 * (c0 - 4) : 512 * (c1 - 4)]
 
         def weave(g, c0, c1, copy=on_vector):
             hf, c = divmod(c0, 4)
@@ -304,8 +310,10 @@ def tile_recomputed_hidden_weight_gradient_s3_kernel(
             )
 
         def quant_h(g, c0, c1):
-            values = woven(g, c0, c1)
-            quantise(h_codes[g], h_plane[g], values, P * c0, P * c1)
+            quantise(group_codes[g], group_plane[g], woven(g, c0, c1), P * (c0 - 4), P * (c1 - 4))
+
+        def quant_chunk(c):
+            quantise(chunk_codes[c], chunk_plane[c], by_chunk[c], 0, GROUPS * P)
 
         pieces = {}
 
@@ -314,10 +322,14 @@ def tile_recomputed_hidden_weight_gradient_s3_kernel(
                 pieces[c, n0] = (bank(b), width)
             acc = pieces[c, n0][0]
             for g in groups:
+                if c < 4:
+                    codes, scales, w0 = chunk_codes[c], chunk_plane[c], P * g
+                else:
+                    codes, scales, w0 = group_codes[g], group_plane[g], P * (c - 4)
                 nc.tensor.matmul_mx(
                     out=acc[:, 0:width],
-                    lhsT=h_codes[g][:, P * c : P * c + P].bitcast(FP8X4),
-                    lhsT_scale=h_plane[g][:, P * c : P * c + P],
+                    lhsT=codes[:, w0 : w0 + P].bitcast(FP8X4),
+                    lhsT_scale=scales[:, w0 : w0 + P],
                     rhs=dy_codes[:, g, 2 * n0 : 2 * n0 + 2 * width].bitcast(FP4X4),
                     rhs_scale=dy_plane[:, g, n0 : n0 + width],
                     start=(g == 0),
@@ -355,9 +367,10 @@ def tile_recomputed_hidden_weight_gradient_s3_kernel(
         load_xo(1)
         load_xo(2)
         load_wo(4, 8)
-        load_gates()
-        load_x(6, 8)
+        load_gates(0, 1)
         load_xo(3)
+        load_x(6, 8)
+        load_gates(1, 3)
         load_x(8, 12)
         load_xo(4)
         load_xo(5)
@@ -401,7 +414,7 @@ def tile_recomputed_hidden_weight_gradient_s3_kernel(
         turn_xo(2, 2)
         empty_xo(1)
         empty_xo(2)
-        split_gate()
+        split_gate(0, 1)
         quant_wo(0)
         quant_x(1, 0, 4)
         unit(0, 0, XO)
@@ -417,10 +430,7 @@ def tile_recomputed_hidden_weight_gradient_s3_kernel(
         waiting = [(2, 0, X), (3, 0, X), (2, 0, XO), (3, 0, XO), (2, 1, X), (3, 1, X)]
         waiting += [(s, 1, XO) for s in range(4)]
         opens_in = {(2, 0): 3, (3, 0): 2, (2, 1): 7, (3, 1): 0}
-        prep = {
-            3: [(s, 1) for s in (3, 2, 1, 0)],
-            4: [(s, 0) for s in range(4)],
-        }
+        prep = {4: [(s, 1) for s in (3, 2, 1, 0)]}
         unit_banks = {2: (2, 5, 1, 7), 3: (0, 2, 5, 1), 4: (7, 0, 2, 5), 5: (1, 7, 0, 2)}
         for j in range(2, PAIRS):
             if j == 3:
@@ -438,7 +448,7 @@ def tile_recomputed_hidden_weight_gradient_s3_kernel(
             elif j + 1 < PAIRS:
                 widen_writing(widen_on_gpsimd, 2 * j + 2, 0, 3, ahead[:, 0:1536])
             else:
-                h_moved[0, 1] = ahead
+                by_group[0] = ahead
                 weave(0, 4, 7, on_gpsimd)
             for i, (s, hf, passes) in enumerate(waiting):
                 if (s, hf) in sums:
@@ -447,12 +457,11 @@ def tile_recomputed_hidden_weight_gradient_s3_kernel(
                     unit(s, hf, passes, opens_in[s, hf])
                 if i == 0 and j > 2:
                     empty_xo(j)
-                    if j + 1 == PAIRS:
-                        weave(0, 0, 2, on_scalar)
                 if passes != X:
                     empty(s, hf)
                 if j == 2 and i == 2:
                     widen_reading(7, 0, 2, own[1][:])
+                    split_gate(1, 3)
                 if i == 0 and 2 < j < PAIRS - 1:
                     widen_reading(2 * j + 3, 1, 1, ahead[:, 1536:2048])
             if 2 < j < PAIRS - 1:
@@ -488,18 +497,21 @@ def tile_recomputed_hidden_weight_gradient_s3_kernel(
             sign(s, 1)
         weave(0, 7, 8)
         quant_h(1, 4, 6)
+        for s in range(4):
+            sign(s, 0, 0, 256)
         for s in (10, 11):
             sign(s, 1)
         quant_h(0, 6, 8)
         weave(2, 4, 6)
-        sign(4, 0)
-        sign(5, 0)
+        weave(1, 6, 8, on_scalar)
+        for s in range(4, 8):
+            sign(s, 0, 0, 256)
         quant_h(2, 4, 6)
-        weave(1, 6, 8)
         weave(2, 6, 8)
+        for s in (11, 10, 9, 8):
+            sign(s, 0, 0, 256)
         quant_h(1, 6, 8)
         quant_h(2, 6, 8)
-        weave(0, 2, 4, on_scalar)
 
         opened = ((4, 0, 6), (4, BANK, 4), (5, 0, 3))
         for c, n0, b in opened:
@@ -509,20 +521,28 @@ def tile_recomputed_hidden_weight_gradient_s3_kernel(
             store(on_scalar, c, n0)
         piece(5, BANK, BANK, 5)
         store(on_scalar, 5, BANK)
-        for s in range(SLOTS - 1, 5, -1):
-            sign(s, 0)
+        for g in range(GROUPS):
+            weave(g, 0, 1)
+        weave(0, 1, 2, on_scalar)
+        weave(1, 1, 2)
+        quant_chunk(0)
+        weave(2, 1, 2)
+        for s in range(SLOTS):
+            sign(s, 0, 256, BANK)
+            if s == 1:
+                quant_chunk(1)
         gradient(6, (1, 7))
-        weave(1, 2, 4, on_scalar)
         gradient(7, (0, 2))
-        for g in (1, 2):
-            weave(g, 0, 2)
-        for g in (0, 1, 2):
-            quant_h(g, 0, 2)
+        weave(0, 2, 3, on_scalar)
+        weave(1, 2, 3)
+        weave(2, 2, 3)
+        weave(0, 3, 4)
+        quant_chunk(2)
+        weave(1, 3, 4)
+        weave(2, 3, 4)
+        quant_chunk(3)
         gradient(0, (6, 4))
         gradient(1, (3, 5))
-        weave(2, 2, 4)
-        for g in (0, 1, 2):
-            quant_h(g, 2, 4)
         piece(2, 0, BANK, 1)
         store(on_scalar, 2, 0)
         last_pieces = [(2, 512, 256), (2, 768, 256), (3, 0, 256), (3, 256, 256), (3, 512, 256)]

@@ -86,17 +86,20 @@ def tile_recomputed_hidden_weight_gradient_s3_kernel(
         wo_v = wo.rearrange("(p j) f -> p j f", j=4)
         x_raw, wo_raw = {}, {}
 
-        def load_x(*edges):
-            rows_in = kept("x_raw%d" % edges[0], [P, (edges[-1] - edges[0]) * K], U8)
-            for s in range(edges[0], edges[-1]):
-                x_raw[s] = (rows_in, K * (s - edges[0]))
-            for s0, s1 in zip(edges, edges[1:]):
-                g, t0 = divmod(s0, 4)
-                c0 = x_raw[s0][1]
-                nc.sync.dma_start(
-                    out=rows_in[:, c0 : c0 + K * (s1 - s0)].rearrange("p (t k) -> p t k", k=K),
-                    in_=x_v[g][:, t0 : t0 + s1 - s0, :],
-                )
+        head_rows = kept("head_rows", [P, 4 * K], U8)
+
+        def load_x(s0, s1):
+            if 2 <= s0 < 6:
+                rows_in, c0 = head_rows, K * (s0 - 2)
+            else:
+                rows_in, c0 = kept("x_raw%d" % s0, [P, (s1 - s0) * K], U8), 0
+            for s in range(s0, s1):
+                x_raw[s] = (rows_in, c0 + K * (s - s0))
+            g, t0 = divmod(s0, 4)
+            nc.sync.dma_start(
+                out=rows_in[:, c0 : c0 + K * (s1 - s0)].rearrange("p (t k) -> p t k", k=K),
+                in_=x_v[g][:, t0 : t0 + s1 - s0, :],
+            )
 
         def load_xo(j):
             g, h = divmod(j, 2)
@@ -358,10 +361,11 @@ def tile_recomputed_hidden_weight_gradient_s3_kernel(
         load_x(0, 1)
         load_x(1, 2)
         load_x_scale()
-        load_x(2, 4, 6)
+        load_x(2, 4)
         load_xo(0)
         load_w(0)
         load_scale_bytes(w_plane, w_scales)
+        load_x(4, 6)
         load_wo(0, 4)
         load_w(1)
         load_xo(1)
@@ -378,43 +382,45 @@ def tile_recomputed_hidden_weight_gradient_s3_kernel(
         nc.sync.dma_start(out=dy_codes[:], in_=dy_words.rearrange("g p n -> p g n"))
 
         first = [kept("first%d" % i, [P, 512], BF16) for i in range(2)]
-        early = kept("early", [P, 512], BF16)
         own = {s: kept("wide%d" % s, [P, K], BF16) for s in range(1, 6)}
         warm_up(4, 6)
         widen_writing(on_vector, 0, 0, 1, first[0][:])
         widen_plainly(on_scalar, 0, 1, 1, first[1][:])
         widen_plainly(on_vector, 1, 0, 2, own[1][:])
-        widen_plainly(on_scalar, 2, 0, 2, own[2][:])
+        widen_reading(2, 0, 2, own[2][:])
         widen_writing(widen_on_gpsimd, 3, 0, 2, own[3][:])
-        widen_plainly(widen_on_gpsimd, 4, 0, 1, early[:])
-        widen_reading(4, 1, 1, own[4][:, 0:512])
         for kk, b in ((0, 0), (1, 5)):
             turn_x(0, b, (kk,))
             scale_x(0, kk, kk + 1)
+        warm_up(1, 6)
         turn_x(1, 1)
-        warm_up(2, 6)
+        warm_up(1, 6)
         scale_x(1)
         turn_xo(0, 2)
         empty_xo(0)
+        warm_up(1, 6)
         quant_x(0, 0, 2)
-        quant_x(0, 2, 6)
+        quant_x(0, 2, 4)
         turn_x(2, 3)
         turn_x(3, 4)
-        turn_x(4, 6)
         scale_x(2)
         scale_x(3)
+        widen_reading(4, 0, 2, own[4][:])
         widen_reading(5, 0, 2, own[5][:])
-        lay_wo(on_scalar, 0, 256)
-        lay_wo(on_gpsimd, 256, 512)
+        lay_wo(on_scalar, 0, 192)
+        lay_wo(on_gpsimd, 192, 512)
         sort_xo(on_scalar, 2)
         for s, hf, b in ((0, 0, 7), (1, 0, 0), (0, 1, 5), (1, 1, 1)):
             unit(s, hf, X, b)
+            if (s, hf) == (1, 0):
+                turn_x(4, 6)
         turn_xo(1, 3)
         turn_x(5, 4)
         turn_xo(2, 2)
         empty_xo(1)
         empty_xo(2)
         split_gate(0, 1)
+        quant_x(0, 4, 6)
         quant_wo(0)
         quant_x(1, 0, 4)
         unit(0, 0, XO)

@@ -339,11 +339,14 @@ def tile_recomputed_hidden_weight_gradient_s3_kernel(
                     stop=(g == GROUPS - 1),
                 )
 
-        def store(copy, c, n0):
+        results = [kept("result%d" % c, [P, N], F32) for c in range(F // P)]
+
+        def copy_out(copy, c, n0):
             acc, width = pieces[c, n0]
-            result = kept("result%d_%d" % (c, n0), [P, width], F32)
-            copy(out=result[:, 0:width], in_=acc[:, 0:width])
-            nc.sync.dma_start(out=out[P * c : P * c + P, n0 : n0 + width], in_=result[:, 0:width])
+            copy(out=results[c][:, n0 : n0 + width], in_=acc[:, 0:width])
+
+        def store(c, n0, n1):
+            nc.sync.dma_start(out=out[P * c : P * c + P, n0:n1], in_=results[c][:, n0:n1])
 
         def warm_up(count, b, width=BANK):
             ps = bank(b)
@@ -490,10 +493,16 @@ def tile_recomputed_hidden_weight_gradient_s3_kernel(
             unit(s, hf, ALL, opens_in[s, hf])
             empty(s, hf)
 
+        WHOLE = (6, 7, 0, 1)
+
         def gradient(c, banks):
             for h in range(2):
                 piece(c, BANK * h, BANK, banks[h])
-                store(on_scalar, c, BANK * h)
+                copy_out(on_scalar, c, BANK * h)
+                if c not in WHOLE:
+                    store(c, BANK * h, BANK * h + BANK)
+            if c in WHOLE:
+                store(c, 0, N)
 
         for s in (7, 6, 5, 4):
             sign(s, 1)
@@ -524,9 +533,12 @@ def tile_recomputed_hidden_weight_gradient_s3_kernel(
             piece(c, n0, BANK, b, (0, 1))
         for c, n0, b in opened:
             piece(c, n0, BANK, b, (2,))
-            store(on_scalar, c, n0)
+            copy_out(on_scalar, c, n0)
+            if (c, n0) == (4, BANK):
+                store(4, 0, N)
         piece(5, BANK, BANK, 5)
-        store(on_scalar, 5, BANK)
+        copy_out(on_scalar, 5, BANK)
+        store(5, 0, N)
         for g in range(GROUPS):
             weave(g, 0, 1)
         weave(0, 1, 2, on_scalar)
@@ -549,10 +561,8 @@ def tile_recomputed_hidden_weight_gradient_s3_kernel(
         quant_chunk(3)
         gradient(0, (6, 4))
         gradient(1, (3, 5))
-        piece(2, 0, BANK, 1)
-        store(on_scalar, 2, 0)
-        last_pieces = [(2, 512, 256), (2, 768, 256), (3, 0, 256), (3, 256, 256), (3, 512, 256)]
-        last_pieces += [(3, 768, P), (3, 896, P)]
-        for i, (c, n0, width) in enumerate(last_pieces):
-            piece(c, n0, width, (7, 0, 2, 6, 4, 3, 5)[i])
-            store(on_scalar if i % 2 else on_vector, c, n0)
+        for i, (c, n0) in enumerate((c, n0) for c in (2, 3) for n0 in range(0, N, 256)):
+            piece(c, n0, 256, (1, 7, 0, 2, 6, 4, 3, 5)[i])
+            copy_out(on_vector if i % 2 else on_scalar, c, n0)
+            if i % 2:
+                store(c, n0 - 256, n0 + 256)

@@ -512,21 +512,21 @@ def tile_recomputed_hidden_weight_gradient_s3_kernel(
             sign(s, 1)
         weave(0, 7, 8)
         quant_h(1, 4, 6)
-        for s in range(4):
-            sign(s, 0, 0, 256)
         for s in (10, 11):
             sign(s, 1)
         quant_h(0, 6, 8)
         weave(2, 4, 6)
         weave(1, 6, 8, on_scalar)
-        for s in range(4, 8):
-            sign(s, 0, 0, 256)
+        for s in range(2):
+            sign(s, 0)
         quant_h(2, 4, 6)
         weave(2, 6, 8)
-        for s in (11, 10, 9, 8):
-            sign(s, 0, 0, 256)
+        for s in range(2, 4):
+            sign(s, 0)
         quant_h(1, 6, 8)
         quant_h(2, 6, 8)
+        for s in (4, 5, 6, 7, 11, 10, 9, 8):
+            sign(s, 0)
 
         opened = ((4, 0, 6), (4, BANK, 4), (5, 0, 3))
         for c, n0, b in opened:
@@ -536,29 +536,20 @@ def tile_recomputed_hidden_weight_gradient_s3_kernel(
             copy_out(on_scalar, c, n0)
             if (c, n0) == (4, BANK):
                 store(4, 0, N)
+                weave(0, 0, 1, on_scalar)
         piece(5, BANK, BANK, 5)
         copy_out(on_scalar, 5, BANK)
         store(5, 0, N)
-        for g in range(GROUPS):
-            weave(g, 0, 1)
-        weave(0, 1, 2, on_scalar)
-        weave(1, 1, 2)
-        quant_chunk(0)
-        weave(2, 1, 2)
-        for s in range(SLOTS):
-            sign(s, 0, 256, BANK)
-            if s == 1:
-                quant_chunk(1)
+        weave(1, 0, 1)
+        weave(2, 0, 1)
+        for c in range(1, 4):
+            weave(0, c, c + 1)
+            quant_chunk(c - 1)
+            weave(1, c, c + 1)
+            weave(2, c, c + 1)
+        quant_chunk(3)
         gradient(6, (1, 7))
         gradient(7, (0, 2))
-        weave(0, 2, 3, on_scalar)
-        weave(1, 2, 3)
-        weave(2, 2, 3)
-        weave(0, 3, 4)
-        quant_chunk(2)
-        weave(1, 3, 4)
-        weave(2, 3, 4)
-        quant_chunk(3)
         gradient(0, (6, 4))
         gradient(1, (3, 5))
         for i, (c, n0) in enumerate((c, n0) for c in (2, 3) for n0 in range(0, N, 256)):

from contextlib import ExitStack

import concourse.mybir as mybir
from concourse.masks import make_identity

T, K, O, F, N = 1536, 1024, 512, 1024, 1024
FLOPS = 2 * T * F * (K + O) + 2 * T * F * N

F32 = mybir.dt.float32
BF16 = mybir.dt.bfloat16
U32 = mybir.dt.uint32
U8 = mybir.dt.uint8
I32 = mybir.dt.int32
FP8 = mybir.dt.float8_e4m3fn
FP8X4 = mybir.dt.float8_e4m3fn_x4
FP4X4 = mybir.dt.float4_e2m1fn_x4
MULT = mybir.AluOpType.mult
ADD = mybir.AluOpType.add
ACT = mybir.ActivationFunctionType

P = 128
BANK = 512
BANKS = 8
GROUPS = T // 512
SLOTS = 4 * GROUPS
PAIRS = SLOTS // 2
XO_PASS = 2
GPSIMD_SHARE = 1280
BF16_ONES = 0x3F803F80


def tile_recomputed_hidden_weight_gradient_s3_kernel(
    tc, x_bytes, x_scale, xo, w_words, w_scales, wo, gate, dy_words, dy_scales, out
):
    nc = tc.nc
    on_vector, on_scalar = nc.vector.tensor_copy, nc.scalar.copy

    def on_gpsimd(out, in_):
        nc.gpsimd.tensor_scalar(out=out, in0=in_, scalar1=1.0, scalar2=0.0, op0=MULT, op1=ADD)

    with ExitStack() as ctx:
        keep = ctx.enter_context(tc.tile_pool(name="keep", bufs=1))
        ring = ctx.enter_context(tc.tile_pool(name="ring", bufs=2))
        psum = ctx.enter_context(tc.psum_pool(name="psum", bufs=1))
        ctx.enter_context(tc.manual_schedule())

        def kept(name, shape, dtype):
            return keep.tile(shape, dtype, name=name, align_bytes=64)

        def passing(name, shape, dtype, bufs):
            return ring.tile(shape, dtype, name=name, align_bytes=64, bufs=bufs)

        def bank(b):
            return psum.tile([P, BANK], F32, name="bank%d" % b)

        ident = kept("ident", [P, P], F32)
        ones = kept("ones", [P, BANK], BF16)
        w_codes = [kept("w_codes%d" % hf, [P, 2, F], U8) for hf in range(2)]
        w_plane = kept("w_plane", [P, 2, F], U8)
        dy_codes = kept("dy_codes", [P, GROUPS, 2 * N], U8)
        dy_plane = kept("dy_plane", [P, GROUPS, N], U8)
        scale_by_k = kept("scale_by_k", [P, 2, 8], F32)[:, :, 0:4]
        gates = kept("gates", [P, GROUPS, 16], BF16)[:, :, 0:4]
        gate_abs = kept("gate_abs", [P, SLOTS], F32)
        gate_sign = kept("gate_sign", [P, SLOTS], F32)
        wo_codes = kept("wo_codes", [P, F], U32)
        wo_plane = kept("wo_plane", [P, F], U8)
        wo_rest = kept("wo_rest", [P, 4 * BANK], BF16)
        x_codes = [kept("x_codes%d" % j, [P, 6 * P], U32) for j in range(PAIRS)]
        x_plane = [kept("x_plane%d" % j, [P, 6 * P], U8) for j in range(PAIRS)]
        xo_raw = [kept("xo_raw%d" % j, [P, K], BF16) for j in range(PAIRS)]
        stage = [kept("stage%d" % i, [P, 3 * K], BF16) for i in range(3)]
        by_group = [kept("by_group%d" % g, [P, 4 * BANK], BF16)[:] for g in range(GROUPS)]
        by_chunk = [kept("by_chunk%d" % c, [P, GROUPS * 512], BF16)[:] for c in range(4)]
        group_codes = [kept("group_codes%d" % g, [P, BANK], U32) for g in range(GROUPS)]
        group_plane = [kept("group_plane%d" % g, [P, BANK], U8) for g in range(GROUPS)]
        chunk_codes = [kept("chunk_codes%d" % c, [P, GROUPS * P], U32) for c in range(4)]
        chunk_plane = [kept("chunk_plane%d" % c, [P, GROUPS * P], U8) for c in range(4)]
        planes = [
            [kept("planes%d_%d" % (g, hf), [P, 4 * BANK], BF16) for hf in range(2)]
            for g in range(GROUPS)
        ]

        x_v = x_bytes.rearrange("(g m t) k -> g m t k", m=P, t=4)
        xo_v = xo.rearrange("(g m t) k -> g m t k", m=P, t=4)
        wo_v = wo.rearrange("(p j) f -> p j f", j=4)
        x_raw, wo_raw = {}, {}

        head_rows = kept("head_rows", [P, 4 * K], U8)

        def load_x(s0, s1):
            if 2 <= s0 < 6:
                rows_in, c0 = head_rows, K * (s0 - 2)
            else:
                rows_in, c0 = kept("x_raw%d" % s0, [P, (s1 - s0) * K], U8), 0
            for s in range(s0, s1):
                x_raw[s] = (rows_in, c0 + K * (s - s0))
            g, t0 = divmod(s0, 4)
            nc.sync.dma_start(
                out=rows_in[:, c0 : c0 + K * (s1 - s0)].rearrange("p (t k) -> p t k", k=K),
                in_=x_v[g][:, t0 : t0 + s1 - s0, :],
            )

        def load_xo(j):
            g, h = divmod(j, 2)
            nc.sync.dma_start(
                out=xo_raw[j][:].rearrange("p (t k) -> p t k", t=2),
                in_=xo_v[g][:, 2 * h : 2 * h + 2, :],
            )

        def load_wo(c0, c1):
            rows_in = kept("wo_raw%d" % c0, [P, 4, P * (c1 - c0)], BF16)
            nc.sync.dma_start(out=rows_in[:], in_=wo_v[:, :, P * c0 : P * c1])
            for c in range(c0, c1):
                wo_raw[c] = (rows_in, P * (c - c0))

        def load_w(hf):
            nc.sync.dma_start(
                out=w_codes[hf][:],
                in_=w_words.rearrange("g p n -> p g n")[:, :, F * hf : F * hf + F],
            )

        def load_scale_bytes(dst, src):
            for r in range(4):
                nc.sync.dma_start(
                    out=dst[r:P:32, :, :].bitcast(I32),
                    in_=src.rearrange("g (q r) n -> r q g n", r=4)[r].bitcast(I32),
                )

        def load_x_scale():
            nc.sync.dma_start(
                out=scale_by_k, in_=x_scale.rearrange("o (g p t) -> p (o g) t", p=P, t=4)
            )

        def load_gates(g0, g1):
            nc.sync.dma_start(
                out=gates[:, g0:g1, :], in_=gate.rearrange("(g m t) -> m g t", m=P, t=4)[:, g0:g1, :]
            )

        wide, xo_sorted, turned = {}, {}, {}

        def raw_passes(s, kk, count):
            rows_in, c0 = x_raw[s]
            return rows_in[:, c0 + 512 * kk : c0 + 512 * (kk + count)].bitcast(FP8)

        def place(s, kk, count, values):
            words = values.bitcast(F32).rearrange("p (u w) -> p u w", u=2)
            for i in range(count):
                wide[s + (kk + i) // 2, (kk + i) % 2] = words[:, :, P * i : P * i + P]

        def widen_writing(copy, s, kk, count, values, k0=0, k1=None):
            place(s, kk, count, values)
            k1 = 512 * count if k1 is None else k1
            copy(
                out=values.rearrange("p (u m e) -> p m u e", u=2, e=2)[:, k0 // 4 : k1 // 4, :, :],
                in_=raw_passes(s, kk, count)[:, k0:k1].rearrange("p (m u e) -> p m u e", u=2, e=2),
            )

        def widen_plainly(copy, s, kk, count, values):
            words = values.bitcast(F32).rearrange("p (w u) -> p u w", u=2)
            for i in range(count):
                wide[s + (kk + i) // 2, (kk + i) % 2] = words[:, :, P * i : P * i + P]
            copy(out=values, in_=raw_passes(s, kk, count))

        def widen_reading(s, kk, count, values, k0=0):
            place(s, kk, count, values)
            on_scalar(
                out=values.rearrange("p (u m e) -> p u m e", u=2, e=2)[:, :, k0 // 4 :, :],
                in_=raw_passes(s, kk, count)[:, k0:].rearrange("p (m u e) -> p u m e", u=2, e=2),
            )

        def sort_xo(copy, j):
            xo_sorted[j] = passing("xo_sorted", [P, 512], F32, 2)
            copy(
                out=xo_sorted[j][:].rearrange("p (i u m) -> p i u m", i=2, u=2),
                in_=xo_raw[j][:].bitcast(F32).rearrange("p (i m u) -> p i u m", i=2, u=2),
            )

        def turn_x(s, b, runs=(0, 1)):
            ps = bank(b)
            for kk in runs:
                for u in range(2):
                    o0 = 256 * u + P * kk
                    src = wide[s, kk][:, u, :]
                    nc.tensor.transpose(ps[:, o0 : o0 + P], src, ident[:])
                turned[s, kk] = ps

        def turn_xo(j, b):
            ps = bank(b)
            for i in range(2):
                for u in range(2):
                    o0 = 256 * u + P * i
                    if j in xo_sorted:
                        src = xo_sorted[j][:, 256 * i + P * u : 256 * i + P * u + P]
                    else:
                        src = xo_raw[j][:].bitcast(F32)[:, 256 * i + u : 256 * i + 256 : 2]
                    nc.tensor.transpose(ps[:, o0 : o0 + P], src, ident[:])
            turned["xo", j] = ps

        def laid_x(s):
            return stage[s // 2 % 3][:, K * (s % 2) : K * (s % 2) + K]

        def laid_xo(j):
            return stage[j % 3][:, 2 * K : 3 * K]

        def empty_xo(j, copy=on_scalar):
            copy(
                out=laid_xo(j).bitcast(F32).rearrange("p (r u) -> p r u", u=2),
                in_=turned["xo", j][:].rearrange("p (u r) -> p r u", u=2),
            )

        def scale_x(s, k0=0, k1=2):
            nc.vector.tensor_tensor(
                out=laid_x(s)[:, 512 * k0 : 512 * k1].rearrange(
                    "p (g r u e) -> p g r u e", r=P, u=2, e=2
                ),
                in0=turned[s, k0][:]
                .bitcast(BF16)
                .rearrange("p (u g r e) -> p g r u e", u=2, g=2, e=2)[:, k0:k1, :, :, :],
                in1=scale_by_k[:, k0:k1, :]
                .rearrange("p g (u e) -> p g u e", e=2)
                .unsqueeze(2)
                .to_broadcast([P, k1 - k0, P, 2, 2]),
                op=MULT,
            )

        def quantise(codes, plane, values, w0, w1):
            nc.vector.quantize_mx(
                out=codes[:, w0:w1].bitcast(FP8X4), scales=plane[:, w0:w1], in_=values
            )

        def quant_x(j, run0, run1):
            values = stage[j % 3][:, 512 * run0 : 512 * run1]
            quantise(x_codes[j], x_plane[j], values, P * run0, P * run1)

        def wo_laid(hf):
            return wo_rest[:] if hf else stage[0][:, 0 : 2 * K]

        def lay_wo(copy, f0, f1):
            rows_in, c0 = wo_raw[f0 // P]
            c0 += f0 % P
            hf, f = divmod(f0, BANK)
            copy(
                out=wo_laid(hf)[:, 4 * f : 4 * (f + f1 - f0)].rearrange(
                    "p (c i e) -> p c e i", i=4, e=4
                ),
                in_=rows_in[:, :, c0 : c0 + f1 - f0].rearrange("p e (c i) -> p c e i", i=4),
            )

        def quant_wo(hf):
            quantise(wo_codes, wo_plane, wo_laid(hf), BANK * hf, BANK * hf + BANK)

        sums = {}

        def unit(s, hf, passes, b=None):
            if b is not None:
                sums[s, hf] = (bank(b), [])
            ps, done = sums[s, hf]
            cols = slice(BANK * hf, BANK * hf + BANK)
            for kk in passes:
                if kk == XO_PASS:
                    w0 = P * (4 + s % 2)
                    rhs, rhs_scale = wo_codes[:, cols].bitcast(FP8X4), wo_plane[:, cols]
                else:
                    w0 = P * (2 * (s % 2) + kk)
                    rhs = w_codes[hf][:, kk, :].bitcast(FP4X4)
                    rhs_scale = w_plane[:, kk, cols]
                done.append(kk)
                nc.tensor.matmul_mx(
                    out=ps[:],
                    lhsT=x_codes[s // 2][:, w0 : w0 + P].bitcast(FP8X4),
                    lhsT_scale=x_plane[s // 2][:, w0 : w0 + P],
                    rhs=rhs,
                    rhs_scale=rhs_scale,
                    start=(len(done) == 1),
                    stop=(len(done) == 3),
                )

        def split_gate(g0, g1):
            for dst, func in ((gate_abs, ACT.Abs), (gate_sign, ACT.Sign)):
                nc.scalar.activation(
                    out=dst[:, 4 * g0 : 4 * g1].rearrange("p (g t) -> p g t", t=4),
                    in_=gates[:, g0:g1, :],
                    func=func,
                )

        def plane(s, hf):
            g, t = divmod(s, 4)
            return planes[g][hf][:, BANK * t : BANK * t + BANK]

        def empty(s, hf):
            nc.scalar.activation(
                out=plane(s, hf), in_=sums[s, hf][0][:], func=ACT.Relu, scale=gate_abs[:, s : s + 1]
            )

        def sign(s, hf, f0=0, f1=BANK):
            row = plane(s, hf)[:, f0:f1]
            nc.vector.tensor_scalar(
                out=row, in0=row, scalar1=gate_sign[:, s : s + 1], scalar2=None, op0=MULT
            )

        def woven(g, c0, c1):
            if c0 < 4:
                return by_chunk[c0][:, 512 * g : 512 * g + 512]
            return by_group[g][:, 512 * (c0 - 4) : 512 * (c1 - 4)]

        def weave(g, c0, c1, copy=on_vector):
            hf, c = divmod(c0, 4)
            rows = planes[g][hf][:].rearrange("p (t f) -> p t f", t=4)
            copy(
                out=woven(g, c0, c1).rearrange("p (c i t) -> p c t i", i=4, t=4),
                in_=rows[:, :, P * c : P * (c + c1 - c0)].rearrange("p t (c i) -> p c t i", i=4),
            )

        def quant_h(g, c0, c1):
            quantise(group_codes[g], group_plane[g], woven(g, c0, c1), P * (c0 - 4), P * (c1 - 4))

        def quant_chunk(c):
            quantise(chunk_codes[c], chunk_plane[c], by_chunk[c], 0, GROUPS * P)

        pieces = {}

        def piece(c, n0, width, b, groups=(0, 1, 2)):
            if groups[0] == 0:
                pieces[c, n0] = (bank(b), width)
            acc = pieces[c, n0][0]
            for g in groups:
                if c < 4:
                    codes, scales, w0 = chunk_codes[c], chunk_plane[c], P * g
                else:
                    codes, scales, w0 = group_codes[g], group_plane[g], P * (c - 4)
                nc.tensor.matmul_mx(
                    out=acc[:, 0:width],
                    lhsT=codes[:, w0 : w0 + P].bitcast(FP8X4),
                    lhsT_scale=scales[:, w0 : w0 + P],
                    rhs=dy_codes[:, g, 2 * n0 : 2 * n0 + 2 * width].bitcast(FP4X4),
                    rhs_scale=dy_plane[:, g, n0 : n0 + width],
                    start=(g == 0),
                    stop=(g == GROUPS - 1),
                )

        results = [kept("result%d" % c, [P, N], F32) for c in range(F // P)]

        def copy_out(copy, c, n0):
            acc, width = pieces[c, n0]
            copy(out=results[c][:, n0 : n0 + width], in_=acc[:, 0:width])

        def store(c, n0, n1):
            nc.sync.dma_start(out=out[P * c : P * c + P, n0:n1], in_=results[c][:, n0:n1])

        def warm_up(count, b, width=BANK):
            ps = bank(b)
            for j in range(count):
                nc.tensor.matmul(ps[:, 0:width], lhsT=ones[:, 0:P], rhs=ones[:, 0:width], start=True, stop=True)

        X, XO, ALL = (0, 1), (XO_PASS,), (0, 1, XO_PASS)
        widen_on_gpsimd = nc.gpsimd.tensor_copy

        nc.vector.memset(ones[:].bitcast(I32), BF16_ONES)
        nc.vector.memset(w_plane[:].rearrange("p g n -> p (g n)").bitcast(I32), 0)
        nc.vector.memset(dy_plane[:].rearrange("p g n -> p (g n)").bitcast(I32), 0)
        make_identity(nc, ident[:])

        load_x(0, 1)
        load_x(1, 2)
        load_x_scale()
        load_x(2, 4)
        load_xo(0)
        load_w(0)
        load_scale_bytes(w_plane, w_scales)
        load_x(4, 6)
        load_wo(0, 4)
        load_w(1)
        load_xo(1)
        load_xo(2)
        load_wo(4, 8)
        load_gates(0, 1)
        load_xo(3)
        load_x(6, 8)
        load_gates(1, 3)
        load_x(8, 12)
        load_xo(4)
        load_xo(5)
        load_scale_bytes(dy_plane, dy_scales)
        nc.sync.dma_start(out=dy_codes[:], in_=dy_words.rearrange("g p n -> p g n"))

        first = [kept("first%d" % i, [P, 512], BF16) for i in range(2)]
        own = {s: kept("wide%d" % s, [P, K], BF16) for s in range(1, 6)}
        warm_up(4, 6)
        widen_writing(on_vector, 0, 0, 1, first[0][:])
        widen_plainly(on_scalar, 0, 1, 1, first[1][:])
        widen_plainly(on_vector, 1, 0, 2, own[1][:])
        widen_reading(2, 0, 2, own[2][:])
        widen_writing(widen_on_gpsimd, 3, 0, 2, own[3][:])
        for kk, b in ((0, 0), (1, 5)):
            turn_x(0, b, (kk,))
            scale_x(0, kk, kk + 1)
        warm_up(1, 6)
        turn_x(1, 1)
        warm_up(1, 6)
        scale_x(1)
        turn_xo(0, 2)
        empty_xo(0)
        warm_up(1, 6)
        quant_x(0, 0, 2)
        quant_x(0, 2, 4)
        turn_x(2, 3)
        turn_x(3, 4)
        scale_x(2)
        scale_x(3)
        widen_reading(4, 0, 2, own[4][:])
        widen_reading(5, 0, 2, own[5][:])
        lay_wo(on_scalar, 0, 192)
        lay_wo(on_gpsimd, 192, 512)
        sort_xo(on_scalar, 2)
        for s, hf, b in ((0, 0, 7), (1, 0, 0), (0, 1, 5), (1, 1, 1)):
            unit(s, hf, X, b)
            if (s, hf) == (1, 0):
                turn_x(4, 6)
        turn_xo(1, 3)
        turn_x(5, 4)
        turn_xo(2, 2)
        empty_xo(1)
        empty_xo(2)
        split_gate(0, 1)
        quant_x(0, 4, 6)
        quant_wo(0)
        quant_x(1, 0, 4)
        unit(0, 0, XO)
        unit(1, 0, XO)
        lay_wo(on_vector, 512, 768)
        quant_x(1, 4, 6)
        lay_wo(on_vector, 768, 1024)
        sort_xo(on_vector, 3)
        empty(0, 0)
        empty(1, 0)
        quant_wo(1)

        waiting = [(2, 0, X), (3, 0, X), (2, 0, XO), (3, 0, XO), (2, 1, X), (3, 1, X)]
        waiting += [(s, 1, XO) for s in range(4)]
        opens_in = {(2, 0): 3, (3, 0): 2, (2, 1): 7, (3, 1): 0}
        prep = {4: [(s, 1) for s in (3, 2, 1, 0)]}
        unit_banks = {2: (2, 5, 1, 7), 3: (0, 2, 5, 1), 4: (7, 0, 2, 5), 5: (1, 7, 0, 2)}
        for j in range(2, PAIRS):
            if j == 3:
                turn_xo(j, 3)
            if j > 2:
                turn_x(2 * j, 6)
                if j > 3:
                    turn_xo(j, 3)
                turn_x(2 * j + 1, 4)
            scale_x(2 * j)
            scale_x(2 * j + 1)
            ahead = wo_rest[:] if j == 2 else stage[(j - 1) % 3][:, 0 : 2 * K]
            if j == 2:
                widen_writing(widen_on_gpsimd, 6, 0, 2, ahead[:, 0:K])
            elif j + 1 < PAIRS:
                widen_writing(widen_on_gpsimd, 2 * j + 2, 0, 3, ahead[:, 0:1536])
            else:
                by_group[0] = ahead
                weave(0, 4, 7, on_gpsimd)
            for i, (s, hf, passes) in enumerate(waiting):
                if (s, hf) in sums:
                    unit(s, hf, passes)
                else:
                    unit(s, hf, passes, opens_in[s, hf])
                if i == 0 and j > 2:
                    empty_xo(j)
                if passes != X:
                    empty(s, hf)
                if j == 2 and i == 2:
                    widen_reading(7, 0, 2, own[1][:])
                    split_gate(1, 3)
                if i == 0 and 2 < j < PAIRS - 1:
                    widen_reading(2 * j + 3, 1, 1, ahead[:, 1536:2048])
            if 2 < j < PAIRS - 1:
                sort_xo(on_vector, j + 1)
            for s, hf in prep.get(j, []):
                sign(s, hf)
            if j == 2:
                quant_x(j, 0, 2)
                quant_x(j, 2, 6)
            elif j + 1 < PAIRS:
                quant_x(j, 0, 4)
                quant_x(j, 4, 6)
            else:
                for run0 in (0, 4, 2):
                    quant_x(j, run0, run0 + 2)
            waiting = [(2 * j, 1, ALL), (2 * j + 1, 1, ALL), (2 * j, 0, ALL), (2 * j + 1, 0, ALL)]
            for (s, hf, passes), b in zip(waiting, unit_banks[j]):
                opens_in[s, hf] = b
        for s, hf, passes in waiting:
            unit(s, hf, ALL, opens_in[s, hf])
            empty(s, hf)

        WHOLE = (6, 7, 0, 1)

        def gradient(c, banks):
            for h in range(2):
                piece(c, BANK * h, BANK, banks[h])
                copy_out(on_scalar, c, BANK * h)
                if c not in WHOLE:
                    store(c, BANK * h, BANK * h + BANK)
            if c in WHOLE:
                store(c, 0, N)

        for s in (7, 6, 5, 4):
            sign(s, 1)
        quant_h(0, 4, 6)
        weave(1, 4, 6)
        for s in (9, 8):
            sign(s, 1)
        weave(0, 7, 8)
        quant_h(1, 4, 6)
        for s in (10, 11):
            sign(s, 1)
        quant_h(0, 6, 8)
        weave(2, 4, 6)
        weave(1, 6, 8, on_scalar)
        for s in range(2):
            sign(s, 0)
        quant_h(2, 4, 6)
        weave(2, 6, 8)
        for s in range(2, 4):
            sign(s, 0)
        quant_h(1, 6, 8)
        quant_h(2, 6, 8)
        for s in (4, 5, 6, 7, 11, 10, 9, 8):
            sign(s, 0)

        opened = ((4, 0, 6), (4, BANK, 4), (5, 0, 3))
        for c, n0, b in opened:
            piece(c, n0, BANK, b, (0, 1))
        for c, n0, b in opened:
            piece(c, n0, BANK, b, (2,))
            copy_out(on_scalar, c, n0)
            if (c, n0) == (4, BANK):
                store(4, 0, N)
                weave(0, 0, 1, on_scalar)
        piece(5, BANK, BANK, 5)
        copy_out(on_scalar, 5, BANK)
        store(5, 0, N)
        weave(1, 0, 1)
        weave(2, 0, 1)
        for c in range(1, 4):
            weave(0, c, c + 1)
            quant_chunk(c - 1)
            weave(1, c, c + 1)
            weave(2, c, c + 1)
        quant_chunk(3)
        gradient(6, (1, 7))
        gradient(7, (0, 2))
        gradient(0, (6, 4))
        gradient(1, (3, 5))
        for i, (c, n0) in enumerate((c, n0) for c in (2, 3) for n0 in range(0, N, 256)):
            piece(c, n0, 256, (1, 7, 0, 2, 6, 4, 3, 5)[i])
            copy_out(on_vector if i % 2 else on_scalar, c, n0)
            if i % 2:
                store(c, n0 - 256, n0 + 256)
